import numpy as np, ml_dtypes
CORES = [1,5,17,21,33,37,49,53]
N = 8
BF = ml_dtypes.bfloat16
V, M, S, CAP, P, RO, STEP, LN = 2048, 4096, 256, 40, 12, 2, 950, 3
W1 = 13 * np.arange(16) + 5; W2 = 255 - 14 * np.arange(16); A = N * CAP
def mix(d):
    u = np.add.reduce(W1[:, None] * d, axis=2) & 4095; w = np.add.reduce(W2[:, None] * d, axis=2) & 4095
    return u, (u * w) >> 5
def kid(d, c, hm, t):
    R, n = d.shape[0], d.shape[3]
    hv = np.take_along_axis(hm, d.reshape(R, 8, 1, 16 * n), 3).reshape(R, 8, 16, 16, n)
    e = np.add.reduce(np.minimum(hv, np.abs(c)[:, :, :, None]), axis=2)
    k = np.argmax(e, axis=2); u, h = mix(d); v = (h + 37 * np.max(e, axis=2) + t) & 4095
    void = np.any(d == v[:, :, None], axis=2) | (v >= M)
    new = np.where(np.arange(16)[:, None] == k[:, :, None], v[:, :, None], d)
    q = np.add.reduce((new < v[:, :, None]).astype(np.int64), axis=2)
    return ~void, np.sort(new, axis=2), np.where((((q - k) & 1) == 1)[:, :, None], -(c >> 2), c >> 2)
def spawn(D, C, hm, t):
    start = STEP * (t + 1); a = np.roll(np.any(C != 0, axis=2), -start, axis=2)
    o = np.argsort(~a, axis=2, kind="stable")[:, :, :S]; on = np.take_along_axis(a, o, 2); pl = (o + start) & (V - 1)
    good, ch, c = kid(np.take_along_axis(D, pl[:, :, None], 3), np.take_along_axis(C, pl[:, :, None], 3), hm, t)
    return pl, on, on & good, ch, c
def recs(rng, shape):
    return np.sort(rng.integers(0, M - 15, shape), axis=-2) + np.arange(16)[:, None]
def base(rng, share=None):
    lim = rng.choice(np.array([1, 3, 20, 127]), (N, 8, 1, V), p=[0.15, 0.15, 0.2, 0.5]); C = rng.integers(-lim, lim + 1, (N, 8, 16, V))
    if share is None: share = rng.choice(np.array([0.4, 0.55, 0.75, 0.92]), (N, 8, 1, 1))
    C = C * (rng.random((N, 8, 1, V)) < share)
    return recs(rng, (N, 8, 16, V)), C, rng.integers(0, 128, (N, 8, 16, M))
def plant(rng, D, C, hm, part, twin=False, t=0, own=False):
    live = np.any(C != 0, axis=2); pl, on, good, ch, c = spawn(D, C, hm, t); u, h = mix(ch)
    busy = np.zeros((N, 8, V), bool); np.put_along_axis(busy, pl, on, 2)
    q, g, s = np.nonzero(good & (rng.random(good.shape) < part)); r = h[q, g, s] & (N - 1)
    p = ((h[q, g, s] >> LN) + rng.integers(0, P, q.size) * (2 * u[q, g, s] + 1)) & (V - 1)
    one = np.unique((r * 8 + g) * V + p, return_index=True)[1]
    if not own: one = one[~busy[r[one], g[one], p[one]]]
    q, g, s, r, p = q[one], g[one], s[one], r[one], p[one]
    rec = ch[q, g, :, s]; w = c[q, g, :, s]; lv = live[r, g, p][:, None]; bs = busy[r, g, p][:, None]; n = one.size
    if twin:
        nxt = np.concatenate([rec[:, 1:], np.full((n, 1), M)], axis=1); way = rng.random(n)
        fit = (rec[:, :14] + 1 < rec[:, 1:15] - 2) & (rec[:, 2:] + 1 < nxt[:, 2:]); i = np.argmax(fit * (0.01 + rng.random(fit.shape)), axis=1)
        z = np.nonzero(np.any(fit, axis=1) & (way < 0.4))[0]
        rec[z, i[z]] += 1; rec[z, i[z] + 1] -= 2; rec[z, i[z] + 2] += 1
        i = np.where(rng.random(n) < 0.3, 15, rng.integers(0, 16, n))
        z = np.nonzero((way > 0.6) & (rec[np.arange(n), i] + 1 < nxt[np.arange(n), i]))[0]
        rec[z, i[z]] += 1
    D[r, g, :, p] = rec
    mode = rng.integers(0, 4, (n, 1)); old = C[r, g, :, p]; some = np.any(w != 0, axis=1)[:, None]
    new = np.where(lv & (mode == 0) & some, -w, np.where(lv & (mode == 1), np.where(w < 0, -127, 127), old))
    C[r, g, :, p] = np.where(bs & (mode == 3), rng.choice(np.array([-1, 1]), (n, 16)), new)
def pack(D, C, hm):
    return {"det": np.ascontiguousarray((256 * D + C + 128).reshape(N, 128, V)).astype(np.int32), "ham": np.ascontiguousarray(hm.reshape(N, 128, M)).astype(np.float32).astype(BF)}
def setup_inputs(rng):
    D, C, hm = base(rng)
    for t in range(RO - 1, -1, -1): plant(rng, D, C, hm, 0.35, False, t, True)
    return pack(D, C, hm)
def setup_inputs_slots(rng):
    D, C, hm = base(rng, 2.0); C[:, :, 0] = np.where(np.any(C != 0, axis=2), C[:, :, 0], 1)
    for q in range(N):
        good, ch, c = kid(D[q:q + 1], C[q:q + 1], hm[q:q + 1], 0); mine = good[0] & ((mix(ch)[1][0] & (N - 1)) == ((q + 1) & (N - 1)))
        for g in range(8):
            hit = rng.permutation(np.nonzero(mine[g])[0]); rest = rng.permutation(np.nonzero(~mine[g])[0])
            n = min((CAP, CAP + 1, CAP - 1, S, 0, 1, CAP, CAP + 1)[g], len(hit))
            seq = np.concatenate([rng.permutation(np.concatenate([hit[:n], rest[:S - n]])), rng.permutation(np.concatenate([hit[n:], rest[S - n:]]))])
            k = int(rng.integers(S, V - 63)); o = rng.permutation(V); at = (np.concatenate([np.sort(o[:k]), o[k:]]) + STEP) & (V - 1)
            d2 = np.zeros_like(D[q, g]); c2 = np.zeros_like(C[q, g])
            d2[:, at] = D[q, g][:, seq]; c2[:, at[:k]] = C[q, g][:, seq[:k]]; D[q, g] = d2; C[q, g] = c2
    return pack(D, C, hm)
def setup_inputs_ties(rng):
    D, C, hm = base(rng); ev = np.ascontiguousarray(D[:, ::2]); u, h = mix(ev)
    x = np.take_along_axis(ev, rng.integers(0, 16, (N, 4, 1, V)), 2); y = np.take_along_axis(ev, rng.integers(0, 16, (N, 4, 1, V)), 2)
    goal = rng.permuted(np.concatenate([x, x + 1, x - 1, y, y + 1, ev[:, :, :1], ev[:, :, 15:], 0 * x, 0 * x + M - 1, 0 * x + 4095], axis=2), axis=2)
    e = ((goal - h[:, :, None]) * pow(37, -1, 4096)) & 4095; ok = (e >= 1) & (e <= 2032)
    e = np.take_along_axis(e, np.argmax(ok, axis=2)[:, :, None], 2); ok = np.any(ok, axis=2)[:, :, None]
    z = (np.arange(16)[:, None] + rng.integers(0, 16, (N, 4, 1, V))) & 15
    new = ((e >> 4) + (z < (e & 15))) * rng.choice(np.array([-1, 1]), (N, 4, 16, V)); live = np.any(C[:, ::2] != 0, axis=2)[:, :, None]
    C[:, ::2] = np.where(ok & live, new, C[:, ::2])
    hm[:, ::2] = 127; hm[:, 1::2] = rng.choice(np.array([0, 9, 60]), (N, 4, 1, M))
    hm[np.arange(N), 2 * rng.integers(0, 4, N) + 1] = 0
    plant(rng, D, C, hm, 0.2)
    return pack(D, C, hm)
def setup_inputs_twins(rng):
    D, C, hm = base(rng); hm = np.repeat(hm[:1], N, axis=0); ix = rng.integers(0, 40, (N, 8, 1, V))
    pd = np.repeat(recs(rng, (1, 8, 16, 40)), N, axis=0)
    pc = np.repeat(np.where(np.arange(40) < 12, rng.integers(0, 4, (1, 8, 16, 40)), rng.integers(4, 128, (1, 8, 16, 40))), N, axis=0)
    use = rng.random((N, 8, 1, V)) < 0.6; live = np.any(C != 0, axis=2)[:, :, None]
    sign = np.where(rng.random((N, 8, 1, V)) < 0.4, 1, rng.choice(np.array([-1, 1]), (N, 8, 16, V)))
    D = np.where(use, np.take_along_axis(pd, ix, 3), D)
    C = np.where(use & live, np.take_along_axis(pc, ix, 3) * sign, C)
    plant(rng, D, C, hm, 0.5); plant(rng, D, C, hm, 0.4); plant(rng, D, C, hm, 0.4, True)
    return pack(D, C, hm)
def setup_inputs_thin(rng):
    D, C, hm = base(rng, 2.0); lone = np.arange(16)[:, None] == rng.integers(0, 16, (N, 8, 1, V))
    C[:, 1::2] = np.where(lone, np.where(C == 0, -1, C), 0)[:, 1::2]
    C[:, :, 0] = np.where(np.any(C != 0, axis=2), C[:, :, 0], 1); sizes = np.array([0, 1, 5, S - 1, S, S + 1, V - 1, V])
    for q in range(N):
        for g in range(8):
            n = int(sizes[g]) if q == 0 else int(rng.choice(sizes)); o = rng.permutation(V)
            if n == 5: o = np.array([0, V - 1, STEP - 1, STEP, STEP + 1])
            keep = np.zeros(V, np.int64); keep[o[:n]] = 1; C[q, g] = C[q, g] * keep
    plant(rng, D, C, hm, 0.3)
    return pack(D, C, hm)
def setup_inputs_spread(rng):
    D, C, hm = base(rng)
    D = np.sort(((M - 15) * rng.random((N, 8, 16, V)) ** rng.choice(np.array([1.0, 4.0]), (N, 8, 1, V))).astype(np.int64), axis=2) + np.arange(16)[:, None]
    size = np.exp2(7 * rng.random((N, 8, 1, V))); live = np.any(C != 0, axis=2)[:, :, None]
    C = np.minimum((size * rng.random((N, 8, 16, V))).astype(np.int64), 127) * rng.choice(np.array([-1, 1]), (N, 8, 16, V)) * live
    hm = np.minimum((np.exp2(7 * rng.random((N, 8, 1, M))) * rng.random((N, 8, 16, M))).astype(np.int64), 127)
    plant(rng, D, C, hm, 0.3)
    return pack(D, C, hm)
def check_inputs(d):
    bad = []
    x = d["det"].astype(np.int64).reshape(N, 8, 16, V); o = x >> 8
    if np.min(o) < 0 or np.max(o) > M - 1: bad.append("orbitals of det")
    if np.min(x & 255) < 1: bad.append("counts of det")
    if not np.all(o[:, :, 1:] > o[:, :, :-1]): bad.append("rising orbitals of det")
    h = d["ham"].astype(np.float32)
    if not np.all((h >= 0) & (h <= 127) & (h == np.floor(h))): bad.append("numbers of ham")
    return bad
def reference(det, ham):
    x = det.astype(np.int64).reshape(N, 8, 16, V); D = x >> 8; C = (x & 255) - 128
    hm = ham.astype(np.float32).astype(np.int64).reshape(N, 8, 16, M); num = np.arange(P)[:, None]
    for t in range(RO):
        pl, on, good, ch, c = spawn(D, C, hm, t)
        sel = np.zeros((N, 8, V), bool); np.put_along_axis(sel, pl, on, 2)
        C = C - np.sign(C) * sel[:, :, None]
        f = good[:, :, None] & ((mix(ch)[1] & (N - 1))[:, :, None] == np.arange(N)[:, None])
        before = np.add.accumulate(f.astype(np.int64), axis=3) - f.astype(np.int64)
        q, g, r, s = np.nonzero(f & (before < CAP)); a = q * CAP + before[q, g, r, s]
        ad = np.zeros((N, 8, 16, A), np.int64); ac = np.zeros((N, 8, 16, A), np.int64); there = np.zeros((N, 8, A), bool)
        ad[r, g, :, a] = ch[q, g, :, s]; ac[r, g, :, a] = c[q, g, :, s]; there[r, g, a] = True
        u, h = mix(ad)
        p = ((h >> LN)[:, :, None] + num * (2 * u + 1)[:, :, None]) & (V - 1)
        live = np.any(C != 0, axis=2); lp = np.take_along_axis(live, p.reshape(N, 8, P * A), 2).reshape(N, 8, P, A)
        dp = np.take_along_axis(D, p.reshape(N, 8, 1, P * A), 3).reshape(N, 8, 16, P, A)
        same = np.all(dp == ad[:, :, :, None], axis=2) & lp
        score = np.where(same, num, np.where(lp, 2 * P, P + num))
        ok = there & (np.min(score, axis=2) < 2 * P); place = np.take_along_axis(p, np.argmin(score, axis=2)[:, :, None], 2)[:, :, 0]
        r, g, a = np.nonzero(ok); low = np.full((N, 8, V), A); np.minimum.at(low, (r, g, place[r, g, a]), a)
        r, g, a = np.nonzero(ok & (np.take_along_axis(low, place, 2) == np.arange(A))); b = place[r, g, a]
        D[r, g, :, b] = ad[r, g, :, a]; C[r, g, :, b] = np.clip(C[r, g, :, b] + ac[r, g, :, a], -127, 127)
    return {"y": (256 * D + C + 128).reshape(N, 128, V).astype(np.float32)}

@@ -1,0 +1,703 @@
+from concourse.bass import DstId, RemoteDMATransfer
+from concourse.mybir import AluOpType as A, AxisListType, ActivationFunctionType as F
+
+N, V, CAP, S, RO, STEP, NP = 8, 2048, 40, 256, 2, 950, 12
+AR = N * CAP
+TR = 320
+M31 = 1.5 * 2.0 ** 31
+M27 = 1.5 * 2.0 ** 27
+M23 = 1.5 * 2.0 ** 23
+OFF = 2.0 ** 22
+SENT = -22528
+THETA = 1.14e10
+
+_DT = {"f": "float32", "b": "bfloat16", "h": "float16", "i": "int32", "u": "uint16"}
+_SBUF = """
+f X:2368 Y:2368 J:256 JI:128 JG:128 PD:128 jm6:144 jm15:144 jm11:144 tm:144 tm2:144 tm3:144 tm4:144 col:32 ones:128 sw:20 swh:16
+f Jp:256 dtr:20 c9f:144 m16:256 MX:16 E:128 U:136 acc:16 cb:16 vw:16 dm8:16 fo:16 fo2:16 fo3:16 T6:256 Sx:256 C:256 Ks:256 hb:16
+f rk:16 VK:512 R1:256 R2:256 m1:256 FK:256 cc:256 PK:256 iv:16 iv2:16 own:16 I9:144 A9:144 plS:20 swS:20 t1:20 t2:20 t3:20 iv3:20
+f SL0:2304 SL1:2304 LA0:320 LA1:320 Cf:256 xf:256 xg:256 Q1:320 ac:320 st:24 s2:32 s4:64 s8:64 dd:3840 KS:60 K1:60 K2:60 K3:32
+f pv:20 lw:20 w1:320 xm:320 cn:320 ck:320 cq:320 xn:320 xo:320 R4:4,32 R5:5,32
+i XI:2048 X1:2048 pp_i:1 pq_i:1 ai:16 pl:16 hp:16 hq:16 vi:16 vv:16 Fl:256 ch:16 ow:16 ah:16 Z:192 Zm:192 km:20 pm:20
+i hi:2,16 ha:2,16 ci:4,8 ca:4,8 ai5:5,8 aa5:5,8
+h NZ:2048 BH:128 NU:128 SU:128 SD:128 ID:128 BI:128 PAR:128 PK1:128 PK2:128 WT:16 EH:144 OH:144 E1:144 O1:144 e0h:128 RX:2048 CM:320
+h c9:144 s9:144 Lb:128 G:256 Dh:256 VB:512 mA:256 mB:256 ow1:256 O:144 pvh:20 Pr:320
+h CH:16,16 eq:16,16 A16:20,16 ZH0:12,6 ZH1:12,16
+b HM:4096 SG:2064 SR:2048 BB:128 AL:128 ZS:144 I592:8 e0b:128 kc:128 kcm:240 ID32:128 ID8:128 m16b:320 cmp:1040 jnk:3040 Lg:4096
+b Mn:4096 fsq:256 fsg:256 sq:3840 k1:240 k2:240 EQ:3040 DG:320 DS:320 esq:320 esg:320
+u cu:16 plu:16 fou:16 Du:256 slu:16 zu:256 pu:20 eou:20
+"""
+_ALL, SCRATCH, _AT = {}, {}, {}
+for _line in _SBUF.split("\n"):
+    _w = _line.split()
+    for _e in _w[1:]:
+        _n, _s = _e.split(":")
+        _ALL[_n] = ("sbuf", [128] + [int(_k) for _k in _s.split(",")], _DT[_w[0]])
+for _n in ("P0", "P1", "P2", "P3", "P4", "P5"):
+    _ALL[_n] = ("psum", [128, 512], "float32")
+for _n in ("Q0", "Q1p"):
+    _ALL[_n] = ("psum", [128, 16, 32], "float32")
+_wide = {}
+for _n, (_w, _sh, _d) in _ALL.items():
+    if _w == "sbuf" and len(_sh) == 2 and _sh[1] <= 144:
+        _AT[_n] = ("pack_" + _d, _wide.get(_d, 0))
+        _wide[_d] = _AT[_n][1] + -(-_sh[1] // 16) * 16
+    else:
+        SCRATCH[_n] = (_w, _sh, _d)
+for _d, _c in _wide.items():
+    SCRATCH["pack_" + _d] = ("sbuf", [128, _c], _d)
+SEMAPHORES = ["sv", "ss", "sp", "sg", "loc", "ar0", "ar1", "an0", "an1"] + ["d%d" % k for k in range(7)]
+_PSUM = ("P0", "P1", "P2", "P3", "P4", "P5", "Q0", "Q1p")
+
+
+def routes(src, T, topo):
+    r = T.rank_of(src)
+    ring = [T.cores[(r + k) % N] for k in range(1, N)]
+    near = [d for d in ring if topo.chip(d) == topo.chip(src)]
+    far = [d for d in ring if topo.chip(d) != topo.chip(src)]
+    eng = topo.engines(src, far[0])
+    n = len(eng)
+    out = [(0, d, eng[k * n // 4:(k + 1) * n // 4]) for k, d in enumerate(far[:4])]
+    out += [(1, d, eng[k * n // 2:(k + 1) * n // 2]) for k, d in enumerate(far[4:])]
+    return out + [(0, d, [e for e in topo.engines(src, d) if e not in eng][:4]) for d in near]
+
+
+def landing(dst, T, topo):
+    near = [c for c in T.cores if topo.chip(c) == topo.chip(dst)]
+    return [T.rank_of(c) for c in near + [c for c in T.cores if c not in near]]
+
+
+def rank_program(g, core, T, topo):
+    me = T.rank_of(core)
+    if me is None:
+        return
+    queue = {"v": g.vector, "s": g.scalar, "p": g.tensor, "g": g, "y": g.sync}
+    semof = {"v": "sv", "s": "ss", "p": "sp", "g": "sg"}
+    cnt, known, snap, acc = {}, {e: {} for e in queue}, {}, {}
+    BIGC = 1000000
+
+    def b(n, lo=0, hi=None, step=1):
+        if hi is None:
+            hi = _ALL[n][1][1]
+        if n in _AT:
+            w, at = _AT[n]
+            return T[w][:, at + lo:at + hi:step], [(w, at + lo, at + hi)]
+        return T[n][:, lo:hi:step], [(n, lo, hi)]
+
+    full = slice(None)
+
+    def b3(n, s1=full, s2=full):
+        return T[n][:, s1, s2], [(n, 0, BIGC)]
+
+    def ind(w, o):
+        return w[0].indirect(o[0]), w[1] + o[1]
+
+    def need(e, reads, writes):
+        want = {}
+        for kind, keys in ((0, reads), (1, writes)):
+            for (n, lo, hi) in keys:
+                ps = n in _PSUM
+                for lo2, hi2, k2, sem, val, e2 in acc.get(n, []):
+                    if not ps and not (lo < hi2 and lo2 < hi):
+                        continue
+                    if e == "p" and e2 == "p" or not (kind or k2 or ps and e != e2):
+                        continue
+                    want[sem] = max(want.get(sem, 0), val)
+        kn = known[e]
+        for s, v in sorted(want.items(), key=lambda x: (x[0] == semof.get(e), x[0])):
+            if kn.get(s, 0) >= v:
+                continue
+            queue[e].wait_ge(T.sem[s], v)
+            kn[s] = v
+            for s2, v2 in snap.get((s, v), {}).items():
+                kn[s2] = max(kn.get(s2, 0), v2)
+
+    def note(e, reads, writes, sem, val):
+        for kind, keys in ((0, reads), (1, writes)):
+            for (n, lo, hi) in keys:
+                if n in _PSUM:
+                    lo, hi = 0, BIGC
+                lst = acc.setdefault(n, [])
+                lst[:] = [r for r in lst if not (kind and lo <= r[0] and r[1] <= hi)
+                          and not (r[5] == e and r[2] == kind and r[3] == sem and r[0] == lo and r[1] == hi)]
+                lst.append((lo, hi, kind, sem, val, e))
+
+    def op(e, call, outs, ins):
+        reads = [k for x in ins for k in x[1]]
+        writes = [k for x in outs for k in x[1]]
+        need(e, reads, writes)
+        s = semof[e]
+        cnt[s] = v = cnt.get(s, 0) + 1
+        call().then_inc(T.sem[s], 1)
+        snap[(s, v)] = dict(known[e])
+        note(e, reads, writes, s, v)
+
+    def dma(e, out, in_, sem):
+        need(e, in_[1], out[1])
+        queue[e].dma_start(out=out[0], in_=in_[0]).then_inc(T.sem[sem], 16)
+        snap[(sem, 16)] = dict(known[e])
+        note(e, in_[1], out[1], sem, 16)
+
+    def sc(x):
+        return x[0] if isinstance(x, tuple) else x
+
+    def ts(out, in0, s1, s2, op0, op1=None):
+        ins = [in0] + [x for x in (s1, s2) if isinstance(x, tuple)]
+        if op1 is None:
+            op("v", lambda: g.vector.tensor_scalar(out[0], in0[0], sc(s1), None, op0), [out], ins)
+        else:
+            op("v", lambda: g.vector.tensor_scalar(out[0], in0[0], sc(s1), sc(s2), op0, op1), [out], ins)
+
+    def tt(out, in0, in1, o):
+        op("v", lambda: g.vector.tensor_tensor(out[0], in0[0], in1[0], o), [out], [in0, in1])
+
+    def cp(out, in_):
+        op("v", lambda: g.vector.tensor_copy(out[0], in_[0]), [out], [in_])
+
+    def scan(out, d0, d1, o0, o1):
+        op("v", lambda: g.vector.tensor_tensor_scan(out[0], d0[0], d1[0], 0.0, o0, o1), [out], [d0, d1])
+
+    def red(out, in_, o):
+        op("v", lambda: g.vector.tensor_reduce(out[0], in_[0], AxisListType.X, o), [out], [in_])
+
+    def vtr(out, in_):
+        op("v", lambda: g.vector.transpose(out[0], in_[0]), [out], [in_])
+
+    def act(out, in_, f, bias=0.0, scale=1.0, accum=None):
+        ins = [in_] + [x for x in (bias, scale) if isinstance(x, tuple)]
+        if accum is None:
+            op("s", lambda: g.scalar.activation(out[0], in_[0], f, bias=sc(bias), scale=sc(scale)), [out], ins)
+        else:
+            op("s", lambda: g.scalar.activation(out[0], in_[0], f, bias=sc(bias), scale=sc(scale), accum_out=accum[0]), [out, accum], ins)
+
+    def mm(out, l, r, start=True, stop=True):
+        op("p", lambda: g.tensor.matmul(out[0], l[0], r[0], start, stop), [out], [l, r])
+
+    def iota(n, pat, base, cm, lo=0, hi=None):
+        out = b(n, lo, hi)
+        if _ALL[n][2] == "int32":
+            op("g", lambda: g.iota(out[0], pat, base, cm), [out], [])
+        else:
+            op("g", lambda: g.iota(out[0], pat, base, cm, allow_small_or_imprecise_dtypes=True), [out], [])
+
+    def gsel(out, in_):
+        op("g", lambda: g.affine_select(out[0], in_[0], [[0, 8], [1, 16]], A.is_gt, 0.0, 0, 0), [out], [in_])
+
+    for k in range(4):
+        dma("y", b("XI", 512 * k, 512 * k + 512), (T.det[:, 512 * k:512 * k + 512], []), "d%d" % k)
+    dma("s", b("HM"), (T.ham[:], []), "d4")
+
+    iota("pp_i", [[0, 1]], 0, 1)
+    iota("JG", [[1, 8], [0, 16]], 0, 0)
+    iota("jm15", [[1, 144]], -15, 0)
+    iota("JI", [[0, 8], [1, 16]], 0, 0)
+    iota("PD", [[1, 128]], 0, -1)
+    iota("J", [[1, 256]], 0, 0)
+    iota("jm11", [[1, 144]], -11, 0)
+    iota("ones", [[0, 128]], 1, 0)
+    for k in range(6):
+        iota("cmp", [[0, 1]], 128, 0, 144 * k + 128, 144 * k + 129)
+    iota("U", [[0, 8]], -1, 0, 128, 136)
+    iota("Jp", [[16, 4], [64, 4], [1, 16]], 0, 0)
+    iota("jm6", [[1, 144]], -6, 0)
+    iota("c9f", [[256, 9], [0, 16]], -1025, 0)
+    for h in (0, 128):
+        gsel(b("m16", h, h + 128), b("ones"))
+    iota("VK", [[0, 512]], 0, 0)
+    for o in range(N):
+        iota("SL0", [[0, CAP]], SENT, 0, 256 * o, 256 * o + CAP)
+    iota("kcm", [[2048, 12], [0, 5]], -16384, 0, 0, 60)
+    iota("kcm", [[2048, 12], [0, 15]], -16384, 0, 60, 240)
+    iota("lw", [[0, 20]], 0, 0)
+    iota("st", [[0, 24]], 0, 0)
+    iota("Z", [[0, 192]], 0, 0)
+    for o in range(N):
+        iota("SL1", [[0, CAP]], SENT, 0, 256 * o, 256 * o + CAP)
+
+    PI, PG16, PGE, PGO, IM, ACOL, BCOL, W1, W2, SIG, WAL, P0C, PGE1, PGO1, SIGK, SIGM, E0C, N15, OD, N0 = \
+        [b("col", k, k + 1) for k in range(20)]
+    q_i = b("pq_i")
+    ts(q_i, b("pp_i"), 15, None, A.bitwise_and)
+    ts(PI, q_i, 1.0, None, A.mult)
+    ts(q_i, b("pp_i"), 4, None, A.arith_shift_right)
+    ts(PG16, q_i, 16.0, None, A.mult)
+    ts(OD, q_i, 1.0, None, A.mult)
+    ts(b("BH"), b("JG"), OD, None, A.is_equal)
+    fill = [(ts, (b("ZS"), b("jm15"), PG16, None, A.is_equal)),
+            (ts, (E0C, PI, 0.0, OFF, A.is_equal, A.mult)),
+            (ts, (WAL, PI, 1.0, -128.0, A.is_equal, A.mult)),
+            (ts, (b("tm", 0, 128), b("PD"), 0.0, -1.0, A.is_lt, A.mult)),
+            (ts, (b("sw"), b("J", 0, 20), 16.0, PI, A.mult, A.add)),
+            (ts, (q_i, q_i, 1, None, A.bitwise_and)),
+            (tt, (WAL, WAL, E0C, A.add)),
+            (tt, (b("NU"), b("tm", 0, 128), b("BH"), A.mult)),
+            (cp, (OD, q_i)),
+            (ts, (b("AL"), b("BH"), WAL, None, A.mult)),
+            (ts, (PGE, OD, 100000.0, PG16, A.mult, A.add)),
+            (ts, (PGO, OD, -100000.0, 100000.0 - 16.0, A.mult, A.add)),
+            (ts, (b("swh"), b("sw", 0, 16), 0.5, None, A.add)),
+            (tt, (PGO, PGO, PG16, A.add)),
+            (ts, (b("E1"), b("jm11"), PGE, None, A.is_equal)),
+            (ts, (b("O1"), b("jm11"), PGO, None, A.is_equal))]
+
+    def filler(n):
+        for f, a in fill[:n]:
+            f(*a)
+        del fill[:n]
+
+    def spawn_constants():
+        ts(q_i, b("pp_i"), 1, None, A.bitwise_and)
+        ts(W1, PI, 13.0, 5.0, A.mult, A.add)
+        ts(W2, PI, -14.0, 255.0, A.mult, A.add)
+        ts(P0C, b("pp_i"), 0.0, None, A.is_equal)
+        ts(SIG, q_i, -2.0, 1.0, A.mult, A.add)
+        ts(IM, PI, -7.5, None, A.add)
+        ts(N0, PI, 0.0, None, A.is_gt)
+        ts(N15, PI, 15.0, None, A.is_lt)
+        ts(SIGK, SIG, 1.0 / 256.0, None, A.mult)
+        ts(SIGM, SIG, -1.0 / 256.0, None, A.mult)
+        ts(PGE1, PGE, 1.0, None, A.add)
+        ts(PGO1, PGO, 1.0, None, A.add)
+        ts(b("WT", 0, 8), b("BH", 0, 128, 16), W1, None, A.mult)
+        ts(b("WT", 8, 16), b("BH", 0, 128, 16), W2, None, A.mult)
+        ts(b("e0b"), b("J", 0, 128), 0.0, P0C, A.mult, A.add)
+        ts(b("kc"), b("JI"), -1.0, 7.5, A.mult, A.add)
+        ts(b("I592"), b("BH", 0, 128, 16), 592.0, None, A.mult)
+        ts(ACOL, N15, -1.0, None, A.mult)
+        ts(BCOL, N0, -1.0, None, A.add)
+        ts(b("dtr"), b("sw"), -1.0, float(TR), A.mult, A.add)
+        ts(b("ID"), b("PD"), 0.0, None, A.is_equal)
+        ts(b("SU"), b("PD"), -1.0, N0, A.is_equal, A.mult)
+        ts(b("SD"), b("PD"), 1.0, N15, A.is_equal, A.mult)
+        ts(b("BI"), b("PD"), 0.0, 8192.0, A.is_equal, A.mult)
+
+    def child_constants():
+        ts(b("tm2"), b("jm6"), PGE, W1, A.is_equal, A.mult)
+        ts(b("tm"), b("jm6"), PGE1, W2, A.is_equal, A.mult)
+        ts(b("tm3"), b("jm6"), PGO, W1, A.is_equal, A.mult)
+        ts(b("tm4"), b("jm6"), PGO1, W2, A.is_equal, A.mult)
+        ts(b("PAR"), b("BH"), SIG, None, A.mult)
+        tt(b("EH"), b("tm"), b("tm2"), A.add)
+        tt(b("OH"), b("tm3"), b("tm4"), A.add)
+        ts(b("PK1"), b("BH"), SIGK, None, A.mult)
+        ts(b("PK2"), b("BH"), SIGM, None, A.mult)
+        cp(b("BB"), b("BH"))
+        cp(b("e0h"), b("e0b"))
+        cp(b("c9"), b("c9f"))
+
+    def arrival_constants():
+        ts(b("ID32"), b("ID"), -65536.0, None, A.mult)
+        ts(b("ID8"), b("ID"), -16384.0, None, A.mult)
+        ts(b("MX"), b("J", 0, 16), PI, None, A.is_equal)
+        for lo, hi in ((0, 128), (128, 256), (256, 320)):
+            ts(b("CM", lo, hi), b("JI", 0, hi - lo), PI, 0.5, A.is_ge, A.mult)
+            cp(b("m16b", lo, hi), b("m16", 0, hi - lo))
+        ts(b("swS"), b("sw"), 1.0 / 65536.0, None, A.mult)
+        for x in range(16):
+            ts(b("RX", 128 * x, 128 * x + 128), b("BH"), b("MX", x, x + 1), None, A.mult)
+
+    def q4(k):
+        return 512 * k, 512 * k + 512
+    filler(5)
+    for k in range(4):
+        if k == 0:
+            ts(b("X1", *q4(0)), b("XI", *q4(0)), 255, None, A.bitwise_and)
+        if k < 3:
+            ts(b("X1", *q4(k + 1)), b("XI", *q4(k + 1)), 255, None, A.bitwise_and)
+        filler(1)
+        ts(b("NZ", *q4(k)), b("X1", *q4(k)), 128.0, None, A.not_equal)
+        filler(2)
+        mm(b("P%d" % k), b("BH"), b("NZ", *q4(k)))
+        act(b("SG", *q4(k)), b("P%d" % k), F.Sign, bias=-0.5)
+        if k == 0:
+            act(b("SG", V, V + 16), b("P0", 0, 16), F.Sign, bias=-0.5)
+
+    XW = b("X", TR, TR + V)
+    plan = {d: routes(d, T, topo) for d in T.cores}
+    land = {d: landing(d, T, topo) for d in T.cores}
+    near = sum(topo.chip(d) == topo.chip(core) for d in T.cores)
+    own0 = min(land[core][:near])
+    PART = ((0, near * CAP // 16), (near * CAP // 16, AR // 16))
+    sent = [0]
+    EQW, CHW = b3("eq"), b3("CH")
+
+    for t in range(RO):
+        start = STEP * (t + 1)
+        if t:
+            for k, (lo, hi) in enumerate(((0, V - start), (512, 1024), (V - start, 512), (1536, V), (1024, 1536))):
+                x = b("X", TR + (lo + start) % V, TR + (hi - 1 + start) % V + 1)
+                if k % 2:
+                    act(b("SR", lo, hi), x, F.Sign)
+                else:
+                    ts(b("SR", lo, hi), x, 0.0, None, A.is_gt)
+            for h in (0, 64):
+                for x in range(16):
+                    mm(b("P4", h, h + 64), b("ZS", 15 - x, 143 - x), b("SR", 16 * h + x, 16 * h + 1024, 16), x == 0, x == 15)
+        else:
+            c1 = (V - start + 15) // 16
+            e1 = start + 16 * c1 - V
+            for x in range(16):
+                mm(b("P4", 0, c1), b("ZS", 15 - x, 143 - x), b("SG", start + x, start + x + 16 * (c1 - 1) + 1, 16), x == 0, x == 15)
+            for x in range(16):
+                mm(b("P4", c1, 128), b("ZS", 15 - x, 143 - x), b("SG", e1 + x, e1 + x + 16 * (127 - c1) + 1, 16), x == 0, x == 15)
+            spawn_constants()
+            child_constants()
+        ts(b("Lb"), b("P4", 0, 128), 0.0, None, A.is_gt)
+        mm(b("P5", 0, 128), b("BH"), b("Lb"))
+        mm(b("P4", 128, 256), b("NU"), b("Lb"))
+        if t == 0:
+            for k in range(4):
+                mm(b("P%d" % k), b("AL"), b("SG", *q4(k)))
+        scan(b("E"), b("ones"), b("P5", 0, 128), A.mult, A.add)
+        NA = 10
+        for k in range(NA):
+            act(b("jnk", 128 * k, 128 * k + 128), b("E"), F.Sign, bias=b("swh", k, k + 1), scale=-1.0, accum=b("acc", k, k + 1))
+        tt(b("U", 0, 128), b("E"), b("P4", 128, 256), A.add)
+        for k in range(NA, 17):
+            o = 144 * (k - NA)
+            if k < 16:
+                ts(b("cmp", o, o + 128), b("E"), b("sw", k, k + 1), -2.0, A.is_gt, A.mult)
+            if k > NA:
+                red(b("acc", k - 1, k), b("cmp", o - 144, o - 15), A.add)
+        ts(b("vw"), b("sw", 0, 16), b("E", 127, 128), None, A.is_lt)
+        for j in range(4):
+            ts(b("cu", 4 * j, 4 * j + 4), b("acc", j, 16, 4), 0.5, 64.0, A.mult, A.add)
+        tt(b("G"), ind(b("U"), b("cu")), b("Jp"), A.is_le)
+        ts(b("cb"), b("acc"), 8.0, 1024.0 + start, A.mult, A.add)
+        ts(b("dm8"), b("vw"), -8.0, 8.0, A.mult, A.add)
+        for par, n in ((0, "E1"), (16, "O1")):
+            for j in range(4):
+                mm(b3("Q0", slice(0, 4), slice(par, par + 16)), b(n, 11 - j, 139 - j), b("G", 64 * j, 64 * j + 64), j == 0, j == 3)
+        if t == 0:
+            for k in range(4):
+                tt(b("X", TR + 512 * k, TR + 512 * k + 512), b("XI", *q4(k)), b("P%d" % k), A.add)
+        vtr(b3("R4"), b3("Q0", slice(0, 4), full))
+        tt(b("ai"), b("cb"), b3("R4", full, slice(0, 4)), A.add)
+        ts(b("pl"), b("ai"), V - 1, None, A.bitwise_and)
+        cp(b("plu"), b("pl"))
+        act(b("Sx"), ind(XW, b("plu")), F.Identity, bias=-OFF)
+        ts(b("T6"), ind(XW, b("plu")), M31, -(M31 + OFF), A.add, A.add)
+        ts(b("Du"), b("T6"), 1.0 / 256.0, 4095.0, A.mult, A.min)
+        tt(b("C"), b("Sx"), b("T6"), A.subtract)
+        for lo, hi in ((64, 96), (0, 0), (96, 128), (128, 192), (192, 256)):
+            if lo == hi:
+                act(b("P0", 0, 256), b("C"), F.Abs)
+            else:
+                act(b("Lg", 16 * lo, 16 * hi), ind(b("HM"), b("Du", lo, hi)), F.Copy)
+        act(b("P4", 0, 256), b("C"), F.Sign)
+        act(b("P5", 0, 256), b("T6"), F.Identity, bias=128.0)
+        ts(b("Dh"), b("T6"), 1.0 / 256.0, -2048.0, A.mult, A.add)
+        cp(b("Lg", 0, 1024), ind(b("HM"), b("Du", 0, 64)))
+        for h in range(2):
+            mm(b("P3", 16 * h, 16 * h + 16), b("Dh", 128 * h, 128 * h + 128), b("WT"))
+        for h in range(2):
+            mm(b("P%d" % (1 + h), 0, 128), b("e0b"), b("kc"), True, False)
+
+        def hash_step(k):
+            if k == 0:
+                cp(b3("hi"), b("P3", 0, 32))
+            elif k == 1:
+                ts(b3("ha"), b3("hi"), 4095, None, A.bitwise_and)
+            elif k == 2:
+                tt(b("hp"), b3("ha", full, slice(0, 8)), b3("ha", full, slice(8, 16)), A.mult)
+            elif k == 3:
+                ts(b("hq"), b("hp"), 5, None, A.arith_shift_right)
+            elif k == 4:
+                ts(b("hb"), b("hq"), 16.0, M27 + 16.0 * t, A.mult, A.add)
+            else:
+                ts(b("Fl"), b("C"), 0.25, -0.375, A.mult, A.add)
+
+        for qd in range(4):
+            lo, h = 64 * qd, qd // 2
+            for k in range(16):
+                tt(b("Mn", 256 * k + lo, 256 * k + lo + 64), b("Lg", 16 * lo + k, 16 * lo + 1024, 16), b("P0", lo, lo + 64), A.min)
+                if qd == 1 and k % 2 == 0 and k < 12:
+                    hash_step(k // 2)
+                if qd % 2:
+                    mm(b("P%d" % (1 + h), k, 128, 16), b("Mn", 256 * k + 128 * h, 256 * k + 128 * h + 128), b("I592"), False, k == 15)
+            if qd == 2:
+                scan(b("Ks", 0, 128), b("m16", 0, 128), b("P1", 0, 128), A.mult, A.max)
+        tt(b("Cf"), b("C"), b("P4", 0, 256), A.subtract)
+        act(b("fsq"), b("Cf"), F.Square)
+        tt(b("xf"), b("Cf"), b("P5", 0, 256), A.add)
+        mm(b("P0", 0, 256), b("BB"), b("fsq"))
+        act(b("fsg"), b("P0", 0, 256), F.Sign, bias=-0.5)
+        scan(b("Ks", 128, 256), b("m16", 0, 128), b("P2", 0, 128), A.mult, A.max)
+        kmx = b("Ks", 15, 256, 16)
+        tt(b("vi"), kmx, b("hb"), A.add)
+        ts(b("rk"), kmx, M27, -M27, A.add, A.add)
+        ts(b("vv"), b("vi"), 4, 4095, A.arith_shift_right, A.bitwise_and)
+        tt(b("VK", 256, 512, 16), b("rk"), kmx, A.subtract)
+        ts(b("VK", 0, 256, 16), b("vv"), -2048.0, None, A.add)
+        scan(b("VB", 256, 512), b("m16"), b("VK", 256, 512), A.mult, A.add)
+        scan(b("VB", 0, 256), b("m16"), b("VK", 0, 256), A.mult, A.add)
+        tt(b("fo"), b("pl"), b("dtr", 0, 16), A.add)
+        mm(b("P5", 0, 256), b("SU"), b("Dh"), True, False)
+        mm(b("P1", 0, 256), b("SD"), b("Dh"), True, False)
+        for x in (2, 3, 0, 1):
+            mm(b("P4" if x > 1 else "P3", 128 * (x % 2), 128 * (x % 2) + 128), b("VB", 128 * x, 128 * x + 128), b("ID"))
+        kr, vr = b("P4", 0, 256), b("P3", 0, 256)
+        ts(b("mA"), kr, IM, ACOL, A.is_le, A.add)
+        ts(b("mB"), kr, IM, BCOL, A.is_lt, A.add)
+        mm(b("P5", 0, 256), b("BI"), b("mA"), False, True)
+        mm(b("P1", 0, 256), b("BI"), b("mB"), False, True)
+        mm(b("P2", 0, 256), b("PK1"), b("mA"), True, False)
+        mm(b("P2", 0, 256), b("PK2"), b("mB"), False, True)
+        mm(b("P0", 256, 512), b("AL"), b("fsg"))
+        tt(b("fo2"), b("fo"), b("vw"), A.mult)
+        tt(b("R1"), b("Dh"), b("P5", 0, 256), A.max)
+        tt(b("R2"), b("Dh"), b("P1", 0, 256), A.min)
+        tt(b("m1"), b("R1"), vr, A.min)
+        tt(EQW, b("Dh"), vr, A.is_equal)
+        tt(b("fo3"), b("fo2"), b("sw", 0, 16), A.add)
+        tt(CHW, b("R2"), b("m1"), A.max)
+        for par, ns, nh in ((0, "E1", "EH"), (16, "O1", "OH")):
+            for j in range(4):
+                mm(b3("Q0", slice(0, 4), slice(par, par + 16)), b(ns, 3 - j, 131 - j), b3("eq", slice(j, None, 4), full), j == 0, False)
+            for j in range(4):
+                mm(b3("Q0", slice(0, 4), slice(par, par + 16)), b(nh, 6 - 2 * j, 134 - 2 * j), b3("CH", slice(j, None, 4), full), False, j == 3)
+        cp(b("fou"), b("fo3"))
+        tt(b("ow1"), CHW, vr, A.is_equal)
+        mm(b("P4", 0, 256), b("PAR"), b("ow1"))
+        tt(b("FK"), b("Fl"), b("P2", 0, 256), A.mult)
+        vtr(b3("R4"), b3("Q0", slice(0, 4), full))
+        cp(b3("ci"), b3("R4", full, slice(0, 8)))
+        ts(b("iv"), b3("R4", full, slice(8, 12)), 0.0, 8.0, A.is_gt, A.mult)
+        ts(b3("ca"), b3("ci"), 4095, None, A.bitwise_and)
+        tt(b("iv2"), b("iv"), b("dm8"), A.max)
+        tt(b("ch"), b3("ca", full, slice(0, 8, 2)), b3("ca", full, slice(1, 8, 2)), A.mult)
+        tt(b("xg"), b("xf"), b("P0", 256, 512), A.add)
+        ts(b("ow"), b("ch"), 5, 7, A.arith_shift_right, A.bitwise_and)
+        tt(b("cc"), b("FK"), b("P4", 0, 256), A.mult)
+        tt(b("own"), b("ow"), b("iv2"), A.add)
+        for o in range(9):
+            ts(b("O", 16 * o, 16 * o + 16), b("own"), float(o), None, A.is_equal if o < 8 else A.is_ge)
+        mm(b("P3", 0, 144), b("BH"), b("O"))
+        mm(b("P5", 0, 144), b("NU"), b("O"), True, False)
+        mm(b("P5", 0, 144), b("e0h"), b("c9"), False, True)
+        tt(b("PK"), b("cc"), CHW, A.add)
+        scan(b("I9"), b("m16", 0, 144), b("P3", 0, 144), A.mult, A.add)
+        tt(b("A9"), b("I9"), b("P5", 0, 144), A.add)
+        tt(b("s9"), b("A9"), b("O"), A.mult)
+        for o in range(9):
+            mm(b("P2", 0, 16), b("ID"), b("s9", 16 * o, 16 * o + 16), o == 0, o == 8)
+        cp(ind(b("X"), b("fou")), b("xg"))
+        ts(b("slu"), b("P2", 0, 16), 1024.0, None, A.add)
+        SL, LA = "SL%d" % t, "LA%d" % t
+        cp(ind(b(SL), b("slu")), b("PK"))
+        for call in (0, 1):
+            tr = []
+            for cl, d, eng in plan[core]:
+                if cl != call:
+                    continue
+                o, at = T.rank_of(d), CAP * land[d].index(me)
+                need("g", b(SL, 256 * o, 256 * o + CAP)[1], [])
+                tr.append(RemoteDMATransfer(
+                    dst_ids=[DstId(rid=topo.addr(d)[0], pnc=topo.addr(d)[1])], dma_engine_mask=sum(1 << e for e in eng),
+                    remote_sem=T.sem[("an%d" if topo.chip(d) == topo.chip(core) else "ar%d") % t],
+                    src=T[SL][:, 256 * o:256 * o + CAP], dst=T[LA][:, at:at + CAP]))
+                sent[0] += len(eng)
+            g.remote_dma_fused(tr, local_sem=T.sem.loc)
+        for d in T.cores:
+            if d != core:
+                nr = topo.chip(d) == topo.chip(core)
+                tot = sum(len(e) for s in T.cores if s != core and (topo.chip(s) == topo.chip(core)) == nr
+                          for _, x, e in plan[s] if x == core)
+                at = CAP * land[core].index(T.rank_of(d))
+                acc.setdefault(LA, []).append((at, at + CAP, 1, ("an%d" if nr else "ar%d") % t, tot, "r"))
+        at = CAP * land[core].index(me)
+        cp(b(LA, at, at + CAP), b(SL, 256 * me, 256 * me + CAP))
+        if t == 0:
+            arrival_constants()
+        else:
+            for k in range(4):
+                act(b("SG", *q4(k)), b("X", TR + 512 * k, TR + 512 * k + 512), F.Sign)
+                mm(b("P%d" % (1 + k)), b("AL"), b("SG", *q4(k)))
+            for k in range(4):
+                q = (TR + 512 * k, TR + 512 * k + 512)
+                tt(b("Y", *q), b("X", *q), b("P%d" % (1 + k)), A.subtract)
+
+        def score(bank, lo):
+            q = (lo, lo + 60)
+            ts(b("k1", *q), b(bank, 0, 60), 0.0, None, A.is_equal)
+            act(b("k2", *q), b(bank, 0, 60), F.Sign, bias=-THETA)
+            mm(b("P4", *q), b("e0b"), b("kcm", *q), True, False)
+            k = lo // 60 - 1
+            mm(b("P4", *q), b("ID"), b3("ZH1", slice(4 * k, 4 * k + 4), slice(0, 15)) if lo else b3("ZH0", full, slice(0, 5)), False, False)
+            mm(b("P4", *q), b("ID32"), b("k1", *q), False, False)
+            mm(b("P4", *q), b("ID8"), b("k2", *q), False, True)
+
+        def sums(k):
+            for x in range(16):
+                mm(b("P%d" % k, 0, 60), b("ZS", 15 - x, 143 - x), b("sq", 960 * k + x, 960 * k + 960, 16), x == 0, x == 15)
+
+        def part0_tail(k):
+            if k == 0:
+                score("P0", 0)
+                act(b("K3", 0, 30), b("P4", 0, 30), F.Copy)
+            elif k == 2:
+                tt(b("K2", 0, 30), b("K3", 0, 30), b("P4", 30, 60), A.min)
+            elif k == 3:
+                tt(b("K1", 0, 15), b("K2", 0, 15), b("K2", 15, 30), A.min)
+            elif k == 4:
+                tt(b("K2", 30, 35), b("K1", 0, 5), b("K1", 5, 10), A.min)
+            elif k == 5:
+                tt(b("km", 0, 5), b("K2", 30, 35), b("K1", 10, 15), A.min)
+
+        def arrivals(part):
+            c0, c2 = PART[part]
+            w = c2 - c0
+            wp, n, ways = w + 1, 16 * w, w // 5
+            a0, z0 = 16 * c0, 960 * part
+            A16 = b3("A16", slice(c0, c2), full)
+            s0 = 6 * part
+            st = b("st", s0, s0 + wp)
+            u1, u2 = b3("aa5", full, slice(0, 2 * ways, 2)), b3("aa5", full, slice(1, 2 * ways, 2))
+            ai5, aa5, R5 = [b3(x, full, slice(0, 2 * ways)) for x in ("ai5", "aa5", "R5")]
+
+            def orbitals():
+                ts(A16, b(LA, a0, a0 + n), M23, -M23, A.add, A.add)
+                for par, nh in ((0, "EH"), (16, "OH")):
+                    for j in range(ways):
+                        mm(b3("Q1p", slice(0, 5), slice(par, par + 16)), b(nh, 6 - 2 * j, 134 - 2 * j),
+                           b3("A16", slice(c0 + j, c2, ways), full), j == 0, j == ways - 1)
+
+            def numbers():
+                ts(b("st", s0, s0 + w), u1, 2.0, 1.0, A.mult, A.add)
+                tt(b("ah", 0, w), u1, u2, A.mult)
+                act(b("s2", 0, wp), st, F.Copy, scale=2.0)
+                act(b("s2", wp, 2 * wp), st, F.Copy, scale=2.0)
+                act(b("s4", 0, 2 * wp), b("s2", 0, 2 * wp), F.Copy, scale=2.0)
+                act(b("s4", 2 * wp, 4 * wp), b("s2", 0, 2 * wp), F.Copy, scale=2.0)
+                act(b("s8", 0, 4 * wp), b("s4", 0, 4 * wp), F.Copy, scale=2.0)
+
+            def first():
+                ts(b("Z", 0, w), b("ah", 0, w), 8, V - 1, A.arith_shift_right, A.bitwise_and)
+                cp(b("zu", 0, wp), b("Z", 0, wp))
+                tt(b("Z", wp, 2 * wp), b("Z", 0, wp), st, A.add)
+                if part:
+                    sums(0)
+
+            def zm(lo, hi):
+                ts(b("Zm", lo * wp, hi * wp), b("Z", lo * wp, hi * wp), V - 1, None, A.bitwise_and)
+
+            def zc(lo, hi):
+                cp(b("zu", lo * wp, hi * wp), b("Zm", lo * wp, hi * wp))
+
+            def probe(m):
+                if m == 1:
+                    zm(0, 2)
+                    tt(b("Z", 2 * wp, 4 * wp), b("Z", 0, 2 * wp), b("s2", 0, 2 * wp), A.add)
+                    zc(1, 2)
+                    zm(2, 4)
+                if m == 2:
+                    tt(b("Z", 4 * wp, 8 * wp), b("Z", 0, 4 * wp), b("s4", 0, 4 * wp), A.add)
+                    zc(2, 4)
+                    tt(b("Z", 8 * wp, 12 * wp), b("Z", 0, 4 * wp), b("s8", 0, 4 * wp), A.add)
+                if m == 3:
+                    zm(4, 12)
+                if m == 4:
+                    zc(4, 12)
+                    cp(b3("ZH%d" % part), b("Zm", 0, 12 * wp))
+                if part and m > 2:
+                    part0_tail(m - 3)
+                d = (z0 + n * m, z0 + n * m + n)
+                tt(b("dd", *d), ind(XW, b("zu", wp * m, wp * m + w)), b("Q1", a0, a0 + n), A.subtract)
+                if part or m % 4 == 3:
+                    d = d if part else (z0 + n * (m - 3), z0 + n * m + n)
+                    act(b("sq", *d), b("dd", *d), F.Square, bias=-M31 / 256.0, scale=1.0 / 256.0)
+                if part and m % 4 == 3:
+                    k = m // 4 + 1
+                    if k > 1:
+                        score("P%d" % (k - 1), 60 * (k - 1))
+                    sums(k)
+                    if k == 2:
+                        act(b("KS"), b("P4", 60, 120), F.Copy)
+
+            pre = [orbitals, lambda: ts(b("Q1", a0, a0 + n), A16, 256.0, 524288.0 + OFF - M31, A.mult, A.add),
+                   lambda: vtr(b3("R5"), b3("Q1p", slice(0, 5), full)), lambda: cp(ai5, R5),
+                   lambda: ts(aa5, ai5, 4095, None, A.bitwise_and), numbers, first]
+            return pre, probe
+
+        pre0, probe0 = arrivals(0)
+        pre1, probe1 = arrivals(1)
+        for f in pre0:
+            f()
+        for m in range(NP):
+            probe0(m)
+            if m > 5:
+                pre1.pop(0)()
+        for f in pre1:
+            f()
+        for m in range(NP):
+            probe1(m)
+        tt(b("ac"), b(LA), b3("A16"), A.subtract)
+        act(b("cq"), b("ac"), F.Identity, bias=128.0, scale=256.0)
+        tt(b("K1"), b("KS"), b("P4", 120, 180), A.min)
+        score("P3", 180)
+        tt(b("K2"), b("K1"), b("P4", 180, 240), A.min)
+        tt(b("K3", 0, 30), b("K2", 0, 30), b("K2", 30, 60), A.min)
+        tt(b("km", 5, 20), b("K3", 0, 15), b("K3", 15, 30), A.min)
+        ts(b("pm"), b("km"), V - 1, None, A.bitwise_and)
+        ts(b("iv3"), b("km"), 0.0, -4096.0, A.is_ge, A.mult)
+        cp(b("pu"), b("pm"))
+        tt(b("pvh"), b("pm"), b("iv3"), A.add)
+        tt(b("pv"), b("pm"), b("iv3"), A.add)
+        for x in range(16):
+            mm(b("P5", x, AR, 16), b("RX", 128 * x, 128 * x + 128), b("pvh"))
+        mm(b("P0", 0, AR), b("ID"), b("CM"), True, False)
+        for x in range(16):
+            mm(b("P0", x, AR, 16), b("ID"), b("pvh"), False, x == 15)
+        act(b("xm"), ind(XW, b("pu")), F.Identity, bias=M31)
+        act(b("P1", 0, AR), b("xm"), F.Identity, bias=-M31)
+        tt(b("w1"), ind(XW, b("pu")), b("cq"), A.add)
+        act(b("P2", 0, AR), b("Q1"), F.Identity, bias=M31 - OFF)
+        ts(b("plS"), b("pv"), float(TR), 1.0 / 65536.0, A.add, A.mult)
+        tt(b("cn"), b("w1"), b("P1", 0, AR), A.subtract)
+        cp(b("Pr"), b("P5", 0, AR))
+        ts(b("ck"), b("cn"), 255.0, 1.0, A.min, A.max)
+        if t < RO - 1:
+            act(b("esq"), b("ck"), F.Square, bias=-128.0)
+            mm(b("P3", 0, AR), b("BB"), b("esq"))
+            act(b("esg"), b("P3", 0, AR), F.Sign, bias=-0.5)
+            mm(b("P4", 0, AR), b("AL"), b("esg"))
+        o5 = own0 // near * PART[0][1]
+        n5 = PART[0][1]
+        rng = []
+        for k in range(20):
+            r = [(0, k), (n5, n5 + o5)] if k < n5 else [(n5 if k < n5 + o5 else 0, k)]
+            rng.append((sum(y - x for x, y in r), k, [(x, y) for x, y in r if x < y]))
+        at, small = 0, []
+        for size, k, rs in sorted(rng, reverse=True):
+            if not size:
+                continue
+            e0 = at
+            for x, y in rs:
+                ts(b("EQ", at, at + 16 * (y - x)), b("Pr", 16 * x, 16 * y), b("pv", k, k + 1), None, A.is_equal)
+                at += 16 * (y - x)
+            if size > (10 if t < RO - 1 else 9):
+                act(b("jnk", e0, at), b("EQ", e0, at), F.Copy, accum=b("lw", k, k + 1))
+            else:
+                small.append((k, e0, at))
+        tt(b("DG"), b("Pr"), b("P0", 0, AR), A.is_equal)
+        for k, e0, e2 in small:
+            red(b("lw", k, k + 1), b("EQ", e0, e2), A.add)
+        scan(b("DS"), b("m16b"), b("DG"), A.mult, A.max)
+        tt(b("xn"), b("ck"), b("P2", 0, AR), A.add)
+        if t < RO - 1:
+            tt(b("xo"), b("xn"), b("P4", 0, AR), A.add)
+        tt(b("t1"), b("plS"), b("DS", 15, AR, 16), A.subtract)
+        tt(b("t2"), b("t1"), b("lw"), A.subtract)
+        tt(b("t3"), b("t2"), b("swS"), A.max)
+        ts(b("eou"), b("t3"), 65536.0, None, A.mult)
+        if t < RO - 1:
+            cp(ind(b("X"), b("eou")), b("xo"))
+        else:
+            cp(ind(b("Y"), b("eou")), b("xn"))
+    for k, e in ((0, "y"), (1, "s")):
+        dma(e, (T.y[:, 1024 * k:1024 * k + 1024], []), b("Y", TR + 1024 * k, TR + 1024 * k + 1024), "d%d" % (5 + k))
+    for s in ("sv", "ss", "sp", "sg"):
+        g.wait_ge(T.sem[s], cnt[s])
+    for k in range(7):
+        g.wait_ge(T.sem["d%d" % k], 16)
+    g.wait_ge(T.sem.loc, sent[0])

@@ -1,3 +1,4 @@
+import numpy as np
 from concourse.bass import DstId, RemoteDMATransfer
 from concourse.mybir import AluOpType as A, AxisListType, ActivationFunctionType as F
 
@@ -10,22 +11,23 @@ M23 = 1.5 * 2.0 ** 23
 OFF = 2.0 ** 22
 SENT = -22528
 THETA = 1.14e10
+NS = 5
 
 _DT = {"f": "float32", "b": "bfloat16", "h": "float16", "i": "int32", "u": "uint16"}
 _SBUF = """
-f X:2368 Y:2368 J:256 JI:128 JG:128 PD:128 jm6:144 jm15:144 jm11:144 tm:144 tm2:144 tm3:144 tm4:144 col:32 ones:128 sw:20 swh:16
-f Jp:256 dtr:20 c9f:144 m16:256 MX:16 E:128 U:136 acc:16 cb:16 vw:16 dm8:16 fo:16 fo2:16 fo3:16 T6:256 Sx:256 C:256 Ks:256 hb:16
-f rk:16 VK:512 R1:256 R2:256 m1:256 FK:256 cc:256 PK:256 iv:16 iv2:16 own:16 I9:144 A9:144 plS:20 swS:20 t1:20 t2:20 t3:20 iv3:20
-f SL0:2304 SL1:2304 LA0:320 LA1:320 Cf:256 xf:256 xg:256 Q1:320 ac:320 st:24 s2:32 s4:64 s8:64 dd:3840 KS:60 K1:60 K2:60 K3:32
-f pv:20 lw:20 w1:320 xm:320 cn:320 ck:320 cq:320 xn:320 xo:320 R4:4,32 R5:5,32
-i XI:2048 X1:2048 pp_i:1 pq_i:1 ai:16 pl:16 hp:16 hq:16 vi:16 vv:16 Fl:256 ch:16 ow:16 ah:16 Z:192 Zm:192 km:20 pm:20
+f X:2368 Y:2368 J:256 col:32 sw:20 swa:20 swb:20 U:136 dm:16 fo:16 fo2:16 Sx:256 Ks:256 hb:16 rk:16 RT:128 cc:256 CHf:256 xg:256
+f iv:16 iv2:16 own:16 R4:4,32 R5:5,32 SL0:2304 SL1:2304 LA0:320 LA1:320 Q0:320 Q1:480 QW:320 Q2:320 dd:3840 KM:320 iv3:20 w1:320
+f MX:16 ck:320 DS:320 t3:20 IF:128 Pr:20,16
+i XI:2048 X1:2048 pp_i:1 pq_i:1 pr_i:1 hp:16 hq:16 vi:16 vv:16 ch:16 ow:16 ah:16 Z:16 ki:20 pm:20 Zi:192 Zm:192
 i hi:2,16 ha:2,16 ci:4,8 ca:4,8 ai5:5,8 aa5:5,8
-h NZ:2048 BH:128 NU:128 SU:128 SD:128 ID:128 BI:128 PAR:128 PK1:128 PK2:128 WT:16 EH:144 OH:144 E1:144 O1:144 e0h:128 RX:2048 CM:320
-h c9:144 s9:144 Lb:128 G:256 Dh:256 VB:512 mA:256 mB:256 ow1:256 O:144 pvh:20 Pr:320
-h CH:16,16 eq:16,16 A16:20,16 ZH0:12,6 ZH1:12,16
-b HM:4096 SG:2064 SR:2048 BB:128 AL:128 ZS:144 I592:8 e0b:128 kc:128 kcm:240 ID32:128 ID8:128 m16b:320 cmp:1040 jnk:3040 Lg:4096
-b Mn:4096 fsq:256 fsg:256 sq:3840 k1:240 k2:240 EQ:3040 DG:320 DS:320 esq:320 esg:320
-u cu:16 plu:16 fou:16 Du:256 slu:16 zu:256 pu:20 eou:20
+h cnt:128 EB:128 cb:16 Dh:16,16 VK:256 VV:256 TK:256 VB:256 R1:256 m1:256 CH:16,16 s9:153 A16:20,16 uh:16 ZH0:64 ZH1:192 pvh:20
+b HM:4096 NZ:2064 SG:2048 SR:16,130 Lb:130 cmp:2048 G:256 Ca:256 Cr:256 Cb:256 sC:256 Fb:256 Fl:256 Lg:2048 Mn:16,128 MV:2048 th:256 sD:16,16
+b sE:256 ab:256 fsq:256 fsg:256 O:153 m17:153 sq:20,12,16 k1:20,16 k2:20,16 k3:16 k4:16 ra:320 rs:320 esq:320 esg:320 EQ:320 EQ3:16,64
+b Jb:256 JI:320 JG:128 PD:128 zero:128 ones:256 BH:128 ZS:144 TX0:130 TX1:130 MK:4 WL:8 base:64 kx:128 kc:128 e0:128 TI:128 NU:128
+b SU:128 SD:128 PAR:128 PA2:128 AL:128 B592:128 I592:8 WT:16 EH:144 OH:144 E1:144 O1:144 TE:130 TO:130 CR1:128 CR2:128 c9:16
+b m16:320 dk:256 mB:320 CM:320 RX:2048 IM:1408 cz0:64 cz1:192 kc2:20,16 I1:128 Im1:128 I256n:128 I256:128 I4kn:128
+b I64k:128 I16kn:128 I64n:128
+u cu:16 plu:16 fou:16 Du:256 DT:128 slu:16 zu0:64 zu1:192 pu:20 eou:4,6
 """
 _ALL, SCRATCH, _AT = {}, {}, {}
 for _line in _SBUF.split("\n"):
@@ -33,10 +35,9 @@ for _line in _SBUF.split("\n"):
     for _e in _w[1:]:
         _n, _s = _e.split(":")
         _ALL[_n] = ("sbuf", [128] + [int(_k) for _k in _s.split(",")], _DT[_w[0]])
-for _n in ("P0", "P1", "P2", "P3", "P4", "P5"):
-    _ALL[_n] = ("psum", [128, 512], "float32")
-for _n in ("Q0", "Q1p"):
-    _ALL[_n] = ("psum", [128, 16, 32], "float32")
+for _k in range(4):
+    _ALL["B%d" % _k] = ("psum", [128, 512], "float32")
+    _ALL["C%d" % _k] = ("psum", [128, 32, 16], "float32")
 _wide = {}
 for _n, (_w, _sh, _d) in _ALL.items():
     if _w == "sbuf" and len(_sh) == 2 and _sh[1] <= 144:
@@ -47,7 +48,9 @@ for _n, (_w, _sh, _d) in _ALL.items():
 for _d, _c in _wide.items():
     SCRATCH["pack_" + _d] = ("sbuf", [128, _c], _d)
 SEMAPHORES = ["sv", "ss", "sp", "sg", "loc", "ar0", "ar1", "an0", "an1"] + ["d%d" % k for k in range(7)]
-_PSUM = ("P0", "P1", "P2", "P3", "P4", "P5", "Q0", "Q1p")
+
+CYC, PE, WAKE, GATHER, SCATTER = 0.83, 0.42, 80.0, 1.56, 3.0
+LOAD, SEND, NEAR, FAR, FIRST = 1500.0, 700.0, 2200.0, 4200.0, 2500.0
 
 
 def routes(src, T, topo):
@@ -67,637 +70,555 @@ def landing(dst, T, topo):
     return [T.rank_of(c) for c in near + [c for c in T.cores if c not in near]]
 
 
+def order_calls(calls):
+    n = len(calls)
+    tail, users = [0.0] * n, [[] for _ in range(n)]
+    for i, c in enumerate(calls):
+        for d in c[3]:
+            users[d].append(i)
+    gap = lambda d, i: 0.0 if calls[d][0] == calls[i][0] == "p" else WAKE
+    for i in range(n - 1, -1, -1):
+        tail[i] = calls[i][2] + max([tail[u] + gap(i, u) for u in users[i]], default=0.0)
+    start, busy = [0.0] * n, {}
+    for i in sorted(range(n), key=lambda i: (-tail[i], i)):
+        t = max([start[d] + calls[d][2] + gap(d, i) for d in calls[i][3]], default=0.0)
+        line, k = busy.setdefault(calls[i][0], []), 0
+        while k < len(line) and line[k][0] < t + calls[i][1]:
+            t, k = max(t, line[k][1]), k + 1
+        line.insert(k, (t, t + calls[i][1]))
+        start[i] = t
+    return sorted(range(n), key=lambda i: (start[i], i))
+
+
+_ORDER = []
+
+
 def rank_program(g, core, T, topo):
     me = T.rank_of(core)
     if me is None:
         return
     queue = {"v": g.vector, "s": g.scalar, "p": g.tensor, "g": g, "y": g.sync}
     semof = {"v": "sv", "s": "ss", "p": "sp", "g": "sg"}
-    cnt, known, snap, acc = {}, {e: {} for e in queue}, {}, {}
-    BIGC = 1000000
-
-    def b(n, lo=0, hi=None, step=1):
-        if hi is None:
-            hi = _ALL[n][1][1]
-        if n in _AT:
-            w, at = _AT[n]
-            return T[w][:, at + lo:at + hi:step], [(w, at + lo, at + hi)]
-        return T[n][:, lo:hi:step], [(n, lo, hi)]
-
+    calls, emit, acc = [], [], {}
     full = slice(None)
 
-    def b3(n, s1=full, s2=full):
-        return T[n][:, s1, s2], [(n, 0, BIGC)]
+    def b3(n, *ix):
+        w, sh, dt = SCRATCH[n]
+        ix = ix + (full,) * (len(sh) - 1 - len(ix))
+        on = np.zeros(sh[1:], bool)
+        on[ix] = True
+        bits = -1 if w == "psum" else int.from_bytes(np.packbits(on).tobytes(), "little")
+        return T[n][(full,) + ix], [(n, bits)], int(on.sum()), dt in ("bfloat16", "float16", "uint16"), w == "psum", False
+
+    def b(n, lo=0, hi=None, step=1):
+        sh = _ALL[n][1]
+        if hi is None:
+            hi = int(np.prod(sh[1:]))
+        if n in _AT:
+            w, at = _AT[n]
+            return b3(w, slice(at + lo, at + hi, step))
+        if len(sh) == 2:
+            return b3(n, slice(lo, hi, step))
+        k = sh[2]
+        if step == 1:
+            return b3(n, slice(lo // k, hi // k))
+        return b3(n, slice(lo // k, -(-hi // k)), lo % k)
 
     def ind(w, o):
-        return w[0].indirect(o[0]), w[1] + o[1]
+        return w[0].indirect(o[0]), w[1] + o[1], 16 * o[2], False, False, True
 
-    def need(e, reads, writes):
-        want = {}
-        for kind, keys in ((0, reads), (1, writes)):
-            for (n, lo, hi) in keys:
-                ps = n in _PSUM
-                for lo2, hi2, k2, sem, val, e2 in acc.get(n, []):
-                    if not ps and not (lo < hi2 and lo2 < hi):
-                        continue
-                    if e == "p" and e2 == "p" or not (kind or k2 or ps and e != e2):
-                        continue
-                    want[sem] = max(want.get(sem, 0), val)
-        kn = known[e]
-        for s, v in sorted(want.items(), key=lambda x: (x[0] == semof.get(e), x[0])):
-            if kn.get(s, 0) >= v:
-                continue
-            queue[e].wait_ge(T.sem[s], v)
-            kn[s] = v
-            for s2, v2 in snap.get((s, v), {}).items():
-                kn[s2] = max(kn.get(s2, 0), v2)
-
-    def note(e, reads, writes, sem, val):
-        for kind, keys in ((0, reads), (1, writes)):
-            for (n, lo, hi) in keys:
-                if n in _PSUM:
-                    lo, hi = 0, BIGC
+    def op(e, call, outs, ins, cost, late=None, sem=None):
+        i, need = len(calls), set()
+        outs = [(x[1][:1] if x[5] else x[1]) for x in outs], [x[1][1:] for x in outs if x[5]]
+        for kind, keys in ((0, sum([x[1] for x in ins] + outs[1], [])), (1, sum(outs[0], []))):
+            for n, bits in keys:
                 lst = acc.setdefault(n, [])
-                lst[:] = [r for r in lst if not (kind and lo <= r[0] and r[1] <= hi)
-                          and not (r[5] == e and r[2] == kind and r[3] == sem and r[0] == lo and r[1] == hi)]
-                lst.append((lo, hi, kind, sem, val, e))
+                need.update(j for b2, k2, j, e2 in lst if bits & b2 and (kind or k2 or bits == -1 and e != e2) and j != i)
+                if kind:
+                    lst[:] = [r for r in lst if r[0] & ~bits]
+                lst.append((bits, kind, i, e))
+        calls.append((e, cost, cost if late is None else late, sorted(need)))
+        emit.append((call, sem))
+        return i
 
-    def op(e, call, outs, ins):
-        reads = [k for x in ins for k in x[1]]
-        writes = [k for x in outs for k in x[1]]
-        need(e, reads, writes)
-        s = semof[e]
-        cnt[s] = v = cnt.get(s, 0) + 1
-        call().then_inc(T.sem[s], 1)
-        snap[(s, v)] = dict(known[e])
-        note(e, reads, writes, s, v)
+    def vec(out, ins, per, fix=50.0):
+        if out[5]:
+            return fix + out[2] * SCATTER * CYC
+        return fix + out[2] * GATHER * CYC if ins[0][5] else max(64, ins[0][2] * per) * CYC
 
-    def dma(e, out, in_, sem):
-        need(e, in_[1], out[1])
-        queue[e].dma_start(out=out[0], in_=in_[0]).then_inc(T.sem[sem], 16)
-        snap[(sem, 16)] = dict(known[e])
-        note(e, in_[1], out[1], sem, 16)
+    def half(*x):
+        return 0.5 if all(k[3] for k in x) else 1.0
 
     def sc(x):
         return x[0] if isinstance(x, tuple) else x
 
     def ts(out, in0, s1, s2, op0, op1=None):
         ins = [in0] + [x for x in (s1, s2) if isinstance(x, tuple)]
-        if op1 is None:
-            op("v", lambda: g.vector.tensor_scalar(out[0], in0[0], sc(s1), None, op0), [out], ins)
-        else:
-            op("v", lambda: g.vector.tensor_scalar(out[0], in0[0], sc(s1), sc(s2), op0, op1), [out], ins)
+        more = () if op1 is None else (op1,)
+        op("v", lambda: g.vector.tensor_scalar(out[0], in0[0], sc(s1), sc(s2), op0, *more), [out], ins, vec(out, ins, half(out, in0)))
 
     def tt(out, in0, in1, o):
-        op("v", lambda: g.vector.tensor_tensor(out[0], in0[0], in1[0], o), [out], [in0, in1])
+        op("v", lambda: g.vector.tensor_tensor(out[0], in0[0], in1[0], o), [out], [in0, in1], vec(out, [in0], 1 if in0[4] or in1[4] else 2))
 
     def cp(out, in_):
-        op("v", lambda: g.vector.tensor_copy(out[0], in_[0]), [out], [in_])
+        op("v", lambda: g.vector.tensor_copy(out[0], in_[0]), [out], [in_], vec(out, [in_], half(out, in_)))
 
     def scan(out, d0, d1, o0, o1):
-        op("v", lambda: g.vector.tensor_tensor_scan(out[0], d0[0], d1[0], 0.0, o0, o1), [out], [d0, d1])
-
-    def red(out, in_, o):
-        op("v", lambda: g.vector.tensor_reduce(out[0], in_[0], AxisListType.X, o), [out], [in_])
+        op("v", lambda: g.vector.tensor_tensor_scan(out[0], d0[0], d1[0], 0.0, o0, o1), [out], [d0, d1], vec(out, [d0], half(out, d0, d1)))
 
     def vtr(out, in_):
-        op("v", lambda: g.vector.transpose(out[0], in_[0]), [out], [in_])
+        op("v", lambda: g.vector.transpose(out[0], in_[0]), [out], [in_], vec(out, [in_], 1))
 
-    def act(out, in_, f, bias=0.0, scale=1.0, accum=None):
+    def act(out, in_, f=F.Identity, bias=0.0, scale=1.0):
         ins = [in_] + [x for x in (bias, scale) if isinstance(x, tuple)]
-        if accum is None:
-            op("s", lambda: g.scalar.activation(out[0], in_[0], f, bias=sc(bias), scale=sc(scale)), [out], ins)
-        else:
-            op("s", lambda: g.scalar.activation(out[0], in_[0], f, bias=sc(bias), scale=sc(scale), accum_out=accum[0]), [out, accum], ins)
+        op("s", lambda: g.scalar.activation(out[0], in_[0], f, bias=sc(bias), scale=sc(scale)), [out], ins, vec(out, ins, 1, 65.0))
 
-    def mm(out, l, r, start=True, stop=True):
-        op("p", lambda: g.tensor.matmul(out[0], l[0], r[0], start, stop), [out], [l, r])
+    def mm(out, terms):
+        for k, (l, r, *part) in enumerate(terms):
+            o = part[0] if part else out
+            op("p", lambda o=o, l=l, r=r, k=k: g.tensor.matmul(o[0], l[0], r[0], k == 0, k == len(terms) - 1), [o], [l, r],
+               max(min(64, l[2]), r[2]) * PE * (1 if l[3] else 4))
 
-    def iota(n, pat, base, cm, lo=0, hi=None):
-        out = b(n, lo, hi)
-        if _ALL[n][2] == "int32":
-            op("g", lambda: g.iota(out[0], pat, base, cm), [out], [])
-        else:
-            op("g", lambda: g.iota(out[0], pat, base, cm, allow_small_or_imprecise_dtypes=True), [out], [])
+    def iota(out, pat, base, cm=0):
+        small = {} if out[1][0][0] == "pack_int32" else {"allow_small_or_imprecise_dtypes": True}
+        op("g", lambda: g.iota(out[0], pat, base, cm, **small), [out], [], 130 + 2 * CYC * out[2])
 
-    def gsel(out, in_):
-        op("g", lambda: g.affine_select(out[0], in_[0], [[0, 8], [1, 16]], A.is_gt, 0.0, 0, 0), [out], [in_])
+    def sel(out, in_, pat, cmp_, fill, base, cm):
+        op("g", lambda: g.affine_select(out[0], in_[0], pat, cmp_, fill, base, cm), [out], [in_], 170 + 2 * CYC * out[2])
 
-    for k in range(4):
-        dma("y", b("XI", 512 * k, 512 * k + 512), (T.det[:, 512 * k:512 * k + 512], []), "d%d" % k)
-    dma("s", b("HM"), (T.ham[:], []), "d4")
+    def dma(e, out, in_, sem, late):
+        op(e, lambda: queue[e].dma_start(out=out[0], in_=in_[0]), [out], [in_], 50.0, late, (sem, 16))
 
-    iota("pp_i", [[0, 1]], 0, 1)
-    iota("JG", [[1, 8], [0, 16]], 0, 0)
-    iota("jm15", [[1, 144]], -15, 0)
-    iota("JI", [[0, 8], [1, 16]], 0, 0)
-    iota("PD", [[1, 128]], 0, -1)
-    iota("J", [[1, 256]], 0, 0)
-    iota("jm11", [[1, 144]], -11, 0)
-    iota("ones", [[0, 128]], 1, 0)
-    for k in range(6):
-        iota("cmp", [[0, 1]], 128, 0, 144 * k + 128, 144 * k + 129)
-    iota("U", [[0, 8]], -1, 0, 128, 136)
-    iota("Jp", [[16, 4], [64, 4], [1, 16]], 0, 0)
-    iota("jm6", [[1, 144]], -6, 0)
-    iota("c9f", [[256, 9], [0, 16]], -1025, 0)
-    for h in (0, 128):
-        gsel(b("m16", h, h + 128), b("ones"))
-    iota("VK", [[0, 512]], 0, 0)
-    for o in range(N):
-        iota("SL0", [[0, CAP]], SENT, 0, 256 * o, 256 * o + CAP)
-    iota("kcm", [[2048, 12], [0, 5]], -16384, 0, 0, 60)
-    iota("kcm", [[2048, 12], [0, 15]], -16384, 0, 60, 240)
-    iota("lw", [[0, 20]], 0, 0)
-    iota("st", [[0, 24]], 0, 0)
-    iota("Z", [[0, 192]], 0, 0)
-    for o in range(N):
-        iota("SL1", [[0, CAP]], SENT, 0, 256 * o, 256 * o + CAP)
-
-    PI, PG16, PGE, PGO, IM, ACOL, BCOL, W1, W2, SIG, WAL, P0C, PGE1, PGO1, SIGK, SIGM, E0C, N15, OD, N0 = \
-        [b("col", k, k + 1) for k in range(20)]
-    q_i = b("pq_i")
-    ts(q_i, b("pp_i"), 15, None, A.bitwise_and)
-    ts(PI, q_i, 1.0, None, A.mult)
-    ts(q_i, b("pp_i"), 4, None, A.arith_shift_right)
-    ts(PG16, q_i, 16.0, None, A.mult)
-    ts(OD, q_i, 1.0, None, A.mult)
-    ts(b("BH"), b("JG"), OD, None, A.is_equal)
-    fill = [(ts, (b("ZS"), b("jm15"), PG16, None, A.is_equal)),
-            (ts, (E0C, PI, 0.0, OFF, A.is_equal, A.mult)),
-            (ts, (WAL, PI, 1.0, -128.0, A.is_equal, A.mult)),
-            (ts, (b("tm", 0, 128), b("PD"), 0.0, -1.0, A.is_lt, A.mult)),
-            (ts, (b("sw"), b("J", 0, 20), 16.0, PI, A.mult, A.add)),
-            (ts, (q_i, q_i, 1, None, A.bitwise_and)),
-            (tt, (WAL, WAL, E0C, A.add)),
-            (tt, (b("NU"), b("tm", 0, 128), b("BH"), A.mult)),
-            (cp, (OD, q_i)),
-            (ts, (b("AL"), b("BH"), WAL, None, A.mult)),
-            (ts, (PGE, OD, 100000.0, PG16, A.mult, A.add)),
-            (ts, (PGO, OD, -100000.0, 100000.0 - 16.0, A.mult, A.add)),
-            (ts, (b("swh"), b("sw", 0, 16), 0.5, None, A.add)),
-            (tt, (PGO, PGO, PG16, A.add)),
-            (ts, (b("E1"), b("jm11"), PGE, None, A.is_equal)),
-            (ts, (b("O1"), b("jm11"), PGO, None, A.is_equal))]
-
-    def filler(n):
-        for f, a in fill[:n]:
-            f(*a)
-        del fill[:n]
-
-    def spawn_constants():
-        ts(q_i, b("pp_i"), 1, None, A.bitwise_and)
-        ts(W1, PI, 13.0, 5.0, A.mult, A.add)
-        ts(W2, PI, -14.0, 255.0, A.mult, A.add)
-        ts(P0C, b("pp_i"), 0.0, None, A.is_equal)
-        ts(SIG, q_i, -2.0, 1.0, A.mult, A.add)
-        ts(IM, PI, -7.5, None, A.add)
-        ts(N0, PI, 0.0, None, A.is_gt)
-        ts(N15, PI, 15.0, None, A.is_lt)
-        ts(SIGK, SIG, 1.0 / 256.0, None, A.mult)
-        ts(SIGM, SIG, -1.0 / 256.0, None, A.mult)
-        ts(PGE1, PGE, 1.0, None, A.add)
-        ts(PGO1, PGO, 1.0, None, A.add)
-        ts(b("WT", 0, 8), b("BH", 0, 128, 16), W1, None, A.mult)
-        ts(b("WT", 8, 16), b("BH", 0, 128, 16), W2, None, A.mult)
-        ts(b("e0b"), b("J", 0, 128), 0.0, P0C, A.mult, A.add)
-        ts(b("kc"), b("JI"), -1.0, 7.5, A.mult, A.add)
-        ts(b("I592"), b("BH", 0, 128, 16), 592.0, None, A.mult)
-        ts(ACOL, N15, -1.0, None, A.mult)
-        ts(BCOL, N0, -1.0, None, A.add)
-        ts(b("dtr"), b("sw"), -1.0, float(TR), A.mult, A.add)
-        ts(b("ID"), b("PD"), 0.0, None, A.is_equal)
-        ts(b("SU"), b("PD"), -1.0, N0, A.is_equal, A.mult)
-        ts(b("SD"), b("PD"), 1.0, N15, A.is_equal, A.mult)
-        ts(b("BI"), b("PD"), 0.0, 8192.0, A.is_equal, A.mult)
-
-    def child_constants():
-        ts(b("tm2"), b("jm6"), PGE, W1, A.is_equal, A.mult)
-        ts(b("tm"), b("jm6"), PGE1, W2, A.is_equal, A.mult)
-        ts(b("tm3"), b("jm6"), PGO, W1, A.is_equal, A.mult)
-        ts(b("tm4"), b("jm6"), PGO1, W2, A.is_equal, A.mult)
-        ts(b("PAR"), b("BH"), SIG, None, A.mult)
-        tt(b("EH"), b("tm"), b("tm2"), A.add)
-        tt(b("OH"), b("tm3"), b("tm4"), A.add)
-        ts(b("PK1"), b("BH"), SIGK, None, A.mult)
-        ts(b("PK2"), b("BH"), SIGM, None, A.mult)
-        cp(b("BB"), b("BH"))
-        cp(b("e0h"), b("e0b"))
-        cp(b("c9"), b("c9f"))
-
-    def arrival_constants():
-        ts(b("ID32"), b("ID"), -65536.0, None, A.mult)
-        ts(b("ID8"), b("ID"), -16384.0, None, A.mult)
-        ts(b("MX"), b("J", 0, 16), PI, None, A.is_equal)
-        for lo, hi in ((0, 128), (128, 256), (256, 320)):
-            ts(b("CM", lo, hi), b("JI", 0, hi - lo), PI, 0.5, A.is_ge, A.mult)
-            cp(b("m16b", lo, hi), b("m16", 0, hi - lo))
-        ts(b("swS"), b("sw"), 1.0 / 65536.0, None, A.mult)
-        for x in range(16):
-            ts(b("RX", 128 * x, 128 * x + 128), b("BH"), b("MX", x, x + 1), None, A.mult)
+    def hbm(ap):
+        return ap, [], 0, False, False, False
 
     def q4(k):
         return 512 * k, 512 * k + 512
-    filler(5)
+
     for k in range(4):
-        if k == 0:
-            ts(b("X1", *q4(0)), b("XI", *q4(0)), 255, None, A.bitwise_and)
-        if k < 3:
-            ts(b("X1", *q4(k + 1)), b("XI", *q4(k + 1)), 255, None, A.bitwise_and)
-        filler(1)
-        ts(b("NZ", *q4(k)), b("X1", *q4(k)), 128.0, None, A.not_equal)
-        filler(2)
-        mm(b("P%d" % k), b("BH"), b("NZ", *q4(k)))
-        act(b("SG", *q4(k)), b("P%d" % k), F.Sign, bias=-0.5)
-        if k == 0:
-            act(b("SG", V, V + 16), b("P0", 0, 16), F.Sign, bias=-0.5)
+        queue["y"].dma_start(out=T.XI[:, 512 * k:512 * k + 512], in_=T.det[:, 512 * k:512 * k + 512]).then_inc(T.sem["d%d" % k], 16)
+        op("r", None, [b("XI", *q4(k))], [], 0.0, LOAD + 1050 * (k + 1), ("d%d" % k, 16))
+    queue["y"].dma_start(out=T.HM[:], in_=T.ham[:]).then_inc(T.sem.d4, 16)
+    op("r", None, [b("HM")], [], 0.0, LOAD + 8000, ("d4", 16))
+
+    cell = [divmod(STEP * (t + 1), 16) for t in range(RO)]
+    PP, PI, PG, PG16, OD, SIG, SI2, W1, W2, PGE, PGO, CE, CO, CE1, CO1, CTE, CTO, CA, CB, P2 = [b("col", k, k + 1) for k in range(20)]
+    diag = [[-1, 128]]
+    blk = [[-16, 8], [0, 16]]
+    iota(b("pp_i"), [[0, 1]], 0, 1)
+    iota(b("Jb"), [[1, 256]], 0)
+    iota(b("JG"), [[1, 8], [0, 16]], 0)
+    iota(b("PD"), [[1, 128]], 0, -1)
+    iota(b("kx"), [[0, 8], [-1, 16]], 0)
+    op("v", lambda: g.vector.memset(b("zero")[0], 0.0), [b("zero")], [], 64 * CYC)
+    op("v", lambda: g.vector.memset(b("ones")[0], 1.0), [b("ones")], [], 128 * CYC)
+    ts(b("pq_i"), b("pp_i"), 15, None, A.bitwise_and)
+    ts(b("pr_i"), b("pp_i"), 4, None, A.arith_shift_right)
+    act(PP, b("pp_i"))
+    act(PI, b("pq_i"))
+    act(PG, b("pr_i"))
+    act(PG16, b("pr_i"), scale=16.0)
+    ts(b("ZS"), b("Jb", 0, 144), -15.0, PG16, A.add, A.is_equal)
+    ts(b("BH"), b("JG"), PG, None, A.is_equal)
+    ts(b("I1"), b("PD"), 0.0, None, A.is_equal)
+    ts(b("e0"), b("ones", 0, 128), PP, 0.0, A.mult, A.is_equal)
+    sel(b("TI"), b("BH"), [[1, 128]], A.is_ge, 0.0, 0, -1)
+    act(b("J"), b("Jb"))
+    ts(b("sw"), b("Jb", 0, 20), 16.0, PI, A.mult, A.add)
+    for t, (c0, r0) in enumerate(cell):
+        TX = "TX%d" % t
+        ts(b("MK", 2 * t, 2 * t + 1), PI, float(r0), -2.0 ** 19, A.is_lt, A.mult)
+        ts(b("MK", 2 * t + 1, 2 * t + 2), PI, float(r0), -2.0 ** 19, A.is_ge, A.mult)
+        ts(CA, PP, float(c0), None, A.is_ge)
+        ts(CB, PP, float(c0), -1.0, A.is_ge, A.add)
+        ts(b(TX, 0, c0), b("PD", 0, c0), 0.0, CA, A.is_gt, A.add)
+        ts(b(TX, c0, 128), b("PD", c0, 128), 0.0, CB, A.is_gt, A.add)
+        cp(b(TX, 128, 130), b("ones", 0, 2))
+        w0, w1 = b("WL", 4 * t, 4 * t + 1), b("WL", 4 * t + 1, 4 * t + 2)
+        sel(w0, b("ones", 0, 1), [[0, 1]], A.not_equal, -127.0, -127, 1)
+        act(w1, w0, scale=16.0)
+        sel(w0, w0, [[0, 1]], A.not_equal, 129.0 - c0, 1 - c0, 1)
+        act(b("WL", 4 * t + 2, 4 * t + 4), b("WL", 4 * t, 4 * t + 2), scale=0.5)
+        act(b("base", 32 * t, 32 * t + 16 - NS), b("zero", 0, 16 - NS), bias=float(c0))
+        act(b("base", 32 * t + 16 - NS, 32 * t + 16), b("zero", 0, NS), bias=(128 + c0) / 2.0)
+        act(b("base", 32 * t + 16, 32 * t + 32), b("zero", 0, 16), bias=16.0 * c0)
+    iota(b("JI"), [[0, 20], [1, 16]], 0)
+    for n, c in (("I256n", -256.0), ("Im1", -1.0), ("IF", 256.0), ("I4kn", -4096.0), ("I256", 256.0), ("I64k", 65536.0),
+                 ("I16kn", -16384.0), ("I64n", -64.0)):
+        ts(b(n), b("I1"), c, None, A.mult)
+    ts(b("pq_i"), b("pp_i"), 1, None, A.bitwise_and)
+    ts(b("pr_i"), b("pr_i"), 1, None, A.bitwise_and)
+    act(SIG, b("pq_i"), scale=-2.0, bias=1.0)
+    act(SI2, b("pq_i"), scale=4.0, bias=-2.0)
+    act(W1, PI, scale=13.0, bias=5.0)
+    act(W2, PI, scale=-14.0, bias=255.0)
+    act(P2, PI, scale=2.0, bias=1.0)
+    act(PGE, b("pr_i"), scale=100000.0, bias=PG16)
+    act(OD, b("pr_i"), scale=-100000.0, bias=100000.0 - 16.0)
+    act(PGO, OD, bias=PG16)
+    for pg, ce, c1, ct, nh, n1, nt in ((PGE, CE, CE1, CTE, "EH", "E1", "TE"), (PGO, CO, CO1, CTO, "OH", "O1", "TO")):
+        act(ce, pg, scale=0.5, bias=3.0)
+        act(c1, pg, bias=11.0)
+        act(ct, pg, bias=P2)
+        ts(b(nt), b("Jb", 0, 130), ct, None, A.is_equal)
+        ts(b(nh, 0, 144, 2), b("Jb", 0, 72), ce, W1, A.is_equal, A.mult)
+        ts(b(nh, 1, 144, 2), b("Jb", 0, 72), ce, W2, A.is_equal, A.mult)
+        ts(b(n1), b("Jb", 0, 144), c1, SIG, A.is_equal, A.mult)
+    act(b("WT", 0, 8), b("BH", 0, 128, 16), scale=W1)
+    act(b("WT", 8, 16), b("BH", 0, 128, 16), scale=W2)
+    act(b("B592"), b("BH"), scale=592.0)
+    act(b("I592"), b("BH", 0, 128, 16), scale=-592.0)
+    act(b("kc"), b("kx"), bias=7.5)
+    act(b("PAR"), b("BH"), scale=SIG)
+    act(b("PA2"), b("BH"), scale=SI2)
+    act(b("swa"), b("sw"), bias=-float(TR))
+    act(b("swb"), b("sw"), bias=-float(TR + 1024))
+    ts(b("m16"), b("JI"), 0.0, None, A.is_gt)
+    ts(b("dk"), b("m16", 0, 256), 1023.0, -1024.0, A.mult, A.add)
+    sel(b("SU"), b("BH"), diag, A.is_equal, 0.0, -1, 1)
+    sel(b("SD"), b("BH"), diag, A.is_equal, 0.0, 1, 1)
+    iota(b("CR1"), [[0, 128]], -240)
+    sel(b("CR1"), b("CR1"), [[0, 8], [1, 16]], A.not_equal, -176.0, -15, 0)
+    sel(b("CR2"), b("zero"), [[0, 8], [1, 16]], A.not_equal, -64.0, 0, 0)
+    act(b("VK"), b("ones"), scale=-7.5)
+    act(b("VV"), b("ones"), scale=0.0)
+    sel(b("NU"), b("BH"), diag, A.is_gt, 0.0, 0, 1)
+    iota(b("c9", 0, 9), [[256, 9]], -1024)
+    iota(b("O", 0, 153, 17), [[0, 9]], 0)
+    sel(b("m17"), b("ones", 0, 153), [[0, 9], [1, 17]], A.not_equal, 0.0, -1, 0)
+    iota(b3("k1"), [[0, 320]], 0)
+    iota(b3("k2"), [[0, 320]], 0)
+    sel(b("AL"), b("zero"), blk, A.not_equal, OFF, 0, 1)
+    sel(b("AL"), b("AL"), blk, A.not_equal, -128.0, -1, 1)
+    for o in range(N):
+        iota(b("SL0", 256 * o, 256 * o + CAP), [[0, CAP]], SENT)
+    for m in range(1, NP):
+        ts(b("IM", 128 * m - 128, 128 * m), b("I1"), 2.0 * m, None, A.mult)
+    iota(b("cz0", 6, 61), [[1, 11], [0, 5]], 1)
+    iota(b("cz1", 16, 181), [[1, 11], [0, 15]], 1)
+    iota(b3("kc2", full, slice(0, 12)), [[0, 20], [2048, 12]], -81920)
+    iota(b3("kc2", full, slice(12, 16)), [[0, 80]], 1 << 20)
+    ts(b("mB"), b("JI"), 0.0, 2.0 ** 21, A.is_equal, A.mult)
+    ts(b("CM"), b("JI"), PI, 0.5, A.is_ge, A.mult)
+    ts(b("MX"), b("Jb", 0, 16), PI, None, A.is_equal)
+    for x in range(16):
+        ts(b("RX", 128 * x, 128 * x + 128), b("BH"), b("MX", x, x + 1), None, A.mult)
+    for o in range(N):
+        iota(b("SL1", 256 * o, 256 * o + CAP), [[0, CAP]], SENT)
+
+    def zs(x):
+        return b("ZS", 15 - x, 143 - x)
 
     XW = b("X", TR, TR + V)
     plan = {d: routes(d, T, topo) for d in T.cores}
     land = {d: landing(d, T, topo) for d in T.cores}
     near = sum(topo.chip(d) == topo.chip(core) for d in T.cores)
-    own0 = min(land[core][:near])
-    PART = ((0, near * CAP // 16), (near * CAP // 16, AR // 16))
+    BW = near * CAP // 16
+    PART = ((0, BW), (BW, AR // 16))
     sent = [0]
-    EQW, CHW = b3("eq"), b3("CH")
+    I1, Im1 = b("I1"), b("Im1")
 
     for t in range(RO):
-        start = STEP * (t + 1)
-        if t:
-            for k, (lo, hi) in enumerate(((0, V - start), (512, 1024), (V - start, 512), (1536, V), (1024, 1536))):
-                x = b("X", TR + (lo + start) % V, TR + (hi - 1 + start) % V + 1)
-                if k % 2:
-                    act(b("SR", lo, hi), x, F.Sign)
-                else:
-                    ts(b("SR", lo, hi), x, 0.0, None, A.is_gt)
-            for h in (0, 64):
-                for x in range(16):
-                    mm(b("P4", h, h + 64), b("ZS", 15 - x, 143 - x), b("SR", 16 * h + x, 16 * h + 1024, 16), x == 0, x == 15)
+        c0, r0 = cell[t]
+        TX = "TX%d" % t
+        if t == 0:
+            for k in range(4):
+                ts(b("X1", *q4(k)), b("XI", *q4(k)), 255, None, A.bitwise_and)
+                act(b("NZ", *q4(k)), b("X1", *q4(k)), F.Square, bias=-128.0)
+            act(b("NZ", V, V + 16), b("X1", 16 * c0, 16 * c0 + 16), F.Square, bias=-128.0)
+            for lo, hi, at in ((0, 64, c0), (64, 129, 128)):
+                mm(b("B0", lo, hi), [(zs(x), b("NZ", 16 * lo + x, 16 * hi, 16)) for x in range(16)]
+                   + [(I1, b("MK", at // 128, at // 128 + 1), b("B0", at, at + 1))])
         else:
-            c1 = (V - start + 15) // 16
-            e1 = start + 16 * c1 - V
+            act(b3("SR", full, 128), b("X", TR + 16 * c0, TR + 16 * c0 + 16), F.Sign)
             for x in range(16):
-                mm(b("P4", 0, c1), b("ZS", 15 - x, 143 - x), b("SG", start + x, start + x + 16 * (c1 - 1) + 1, 16), x == 0, x == 15)
-            for x in range(16):
-                mm(b("P4", c1, 128), b("ZS", 15 - x, 143 - x), b("SG", e1 + x, e1 + x + 16 * (127 - c1) + 1, 16), x == 0, x == 15)
-            spawn_constants()
-            child_constants()
-        ts(b("Lb"), b("P4", 0, 128), 0.0, None, A.is_gt)
-        mm(b("P5", 0, 128), b("BH"), b("Lb"))
-        mm(b("P4", 128, 256), b("NU"), b("Lb"))
+                o, i = b3("SR", x, slice(0, 128)), b("X", TR + x, TR + V, 16)
+                act(o, i, F.Sign) if x % 2 else ts(o, i, 0.0, None, A.is_gt)
+            mm(b("B0", 0, 129), [(zs(x), b3("SR", x, slice(0, 129))) for x in range(16)]
+               + [(I1, b("MK", 2, 4), b("B0", c0, 129, 128 - c0))])
+        ts(b("Lb", 0, 129), b("B0", 0, 129), 0.0, None, A.is_gt)
+        mm(b("B1", 0, 128), [(b("Lb", 0, 128), b("BH"))])
+        cp(b("cnt"), b("B1", 0, 128))
+        mm(b("B2", 0, 128), [(b("e0"), b("kx")), (b(TX, 0, 128), b("cnt")), (I1, b("cnt"))])
+        mm(b("B0", 0, 130), [(b("cnt"), b(TX)), (b("TI"), b("Lb", 0, 129), b("B0", 0, 129)), (b("BH"), b("Lb", 128, 129), b("B0", 129, 130))])
+        cp(b("EB"), b("B2", 0, 128))
+        act(b("U", 0, 130), b("B0", 0, 130))
+        for j in range(16):
+            o = b("cmp", 128 * j, 128 * j + 128)
+            if j < 16 - NS:
+                ts(o, b("EB"), 16.0 * j, None, A.is_le)
+            else:
+                act(o, b("EB"), F.Sign, bias=16.0 * j + 0.5, scale=-1.0)
+        turn = sorted(range(16), key=lambda j: j if j < 16 - NS else 2 * (j - 16 + NS) + 1.5)
+        mm(b("B1", 0, 32), [(b("e0"), b("base", 32 * t, 32 * t + 32))]
+           + [(b("cmp", 128 * j, 128 * j + 128), b("WL", 4 * t + 2 * (j >= 16 - NS), 4 * t + 2 * (j >= 16 - NS) + 2), b("B1", j, 32, 16)) for j in turn])
+        cp(b("cu"), b("B1", 0, 16))
+        act(b("cb"), b("B1", 16, 32))
+        tt(b("G"), ind(b("U", 0, 130), b("cu")), b("J"), A.is_le)
+        mm(b("B2", 0, 16), [(zs(x), b("G", x, 256, 16)) for x in range(16)] + [(I1, b("cb"))])
+        cp(b("plu"), b("B2", 0, 16))
+        ts(b("dm"), b("sw", 0, 16), b("U", 129, 130), -8192.0, A.is_ge, A.mult)
         if t == 0:
             for k in range(4):
-                mm(b("P%d" % k), b("AL"), b("SG", *q4(k)))
-        scan(b("E"), b("ones"), b("P5", 0, 128), A.mult, A.add)
-        NA = 10
-        for k in range(NA):
-            act(b("jnk", 128 * k, 128 * k + 128), b("E"), F.Sign, bias=b("swh", k, k + 1), scale=-1.0, accum=b("acc", k, k + 1))
-        tt(b("U", 0, 128), b("E"), b("P4", 128, 256), A.add)
-        for k in range(NA, 17):
-            o = 144 * (k - NA)
-            if k < 16:
-                ts(b("cmp", o, o + 128), b("E"), b("sw", k, k + 1), -2.0, A.is_gt, A.mult)
-            if k > NA:
-                red(b("acc", k - 1, k), b("cmp", o - 144, o - 15), A.add)
-        ts(b("vw"), b("sw", 0, 16), b("E", 127, 128), None, A.is_lt)
-        for j in range(4):
-            ts(b("cu", 4 * j, 4 * j + 4), b("acc", j, 16, 4), 0.5, 64.0, A.mult, A.add)
-        tt(b("G"), ind(b("U"), b("cu")), b("Jp"), A.is_le)
-        ts(b("cb"), b("acc"), 8.0, 1024.0 + start, A.mult, A.add)
-        ts(b("dm8"), b("vw"), -8.0, 8.0, A.mult, A.add)
-        for par, n in ((0, "E1"), (16, "O1")):
-            for j in range(4):
-                mm(b3("Q0", slice(0, 4), slice(par, par + 16)), b(n, 11 - j, 139 - j), b("G", 64 * j, 64 * j + 64), j == 0, j == 3)
-        if t == 0:
-            for k in range(4):
-                tt(b("X", TR + 512 * k, TR + 512 * k + 512), b("XI", *q4(k)), b("P%d" % k), A.add)
-        vtr(b3("R4"), b3("Q0", slice(0, 4), full))
-        tt(b("ai"), b("cb"), b3("R4", full, slice(0, 4)), A.add)
-        ts(b("pl"), b("ai"), V - 1, None, A.bitwise_and)
-        cp(b("plu"), b("pl"))
-        act(b("Sx"), ind(XW, b("plu")), F.Identity, bias=-OFF)
-        ts(b("T6"), ind(XW, b("plu")), M31, -(M31 + OFF), A.add, A.add)
-        ts(b("Du"), b("T6"), 1.0 / 256.0, 4095.0, A.mult, A.min)
-        tt(b("C"), b("Sx"), b("T6"), A.subtract)
-        for lo, hi in ((64, 96), (0, 0), (96, 128), (128, 192), (192, 256)):
-            if lo == hi:
-                act(b("P0", 0, 256), b("C"), F.Abs)
-            else:
-                act(b("Lg", 16 * lo, 16 * hi), ind(b("HM"), b("Du", lo, hi)), F.Copy)
-        act(b("P4", 0, 256), b("C"), F.Sign)
-        act(b("P5", 0, 256), b("T6"), F.Identity, bias=128.0)
-        ts(b("Dh"), b("T6"), 1.0 / 256.0, -2048.0, A.mult, A.add)
-        cp(b("Lg", 0, 1024), ind(b("HM"), b("Du", 0, 64)))
+                mm(b("C%d" % k), [(b("BH"), b("NZ", *q4(k)))])
+                act(b("SG", *q4(k)), b("C%d" % k), F.Sign, bias=-0.5)
+        win, off = (b("XI"), 128.0) if t == 0 else (XW, OFF)
+        ts(b("Du"), ind(win, b("plu")), 1.0 / 256.0, -off / 256.0, A.mult, A.add)
+        act(b("Sx"), ind(win, b("plu")), F.Relu, bias=(128.0 - off) / 256.0, scale=1.0 / 256.0)
+        tt(b("fo"), b("dm"), b("B2", 0, 16), A.add)
+        for h in (0, 128):
+            ts(b("Dh", h, h + 128), b("Du", h, h + 128), -2048.0, None, A.add)
+        CB0 = -524288.0 - 128.0
+        for par, n in ((0, "TE"), (1, "TO")):
+            mm(b3("C0", slice(par, 8, 2)), [(b(n, 1 - u, 129 - u), b("Dh", 64 * u, 64 * u + 64)) for u in (0, 1)])
+        for h in (0, 128):
+            mm(b("B3", h, h + 128), [(b("IF"), b("Sx", h, h + 128)), (b("I256n"), b("Dh", h, h + 128))])
+            act(b("Ca", h, h + 128), b("B3", h, h + 128), F.Abs, bias=CB0)
+        vtr(b("RT"), b("C0", 0, 128))
+        for k in range(4):
+            ts(b("DT", k, 128, 4), b("RT", 32 * k, 32 * k + 32), 2048.0, None, A.add)
+        for h in (0, 128):
+            cp(b("Cr", h, h + 128), b("Ca", 0, 128))
         for h in range(2):
-            mm(b("P3", 16 * h, 16 * h + 16), b("Dh", 128 * h, 128 * h + 128), b("WT"))
+            mm(b("B0", 16 * h, 16 * h + 16), [(b("Dh", 128 * h, 128 * h + 128), b("WT"))])
+        for k in range(0, 16, 2):
+            tt(b("MV", 128 * k, 128 * k + 256), ind(b("HM"), b("DT", 8 * k, 8 * k + 16)), b("Cr"), A.min)
+        mm(b("B1", 0, 128), [(b("e0"), b("kc"))] + [(b("MV", 128 * k, 128 * k + 128), b("B592", 0, 128, 16), b("B1", k, 128, 16)) for k in range(16)])
+        for q in range(4):
+            act(b("Lg", *q4(q)), ind(b("HM"), b("Du", 128 + 32 * q, 160 + 32 * q)), F.Copy)
+        for q, kk, bank in ((0, 0, "C1"), (0, 8, "C2"), (1, 0, "C0"), (1, 8, "C1")):
+            for k in range(8):
+                mm(b(bank, 64 * k, 64 * k + 64), [(Im1, b("Lg", 1024 * q + kk + k, 1024 * q + 1024, 16)), (I1, b("Ca", 128 + 64 * q, 192 + 64 * q))])
+            act(b3("Mn", slice(kk, kk + 8), slice(64 * q, 64 + 64 * q)), b(bank), F.Relu)
+        mm(b("B2", 0, 128), [(b("e0"), b("kc")), (b("Ca", 128, 256), b("B592"))]
+           + [(b3("Mn", k), b("I592"), b("B2", k, 128, 16)) for k in range(16)])
+        cp(b3("hi"), b("B0", 0, 32))
+        ts(b3("ha"), b3("hi"), 4095, None, A.bitwise_and)
+        tt(b("hp"), b3("ha", full, slice(0, 8)), b3("ha", full, slice(8, 16)), A.mult)
+        ts(b("hq"), b("hp"), 5, None, A.arith_shift_right)
+        ts(b("hb"), b("hq"), 16.0, M27 + 16.0 * t, A.mult, A.add)
+        act(b("Cb"), b("B3", 0, 256), bias=CB0)
         for h in range(2):
-            mm(b("P%d" % (1 + h), 0, 128), b("e0b"), b("kc"), True, False)
-
-        def hash_step(k):
-            if k == 0:
-                cp(b3("hi"), b("P3", 0, 32))
-            elif k == 1:
-                ts(b3("ha"), b3("hi"), 4095, None, A.bitwise_and)
-            elif k == 2:
-                tt(b("hp"), b3("ha", full, slice(0, 8)), b3("ha", full, slice(8, 16)), A.mult)
-            elif k == 3:
-                ts(b("hq"), b("hp"), 5, None, A.arith_shift_right)
-            elif k == 4:
-                ts(b("hb"), b("hq"), 16.0, M27 + 16.0 * t, A.mult, A.add)
-            else:
-                ts(b("Fl"), b("C"), 0.25, -0.375, A.mult, A.add)
-
-        for qd in range(4):
-            lo, h = 64 * qd, qd // 2
-            for k in range(16):
-                tt(b("Mn", 256 * k + lo, 256 * k + lo + 64), b("Lg", 16 * lo + k, 16 * lo + 1024, 16), b("P0", lo, lo + 64), A.min)
-                if qd == 1 and k % 2 == 0 and k < 12:
-                    hash_step(k // 2)
-                if qd % 2:
-                    mm(b("P%d" % (1 + h), k, 128, 16), b("Mn", 256 * k + 128 * h, 256 * k + 128 * h + 128), b("I592"), False, k == 15)
-            if qd == 2:
-                scan(b("Ks", 0, 128), b("m16", 0, 128), b("P1", 0, 128), A.mult, A.max)
-        tt(b("Cf"), b("C"), b("P4", 0, 256), A.subtract)
-        act(b("fsq"), b("Cf"), F.Square)
-        tt(b("xf"), b("Cf"), b("P5", 0, 256), A.add)
-        mm(b("P0", 0, 256), b("BB"), b("fsq"))
-        act(b("fsg"), b("P0", 0, 256), F.Sign, bias=-0.5)
-        scan(b("Ks", 128, 256), b("m16", 0, 128), b("P2", 0, 128), A.mult, A.max)
+            scan(b("Ks", 128 * h, 128 * h + 128), b("m16", 0, 128), b("B%d" % (1 + h), 0, 128), A.mult, A.max)
         kmx = b("Ks", 15, 256, 16)
-        tt(b("vi"), kmx, b("hb"), A.add)
         ts(b("rk"), kmx, M27, -M27, A.add, A.add)
+        tt(b("vi"), kmx, b("hb"), A.add)
+        tt(b("VK", 0, 256, 16), b("rk"), kmx, A.subtract)
         ts(b("vv"), b("vi"), 4, 4095, A.arith_shift_right, A.bitwise_and)
-        tt(b("VK", 256, 512, 16), b("rk"), kmx, A.subtract)
-        ts(b("VK", 0, 256, 16), b("vv"), -2048.0, None, A.add)
-        scan(b("VB", 256, 512), b("m16"), b("VK", 256, 512), A.mult, A.add)
-        scan(b("VB", 0, 256), b("m16"), b("VK", 0, 256), A.mult, A.add)
-        tt(b("fo"), b("pl"), b("dtr", 0, 16), A.add)
-        mm(b("P5", 0, 256), b("SU"), b("Dh"), True, False)
-        mm(b("P1", 0, 256), b("SD"), b("Dh"), True, False)
-        for x in (2, 3, 0, 1):
-            mm(b("P4" if x > 1 else "P3", 128 * (x % 2), 128 * (x % 2) + 128), b("VB", 128 * x, 128 * x + 128), b("ID"))
-        kr, vr = b("P4", 0, 256), b("P3", 0, 256)
-        ts(b("mA"), kr, IM, ACOL, A.is_le, A.add)
-        ts(b("mB"), kr, IM, BCOL, A.is_lt, A.add)
-        mm(b("P5", 0, 256), b("BI"), b("mA"), False, True)
-        mm(b("P1", 0, 256), b("BI"), b("mB"), False, True)
-        mm(b("P2", 0, 256), b("PK1"), b("mA"), True, False)
-        mm(b("P2", 0, 256), b("PK2"), b("mB"), False, True)
-        mm(b("P0", 256, 512), b("AL"), b("fsg"))
-        tt(b("fo2"), b("fo"), b("vw"), A.mult)
-        tt(b("R1"), b("Dh"), b("P5", 0, 256), A.max)
-        tt(b("R2"), b("Dh"), b("P1", 0, 256), A.min)
-        tt(b("m1"), b("R1"), vr, A.min)
-        tt(EQW, b("Dh"), vr, A.is_equal)
-        tt(b("fo3"), b("fo2"), b("sw", 0, 16), A.add)
-        tt(CHW, b("R2"), b("m1"), A.max)
-        for par, ns, nh in ((0, "E1", "EH"), (16, "O1", "OH")):
-            for j in range(4):
-                mm(b3("Q0", slice(0, 4), slice(par, par + 16)), b(ns, 3 - j, 131 - j), b3("eq", slice(j, None, 4), full), j == 0, False)
-            for j in range(4):
-                mm(b3("Q0", slice(0, 4), slice(par, par + 16)), b(nh, 6 - 2 * j, 134 - 2 * j), b3("CH", slice(j, None, 4), full), False, j == 3)
-        cp(b("fou"), b("fo3"))
-        tt(b("ow1"), CHW, vr, A.is_equal)
-        mm(b("P4", 0, 256), b("PAR"), b("ow1"))
-        tt(b("FK"), b("Fl"), b("P2", 0, 256), A.mult)
-        vtr(b3("R4"), b3("Q0", slice(0, 4), full))
+        scan(b("TK"), b("dk"), b("VK"), A.add, A.max)
+        ts(b("VV", 0, 256, 16), b("vv"), -2048.0, None, A.add)
+        scan(b("VB"), b("m16", 0, 256), b("VV"), A.mult, A.add)
+
+        def turned(bank, n, w):
+            return [(b(n, h, h + 128), w, b(bank, h, h + 128)) for h in (0, 128)]
+        DH, ONE = b("Dh"), b("ones")
+        mm(b("B0", 0, 256), [(b("SU"), DH), (b("CR1"), ONE)] + turned("B0", "TK", b("I4kn")))
+        tt(b("R1"), DH, b("B0", 0, 256), A.max)
+        for term in turned("B3", "VB", I1):
+            mm(None, [term])
+        mm(b("B1", 0, 256), [(b("CR2"), ONE), (b("SD"), b("R1"))])
+        tt(b("m1"), b("R1"), b("B3", 0, 256), A.min)
+        tt(b("CH"), b("m1"), b("B1", 0, 256), A.max)
+        mm(b("C1", 0, 256), [(I1, DH)] + turned("C1", "VB", Im1))
+        act(b("sD"), b("C1", 0, 256), F.Sign)
+        for par, ns, nh in ((0, "E1", "EH"), (1, "O1", "OH")):
+            mm(b3("C2", slice(par, 8, 2)), [(b(ns, 3 - j, 131 - j), b3("sD", slice(j, None, 4))) for j in range(4)]
+               + [(b(nh, 6 - 2 * j, 134 - 2 * j), b3("CH", slice(j, None, 4))) for j in range(4)])
+        for term in turned("C0", "TK", I1):
+            mm(None, [term])
+        act(b("th"), b("C0", 0, 256), F.Sign, bias=7.5)
+        mm(b("B2", 0, 256), [(I1, b("R1"))] + turned("B2", "VB", Im1))
+        act(b("sE"), b("B2", 0, 256), F.Sign)
+        mm(b("C0", 0, 256), [(b("PA2"), b("th")), (b("PAR"), b("sE"))])
+        act(b("ab"), b("C0", 0, 256), F.Abs, bias=2.0)
+        act(b("C1", 0, 256), b("ab"), bias=-1.0 / 256.0, scale=1.0 / 256.0)
+        act(b("Fb"), b("Cb"), bias=191.625, scale=0.25)
+        act(b("Fl"), b("Fb"), bias=-192.0)
+        act(b("CHf"), b("CH"))
+        tt(b("cc"), b("Fl"), b("C1", 0, 256), A.mult)
+        vtr(b3("R4"), b("C2", 0, 128))
         cp(b3("ci"), b3("R4", full, slice(0, 8)))
-        ts(b("iv"), b3("R4", full, slice(8, 12)), 0.0, 8.0, A.is_gt, A.mult)
+        ts(b("iv"), b3("R4", full, slice(8, 12)), -1.0, -8192.0, A.is_equal, A.mult)
         ts(b3("ca"), b3("ci"), 4095, None, A.bitwise_and)
-        tt(b("iv2"), b("iv"), b("dm8"), A.max)
+        tt(b("iv2"), b("iv"), b("dm"), A.min)
         tt(b("ch"), b3("ca", full, slice(0, 8, 2)), b3("ca", full, slice(1, 8, 2)), A.mult)
-        tt(b("xg"), b("xf"), b("P0", 256, 512), A.add)
+        ts(b("O", 137, 153), b("iv2"), 0.0, None, A.is_lt)
         ts(b("ow"), b("ch"), 5, 7, A.arith_shift_right, A.bitwise_and)
-        tt(b("cc"), b("FK"), b("P4", 0, 256), A.mult)
         tt(b("own"), b("ow"), b("iv2"), A.add)
-        for o in range(9):
-            ts(b("O", 16 * o, 16 * o + 16), b("own"), float(o), None, A.is_equal if o < 8 else A.is_ge)
-        mm(b("P3", 0, 144), b("BH"), b("O"))
-        mm(b("P5", 0, 144), b("NU"), b("O"), True, False)
-        mm(b("P5", 0, 144), b("e0h"), b("c9"), False, True)
-        tt(b("PK"), b("cc"), CHW, A.add)
-        scan(b("I9"), b("m16", 0, 144), b("P3", 0, 144), A.mult, A.add)
-        tt(b("A9"), b("I9"), b("P5", 0, 144), A.add)
-        tt(b("s9"), b("A9"), b("O"), A.mult)
-        for o in range(9):
-            mm(b("P2", 0, 16), b("ID"), b("s9", 16 * o, 16 * o + 16), o == 0, o == 8)
-        cp(ind(b("X"), b("fou")), b("xg"))
-        ts(b("slu"), b("P2", 0, 16), 1024.0, None, A.add)
+        for o in range(8):
+            ts(b("O", 17 * o + 1, 17 * o + 17), b("own"), float(o), None, A.is_equal)
+        mm(b("B3", 0, 153), [(b("TI"), b("O")), (b("e0"), b("c9", 0, 9), b("B3", 1, 153, 17)), (b("NU"), b("O", 0, 152), b("B3", 1, 153))])
+        scan(b("B0", 0, 153), b("m17"), b("B3", 0, 153), A.mult, A.add)
+        tt(b("s9"), b("O"), b("B0", 0, 153), A.mult)
+        mm(b("B1", 0, 16), [(I1, b("s9", 17 * o + 1, 17 * o + 17)) for o in range(9)])
+        ts(b("slu"), b("B1", 0, 16), 1023.0, None, A.add)
         SL, LA = "SL%d" % t, "LA%d" % t
-        cp(ind(b(SL), b("slu")), b("PK"))
+        tt(ind(b(SL), b("slu")), b("cc"), b("CHf"), A.add)
+        sends = []
         for call in (0, 1):
             tr = []
             for cl, d, eng in plan[core]:
                 if cl != call:
                     continue
                 o, at = T.rank_of(d), CAP * land[d].index(me)
-                need("g", b(SL, 256 * o, 256 * o + CAP)[1], [])
                 tr.append(RemoteDMATransfer(
                     dst_ids=[DstId(rid=topo.addr(d)[0], pnc=topo.addr(d)[1])], dma_engine_mask=sum(1 << e for e in eng),
                     remote_sem=T.sem[("an%d" if topo.chip(d) == topo.chip(core) else "ar%d") % t],
                     src=T[SL][:, 256 * o:256 * o + CAP], dst=T[LA][:, at:at + CAP]))
                 sent[0] += len(eng)
-            g.remote_dma_fused(tr, local_sem=T.sem.loc)
-        for d in T.cores:
-            if d != core:
-                nr = topo.chip(d) == topo.chip(core)
-                tot = sum(len(e) for s in T.cores if s != core and (topo.chip(s) == topo.chip(core)) == nr
-                          for _, x, e in plan[s] if x == core)
-                at = CAP * land[core].index(T.rank_of(d))
-                acc.setdefault(LA, []).append((at, at + CAP, 1, ("an%d" if nr else "ar%d") % t, tot, "r"))
+            sends.append(op("g", lambda tr=tr: g.remote_dma_fused(tr, local_sem=T.sem.loc), [], [b(SL)], SEND, None, ("", 0)))
+        for nr in (True, False):
+            there = [d for d in T.cores if d != core and (topo.chip(d) == topo.chip(core)) == nr]
+            tot = sum(len(e) for s in there for _, x, e in plan[s] if x == core)
+            at = [CAP * land[core].index(T.rank_of(d)) for d in there]
+            i = op("r", None, [b(LA, a, a + CAP) for a in at], [], 0.0, (NEAR if nr else FAR) + FIRST * (t == 0), (("an%d" if nr else "ar%d") % t, tot))
+            calls[i][3].append(sends[0 if nr else 1])
         at = CAP * land[core].index(me)
-        cp(b(LA, at, at + CAP), b(SL, 256 * me, 256 * me + CAP))
+        act(b(LA, at, at + CAP), b(SL, 256 * me, 256 * me + CAP))
+        act(b("sC"), b("Cb"), F.Sign)
+        fade = [(I1, b("Cb")), (Im1, b("sC"))]
+        mm(b("C3", 0, 256), fade)
+        act(b("fsq"), b("C3", 0, 256), F.Square)
+        mm(b("C3", 0, 256), [(b("BH"), b("fsq"))])
+        act(b("fsg"), b("C3", 0, 256), F.Sign, bias=-0.5)
+        mm(b("C3", 0, 256), fade + [(b("I256"), DH), (b("AL"), b("fsg"))])
+        act(b("xg"), b("C3", 0, 256), bias=-CB0)
+        tt(b("fo2"), b("fo"), b("swa", 0, 16), A.max)
+        act(b("fou"), b("fo2"), bias=float(TR))
+
+        def flagged(out, in_, at, o):
+            for k in range(4):
+                mm(b("C3"), [(b("AL"), b("SG", *q4(k)))])
+                for h in (0, 256):
+                    lo = 512 * k + h
+                    tt(b(out, TR + lo, TR + lo + 256), b(in_, at + lo, at + lo + 256), b("C3", h, h + 256), o)
         if t == 0:
-            arrival_constants()
-        else:
+            flagged("X", "XI", 0, A.add)
+        cp(ind(b("X"), b("fou")), b("xg"))
+        if t == RO - 1:
             for k in range(4):
                 act(b("SG", *q4(k)), b("X", TR + 512 * k, TR + 512 * k + 512), F.Sign)
-                mm(b("P%d" % (1 + k)), b("AL"), b("SG", *q4(k)))
-            for k in range(4):
-                q = (TR + 512 * k, TR + 512 * k + 512)
-                tt(b("Y", *q), b("X", *q), b("P%d" % (1 + k)), A.subtract)
+            flagged("Y", "X", TR, A.subtract)
 
-        def score(bank, lo):
-            q = (lo, lo + 60)
-            ts(b("k1", *q), b(bank, 0, 60), 0.0, None, A.is_equal)
-            act(b("k2", *q), b(bank, 0, 60), F.Sign, bias=-THETA)
-            mm(b("P4", *q), b("e0b"), b("kcm", *q), True, False)
-            k = lo // 60 - 1
-            mm(b("P4", *q), b("ID"), b3("ZH1", slice(4 * k, 4 * k + 4), slice(0, 15)) if lo else b3("ZH0", full, slice(0, 5)), False, False)
-            mm(b("P4", *q), b("ID32"), b("k1", *q), False, False)
-            mm(b("P4", *q), b("ID8"), b("k2", *q), False, True)
-
-        def sums(k):
-            for x in range(16):
-                mm(b("P%d" % k, 0, 60), b("ZS", 15 - x, 143 - x), b("sq", 960 * k + x, 960 * k + 960, 16), x == 0, x == 15)
-
-        def part0_tail(k):
-            if k == 0:
-                score("P0", 0)
-                act(b("K3", 0, 30), b("P4", 0, 30), F.Copy)
-            elif k == 2:
-                tt(b("K2", 0, 30), b("K3", 0, 30), b("P4", 30, 60), A.min)
-            elif k == 3:
-                tt(b("K1", 0, 15), b("K2", 0, 15), b("K2", 15, 30), A.min)
-            elif k == 4:
-                tt(b("K2", 30, 35), b("K1", 0, 5), b("K1", 5, 10), A.min)
-            elif k == 5:
-                tt(b("km", 0, 5), b("K2", 30, 35), b("K1", 10, 15), A.min)
-
-        def arrivals(part):
-            c0, c2 = PART[part]
-            w = c2 - c0
-            wp, n, ways = w + 1, 16 * w, w // 5
-            a0, z0 = 16 * c0, 960 * part
-            A16 = b3("A16", slice(c0, c2), full)
-            s0 = 6 * part
-            st = b("st", s0, s0 + wp)
+        score = [(b("e0"), b3("kc2"))]
+        banks = ["C0", "C2", "C1", "C0"]
+        for part in range(2):
+            c1, c2 = PART[part]
+            w = c2 - c1
+            n, ways, a0, z0 = 16 * w, w // 5, 16 * c1, 960 * part
+            cs = slice(c1, c2)
+            A16 = b3("A16", cs)
+            zu, ZH, cz, Q = "zu%d" % part, "ZH%d" % part, "cz%d" % part, "Q%d" % part
+            at = [0] + [w + 1 + w * m for m in range(NP)]
             u1, u2 = b3("aa5", full, slice(0, 2 * ways, 2)), b3("aa5", full, slice(1, 2 * ways, 2))
             ai5, aa5, R5 = [b3(x, full, slice(0, 2 * ways)) for x in ("ai5", "aa5", "R5")]
-
-            def orbitals():
-                ts(A16, b(LA, a0, a0 + n), M23, -M23, A.add, A.add)
-                for par, nh in ((0, "EH"), (16, "OH")):
-                    for j in range(ways):
-                        mm(b3("Q1p", slice(0, 5), slice(par, par + 16)), b(nh, 6 - 2 * j, 134 - 2 * j),
-                           b3("A16", slice(c0 + j, c2, ways), full), j == 0, j == ways - 1)
-
-            def numbers():
-                ts(b("st", s0, s0 + w), u1, 2.0, 1.0, A.mult, A.add)
-                tt(b("ah", 0, w), u1, u2, A.mult)
-                act(b("s2", 0, wp), st, F.Copy, scale=2.0)
-                act(b("s2", wp, 2 * wp), st, F.Copy, scale=2.0)
-                act(b("s4", 0, 2 * wp), b("s2", 0, 2 * wp), F.Copy, scale=2.0)
-                act(b("s4", 2 * wp, 4 * wp), b("s2", 0, 2 * wp), F.Copy, scale=2.0)
-                act(b("s8", 0, 4 * wp), b("s4", 0, 4 * wp), F.Copy, scale=2.0)
-
-            def first():
-                ts(b("Z", 0, w), b("ah", 0, w), 8, V - 1, A.arith_shift_right, A.bitwise_and)
-                cp(b("zu", 0, wp), b("Z", 0, wp))
-                tt(b("Z", wp, 2 * wp), b("Z", 0, wp), st, A.add)
-                if part:
-                    sums(0)
-
-            def zm(lo, hi):
-                ts(b("Zm", lo * wp, hi * wp), b("Z", lo * wp, hi * wp), V - 1, None, A.bitwise_and)
-
-            def zc(lo, hi):
-                cp(b("zu", lo * wp, hi * wp), b("Zm", lo * wp, hi * wp))
-
-            def probe(m):
-                if m == 1:
-                    zm(0, 2)
-                    tt(b("Z", 2 * wp, 4 * wp), b("Z", 0, 2 * wp), b("s2", 0, 2 * wp), A.add)
-                    zc(1, 2)
-                    zm(2, 4)
-                if m == 2:
-                    tt(b("Z", 4 * wp, 8 * wp), b("Z", 0, 4 * wp), b("s4", 0, 4 * wp), A.add)
-                    zc(2, 4)
-                    tt(b("Z", 8 * wp, 12 * wp), b("Z", 0, 4 * wp), b("s8", 0, 4 * wp), A.add)
-                if m == 3:
-                    zm(4, 12)
-                if m == 4:
-                    zc(4, 12)
-                    cp(b3("ZH%d" % part), b("Zm", 0, 12 * wp))
-                if part and m > 2:
-                    part0_tail(m - 3)
-                d = (z0 + n * m, z0 + n * m + n)
-                tt(b("dd", *d), ind(XW, b("zu", wp * m, wp * m + w)), b("Q1", a0, a0 + n), A.subtract)
-                if part or m % 4 == 3:
-                    d = d if part else (z0 + n * (m - 3), z0 + n * m + n)
-                    act(b("sq", *d), b("dd", *d), F.Square, bias=-M31 / 256.0, scale=1.0 / 256.0)
-                if part and m % 4 == 3:
-                    k = m // 4 + 1
-                    if k > 1:
-                        score("P%d" % (k - 1), 60 * (k - 1))
-                    sums(k)
-                    if k == 2:
-                        act(b("KS"), b("P4", 60, 120), F.Copy)
-
-            pre = [orbitals, lambda: ts(b("Q1", a0, a0 + n), A16, 256.0, 524288.0 + OFF - M31, A.mult, A.add),
-                   lambda: vtr(b3("R5"), b3("Q1p", slice(0, 5), full)), lambda: cp(ai5, R5),
-                   lambda: ts(aa5, ai5, 4095, None, A.bitwise_and), numbers, first]
-            return pre, probe
-
-        pre0, probe0 = arrivals(0)
-        pre1, probe1 = arrivals(1)
-        for f in pre0:
-            f()
-        for m in range(NP):
-            probe0(m)
-            if m > 5:
-                pre1.pop(0)()
-        for f in pre1:
-            f()
-        for m in range(NP):
-            probe1(m)
-        tt(b("ac"), b(LA), b3("A16"), A.subtract)
-        act(b("cq"), b("ac"), F.Identity, bias=128.0, scale=256.0)
-        tt(b("K1"), b("KS"), b("P4", 120, 180), A.min)
-        score("P3", 180)
-        tt(b("K2"), b("K1"), b("P4", 180, 240), A.min)
-        tt(b("K3", 0, 30), b("K2", 0, 30), b("K2", 30, 60), A.min)
-        tt(b("km", 5, 20), b("K3", 0, 15), b("K3", 15, 30), A.min)
-        ts(b("pm"), b("km"), V - 1, None, A.bitwise_and)
-        ts(b("iv3"), b("km"), 0.0, -4096.0, A.is_ge, A.mult)
-        cp(b("pu"), b("pm"))
+            hb = "C%d" % (2 - part)
+            ts(A16, b(LA, a0, a0 + n), M23, -M23, A.add, A.add)
+            for par, nh in ((0, "EH"), (1, "OH")):
+                mm(b3(hb, slice(par, 10, 2)), [(b(nh, 6 - 2 * j, 134 - 2 * j), b3("A16", slice(c1 + j, c2, ways))) for j in range(ways)])
+            groups = [(0, 1), (1, 3), (3, 5), (5, 7), (7, 9), (9, 11), (11, 12)] if part else [(0, 1), (1, 5), (5, 9), (9, 12)]
+            for k in range(groups[1][1] - 1):
+                act(b(Q, n * k, n * k + n), A16, bias=524288.0 + OFF - M31, scale=256.0)
+            vtr(b3("R5"), b(hb, 0, 160))
+            cp(ai5, R5)
+            ts(aa5, ai5, 4095, None, A.bitwise_and)
+            tt(b("ah", 0, w), u1, u2, A.mult)
+            act(b("uh", 0, w), u1, bias=-2048.0)
+            ts(b("Z", 0, w), b("ah", 0, w), 8, V - 1, A.arith_shift_right, A.bitwise_and)
+            cp(b(zu, 0, w), b("Z", 0, w))
+            act(b(ZH, 0, w), b("Z", 0, w))
+            for m0, m1, bank in ((1, 5, "B0"), (5, NP, "B2")):
+                r = (at[m0], at[m1])
+                mm(b(bank, *r), [(b("e0"), b(cz, *r))]
+                   + [(b("IM", 128 * m - 128, 128 * m), b("uh", 0, w), b(bank, at[m], at[m] + w)) for m in range(m0, m1)]
+                   + [(I1, b(ZH, 0, w), b(bank, at[m], at[m] + w)) for m in range(m0, m1)])
+                act(b("Zi", *r), b(bank, *r))
+                ts(b("Zm", *r), b("Zi", *r), V - 1, None, A.bitwise_and)
+                act(b(zu, *r), b("Zm", *r))
+                act(b(ZH, *r), b("Zm", *r))
+            score += [(I1, b(ZH, at[m], at[m] + w), b("B1", a0 + m, a0 + n, 16)) for m in range(NP)]
+            for m0, m1 in groups:
+                tt(b("dd", z0 + n * m0, z0 + n * m1), ind(XW, b(zu, at[m0], at[m0] + w * (m1 - m0))), b(Q, 0, n * (m1 - m0)), A.subtract)
+                for m in range(m0, m1):
+                    act(b3("sq", cs, m), b("dd", z0 + n * m, z0 + n * m + n), F.Square, bias=-M31 / 256.0, scale=1.0 / 256.0)
+            for ms in (slice(0, 7), slice(7, 11), 11) if part else (slice(0, 12),):
+                bank = b3(banks.pop(0), cs, ms)
+                mm(bank, [(zs(x), b3("sq", cs, ms, x)) for x in range(16)])
+                act(b3("k1", cs, ms) if ms != 11 else b("k3", 0, w), bank, F.Sign)
+                act(b3("k2", cs, ms) if ms != 11 else b("k4", 0, w), bank, F.Sign, bias=-THETA)
+        last = b("B1", a0 + 11, AR, 16)
+        mm(b("B1", 0, AR), score + [(b("I64k"), b3("k1")), (b("I16kn"), b3("k2")), (b("I64k"), b("k3", 0, w), last), (b("I16kn"), b("k4", 0, w), last)])
+        act(b("QW"), b3("A16"), bias=524288.0 + OFF, scale=256.0)
+        scan(b("KM"), b("mB"), b("B1", 0, AR), A.add, A.min)
+        km = b("KM", 15, AR, 16)
+        cp(b("ki"), km)
+        ts(b("iv3"), km, 0.0, -4096.0, A.is_ge, A.mult)
+        ts(b("pm"), b("ki"), V - 1, None, A.bitwise_and)
+        ts(b("iv3"), b("iv3"), -1024.0, None, A.add)
         tt(b("pvh"), b("pm"), b("iv3"), A.add)
-        tt(b("pv"), b("pm"), b("iv3"), A.add)
+        cp(b("pu"), b("pm"))
         for x in range(16):
-            mm(b("P5", x, AR, 16), b("RX", 128 * x, 128 * x + 128), b("pvh"))
-        mm(b("P0", 0, AR), b("ID"), b("CM"), True, False)
+            mm(b("C1", x, AR, 16), [(b("RX", 128 * x, 128 * x + 128), b("pvh"))])
+        act(b3("Pr"), b("C1", 0, AR))
         for x in range(16):
-            mm(b("P0", x, AR, 16), b("ID"), b("pvh"), False, x == 15)
-        act(b("xm"), ind(XW, b("pu")), F.Identity, bias=M31)
-        act(b("P1", 0, AR), b("xm"), F.Identity, bias=-M31)
-        tt(b("w1"), ind(XW, b("pu")), b("cq"), A.add)
-        act(b("P2", 0, AR), b("Q1"), F.Identity, bias=M31 - OFF)
-        ts(b("plS"), b("pv"), float(TR), 1.0 / 65536.0, A.add, A.mult)
-        tt(b("cn"), b("w1"), b("P1", 0, AR), A.subtract)
-        cp(b("Pr"), b("P5", 0, AR))
-        ts(b("ck"), b("cn"), 255.0, 1.0, A.min, A.max)
+            mm(b("C2", x, AR, 16), [(I1, b("pvh"))])
+        mm(b("B0", 0, AR), [(I1, b("CM"))] + [(I1, b("pvh"), b("B0", x, AR, 16)) for x in range(16)])
+        tt(b("w1"), ind(XW, b("pu")), b("QW"), A.subtract)
+        act(b("ra"), b("w1"), F.Relu, bias=128.0)
+        act(b("rs"), b("w1"), F.Sign, bias=128.0)
+        mm(b("B3", 0, AR), [(b("IF"), b(LA)), (b("I256n"), b3("A16")), (I1, b("ra")), (b("I64n"), b("rs"))])
         if t < RO - 1:
-            act(b("esq"), b("ck"), F.Square, bias=-128.0)
-            mm(b("P3", 0, AR), b("BB"), b("esq"))
-            act(b("esg"), b("P3", 0, AR), F.Sign, bias=-0.5)
-            mm(b("P4", 0, AR), b("AL"), b("esg"))
-        o5 = own0 // near * PART[0][1]
-        n5 = PART[0][1]
-        rng = []
-        for k in range(20):
-            r = [(0, k), (n5, n5 + o5)] if k < n5 else [(n5 if k < n5 + o5 else 0, k)]
-            rng.append((sum(y - x for x, y in r), k, [(x, y) for x, y in r if x < y]))
-        at, small = 0, []
-        for size, k, rs in sorted(rng, reverse=True):
-            if not size:
-                continue
-            e0 = at
-            for x, y in rs:
-                ts(b("EQ", at, at + 16 * (y - x)), b("Pr", 16 * x, 16 * y), b("pv", k, k + 1), None, A.is_equal)
-                at += 16 * (y - x)
-            if size > (10 if t < RO - 1 else 9):
-                act(b("jnk", e0, at), b("EQ", e0, at), F.Copy, accum=b("lw", k, k + 1))
-            else:
-                small.append((k, e0, at))
-        tt(b("DG"), b("Pr"), b("P0", 0, AR), A.is_equal)
-        for k, e0, e2 in small:
-            red(b("lw", k, k + 1), b("EQ", e0, e2), A.add)
-        scan(b("DS"), b("m16b"), b("DG"), A.mult, A.max)
-        tt(b("xn"), b("ck"), b("P2", 0, AR), A.add)
+            act(b("esq"), b("B3", 0, AR), F.Square, bias=-64.0)
+        ts(b("ck"), b("B3", 0, AR), 191.0, -63.0, A.min, A.max)
         if t < RO - 1:
-            tt(b("xo"), b("xn"), b("P4", 0, AR), A.add)
-        tt(b("t1"), b("plS"), b("DS", 15, AR, 16), A.subtract)
-        tt(b("t2"), b("t1"), b("lw"), A.subtract)
-        tt(b("t3"), b("t2"), b("swS"), A.max)
-        ts(b("eou"), b("t3"), 65536.0, None, A.mult)
-        if t < RO - 1:
-            cp(ind(b("X"), b("eou")), b("xo"))
+            mm(b("B2", 0, AR), [(b("BH"), b("esq"))])
+            act(b("esg"), b("B2", 0, AR), F.Sign, bias=-0.5)
+            mm(b("C0", 0, AR), [(b("I256"), b3("A16")), (b("AL"), b("esg"))])
+            act(b("Q2"), b("C0", 0, AR), bias=524288.0 + 64.0)
         else:
-            cp(ind(b("Y"), b("eou")), b("xn"))
+            act(b("Q2"), b3("A16"), bias=524288.0 + 64.0, scale=256.0)
+        tt(b("EQ"), b3("Pr"), b("B0", 0, AR), A.is_equal)
+        for d in range(1, BW):
+            for k in range(d, BW):
+                tt(b3("EQ3", slice(4 * d - 4, 4 * d), slice(16 * (k - d), 16 * (k - d + 1))), b3("Pr", slice(k - d, 20, BW)),
+                   b3("C2", slice(k, 20, BW)), A.is_equal)
+        mm(b("B1", 0, AR), [(b("I4kn"), b("EQ")), (I1, b("pvh"), b("B1", 0, AR, 16))]
+           + [(b("I4kn"), b3("EQ3", 4 * d - 4 + k, slice(0, 16 * (BW - d))), b("B1", 16 * (BW * k + d), 16 * BW * (k + 1)))
+              for d in range(1, BW) for k in range(4)])
+        scan(b("DS"), b("m16"), b("B1", 0, AR), A.mult, A.add)
+        tt(b("t3"), b("DS", 15, AR, 16), b("swb"), A.max)
+        ts(b3("eou", full, slice(0, BW)), b("t3"), float(TR + 1024), None, A.add)
+        for k in sorted(range(N // near), key=lambda k: -land[core][near * k]):
+            q = (16 * BW * k, 16 * BW * (k + 1))
+            tt(ind(b("X" if t < RO - 1 else "Y"), b3("eou", k, slice(0, BW))), b("ck", *q), b("Q2", *q), A.add)
     for k, e in ((0, "y"), (1, "s")):
-        dma(e, (T.y[:, 1024 * k:1024 * k + 1024], []), b("Y", TR + 1024 * k, TR + 1024 * k + 1024), "d%d" % (5 + k))
-    for s in ("sv", "ss", "sp", "sg"):
-        g.wait_ge(T.sem[s], cnt[s])
+        dma(e, hbm(T.y[:, 1024 * k:1024 * k + 1024]), b("Y", TR + 1024 * k, TR + 1024 * k + 1024), "d%d" % (5 + k), LOAD + 3000)
+
+    if not _ORDER:
+        _ORDER.extend(order_calls(calls))
+    cnt, known, mark = {}, {e: {} for e in queue}, {}
+    for i in _ORDER:
+        e, (call, sem) = calls[i][0], emit[i]
+        if e == "r":
+            mark[i] = (sem[0], sem[1], {})
+            continue
+        kn = known[e]
+        for s, v, seen in sorted((mark[d] for d in calls[i][3] if not (e == calls[d][0] == "p")), key=lambda x: (x[0] == semof.get(e), -x[1])):
+            if s and kn.get(s, 0) < v:
+                queue[e].wait_ge(T.sem[s], v)
+                for s2, v2 in list(seen.items()) + [(s, v)]:
+                    kn[s2] = max(kn.get(s2, 0), v2)
+        if sem is None:
+            cnt[e] = cnt.get(e, 0) + 1
+            sem = (semof[e], cnt[e])
+            call().then_inc(T.sem[sem[0]], 1)
+        elif sem[0]:
+            call().then_inc(T.sem[sem[0]], sem[1])
+        else:
+            call()
+        mark[i] = (sem[0], sem[1], dict(kn))
+    for e in semof:
+        g.wait_ge(T.sem[semof[e]], cnt[e])
     for k in range(7):
         g.wait_ge(T.sem["d%d" % k], 16)
     g.wait_ge(T.sem.loc, sent[0])

@@ -11,23 +11,24 @@ M23 = 1.5 * 2.0 ** 23
 OFF = 2.0 ** 22
 SENT = -22528
 THETA = 1.14e10
-NS = 5
+NS = 3
+NA, NV = 96, 160
 
 _DT = {"f": "float32", "b": "bfloat16", "h": "float16", "i": "int32", "u": "uint16"}
 _SBUF = """
-f X:2368 Y:2368 J:256 col:32 sw:20 swa:20 swb:20 U:136 dm:16 fo:16 fo2:16 Sx:256 Ks:256 hb:16 rk:16 RT:128 cc:256 CHf:256 xg:256
-f iv:16 iv2:16 own:16 R4:4,32 R5:5,32 SL0:2304 SL1:2304 LA0:320 LA1:320 Q0:320 Q1:480 QW:320 Q2:320 dd:3840 KM:320 iv3:20 w1:320
-f MX:16 ck:320 DS:320 t3:20 IF:128 Pr:20,16
-i XI:2048 X1:2048 pp_i:1 pq_i:1 pr_i:1 hp:16 hq:16 vi:16 vv:16 ch:16 ow:16 ah:16 Z:16 ki:20 pm:20 Zi:192 Zm:192
+f X:2368 Y:2368 J:256 col:32 sw:20 swa:20 swb:20 U:136 dm:16 fo:16 fo2:16 Sx:256 Ks:256 hb:16 rk:16 RT:160 cc:256 CHf:256 xg:256
+f iv:16 iv2:16 own:16 R4:4,32 R50:5,32 R51:5,32 SL0:2304 SL1:2304 LA0:320 LA1:320 Q0:160 Q1:480 QW:320 Q2:320 dd:3840 iv3:20 w1:320
+f MX:16 ck:320 DS:320 t3:20 IF:128
+i XI:2048 X1:2048 pp_i:1 pq_i:1 pr_i:1 hp:16 hq:16 vi:16 vv:16 ch:16 ow:16 ah:24 Z0:10 Z1:30 st0:10 st1:30 pm:20 Zi0:64 Zm0:64 Zi1:192 Zm1:192 KM:240
 i hi:2,16 ha:2,16 ci:4,8 ca:4,8 ai5:5,8 aa5:5,8
-h cnt:128 EB:128 cb:16 Dh:16,16 VK:256 VV:256 TK:256 VB:256 R1:256 m1:256 CH:16,16 s9:153 A16:20,16 uh:16 ZH0:64 ZH1:192 pvh:20
-b HM:4096 NZ:2064 SG:2048 SR:16,130 Lb:130 cmp:2048 G:256 Ca:256 Cr:256 Cb:256 sC:256 Fb:256 Fl:256 Lg:2048 Mn:16,128 MV:2048 th:256 sD:16,16
-b sE:256 ab:256 fsq:256 fsg:256 O:153 m17:153 sq:20,12,16 k1:20,16 k2:20,16 k3:16 k4:16 ra:320 rs:320 esq:320 esg:320 EQ:320 EQ3:16,64
+h cnt:128 EB:128 cb:16 Dh:16,16 VK:256 VV:256 TK:256 VB:256 R1:256 m1:256 CH:16,16 s9:153 A16:20,16 uh:24 ZH0:64 ZH1:192 pvs:320 PB:4,80
+b HM:4096 NZ:2064 SG:2048 SR:16,130 Lb:130 cmp:2048 G:256 Ca:416 Cb:256 sC:256 Fb:256 Fl:256 Lg:1536 Mn:16,96 MV:2560 th:256 sD:16,16
+b sE:256 ab:256 fsq:256 fsg:256 O:153 m17:153 sq:3840 k1:240 k2:240 ra:320 rs:320 esq:320 esg:320 EQ:320 EQ3:16,64
 b Jb:256 JI:320 JG:128 PD:128 zero:128 ones:256 BH:128 ZS:144 TX0:130 TX1:130 MK:4 WL:8 base:64 kx:128 kc:128 e0:128 TI:128 NU:128
 b SU:128 SD:128 PAR:128 PA2:128 AL:128 B592:128 I592:8 WT:16 EH:144 OH:144 E1:144 O1:144 TE:130 TO:130 CR1:128 CR2:128 c9:16
-b m16:320 dk:256 mB:320 CM:320 RX:2048 IM:1408 cz0:64 cz1:192 kc2:20,16 I1:128 Im1:128 I256n:128 I256:128 I4kn:128
-b I64k:128 I16kn:128 I64n:128
-u cu:16 plu:16 fou:16 Du:256 DT:128 slu:16 zu0:64 zu1:192 pu:20 eou:4,6
+b m16:320 dk:256 mB:240 CM:320 RX:2048 IM:1408 cz0:64 cz1:192 kc2:240 I1:128 Im1:128 I256n:128 I256:128 I4kn:128
+b I64k:128 I16kn:128 I32kn:128 I64n:128
+u cu:16 plu:16 fou:16 Du:256 DT:160 slu:16 zu0:64 zu1:192 pu:20 eou:4,6
 """
 _ALL, SCRATCH, _AT = {}, {}, {}
 for _line in _SBUF.split("\n"):
@@ -49,8 +50,8 @@ for _d, _c in _wide.items():
     SCRATCH["pack_" + _d] = ("sbuf", [128, _c], _d)
 SEMAPHORES = ["sv", "ss", "sp", "sg", "loc", "ar0", "ar1", "an0", "an1"] + ["d%d" % k for k in range(7)]
 
-CYC, PE, WAKE, GATHER, SCATTER = 0.83, 0.42, 80.0, 1.56, 3.0
-LOAD, SEND, NEAR, FAR, FIRST = 1500.0, 700.0, 2200.0, 4200.0, 2500.0
+CYC, PE, WAKE, GATHER, SCATTER = 0.83, 0.42, 120.0, 1.56, 3.0
+ACT, LOAD, SEND, NEAR, FAR, FIRST = 100.0, 1500.0, 700.0, 2400.0, 5500.0, 2500.0
 
 
 def routes(src, T, topo):
@@ -62,7 +63,7 @@ def routes(src, T, topo):
     n = len(eng)
     out = [(0, d, eng[k * n // 4:(k + 1) * n // 4]) for k, d in enumerate(far[:4])]
     out += [(1, d, eng[k * n // 2:(k + 1) * n // 2]) for k, d in enumerate(far[4:])]
-    return out + [(0, d, [e for e in topo.engines(src, d) if e not in eng][:4]) for d in near]
+    return out + [(0, d, [e for e in topo.engines(src, d) if e not in eng][::2]) for d in near]
 
 
 def landing(dst, T, topo):
@@ -76,11 +77,11 @@ def order_calls(calls):
     for i, c in enumerate(calls):
         for d in c[3]:
             users[d].append(i)
-    gap = lambda d, i: 0.0 if calls[d][0] == calls[i][0] == "p" else WAKE
+    gap = lambda d, i: 0.0 if calls[d][0] == calls[i][0] == "p" or d == calls[i][5] else WAKE
     for i in range(n - 1, -1, -1):
         tail[i] = calls[i][2] + max([tail[u] + gap(i, u) for u in users[i]], default=0.0)
     start, busy = [0.0] * n, {}
-    for i in sorted(range(n), key=lambda i: (-tail[i], i)):
+    for i in sorted(range(n), key=lambda i: (-tail[i + calls[i][4]], i)):
         t = max([start[d] + calls[d][2] + gap(d, i) for d in calls[i][3]], default=0.0)
         line, k = busy.setdefault(calls[i][0], []), 0
         while k < len(line) and line[k][0] < t + calls[i][1]:
@@ -108,7 +109,7 @@ def rank_program(g, core, T, topo):
         on = np.zeros(sh[1:], bool)
         on[ix] = True
         bits = -1 if w == "psum" else int.from_bytes(np.packbits(on).tobytes(), "little")
-        return T[n][(full,) + ix], [(n, bits)], int(on.sum()), dt in ("bfloat16", "float16", "uint16"), w == "psum", False
+        return T[n][(full,) + ix], [(n, bits)], int(on.sum()), dt in ("bfloat16", "float16", "uint16"), w == "psum", False, ix[0]
 
     def b(n, lo=0, hi=None, step=1):
         sh = _ALL[n][1]
@@ -124,10 +125,13 @@ def rank_program(g, core, T, topo):
             return b3(n, slice(lo // k, hi // k))
         return b3(n, slice(lo // k, -(-hi // k)), lo % k)
 
+    def rows(x, lo, hi):
+        return (T[x[1][0][0]][lo:hi, x[6]],) + x[1:] + (lo,)
+
     def ind(w, o):
         return w[0].indirect(o[0]), w[1] + o[1], 16 * o[2], False, False, True
 
-    def op(e, call, outs, ins, cost, late=None, sem=None):
+    def op(e, call, outs, ins, cost, late=None, sem=None, more=0):
         i, need = len(calls), set()
         outs = [(x[1][:1] if x[5] else x[1]) for x in outs], [x[1][1:] for x in outs if x[5]]
         for kind, keys in ((0, sum([x[1] for x in ins] + outs[1], [])), (1, sum(outs[0], []))):
@@ -137,9 +141,15 @@ def rank_program(g, core, T, topo):
                 if kind:
                     lst[:] = [r for r in lst if r[0] & ~bits]
                 lst.append((bits, kind, i, e))
-        calls.append((e, cost, cost if late is None else late, sorted(need)))
+        calls.append([e, cost, cost if late is None else late, sorted(need), more, None])
         emit.append((call, sem))
         return i
+
+    def row(ids):
+        for d, i in zip(ids, ids[1:]):
+            if d not in calls[i][3]:
+                calls[i][3].append(d)
+                calls[i][5] = d
 
     def vec(out, ins, per, fix=50.0):
         if out[5]:
@@ -155,10 +165,10 @@ def rank_program(g, core, T, topo):
     def ts(out, in0, s1, s2, op0, op1=None):
         ins = [in0] + [x for x in (s1, s2) if isinstance(x, tuple)]
         more = () if op1 is None else (op1,)
-        op("v", lambda: g.vector.tensor_scalar(out[0], in0[0], sc(s1), sc(s2), op0, *more), [out], ins, vec(out, ins, half(out, in0)))
+        return op("v", lambda: g.vector.tensor_scalar(out[0], in0[0], sc(s1), sc(s2), op0, *more), [out], ins, vec(out, ins, half(out, in0)))
 
     def tt(out, in0, in1, o):
-        op("v", lambda: g.vector.tensor_tensor(out[0], in0[0], in1[0], o), [out], [in0, in1], vec(out, [in0], 1 if in0[4] or in1[4] else 2))
+        return op("v", lambda: g.vector.tensor_tensor(out[0], in0[0], in1[0], o), [out], [in0, in1], vec(out, [in0], 1 if in0[4] or in1[4] else 2))
 
     def cp(out, in_):
         op("v", lambda: g.vector.tensor_copy(out[0], in_[0]), [out], [in_], vec(out, [in_], half(out, in_)))
@@ -171,13 +181,15 @@ def rank_program(g, core, T, topo):
 
     def act(out, in_, f=F.Identity, bias=0.0, scale=1.0):
         ins = [in_] + [x for x in (bias, scale) if isinstance(x, tuple)]
-        op("s", lambda: g.scalar.activation(out[0], in_[0], f, bias=sc(bias), scale=sc(scale)), [out], ins, vec(out, ins, 1, 65.0))
+        return op("s", lambda: g.scalar.activation(out[0], in_[0], f, bias=sc(bias), scale=sc(scale)), [out], ins,
+                  vec(out, ins, 1, 65.0) if in_[5] else ACT + in_[2] * CYC)
 
     def mm(out, terms):
         for k, (l, r, *part) in enumerate(terms):
             o = part[0] if part else out
-            op("p", lambda o=o, l=l, r=r, k=k: g.tensor.matmul(o[0], l[0], r[0], k == 0, k == len(terms) - 1), [o], [l, r],
-               max(min(64, l[2]), r[2]) * PE * (1 if l[3] else 4))
+            stop = not out or k == len(terms) - 1 or len(o) > 7 and all(x[2][7:] != o[7:] for x in terms[k + 1:])
+            op("p", lambda o=o, l=l, r=r, k=k, stop=stop: g.tensor.matmul(o[0], l[0], r[0], k == 0 or not out, stop),
+               [o], [l, r], max(min(64, l[2]), r[2]) * PE * (1 if l[3] else 4), more=len(terms) - 1 - k)
 
     def iota(out, pat, base, cm=0):
         small = {} if out[1][0][0] == "pack_int32" else {"allow_small_or_imprecise_dtypes": True}
@@ -244,7 +256,7 @@ def rank_program(g, core, T, topo):
         act(b("base", 32 * t + 16, 32 * t + 32), b("zero", 0, 16), bias=16.0 * c0)
     iota(b("JI"), [[0, 20], [1, 16]], 0)
     for n, c in (("I256n", -256.0), ("Im1", -1.0), ("IF", 256.0), ("I4kn", -4096.0), ("I256", 256.0), ("I64k", 65536.0),
-                 ("I16kn", -16384.0), ("I64n", -64.0)):
+                 ("I16kn", -16384.0), ("I32kn", -32768.0), ("I64n", -64.0)):
         ts(b(n), b("I1"), c, None, A.mult)
     ts(b("pq_i"), b("pp_i"), 1, None, A.bitwise_and)
     ts(b("pr_i"), b("pr_i"), 1, None, A.bitwise_and)
@@ -272,7 +284,6 @@ def rank_program(g, core, T, topo):
     act(b("PAR"), b("BH"), scale=SIG)
     act(b("PA2"), b("BH"), scale=SI2)
     act(b("swa"), b("sw"), bias=-float(TR))
-    act(b("swb"), b("sw"), bias=-float(TR + 1024))
     ts(b("m16"), b("JI"), 0.0, None, A.is_gt)
     ts(b("dk"), b("m16", 0, 256), 1023.0, -1024.0, A.mult, A.add)
     sel(b("SU"), b("BH"), diag, A.is_equal, 0.0, -1, 1)
@@ -286,19 +297,18 @@ def rank_program(g, core, T, topo):
     iota(b("c9", 0, 9), [[256, 9]], -1024)
     iota(b("O", 0, 153, 17), [[0, 9]], 0)
     sel(b("m17"), b("ones", 0, 153), [[0, 9], [1, 17]], A.not_equal, 0.0, -1, 0)
-    iota(b3("k1"), [[0, 320]], 0)
-    iota(b3("k2"), [[0, 320]], 0)
     sel(b("AL"), b("zero"), blk, A.not_equal, OFF, 0, 1)
     sel(b("AL"), b("AL"), blk, A.not_equal, -128.0, -1, 1)
     for o in range(N):
         iota(b("SL0", 256 * o, 256 * o + CAP), [[0, CAP]], SENT)
-    for m in range(1, NP):
-        ts(b("IM", 128 * m - 128, 128 * m), b("I1"), 2.0 * m, None, A.mult)
+    for m in range(3, NP):
+        ts(b("IM", 128 * m - 384, 128 * m - 256), b("I1"), 2.0 * m, None, A.mult)
     iota(b("cz0", 6, 61), [[1, 11], [0, 5]], 1)
     iota(b("cz1", 16, 181), [[1, 11], [0, 15]], 1)
-    iota(b3("kc2", full, slice(0, 12)), [[0, 20], [2048, 12]], -81920)
-    iota(b3("kc2", full, slice(12, 16)), [[0, 80]], 1 << 20)
-    ts(b("mB"), b("JI"), 0.0, 2.0 ** 21, A.is_equal, A.mult)
+    iota(b("kc2"), [[0, 20], [2048, 12]], -81920)
+    ts(b("pvs"), b("JI"), 0.0, None, A.mult)
+    iota(b("mB"), [[0, 240]], 0)
+    iota(b("mB", 0, 240, NP), [[0, 20]], 1 << 21)
     ts(b("CM"), b("JI"), PI, 0.5, A.is_ge, A.mult)
     ts(b("MX"), b("Jb", 0, 16), PI, None, A.is_equal)
     for x in range(16):
@@ -333,7 +343,7 @@ def rank_program(g, core, T, topo):
             act(b3("SR", full, 128), b("X", TR + 16 * c0, TR + 16 * c0 + 16), F.Sign)
             for x in range(16):
                 o, i = b3("SR", x, slice(0, 128)), b("X", TR + x, TR + V, 16)
-                act(o, i, F.Sign) if x % 2 else ts(o, i, 0.0, None, A.is_gt)
+                act(o, i, F.Sign) if x % 3 == 1 else ts(o, i, 0.0, None, A.is_gt)
             mm(b("B0", 0, 129), [(zs(x), b3("SR", x, slice(0, 129))) for x in range(16)]
                + [(I1, b("MK", 2, 4), b("B0", c0, 129, 128 - c0))])
         ts(b("Lb", 0, 129), b("B0", 0, 129), 0.0, None, A.is_gt)
@@ -349,7 +359,7 @@ def rank_program(g, core, T, topo):
                 ts(o, b("EB"), 16.0 * j, None, A.is_le)
             else:
                 act(o, b("EB"), F.Sign, bias=16.0 * j + 0.5, scale=-1.0)
-        turn = sorted(range(16), key=lambda j: j if j < 16 - NS else 2 * (j - 16 + NS) + 1.5)
+        turn = sorted(range(16), key=lambda j: j if j < 16 - NS else 4 * (j - 16 + NS) + 2.5)
         mm(b("B1", 0, 32), [(b("e0"), b("base", 32 * t, 32 * t + 32))]
            + [(b("cmp", 128 * j, 128 * j + 128), b("WL", 4 * t + 2 * (j >= 16 - NS), 4 * t + 2 * (j >= 16 - NS) + 2), b("B1", j, 32, 16)) for j in turn])
         cp(b("cu"), b("B1", 0, 16))
@@ -366,32 +376,33 @@ def rank_program(g, core, T, topo):
         ts(b("Du"), ind(win, b("plu")), 1.0 / 256.0, -off / 256.0, A.mult, A.add)
         act(b("Sx"), ind(win, b("plu")), F.Relu, bias=(128.0 - off) / 256.0, scale=1.0 / 256.0)
         tt(b("fo"), b("dm"), b("B2", 0, 16), A.add)
-        for h in (0, 128):
-            ts(b("Dh", h, h + 128), b("Du", h, h + 128), -2048.0, None, A.add)
+        for lo, hi in ((NA, S), (0, NA)):
+            ts(b("Dh", lo, hi), b("Du", lo, hi), -2048.0, None, A.add)
         CB0 = -524288.0 - 128.0
-        for par, n in ((0, "TE"), (1, "TO")):
-            mm(b3("C0", slice(par, 8, 2)), [(b(n, 1 - u, 129 - u), b("Dh", 64 * u, 64 * u + 64)) for u in (0, 1)])
-        for h in (0, 128):
-            mm(b("B3", h, h + 128), [(b("IF"), b("Sx", h, h + 128)), (b("I256n"), b("Dh", h, h + 128))])
-            act(b("Ca", h, h + 128), b("B3", h, h + 128), F.Abs, bias=CB0)
-        vtr(b("RT"), b("C0", 0, 128))
-        for k in range(4):
-            ts(b("DT", k, 128, 4), b("RT", 32 * k, 32 * k + 32), 2048.0, None, A.add)
-        for h in (0, 128):
-            cp(b("Cr", h, h + 128), b("Ca", 0, 128))
+        mm(b("C0", 0, NV), [(b(n, 1 - u, 129 - u), b("Dh", NA + 80 * u, NA + 80 * u + 80), b3("C0", slice(par, 10, 2)))
+                            for par, n in ((0, "TE"), (1, "TO")) for u in (0, 1)])
+        mm(b("B3", 0, S), [(b("IF"), b("Sx")), (b("I256n"), b("Dh"))])
+        first = act(b("Ca", 0, S), b("B3", 0, S), F.Abs, bias=CB0)
+        vtr(b("RT"), b("C0", 0, NV))
+        for k in range(5):
+            ts(b("DT", k, NV, 5), b("RT", 32 * k, 32 * k + 32), 2048.0, None, A.add)
+        cp(b("Ca", S, S + NV), b("Ca", NA, S))
         for h in range(2):
             mm(b("B0", 16 * h, 16 * h + 16), [(b("Dh", 128 * h, 128 * h + 128), b("WT"))])
-        for k in range(0, 16, 2):
-            tt(b("MV", 128 * k, 128 * k + 256), ind(b("HM"), b("DT", 8 * k, 8 * k + 16)), b("Cr"), A.min)
-        mm(b("B1", 0, 128), [(b("e0"), b("kc"))] + [(b("MV", 128 * k, 128 * k + 128), b("B592", 0, 128, 16), b("B1", k, 128, 16)) for k in range(16)])
-        for q in range(4):
-            act(b("Lg", *q4(q)), ind(b("HM"), b("Du", 128 + 32 * q, 160 + 32 * q)), F.Copy)
-        for q, kk, bank in ((0, 0, "C1"), (0, 8, "C2"), (1, 0, "C0"), (1, 8, "C1")):
-            for k in range(8):
-                mm(b(bank, 64 * k, 64 * k + 64), [(Im1, b("Lg", 1024 * q + kk + k, 1024 * q + 1024, 16)), (I1, b("Ca", 128 + 64 * q, 192 + 64 * q))])
-            act(b3("Mn", slice(kk, kk + 8), slice(64 * q, 64 + 64 * q)), b(bank), F.Relu)
-        mm(b("B2", 0, 128), [(b("e0"), b("kc")), (b("Ca", 128, 256), b("B592"))]
-           + [(b3("Mn", k), b("I592"), b("B2", k, 128, 16)) for k in range(16)])
+        row([tt(b("MV", NV * k0, NV * k1), ind(b("HM"), b("DT", 10 * k0, 10 * k1)), b("Ca", NA, NA + NV * (k1 - k0)), A.min)
+             for k0, k1 in [(0, 1)] + [(k, k + 2) for k in range(1, 15, 2)] + [(15, 16)]])
+        mm(b("B2", 0, 128), [(b("e0"), b("kc"))] + [(b("MV", NV * k + 32, NV * k + NV), b("B592", 0, 128, 16), b("B2", k, 128, 16)) for k in range(16)])
+        look = [act(b("Lg", 16 * lo, 16 * hi), ind(b("HM"), b("Du", lo, hi)), F.Copy) for lo, hi in ((0, 32), (32, NA))]
+        row([first, look[1]])
+        for lo, hi, k0, k1, bank in ((0, 32, 0, 16, "C1"), (32, NA, 0, 8, "C2"), (32, NA, 8, 16, "C0")):
+            w = hi - lo
+            mm(b(bank), [x for k in range(k1 - k0) for x in ((Im1, b("Lg", 16 * lo + k0 + k, 16 * hi, 16), b(bank, w * k, w * k + w)),
+                                                             (I1, b("Ca", lo, hi), b(bank, w * k, w * k + w)))])
+            act(b3("Mn", slice(k0, k1), slice(lo, hi)), b(bank), F.Relu)
+        mm(b("B1", 0, 128), [(b("e0"), b("kc")), (b("Ca", 0, NA), b("B592"), rows(b("B1", 0, 128), 0, NA))]
+           + [(b("MV", NV * k, NV * k + 32), b("B592", 0, 128, 16), rows(b("B1", k, 128, 16), NA, 128)) for k in range(11)]
+           + [(b3("Mn", k), b("I592"), rows(b("B1", k, 128, 16), 0, NA)) for k in range(16)]
+           + [(b("MV", NV * k, NV * k + 32), b("B592", 0, 128, 16), rows(b("B1", k, 128, 16), NA, 128)) for k in range(11, 16)])
         cp(b3("hi"), b("B0", 0, 32))
         ts(b3("ha"), b3("hi"), 4095, None, A.bitwise_and)
         tt(b("hp"), b3("ha", full, slice(0, 8)), b3("ha", full, slice(8, 16)), A.mult)
@@ -414,18 +425,16 @@ def rank_program(g, core, T, topo):
         DH, ONE = b("Dh"), b("ones")
         mm(b("B0", 0, 256), [(b("SU"), DH), (b("CR1"), ONE)] + turned("B0", "TK", b("I4kn")))
         tt(b("R1"), DH, b("B0", 0, 256), A.max)
-        for term in turned("B3", "VB", I1):
-            mm(None, [term])
+        mm(None, turned("B3", "VB", I1))
         mm(b("B1", 0, 256), [(b("CR2"), ONE), (b("SD"), b("R1"))])
         tt(b("m1"), b("R1"), b("B3", 0, 256), A.min)
         tt(b("CH"), b("m1"), b("B1", 0, 256), A.max)
         mm(b("C1", 0, 256), [(I1, DH)] + turned("C1", "VB", Im1))
         act(b("sD"), b("C1", 0, 256), F.Sign)
-        for par, ns, nh in ((0, "E1", "EH"), (1, "O1", "OH")):
-            mm(b3("C2", slice(par, 8, 2)), [(b(ns, 3 - j, 131 - j), b3("sD", slice(j, None, 4))) for j in range(4)]
-               + [(b(nh, 6 - 2 * j, 134 - 2 * j), b3("CH", slice(j, None, 4))) for j in range(4)])
-        for term in turned("C0", "TK", I1):
-            mm(None, [term])
+        mm(b("C2", 0, 128),
+           [(b(n, 3 - j, 131 - j), b3("sD", slice(j, None, 4)), b3("C2", slice(par, 8, 2))) for par, n in ((0, "E1"), (1, "O1")) for j in range(4)]
+           + [(b(n, 6 - 2 * j, 134 - 2 * j), b3("CH", slice(j, None, 4)), b3("C2", slice(par, 8, 2))) for par, n in ((0, "EH"), (1, "OH")) for j in range(4)])
+        mm(None, turned("C0", "TK", I1))
         act(b("th"), b("C0", 0, 256), F.Sign, bias=7.5)
         mm(b("B2", 0, 256), [(I1, b("R1"))] + turned("B2", "VB", Im1))
         act(b("sE"), b("B2", 0, 256), F.Sign)
@@ -467,6 +476,7 @@ def rank_program(g, core, T, topo):
                     src=T[SL][:, 256 * o:256 * o + CAP], dst=T[LA][:, at:at + CAP]))
                 sent[0] += len(eng)
             sends.append(op("g", lambda tr=tr: g.remote_dma_fused(tr, local_sem=T.sem.loc), [], [b(SL)], SEND, None, ("", 0)))
+        row(sends)
         for nr in (True, False):
             there = [d for d in T.cores if d != core and (topo.chip(d) == topo.chip(core)) == nr]
             tot = sum(len(e) for s in there for _, x, e in plan[s] if x == core)
@@ -488,10 +498,11 @@ def rank_program(g, core, T, topo):
 
         def flagged(out, in_, at, o):
             for k in range(4):
-                mm(b("C3"), [(b("AL"), b("SG", *q4(k)))])
+                bank = "C0" if k % 2 else "C3"
+                mm(b(bank), [(b("AL"), b("SG", *q4(k)))])
                 for h in (0, 256):
                     lo = 512 * k + h
-                    tt(b(out, TR + lo, TR + lo + 256), b(in_, at + lo, at + lo + 256), b("C3", h, h + 256), o)
+                    tt(b(out, TR + lo, TR + lo + 256), b(in_, at + lo, at + lo + 256), b(bank, h, h + 256), o)
         if t == 0:
             flagged("X", "XI", 0, A.add)
         cp(ind(b("X"), b("fou")), b("xg"))
@@ -500,69 +511,83 @@ def rank_program(g, core, T, topo):
                 act(b("SG", *q4(k)), b("X", TR + 512 * k, TR + 512 * k + 512), F.Sign)
             flagged("Y", "X", TR, A.subtract)
 
-        score = [(b("e0"), b3("kc2"))]
-        banks = ["C0", "C2", "C1", "C0"]
+        score = [(b("e0"), b("kc2"))]
+        banks, probes = ["C0", "C2", "C1", "C0"], []
         for part in range(2):
             c1, c2 = PART[part]
             w = c2 - c1
-            n, ways, a0, z0 = 16 * w, w // 5, 16 * c1, 960 * part
-            cs = slice(c1, c2)
-            A16 = b3("A16", cs)
-            zu, ZH, cz, Q = "zu%d" % part, "ZH%d" % part, "cz%d" % part, "Q%d" % part
+            n, ways, a0, z0, s0, q0 = 16 * w, w // 5, 16 * c1, 960 * part, 16 - 16 * part, 6 - 6 * part
+            A16 = b3("A16", slice(c1, c2))
+            zu, ZH, Zi, Zm, cz, Q, R, Z, st = [x + str(part) for x in ("zu", "ZH", "Zi", "Zm", "cz", "Q", "R5", "Z", "st")]
             at = [0] + [w + 1 + w * m for m in range(NP)]
-            u1, u2 = b3("aa5", full, slice(0, 2 * ways, 2)), b3("aa5", full, slice(1, 2 * ways, 2))
-            ai5, aa5, R5 = [b3(x, full, slice(0, 2 * ways)) for x in ("ai5", "aa5", "R5")]
+            u1, u2 = b3("aa5", full, slice(q0, q0 + 2 * ways, 2)), b3("aa5", full, slice(q0 + 1, q0 + 2 * ways, 2))
+            ai5, aa5 = [b3(x, full, slice(q0, q0 + 2 * ways)) for x in ("ai5", "aa5")]
+            ah, uh = [b(x, s0, s0 + w) for x in ("ah", "uh")]
             hb = "C%d" % (2 - part)
             ts(A16, b(LA, a0, a0 + n), M23, -M23, A.add, A.add)
-            for par, nh in ((0, "EH"), (1, "OH")):
-                mm(b3(hb, slice(par, 10, 2)), [(b(nh, 6 - 2 * j, 134 - 2 * j), b3("A16", slice(c1 + j, c2, ways))) for j in range(ways)])
-            groups = [(0, 1), (1, 3), (3, 5), (5, 7), (7, 9), (9, 11), (11, 12)] if part else [(0, 1), (1, 5), (5, 9), (9, 12)]
-            for k in range(groups[1][1] - 1):
+            mm(b(hb, 0, 160), [(b(nh, 6 - 2 * j, 134 - 2 * j), b3("A16", slice(c1 + j, c2, ways)), b3(hb, slice(par, 10, 2)))
+                               for par, nh in ((0, "EH"), (1, "OH")) for j in range(ways)])
+            groups = [(0, 1), (1, 3), (3, 5), (5, 7), (7, 9), (9, 11), (11, 12)]
+            for k in range(2):
                 act(b(Q, n * k, n * k + n), A16, bias=524288.0 + OFF - M31, scale=256.0)
-            vtr(b3("R5"), b(hb, 0, 160))
-            cp(ai5, R5)
+            vtr(b3(R), b(hb, 0, 160))
+            cp(ai5, b3(R, full, slice(0, 2 * ways)))
             ts(aa5, ai5, 4095, None, A.bitwise_and)
-            tt(b("ah", 0, w), u1, u2, A.mult)
-            act(b("uh", 0, w), u1, bias=-2048.0)
-            ts(b("Z", 0, w), b("ah", 0, w), 8, V - 1, A.arith_shift_right, A.bitwise_and)
-            cp(b(zu, 0, w), b("Z", 0, w))
-            act(b(ZH, 0, w), b("Z", 0, w))
-            for m0, m1, bank in ((1, 5, "B0"), (5, NP, "B2")):
+            tt(ah, u1, u2, A.mult)
+            ts(uh, u1, -2048.0, None, A.add)
+            for m in (1, 2):
+                ts(b(st, w * m - w, w * m), u1, 2.0 * m, float(m), A.mult, A.add)
+            for m in (0, 1):
+                ts(b(Z, w * m, w * m + w), ah, 8, V - 1, A.arith_shift_right, A.bitwise_and)
+            cp(b(zu, 0, w), b(Z, 0, w))
+            cp(b(ZH, 0, w), b(Z, 0, w))
+            for m0, m1, bank in ((1, 3, None), (3, NP, "B%d" % (2 * part))):
                 r = (at[m0], at[m1])
-                mm(b(bank, *r), [(b("e0"), b(cz, *r))]
-                   + [(b("IM", 128 * m - 128, 128 * m), b("uh", 0, w), b(bank, at[m], at[m] + w)) for m in range(m0, m1)]
-                   + [(I1, b(ZH, 0, w), b(bank, at[m], at[m] + w)) for m in range(m0, m1)])
-                act(b("Zi", *r), b(bank, *r))
-                ts(b("Zm", *r), b("Zi", *r), V - 1, None, A.bitwise_and)
-                act(b(zu, *r), b("Zm", *r))
-                act(b(ZH, *r), b("Zm", *r))
-            score += [(I1, b(ZH, at[m], at[m] + w), b("B1", a0 + m, a0 + n, 16)) for m in range(NP)]
+                if bank:
+                    mm(b(bank, *r), [(b("e0"), b(cz, *r))]
+                       + [(b("IM", 128 * m - 384, 128 * m - 256), uh, b(bank, at[m], at[m] + w)) for m in range(m0, m1)]
+                       + [(I1, b(ZH, 0, w), b(bank, at[m], at[m] + w)) for m in range(m0, m1)])
+                    cp(b(Zi, *r), b(bank, *r))
+                else:
+                    tt(b(Zi, *r), b(Z, 0, 2 * w), b(st, 0, 2 * w), A.add)
+                ts(b(Zm, *r), b(Zi, *r), V - 1, None, A.bitwise_and)
+                cp(b(zu, *r), b(Zm, *r))
+                cp(b(ZH, *r), b(zu, *r))
+            into = [b("B1", NP * c1 + m, NP * c2, NP) for m in range(NP)]
+            score += [(I1, b(ZH, at[m], at[m] + w), into[m]) for m in range(NP)]
             for m0, m1 in groups:
-                tt(b("dd", z0 + n * m0, z0 + n * m1), ind(XW, b(zu, at[m0], at[m0] + w * (m1 - m0))), b(Q, 0, n * (m1 - m0)), A.subtract)
+                d = (z0 + n * m0, z0 + n * m1)
+                probes.append(tt(b("dd", *d), ind(XW, b(zu, at[m0], at[m0] + w * (m1 - m0))), b(Q, 0, n * (m1 - m0)), A.subtract))
+                if part or m1 in (5, NP):
+                    d = d if part else (n * (0 if m1 == 5 else 5), n * m1)
+                    act(b("sq", *d), b("dd", *d), F.Square, bias=-M31 / 256.0, scale=1.0 / 256.0)
+            for m0, m1 in ((0, 5), (5, 9), (9, NP)) if part else ((0, NP),):
+                bank = b3(banks.pop(0), slice(0, m1 - m0), slice(0, w))
+                mm(bank, [(zs(x), b("sq", z0 + n * m0 + x, z0 + n * m1, 16)) for x in range(16)])
+                k = (NP * c1 + w * m0, NP * c1 + w * m1)
+                if m0 < 9:
+                    act(b("k1", *k), bank, F.Sign)
+                    act(b("k2", *k), bank, F.Sign, bias=-THETA)
+                else:
+                    ts(b("k1", *k), bank, 0.0, None, A.is_gt)
+                    ts(b("k2", *k), bank, THETA, -0.5, A.is_gt, A.add)
                 for m in range(m0, m1):
-                    act(b3("sq", cs, m), b("dd", z0 + n * m, z0 + n * m + n), F.Square, bias=-M31 / 256.0, scale=1.0 / 256.0)
-            for ms in (slice(0, 7), slice(7, 11), 11) if part else (slice(0, 12),):
-                bank = b3(banks.pop(0), cs, ms)
-                mm(bank, [(zs(x), b3("sq", cs, ms, x)) for x in range(16)])
-                act(b3("k1", cs, ms) if ms != 11 else b("k3", 0, w), bank, F.Sign)
-                act(b3("k2", cs, ms) if ms != 11 else b("k4", 0, w), bank, F.Sign, bias=-THETA)
-        last = b("B1", a0 + 11, AR, 16)
-        mm(b("B1", 0, AR), score + [(b("I64k"), b3("k1")), (b("I16kn"), b3("k2")), (b("I64k"), b("k3", 0, w), last), (b("I16kn"), b("k4", 0, w), last)])
+                    k = (NP * c1 + w * m, NP * c1 + w * m + w)
+                    score += [(b("I64k"), b("k1", *k), into[m]), (b("I16kn" if m0 < 9 else "I32kn"), b("k2", *k), into[m])]
+        row(probes)
+        mm(b("B1", 0, 240), score)
         act(b("QW"), b3("A16"), bias=524288.0 + OFF, scale=256.0)
-        scan(b("KM"), b("mB"), b("B1", 0, AR), A.add, A.min)
-        km = b("KM", 15, AR, 16)
-        cp(b("ki"), km)
+        scan(b("KM"), b("mB"), b("B1", 0, 240), A.add, A.min)
+        km = b("KM", 11, 240, NP)
+        ts(b("pm"), km, V - 1, None, A.bitwise_and)
         ts(b("iv3"), km, 0.0, -4096.0, A.is_ge, A.mult)
-        ts(b("pm"), b("ki"), V - 1, None, A.bitwise_and)
-        ts(b("iv3"), b("iv3"), -1024.0, None, A.add)
-        tt(b("pvh"), b("pm"), b("iv3"), A.add)
+        pvh = b("pvs", 0, AR, 16)
+        tt(pvh, b("pm"), b("iv3"), A.add)
         cp(b("pu"), b("pm"))
-        for x in range(16):
-            mm(b("C1", x, AR, 16), [(b("RX", 128 * x, 128 * x + 128), b("pvh"))])
-        act(b3("Pr"), b("C1", 0, AR))
-        for x in range(16):
-            mm(b("C2", x, AR, 16), [(I1, b("pvh"))])
-        mm(b("B0", 0, AR), [(I1, b("CM"))] + [(I1, b("pvh"), b("B0", x, AR, 16)) for x in range(16)])
+        for k in range(4):
+            scan(b3("PB", k), b("m16", 0, 80), b("pvs", 80 * k, 80 * k + 80), A.mult, A.add)
+        mm(None, [(b("RX", 128 * x, 128 * x + 128), pvh, b("C2", x, AR, 16)) for x in range(16)])
+        mm(b("B0", 0, AR), [(I1, b("CM"))] + [(b("RX", 128 * x, 128 * x + 128), pvh, b("B0", x, AR, 16)) for x in range(16)])
         tt(b("w1"), ind(XW, b("pu")), b("QW"), A.subtract)
         act(b("ra"), b("w1"), F.Relu, bias=128.0)
         act(b("rs"), b("w1"), F.Sign, bias=128.0)
@@ -571,23 +596,21 @@ def rank_program(g, core, T, topo):
             act(b("esq"), b("B3", 0, AR), F.Square, bias=-64.0)
         ts(b("ck"), b("B3", 0, AR), 191.0, -63.0, A.min, A.max)
         if t < RO - 1:
-            mm(b("B2", 0, AR), [(b("BH"), b("esq"))])
-            act(b("esg"), b("B2", 0, AR), F.Sign, bias=-0.5)
+            mm(b("C1", 0, AR), [(b("BH"), b("esq"))])
+            act(b("esg"), b("C1", 0, AR), F.Sign, bias=-0.5)
             mm(b("C0", 0, AR), [(b("I256"), b3("A16")), (b("AL"), b("esg"))])
             act(b("Q2"), b("C0", 0, AR), bias=524288.0 + 64.0)
         else:
             act(b("Q2"), b3("A16"), bias=524288.0 + 64.0, scale=256.0)
-        tt(b("EQ"), b3("Pr"), b("B0", 0, AR), A.is_equal)
-        for d in range(1, BW):
-            for k in range(d, BW):
-                tt(b3("EQ3", slice(4 * d - 4, 4 * d), slice(16 * (k - d), 16 * (k - d + 1))), b3("Pr", slice(k - d, 20, BW)),
-                   b3("C2", slice(k, 20, BW)), A.is_equal)
-        mm(b("B1", 0, AR), [(b("I4kn"), b("EQ")), (I1, b("pvh"), b("B1", 0, AR, 16))]
+        row([tt(b3("EQ3", slice(4 * d - 4, 4 * d), slice(16 * (k - d), 16 * (k - d + 1))), b3("PB", full, slice(16 * k, 16 * k + 16)),
+                b3("C2", slice(k - d, 20, BW)), A.is_equal) for d in range(1, BW) for k in range(d, BW)]
+            + [tt(b("EQ"), b3("PB"), b("B0", 0, AR), A.is_equal)])
+        mm(b("B1", 0, AR), [(b("zero"), b("m16")), (I1, pvh, b("B1", 0, AR, 16))]
            + [(b("I4kn"), b3("EQ3", 4 * d - 4 + k, slice(0, 16 * (BW - d))), b("B1", 16 * (BW * k + d), 16 * BW * (k + 1)))
-              for d in range(1, BW) for k in range(4)])
+              for d in range(1, BW) for k in range(4)] + [(b("I4kn"), b("EQ"))])
         scan(b("DS"), b("m16"), b("B1", 0, AR), A.mult, A.add)
-        tt(b("t3"), b("DS", 15, AR, 16), b("swb"), A.max)
-        ts(b3("eou", full, slice(0, BW)), b("t3"), float(TR + 1024), None, A.add)
+        tt(b("t3"), b("DS", 15, AR, 16), b("swa"), A.max)
+        ts(b3("eou", full, slice(0, BW)), b("t3"), float(TR), None, A.add)
         for k in sorted(range(N // near), key=lambda k: -land[core][near * k]):
             q = (16 * BW * k, 16 * BW * (k + 1))
             tt(ind(b("X" if t < RO - 1 else "Y"), b3("eou", k, slice(0, BW))), b("ck", *q), b("Q2", *q), A.add)
@@ -603,7 +626,7 @@ def rank_program(g, core, T, topo):
             mark[i] = (sem[0], sem[1], {})
             continue
         kn = known[e]
-        for s, v, seen in sorted((mark[d] for d in calls[i][3] if not (e == calls[d][0] == "p")), key=lambda x: (x[0] == semof.get(e), -x[1])):
+        for s, v, seen in sorted((mark[d] for d in calls[i][3] if not (e == calls[d][0] == "p" or d == calls[i][5])), key=lambda x: (x[0] == semof.get(e), -x[1])):
             if s and kn.get(s, 0) < v:
                 queue[e].wait_ge(T.sem[s], v)
                 for s2, v2 in list(seen.items()) + [(s, v)]:

@@ -10,25 +10,28 @@ M27 = 1.5 * 2.0 ** 27
 M23 = 1.5 * 2.0 ** 23
 OFF = 2.0 ** 22
 SENT = -22528
-THETA = 1.14e10
+THETA = 7.05e8
+VF, VN, SK = (1, 5, 9, 11), ((0, 7),), ()
+PASSES, AHEAD, KA, KB, KC, CN = 2, 2, 13, 17, 21, 5
+ZS_ = 0
 NS = 3
-NA, NV = 96, 160
+NV = 64
 
 _DT = {"f": "float32", "b": "bfloat16", "h": "float16", "i": "int32", "u": "uint16"}
 _SBUF = """
-f X:2368 Y:2368 J:256 col:32 sw:20 swa:20 swb:20 U:136 dm:16 fo:16 fo2:16 Sx:256 Ks:256 hb:16 rk:16 RT:160 cc:256 CHf:256 xg:256
-f iv:16 iv2:16 own:16 R4:4,32 R50:5,32 R51:5,32 SL0:2304 SL1:2304 LA0:320 LA1:320 Q0:160 Q1:480 QW:320 Q2:320 dd:3840 iv3:20 w1:320
-f MX:16 ck:320 DS:320 t3:20 IF:128
+f X:2368 Y:2368 J:256 col:32 sw:20 swa:20 swb:20 U:136 dm:16 fo:16 fo2:16 Sx:256 Ks:256 hb:16 rk:16 cc:256 CHf:256 xg:256
+f iv:16 iv2:16 own:16 R4:4,32 R50:5,32 R51:5,32 SL0:2304 SL1:2304 LA0:320 LA1:320 dd:3840 iv3:20 w1:320
+f MX:16 Q1:480 iv4:20 xq:320 ft:320 cq:320 xm:320 cn:320 DS:320 t3:20 IF:128
 i XI:2048 X1:2048 pp_i:1 pq_i:1 pr_i:1 hp:16 hq:16 vi:16 vv:16 ch:16 ow:16 ah:24 Z0:10 Z1:30 st0:10 st1:30 pm:20 Zi0:64 Zm0:64 Zi1:192 Zm1:192 KM:240
 i hi:2,16 ha:2,16 ci:4,8 ca:4,8 ai5:5,8 aa5:5,8
-h cnt:128 EB:128 cb:16 Dh:16,16 VK:256 VV:256 TK:256 VB:256 R1:256 m1:256 CH:16,16 s9:153 A16:20,16 uh:24 ZH0:64 ZH1:192 pvs:320 PB:4,80
-b HM:4096 NZ:2064 SG:2048 SR:16,130 Lb:130 cmp:2048 G:256 Ca:416 Cb:256 sC:256 Fb:256 Fl:256 Lg:1536 Mn:16,96 MV:2560 th:256 sD:16,16
-b sE:256 ab:256 fsq:256 fsg:256 O:153 m17:153 sq:3840 k1:240 k2:240 ra:320 rs:320 esq:320 esg:320 EQ:320 EQ3:16,64
-b Jb:256 JI:320 JG:128 PD:128 zero:128 ones:256 BH:128 ZS:144 TX0:130 TX1:130 MK:4 WL:8 base:64 kx:128 kc:128 e0:128 TI:128 NU:128
-b SU:128 SD:128 PAR:128 PA2:128 AL:128 B592:128 I592:8 WT:16 EH:144 OH:144 E1:144 O1:144 TE:130 TO:130 CR1:128 CR2:128 c9:16
-b m16:320 dk:256 mB:240 CM:320 RX:2048 IM:1408 cz0:64 cz1:192 kc2:240 I1:128 Im1:128 I256n:128 I256:128 I4kn:128
-b I64k:128 I16kn:128 I32kn:128 I64n:128
-u cu:16 plu:16 fou:16 Du:256 DT:160 slu:16 zu0:64 zu1:192 pu:20 eou:4,6
+h EB:128 cb:16 Dh:16,16 VK:256 VV:256 TK:256 VB:256 R1:256 m1:256 CH:16,16 s9:153 A16:20,16 uh:24 ZH:240 pvs:320 pv0:320 P0:320 PB:4,80
+b HM:4096 NZ:2048 SG:2048 SR:2064 Lb:130 PL:130 cmp:2048 G:256 Cb:256 sC:256 Fb:256 Fl:256 Lg:4096 Mn:16,256 db:3840 th:256 sD:16,16
+b sE:256 ab:256 fsq:256 fsg:256 O:153 m17:153 sq:3840 k1:240 k2:240 ckb:320 esq:320 EQ:320 EQ3:16,64
+b Jb:256 JI:320 JG:128 PD:128 zero:128 ones:256 BH:128 ZS:144 MK:4 WL:8 base:64 kx:128 kc:128 e0:128 TI:128 NU:128
+b SU:128 SD:128 PAR:128 PA2:128 AL:128 I592:8 WT:16 EH:144 OH:144 E1:144 O1:144 CQ:128 CR1:128 CR2:128 c9:16
+b m16:320 dk:256 RX:2048 IM:1408 cz0:64 cz1:192 kc2:240 mB:240 cT:20 I1:128 Im1:128 I256n:128 I256:128 I4kn:128
+b I64k:128 I16kn:128 I32kn:128 NUn:128
+u cu:16 plu:16 fou:16 Du:256 slu:16 zu0:64 zu1:192 pu:20 eou:4,6
 """
 _ALL, SCRATCH, _AT = {}, {}, {}
 for _line in _SBUF.split("\n"):
@@ -50,8 +53,8 @@ for _d, _c in _wide.items():
     SCRATCH["pack_" + _d] = ("sbuf", [128, _c], _d)
 SEMAPHORES = ["sv", "ss", "sp", "sg", "loc", "ar0", "ar1", "an0", "an1"] + ["d%d" % k for k in range(7)]
 
-CYC, PE, WAKE, GATHER, SCATTER = 0.83, 0.42, 120.0, 1.56, 3.0
-ACT, LOAD, SEND, NEAR, FAR, FIRST = 100.0, 1500.0, 700.0, 2400.0, 5500.0, 2500.0
+CYC, PE, WAKE, GATHER, SCATTER = 0.83, 0.42, 200.0, 1.56, 3.0
+ACT, DRAIN, LOAD, SEND, NEAR, FAR, FIRST = 65.0, 0.0, 1000.0, 700.0, 2200.0, 2800.0, 2500.0
 
 
 def routes(src, T, topo):
@@ -77,18 +80,38 @@ def order_calls(calls):
     for i, c in enumerate(calls):
         for d in c[3]:
             users[d].append(i)
-    gap = lambda d, i: 0.0 if calls[d][0] == calls[i][0] == "p" or d == calls[i][5] else WAKE
-    for i in range(n - 1, -1, -1):
+    gap = lambda d, i: calls[d][1] - calls[d][2] if calls[d][0] == calls[i][0] == "p" or d == calls[i][5] else WAKE
+    left = [len(u) for u in users]
+    turn = [i for i in range(n) if not left[i]]
+    for i in turn:
         tail[i] = calls[i][2] + max([tail[u] + gap(i, u) for u in users[i]], default=0.0)
-    start, busy = [0.0] * n, {}
-    for i in sorted(range(n), key=lambda i: (-tail[i + calls[i][4]], i)):
-        t = max([start[d] + calls[d][2] + gap(d, i) for d in calls[i][3]], default=0.0)
-        line, k = busy.setdefault(calls[i][0], []), 0
-        while k < len(line) and line[k][0] < t + calls[i][1]:
-            t, k = max(t, line[k][1]), k + 1
-        line.insert(k, (t, t + calls[i][1]))
-        start[i] = t
-    return sorted(range(n), key=lambda i: (start[i], i))
+        for d in calls[i][3]:
+            left[d] -= 1
+            if not left[d]:
+                turn.append(d)
+
+    def place(turn, back):
+        at, busy = [0.0] * n, {}
+        for i in turn:
+            c = calls[i]
+            if back:
+                t = max([at[u] + calls[u][1] + gap(i, u) for u in users[i]], default=0.0) + c[2] - c[1]
+            else:
+                t = max([at[d] + calls[d][2] + gap(d, i) for d in c[3]], default=0.0)
+            line, k = busy.setdefault(c[0], []), 0
+            while k < len(line) and line[k][0] < t + c[1]:
+                t, k = max(t, line[k][1]), k + 1
+            line.insert(k, (t, t + c[1]))
+            at[i] = t
+        return at
+
+    at = place(sorted(range(n), key=lambda i: (-tail[i + calls[i][4]], i)), False)
+    best = (max(at), at)
+    for _ in range(PASSES):
+        late = place(sorted(range(n), key=lambda i: (-at[i] - calls[i][1], -i)), True)
+        at = place(sorted(range(n), key=lambda i: (-late[i] - calls[i][1], i)), False)
+        best = min(best, (max(at), at))
+    return sorted(range(n), key=lambda i: (best[1][i], i))
 
 
 _ORDER = []
@@ -168,10 +191,11 @@ def rank_program(g, core, T, topo):
         return op("v", lambda: g.vector.tensor_scalar(out[0], in0[0], sc(s1), sc(s2), op0, *more), [out], ins, vec(out, ins, half(out, in0)))
 
     def tt(out, in0, in1, o):
-        return op("v", lambda: g.vector.tensor_tensor(out[0], in0[0], in1[0], o), [out], [in0, in1], vec(out, [in0], 1 if in0[4] or in1[4] else 2))
+        return op("v", lambda: g.vector.tensor_tensor(out[0], in0[0], in1[0], o), [out], [in0, in1],
+                  vec(out, [in0], 1 if in0[4] or in1[4] else 2) + in0[5] * in0[2] * (2 - GATHER) * CYC)
 
     def cp(out, in_):
-        op("v", lambda: g.vector.tensor_copy(out[0], in_[0]), [out], [in_], vec(out, [in_], half(out, in_)))
+        return op("v", lambda: g.vector.tensor_copy(out[0], in_[0]), [out], [in_], vec(out, [in_], half(out, in_)))
 
     def scan(out, d0, d1, o0, o1):
         op("v", lambda: g.vector.tensor_tensor_scan(out[0], d0[0], d1[0], 0.0, o0, o1), [out], [d0, d1], vec(out, [d0], half(out, d0, d1)))
@@ -186,10 +210,10 @@ def rank_program(g, core, T, topo):
 
     def mm(out, terms):
         for k, (l, r, *part) in enumerate(terms):
-            o = part[0] if part else out
+            o, cost = part[0] if part else out, max(min(64, l[2]), r[2]) * PE * (1 if l[3] else 4)
             stop = not out or k == len(terms) - 1 or len(o) > 7 and all(x[2][7:] != o[7:] for x in terms[k + 1:])
             op("p", lambda o=o, l=l, r=r, k=k, stop=stop: g.tensor.matmul(o[0], l[0], r[0], k == 0 or not out, stop),
-               [o], [l, r], max(min(64, l[2]), r[2]) * PE * (1 if l[3] else 4), more=len(terms) - 1 - k)
+               [o], [l, r], cost, cost + DRAIN, more=len(terms) - 1 - k)
 
     def iota(out, pat, base, cm=0):
         small = {} if out[1][0][0] == "pack_int32" else {"allow_small_or_imprecise_dtypes": True}
@@ -207,14 +231,15 @@ def rank_program(g, core, T, topo):
     def q4(k):
         return 512 * k, 512 * k + 512
 
-    for k in range(4):
-        queue["y"].dma_start(out=T.XI[:, 512 * k:512 * k + 512], in_=T.det[:, 512 * k:512 * k + 512]).then_inc(T.sem["d%d" % k], 16)
-        op("r", None, [b("XI", *q4(k))], [], 0.0, LOAD + 1050 * (k + 1), ("d%d" % k, 16))
+    blocks = ((0, 640), (640, 1280), (1280, 1792), (1792, V))
+    for k, (lo, hi) in enumerate(blocks):
+        queue["y"].dma_start(out=T.XI[:, lo:hi], in_=T.det[:, lo:hi]).then_inc(T.sem["d%d" % k], 16)
+        op("r", None, [b("XI", lo, hi)], [], 0.0, LOAD + 80 * (k + 1) + 0.64 * hi, ("d%d" % k, 16))
     queue["y"].dma_start(out=T.HM[:], in_=T.ham[:]).then_inc(T.sem.d4, 16)
-    op("r", None, [b("HM")], [], 0.0, LOAD + 8000, ("d4", 16))
+    op("r", None, [b("HM")], [], 0.0, LOAD + 3500, ("d4", 16))
 
     cell = [divmod(STEP * (t + 1), 16) for t in range(RO)]
-    PP, PI, PG, PG16, OD, SIG, SI2, W1, W2, PGE, PGO, CE, CO, CE1, CO1, CTE, CTO, CA, CB, P2 = [b("col", k, k + 1) for k in range(20)]
+    PP, PI, PG, PG16, OD, SIG, SI2, W1, W2, PGE, PGO, CE, CO, CE1, CO1, FIRSTROW = [b("col", k, k + 1) for k in range(16)]
     diag = [[-1, 128]]
     blk = [[-16, 8], [0, 16]]
     iota(b("pp_i"), [[0, 1]], 0, 1)
@@ -238,25 +263,19 @@ def rank_program(g, core, T, topo):
     act(b("J"), b("Jb"))
     ts(b("sw"), b("Jb", 0, 20), 16.0, PI, A.mult, A.add)
     for t, (c0, r0) in enumerate(cell):
-        TX = "TX%d" % t
-        ts(b("MK", 2 * t, 2 * t + 1), PI, float(r0), -2.0 ** 19, A.is_lt, A.mult)
-        ts(b("MK", 2 * t + 1, 2 * t + 2), PI, float(r0), -2.0 ** 19, A.is_ge, A.mult)
-        ts(CA, PP, float(c0), None, A.is_ge)
-        ts(CB, PP, float(c0), -1.0, A.is_ge, A.add)
-        ts(b(TX, 0, c0), b("PD", 0, c0), 0.0, CA, A.is_gt, A.add)
-        ts(b(TX, c0, 128), b("PD", c0, 128), 0.0, CB, A.is_gt, A.add)
-        cp(b(TX, 128, 130), b("ones", 0, 2))
+        ts(b("MK", 3 * t, 3 * t + 1), PI, float(r0), -2.0 ** 19, A.is_ge, A.mult)
+        ts(b("MK", t + 1, t + 2), PI, float(r0), -2.0 ** 19, A.is_lt, A.mult)
         w0, w1 = b("WL", 4 * t, 4 * t + 1), b("WL", 4 * t + 1, 4 * t + 2)
-        sel(w0, b("ones", 0, 1), [[0, 1]], A.not_equal, -127.0, -127, 1)
-        act(w1, w0, scale=16.0)
-        sel(w0, w0, [[0, 1]], A.not_equal, 129.0 - c0, 1 - c0, 1)
+        iota(b("WL", 4 * t, 4 * t + 2), [[15, 2]], 1)
+        sel(w1, w1, [[0, 1]], A.not_equal, -2032.0, c0 - 127, 1)
         act(b("WL", 4 * t + 2, 4 * t + 4), b("WL", 4 * t, 4 * t + 2), scale=0.5)
-        act(b("base", 32 * t, 32 * t + 16 - NS), b("zero", 0, 16 - NS), bias=float(c0))
-        act(b("base", 32 * t + 16 - NS, 32 * t + 16), b("zero", 0, NS), bias=(128 + c0) / 2.0)
-        act(b("base", 32 * t + 16, 32 * t + 32), b("zero", 0, 16), bias=16.0 * c0)
+        iota(b("base", 32 * t, 32 * t + 32), [[16 * c0, 2], [0, 16]], 0)
+        iota(b("base", 32 * t + 16 - NS, 32 * t + 16), [[0, NS]], 64)
+    sel(b("NU"), b("BH"), diag, A.is_gt, 0.0, 0, 1)
+    ts(b("NUn"), b("NU"), -1.0, None, A.mult)
     iota(b("JI"), [[0, 20], [1, 16]], 0)
     for n, c in (("I256n", -256.0), ("Im1", -1.0), ("IF", 256.0), ("I4kn", -4096.0), ("I256", 256.0), ("I64k", 65536.0),
-                 ("I16kn", -16384.0), ("I32kn", -32768.0), ("I64n", -64.0)):
+                 ("I16kn", -16384.0), ("I32kn", -32768.0)):
         ts(b(n), b("I1"), c, None, A.mult)
     ts(b("pq_i"), b("pp_i"), 1, None, A.bitwise_and)
     ts(b("pr_i"), b("pr_i"), 1, None, A.bitwise_and)
@@ -264,22 +283,18 @@ def rank_program(g, core, T, topo):
     act(SI2, b("pq_i"), scale=4.0, bias=-2.0)
     act(W1, PI, scale=13.0, bias=5.0)
     act(W2, PI, scale=-14.0, bias=255.0)
-    act(P2, PI, scale=2.0, bias=1.0)
     act(PGE, b("pr_i"), scale=100000.0, bias=PG16)
     act(OD, b("pr_i"), scale=-100000.0, bias=100000.0 - 16.0)
     act(PGO, OD, bias=PG16)
-    for pg, ce, c1, ct, nh, n1, nt in ((PGE, CE, CE1, CTE, "EH", "E1", "TE"), (PGO, CO, CO1, CTO, "OH", "O1", "TO")):
+    for pg, ce, c1, nh, n1 in ((PGE, CE, CE1, "EH", "E1"), (PGO, CO, CO1, "OH", "O1")):
         act(ce, pg, scale=0.5, bias=3.0)
         act(c1, pg, bias=11.0)
-        act(ct, pg, bias=P2)
-        ts(b(nt), b("Jb", 0, 130), ct, None, A.is_equal)
         ts(b(nh, 0, 144, 2), b("Jb", 0, 72), ce, W1, A.is_equal, A.mult)
         ts(b(nh, 1, 144, 2), b("Jb", 0, 72), ce, W2, A.is_equal, A.mult)
         ts(b(n1), b("Jb", 0, 144), c1, SIG, A.is_equal, A.mult)
     act(b("WT", 0, 8), b("BH", 0, 128, 16), scale=W1)
     act(b("WT", 8, 16), b("BH", 0, 128, 16), scale=W2)
-    act(b("B592"), b("BH"), scale=592.0)
-    act(b("I592"), b("BH", 0, 128, 16), scale=-592.0)
+    act(b("I592"), b("BH", 0, 128, 16), scale=592.0)
     act(b("kc"), b("kx"), bias=7.5)
     act(b("PAR"), b("BH"), scale=SIG)
     act(b("PA2"), b("BH"), scale=SI2)
@@ -293,7 +308,8 @@ def rank_program(g, core, T, topo):
     sel(b("CR2"), b("zero"), [[0, 8], [1, 16]], A.not_equal, -64.0, 0, 0)
     act(b("VK"), b("ones"), scale=-7.5)
     act(b("VV"), b("ones"), scale=0.0)
-    sel(b("NU"), b("BH"), diag, A.is_gt, 0.0, 0, 1)
+    sel(b("CQ"), b("zero"), [[0, 128]], A.not_equal, M31, 0, 1)
+    sel(b("CQ"), b("CQ"), [[0, 128]], A.not_equal, 524288.0 + OFF, -1, 1)
     iota(b("c9", 0, 9), [[256, 9]], -1024)
     iota(b("O", 0, 153, 17), [[0, 9]], 0)
     sel(b("m17"), b("ones", 0, 153), [[0, 9], [1, 17]], A.not_equal, 0.0, -1, 0)
@@ -306,10 +322,12 @@ def rank_program(g, core, T, topo):
     iota(b("cz0", 6, 61), [[1, 11], [0, 5]], 1)
     iota(b("cz1", 16, 181), [[1, 11], [0, 15]], 1)
     iota(b("kc2"), [[0, 20], [2048, 12]], -81920)
-    ts(b("pvs"), b("JI"), 0.0, None, A.mult)
+    iota(b("cT"), [[0, 20]], TR)
     iota(b("mB"), [[0, 240]], 0)
     iota(b("mB", 0, 240, NP), [[0, 20]], 1 << 21)
-    ts(b("CM"), b("JI"), PI, 0.5, A.is_ge, A.mult)
+    ts(b("pvs"), b("JI"), 0.0, None, A.mult)
+    ts(b("pv0"), b("JI"), PI, 8192.0, A.is_equal, A.mult)
+    ts(FIRSTROW, PI, 0.0, 8192.0, A.is_equal, A.mult)
     ts(b("MX"), b("Jb", 0, 16), PI, None, A.is_equal)
     for x in range(16):
         ts(b("RX", 128 * x, 128 * x + 128), b("BH"), b("MX", x, x + 1), None, A.mult)
@@ -330,27 +348,33 @@ def rank_program(g, core, T, topo):
 
     for t in range(RO):
         c0, r0 = cell[t]
-        TX = "TX%d" % t
         if t == 0:
-            for k in range(4):
-                ts(b("X1", *q4(k)), b("XI", *q4(k)), 255, None, A.bitwise_and)
-                act(b("NZ", *q4(k)), b("X1", *q4(k)), F.Square, bias=-128.0)
-            act(b("NZ", V, V + 16), b("X1", 16 * c0, 16 * c0 + 16), F.Square, bias=-128.0)
-            for lo, hi, at in ((0, 64, c0), (64, 129, 128)):
-                mm(b("B0", lo, hi), [(zs(x), b("NZ", 16 * lo + x, 16 * hi, 16)) for x in range(16)]
-                   + [(I1, b("MK", at // 128, at // 128 + 1), b("B0", at, at + 1))])
+            for q in blocks:
+                ts(b("X1", *q), b("XI", *q), 255, None, A.bitwise_and)
+                if q[1] < V:
+                    act(b("NZ", *q), b("X1", *q), F.Square, bias=-128.0)
+                else:
+                    ts(b("NZ", *q), b("X1", *q), 128.0, None, A.not_equal)
+            terms = [(zs(x), b("NZ", 16 * lo + x, 16 * hi, 16), b("B0", lo + d, hi + d))
+                     for lo, hi, d in ((0, c0 + 1, 0), (c0, 128, 1)) for x in range(16)]
+            mm(b("B0", 0, 129), terms[:18] + [(I1, b("MK", 0, 2), b("B0", c0, c0 + 2))] + terms[18:])
+            parts = ((c0 + 1, 129), (0, c0 + 1))
         else:
-            act(b3("SR", full, 128), b("X", TR + 16 * c0, TR + 16 * c0 + 16), F.Sign)
+            act(b("SR", 128, 16 * 129, 129), b("X", TR + 16 * c0, TR + 16 * c0 + 16), F.Sign)
             for x in range(16):
-                o, i = b3("SR", x, slice(0, 128)), b("X", TR + x, TR + V, 16)
-                act(o, i, F.Sign) if x % 3 == 1 else ts(o, i, 0.0, None, A.is_gt)
-            mm(b("B0", 0, 129), [(zs(x), b3("SR", x, slice(0, 129))) for x in range(16)]
-               + [(I1, b("MK", 2, 4), b("B0", c0, 129, 128 - c0))])
-        ts(b("Lb", 0, 129), b("B0", 0, 129), 0.0, None, A.is_gt)
-        mm(b("B1", 0, 128), [(b("Lb", 0, 128), b("BH"))])
-        cp(b("cnt"), b("B1", 0, 128))
-        mm(b("B2", 0, 128), [(b("e0"), b("kx")), (b(TX, 0, 128), b("cnt")), (I1, b("cnt"))])
-        mm(b("B0", 0, 130), [(b("cnt"), b(TX)), (b("TI"), b("Lb", 0, 129), b("B0", 0, 129)), (b("BH"), b("Lb", 128, 129), b("B0", 129, 130))])
+                o, i = b("SR", 129 * x, 129 * x + 128), b("X", TR + x, TR + V, 16)
+                act(o, i, F.Sign) if x % 8 in (1, 4, 6) else ts(o, i, 0.0, None, A.is_gt)
+            terms = [(zs(x), b("SR", 129 * x, 129 * x + 129)) for x in range(16)]
+            mm(b("B0", 0, 129), terms[:1] + [(I1, b("MK", 2, 4), b("B0", c0, 129, 128 - c0))] + terms[1:])
+            parts = ((c0, 128), (0, c0), (128, 129))
+        at = 0
+        for lo, hi in parts:
+            ts(b("Lb", at, at + hi - lo), b("B0", lo, hi), 0.0, None, A.is_gt)
+            at += hi - lo
+        scan(b("PL", 0, 129), b("ones", 0, 129), b("Lb", 0, 129), A.mult, A.add)
+        mm(b("B2", 0, 128), [(b("e0"), b("kx")), (b("PL", 0, 128), b("BH"))])
+        mm(b("B0", 0, 130), [(b("BH"), b("PL", 0, 129), b("B0", 0, 129)), (b("NUn"), b("Lb", 0, 129), b("B0", 0, 129)),
+                             (b("BH"), b("PL", 128, 129), b("B0", 129, 130))])
         cp(b("EB"), b("B2", 0, 128))
         act(b("U", 0, 130), b("B0", 0, 130))
         for j in range(16):
@@ -365,7 +389,7 @@ def rank_program(g, core, T, topo):
         cp(b("cu"), b("B1", 0, 16))
         act(b("cb"), b("B1", 16, 32))
         tt(b("G"), ind(b("U", 0, 130), b("cu")), b("J"), A.is_le)
-        mm(b("B2", 0, 16), [(zs(x), b("G", x, 256, 16)) for x in range(16)] + [(I1, b("cb"))])
+        mm(b("B2", 0, 16), [(I1, b("cb"))] + [(zs(x), b("G", x, 256, 16)) for x in range(16)])
         cp(b("plu"), b("B2", 0, 16))
         ts(b("dm"), b("sw", 0, 16), b("U", 129, 130), -8192.0, A.is_ge, A.mult)
         if t == 0:
@@ -376,38 +400,27 @@ def rank_program(g, core, T, topo):
         ts(b("Du"), ind(win, b("plu")), 1.0 / 256.0, -off / 256.0, A.mult, A.add)
         act(b("Sx"), ind(win, b("plu")), F.Relu, bias=(128.0 - off) / 256.0, scale=1.0 / 256.0)
         tt(b("fo"), b("dm"), b("B2", 0, 16), A.add)
-        for lo, hi in ((NA, S), (0, NA)):
-            ts(b("Dh", lo, hi), b("Du", lo, hi), -2048.0, None, A.add)
+        dh = ts(b("Dh"), b("Du"), -2048.0, None, A.add)
         CB0 = -524288.0 - 128.0
-        mm(b("C0", 0, NV), [(b(n, 1 - u, 129 - u), b("Dh", NA + 80 * u, NA + 80 * u + 80), b3("C0", slice(par, 10, 2)))
-                            for par, n in ((0, "TE"), (1, "TO")) for u in (0, 1)])
         mm(b("B3", 0, S), [(b("IF"), b("Sx")), (b("I256n"), b("Dh"))])
-        first = act(b("Ca", 0, S), b("B3", 0, S), F.Abs, bias=CB0)
-        vtr(b("RT"), b("C0", 0, NV))
-        for k in range(5):
-            ts(b("DT", k, NV, 5), b("RT", 32 * k, 32 * k + 32), 2048.0, None, A.add)
-        cp(b("Ca", S, S + NV), b("Ca", NA, S))
+        first = act(b("C3", 0, S), b("B3", 0, S), F.Abs, bias=CB0)
         for h in range(2):
             mm(b("B0", 16 * h, 16 * h + 16), [(b("Dh", 128 * h, 128 * h + 128), b("WT"))])
-        row([tt(b("MV", NV * k0, NV * k1), ind(b("HM"), b("DT", 10 * k0, 10 * k1)), b("Ca", NA, NA + NV * (k1 - k0)), A.min)
-             for k0, k1 in [(0, 1)] + [(k, k + 2) for k in range(1, 15, 2)] + [(15, 16)]])
-        mm(b("B2", 0, 128), [(b("e0"), b("kc"))] + [(b("MV", NV * k + 32, NV * k + NV), b("B592", 0, 128, 16), b("B2", k, 128, 16)) for k in range(16)])
-        look = [act(b("Lg", 16 * lo, 16 * hi), ind(b("HM"), b("Du", lo, hi)), F.Copy) for lo, hi in ((0, 32), (32, NA))]
-        row([first, look[1]])
-        for lo, hi, k0, k1, bank in ((0, 32, 0, 16, "C1"), (32, NA, 0, 8, "C2"), (32, NA, 8, 16, "C0")):
-            w = hi - lo
-            mm(b(bank), [x for k in range(k1 - k0) for x in ((Im1, b("Lg", 16 * lo + k0 + k, 16 * hi, 16), b(bank, w * k, w * k + w)),
-                                                             (I1, b("Ca", lo, hi), b(bank, w * k, w * k + w)))])
-            act(b3("Mn", slice(k0, k1), slice(lo, hi)), b(bank), F.Relu)
-        mm(b("B1", 0, 128), [(b("e0"), b("kc")), (b("Ca", 0, NA), b("B592"), rows(b("B1", 0, 128), 0, NA))]
-           + [(b("MV", NV * k, NV * k + 32), b("B592", 0, 128, 16), rows(b("B1", k, 128, 16), NA, 128)) for k in range(11)]
-           + [(b3("Mn", k), b("I592"), rows(b("B1", k, 128, 16), 0, NA)) for k in range(16)]
-           + [(b("MV", NV * k, NV * k + 32), b("B592", 0, 128, 16), rows(b("B1", k, 128, 16), NA, 128)) for k in range(11, 16)])
-        cp(b3("hi"), b("B0", 0, 32))
-        ts(b3("ha"), b3("hi"), 4095, None, A.bitwise_and)
-        tt(b("hp"), b3("ha", full, slice(0, 8)), b3("ha", full, slice(8, 16)), A.mult)
-        ts(b("hq"), b("hp"), 5, None, A.arith_shift_right)
-        ts(b("hb"), b("hq"), 16.0, M27 + 16.0 * t, A.mult, A.add)
+        mine = [cp(b("Lg", 0, 16 * NV), ind(b("HM"), b("Du", 0, NV)))]
+        look = [act(b("Lg", 16 * lo, 16 * hi), ind(b("HM"), b("Du", lo, hi)), F.Copy) for lo, hi in ((NV, 128), (128, 192), (192, S))]
+        row(look[:1] + [first] + look[1:])
+        least = [tt(b3("Mn", k, slice(lo, hi)), b("Lg", 16 * lo + k, 16 * hi, 16), b("C3", lo, hi), A.min)
+                 for lo, hi in ((0, 128), (128, 192), (192, S)) for k in range(16)]
+        for h in range(2):
+            bank = "B%d" % (1 + h)
+            mm(b(bank, 0, 128), [(b("e0"), b("kc"))]
+               + [(b3("Mn", k, slice(128 * h, 128 * h + 128)), b("I592"), b(bank, k, 128, 16)) for k in range(16)])
+        steps = [cp(b3("hi"), b("B0", 0, 32)),
+                 ts(b3("ha"), b3("hi"), 4095, None, A.bitwise_and),
+                 tt(b("hp"), b3("ha", full, slice(0, 8)), b3("ha", full, slice(8, 16)), A.mult),
+                 ts(b("hq"), b("hp"), 5, None, A.arith_shift_right),
+                 ts(b("hb"), b("hq"), 16.0, M27 + 16.0 * t, A.mult, A.add)]
+        row([dh] + mine + [x for k in range(5) for x in [steps[k]] + least[2 * k:2 * k + 2]] + least[10:])
         act(b("Cb"), b("B3", 0, 256), bias=CB0)
         for h in range(2):
             scan(b("Ks", 128 * h, 128 * h + 128), b("m16", 0, 128), b("B%d" % (1 + h), 0, 128), A.mult, A.max)
@@ -494,11 +507,11 @@ def rank_program(g, core, T, topo):
         mm(b("C3", 0, 256), fade + [(b("I256"), DH), (b("AL"), b("fsg"))])
         act(b("xg"), b("C3", 0, 256), bias=-CB0)
         tt(b("fo2"), b("fo"), b("swa", 0, 16), A.max)
-        act(b("fou"), b("fo2"), bias=float(TR))
+        ts(b("fou"), b("fo2"), float(TR), None, A.add)
 
         def flagged(out, in_, at, o):
             for k in range(4):
-                bank = "C0" if k % 2 else "C3"
+                bank = "C0" if k % 2 and k < 3 - 2 * t else "C3"
                 mm(b(bank), [(b("AL"), b("SG", *q4(k)))])
                 for h in (0, 256):
                     lo = 512 * k + h
@@ -511,14 +524,14 @@ def rank_program(g, core, T, topo):
                 act(b("SG", *q4(k)), b("X", TR + 512 * k, TR + 512 * k + 512), F.Sign)
             flagged("Y", "X", TR, A.subtract)
 
-        score = [(b("e0"), b("kc2"))]
-        banks, probes = ["C0", "C2", "C1", "C0"], []
+        banks, looks, fused, tests, score = ["C0", "C2", "C1", "C0"], [], [], [], [(b("e0"), b("kc2"))]
         for part in range(2):
             c1, c2 = PART[part]
             w = c2 - c1
             n, ways, a0, z0, s0, q0 = 16 * w, w // 5, 16 * c1, 960 * part, 16 - 16 * part, 6 - 6 * part
             A16 = b3("A16", slice(c1, c2))
-            zu, ZH, Zi, Zm, cz, Q, R, Z, st = [x + str(part) for x in ("zu", "ZH", "Zi", "Zm", "cz", "Q", "R5", "Z", "st")]
+            zu, Zi, Zm, cz, R, Z, st = [x + str(part) for x in ("zu", "Zi", "Zm", "cz", "R5", "Z", "st")]
+            k0, linear = NP * c1, []
             at = [0] + [w + 1 + w * m for m in range(NP)]
             u1, u2 = b3("aa5", full, slice(q0, q0 + 2 * ways, 2)), b3("aa5", full, slice(q0 + 1, q0 + 2 * ways, 2))
             ai5, aa5 = [b3(x, full, slice(q0, q0 + 2 * ways)) for x in ("ai5", "aa5")]
@@ -527,9 +540,11 @@ def rank_program(g, core, T, topo):
             ts(A16, b(LA, a0, a0 + n), M23, -M23, A.add, A.add)
             mm(b(hb, 0, 160), [(b(nh, 6 - 2 * j, 134 - 2 * j), b3("A16", slice(c1 + j, c2, ways)), b3(hb, slice(par, 10, 2)))
                                for par, nh in ((0, "EH"), (1, "OH")) for j in range(ways)])
-            groups = [(0, 1), (1, 3), (3, 5), (5, 7), (7, 9), (9, 11), (11, 12)]
-            for k in range(2):
-                act(b(Q, n * k, n * k + n), A16, bias=524288.0 + OFF - M31, scale=256.0)
+            groups = [(0, 1), (1, 3), (3, 5), (5, 7), (7, 9), (9, 11), (11, 12)] if part else [(0, 1), (1, 3), (3, 7), (7, NP)]
+            Q = b("B0" if part else "B3", 0, n)
+            mm(Q, [(b("CQ"), b("ones", 0, n)), (b("I256"), A16)])
+            for k in range(2 * part):
+                act(b("Q1", n * k, n * k + n), A16, bias=524288.0 + OFF - M31, scale=256.0)
             vtr(b3(R), b(hb, 0, 160))
             cp(ai5, b3(R, full, slice(0, 2 * ways)))
             ts(aa5, ai5, 4095, None, A.bitwise_and)
@@ -540,80 +555,102 @@ def rank_program(g, core, T, topo):
             for m in (0, 1):
                 ts(b(Z, w * m, w * m + w), ah, 8, V - 1, A.arith_shift_right, A.bitwise_and)
             cp(b(zu, 0, w), b(Z, 0, w))
-            cp(b(ZH, 0, w), b(Z, 0, w))
-            for m0, m1, bank in ((1, 3, None), (3, NP, "B%d" % (2 * part))):
+            cp(b("ZH", k0, k0 + w), b(Z, 0, w))
+            for m0, m1, bank in ((1, 3, None), (3, NP, "B2")):
                 r = (at[m0], at[m1])
                 if bank:
                     mm(b(bank, *r), [(b("e0"), b(cz, *r))]
                        + [(b("IM", 128 * m - 384, 128 * m - 256), uh, b(bank, at[m], at[m] + w)) for m in range(m0, m1)]
-                       + [(I1, b(ZH, 0, w), b(bank, at[m], at[m] + w)) for m in range(m0, m1)])
-                    cp(b(Zi, *r), b(bank, *r))
+                       + [(I1, b("ZH", k0, k0 + w), b(bank, at[m], at[m] + w)) for m in range(m0, m1)])
+                    (act if part else cp)(b(Zi, *r), b(bank, *r))
                 else:
                     tt(b(Zi, *r), b(Z, 0, 2 * w), b(st, 0, 2 * w), A.add)
                 ts(b(Zm, *r), b(Zi, *r), V - 1, None, A.bitwise_and)
-                cp(b(zu, *r), b(Zm, *r))
-                cp(b(ZH, *r), b(zu, *r))
-            into = [b("B1", NP * c1 + m, NP * c2, NP) for m in range(NP)]
-            score += [(I1, b(ZH, at[m], at[m] + w), into[m]) for m in range(NP)]
+                (act if part and bank else cp)(b(zu, *r), b(Zm, *r))
+                (act if part and bank and ZS_ else cp)(b("ZH", k0 + w * m0, k0 + w * m1), b(zu, *r))
             for m0, m1 in groups:
                 d = (z0 + n * m0, z0 + n * m1)
-                probes.append(tt(b("dd", *d), ind(XW, b(zu, at[m0], at[m0] + w * (m1 - m0))), b(Q, 0, n * (m1 - m0)), A.subtract))
-                if part or m1 in (5, NP):
-                    d = d if part else (n * (0 if m1 == 5 else 5), n * m1)
-                    act(b("sq", *d), b("dd", *d), F.Square, bias=-M31 / 256.0, scale=1.0 / 256.0)
-            for m0, m1 in ((0, 5), (5, 9), (9, NP)) if part else ((0, NP),):
-                bank = b3(banks.pop(0), slice(0, m1 - m0), slice(0, w))
-                mm(bank, [(zs(x), b("sq", z0 + n * m0 + x, z0 + n * m1, 16)) for x in range(16)])
-                k = (NP * c1 + w * m0, NP * c1 + w * m1)
-                if m0 < 9:
+                look = ind(XW, b(zu, at[m0], at[m0] + w * (m1 - m0)))
+                if part and m0 in VF:
+                    fused.append(tt(b("dd", *d), look, b("Q1", 0, n * (m1 - m0)), A.subtract))
+                    looks.append(act(b("sq", *d), b("dd", *d), F.Square, bias=-M31 / 1024.0, scale=1.0 / 1024.0))
+                    continue
+                looks.insert(len(looks) - AHEAD * (part and m0 > 0), act(b("dd", *d), look, bias=M31))
+                for m in range(m0, m1):
+                    e = (z0 + n * m, z0 + n * m + n)
+                    fused.append(tt(b("db", *e), Q, b("dd", *e), A.subtract))
+                if part or m1 == NP:
+                    d = d if part else (0, n * NP)
+                    if (part, m0) in VN:
+                        tests.append([ts(b("sq", *d), b("db", *d), 0.0, 37.0 * 2 ** 20, A.not_equal, A.mult)])
+                        linear += range(d[0] // n - 4 * part, d[1] // n - 4 * part)
+                    else:
+                        looks.append(act(b("sq", *d), b("db", *d), F.Square, scale=1.0 / 1024.0))
+            if part:
+                mm(b("B2", 0, AR), [(b("IF"), b(LA)), (b("I256n"), b3("A16"))])
+                act(b("cq"), b("B2", 0, AR))
+            for m0 in (0, 4, 8) if part else (0,):
+                bank = banks.pop(0)
+                k = (k0 + w * m0, k0 + w * m0 + 60)
+                ms = [m for m in linear if m0 <= m < m0 + 60 // w]
+                more = [(zs(x), b("db", z0 + n * ms[0] + x, z0 + n * ms[-1] + n, 16), b3(bank, slice(ms[0] - m0, ms[-1] - m0 + 1), slice(0, w)))
+                        for x in range(16)] if ms else []
+                bank = b3(bank, slice(0, 60 // w), slice(0, w))
+                terms = [(zs(x), b("sq", 16 * k[0] + x, 16 * k[1], 16)) for x in range(16)]
+                mm(bank, terms[:1] + more + terms[1:])
+                if (part, m0) in SK:
                     act(b("k1", *k), bank, F.Sign)
                     act(b("k2", *k), bank, F.Sign, bias=-THETA)
                 else:
-                    ts(b("k1", *k), bank, 0.0, None, A.is_gt)
-                    ts(b("k2", *k), bank, THETA, -0.5, A.is_gt, A.add)
-                for m in range(m0, m1):
-                    k = (NP * c1 + w * m, NP * c1 + w * m + w)
-                    score += [(b("I64k"), b("k1", *k), into[m]), (b("I16kn" if m0 < 9 else "I32kn"), b("k2", *k), into[m])]
-        row(probes)
-        mm(b("B1", 0, 240), score)
-        act(b("QW"), b3("A16"), bias=524288.0 + OFF, scale=256.0)
+                    tests.append([ts(b("k1", *k), bank, 0.0, None, A.is_gt), ts(b("k2", *k), bank, THETA, -0.5, A.is_gt, A.add)])
+                for m in range(m0, m0 + 60 // w):
+                    k, into = (k0 + w * m, k0 + w * m + w), b("B1", k0 + m, NP * c2, NP)
+                    score.insert(1, (I1, b("ZH", *k), into))
+                    score += [(b("I64k"), b("k1", *k), into), (b("I16kn" if (part, m0) in SK else "I32kn"), b("k2", *k), into)]
+        row(looks)
+        tests = [[]] * (5 - len(tests)) + tests
+        row(fused[:KA] + tests[0] + fused[KA:KB] + tests[1] + fused[KB:KC] + tests[2] + fused[KC:])
+        mm(b("B1", 0, 240), score[:1] + score[24:0:-1] + score[25:])
         scan(b("KM"), b("mB"), b("B1", 0, 240), A.add, A.min)
-        km = b("KM", 11, 240, NP)
+        km = b("KM", NP - 1, 240, NP)
         ts(b("pm"), km, V - 1, None, A.bitwise_and)
         ts(b("iv3"), km, 0.0, -4096.0, A.is_ge, A.mult)
+        ts(b("iv4"), b("iv3"), FIRSTROW, None, A.add)
         pvh = b("pvs", 0, AR, 16)
         tt(pvh, b("pm"), b("iv3"), A.add)
+        tt(b("pv0", 0, AR, 16), b("pm"), b("iv4"), A.add)
         cp(b("pu"), b("pm"))
+        mm(None, [(b("RX", 128 * x, 128 * x + 128), pvh, b("C2", x, AR, 16)) for x in range(16)])
         for k in range(4):
             scan(b3("PB", k), b("m16", 0, 80), b("pvs", 80 * k, 80 * k + 80), A.mult, A.add)
-        mm(None, [(b("RX", 128 * x, 128 * x + 128), pvh, b("C2", x, AR, 16)) for x in range(16)])
-        mm(b("B0", 0, AR), [(I1, b("CM"))] + [(b("RX", 128 * x, 128 * x + 128), pvh, b("B0", x, AR, 16)) for x in range(16)])
-        tt(b("w1"), ind(XW, b("pu")), b("QW"), A.subtract)
-        act(b("ra"), b("w1"), F.Relu, bias=128.0)
-        act(b("rs"), b("w1"), F.Sign, bias=128.0)
-        mm(b("B3", 0, AR), [(b("IF"), b(LA)), (b("I256n"), b3("A16")), (I1, b("ra")), (b("I64n"), b("rs"))])
+        scan(b("P0"), b("m16"), b("pv0"), A.mult, A.add)
+        act(b("xm"), ind(XW, b("pu")), bias=M31)
+        act(b("C0", 0, AR), b("xm"), bias=-M31)
+        w1 = tt(b("w1"), ind(XW, b("pu")), b("cq"), A.add)
+        cn = tt(b("cn"), b("w1"), b("C0", 0, AR), A.subtract)
         if t < RO - 1:
-            act(b("esq"), b("B3", 0, AR), F.Square, bias=-64.0)
-        ts(b("ck"), b("B3", 0, AR), 191.0, -63.0, A.min, A.max)
-        if t < RO - 1:
+            act(b("esq"), b("cn"), F.Square)
+            ts(b("ckb"), b("cn"), 127.0, -127.0, A.min, A.max)
+            mm(b("B3", 0, AR), [(b("I256"), b3("A16")), (I1, b("ckb"))])
+            act(b("xq"), b("B3", 0, AR), bias=524288.0 + 256.0 - OFF)
             mm(b("C1", 0, AR), [(b("BH"), b("esq"))])
-            act(b("esg"), b("C1", 0, AR), F.Sign, bias=-0.5)
-            mm(b("C0", 0, AR), [(b("I256"), b3("A16")), (b("AL"), b("esg"))])
-            act(b("Q2"), b("C0", 0, AR), bias=524288.0 + 64.0)
+            ts(b("ft"), b("C1", 0, AR), 0.5, 2.0 * (OFF - 128.0), A.is_gt, A.mult)
         else:
-            act(b("Q2"), b3("A16"), bias=524288.0 + 64.0, scale=256.0)
-        row([tt(b3("EQ3", slice(4 * d - 4, 4 * d), slice(16 * (k - d), 16 * (k - d + 1))), b3("PB", full, slice(16 * k, 16 * k + 16)),
-                b3("C2", slice(k - d, 20, BW)), A.is_equal) for d in range(1, BW) for k in range(d, BW)]
-            + [tt(b("EQ"), b3("PB"), b("B0", 0, AR), A.is_equal)])
-        mm(b("B1", 0, AR), [(b("zero"), b("m16")), (I1, pvh, b("B1", 0, AR, 16))]
+            ts(b("ft"), b("cn"), 127.0, -127.0, A.min, A.max)
+            act(b("xq"), b3("A16"), bias=524288.0 + 128.0, scale=256.0)
+        same = ([tt(b("EQ"), b("P0"), b("C2", 0, AR), A.is_equal)]
+            + [tt(b3("EQ3", slice(4 * d - 4, 4 * d), slice(16 * (k - d), 16 * (k - d + 1))), b3("PB", full, slice(16 * k, 16 * k + 16)),
+                  b3("C2", slice(k - d, 20, BW)), A.is_equal) for d in range(1, BW) for k in range(d, BW)])
+        at = CN if t < RO - 1 else len(same)
+        row([w1] + same[:at] + [cn] + same[at:])
+        mm(b("B1", 0, AR), [(b("I4kn"), b("EQ")), (I1, pvh, b("B1", 0, AR, 16)), (b("e0"), b("cT"), b("B1", 0, AR, 16))]
            + [(b("I4kn"), b3("EQ3", 4 * d - 4 + k, slice(0, 16 * (BW - d))), b("B1", 16 * (BW * k + d), 16 * BW * (k + 1)))
-              for d in range(1, BW) for k in range(4)] + [(b("I4kn"), b("EQ"))])
+              for d in range(1, BW) for k in range(4)])
         scan(b("DS"), b("m16"), b("B1", 0, AR), A.mult, A.add)
-        tt(b("t3"), b("DS", 15, AR, 16), b("swa"), A.max)
-        ts(b3("eou", full, slice(0, BW)), b("t3"), float(TR), None, A.add)
+        tt(b3("eou", full, slice(0, BW)), b("DS", 15, AR, 16), b("sw"), A.max)
         for k in sorted(range(N // near), key=lambda k: -land[core][near * k]):
             q = (16 * BW * k, 16 * BW * (k + 1))
-            tt(ind(b("X" if t < RO - 1 else "Y"), b3("eou", k, slice(0, BW))), b("ck", *q), b("Q2", *q), A.add)
+            tt(ind(b("X" if t < RO - 1 else "Y"), b3("eou", k, slice(0, BW))), b("xq", *q), b("ft", *q), A.add)
     for k, e in ((0, "y"), (1, "s")):
         dma(e, hbm(T.y[:, 1024 * k:1024 * k + 1024]), b("Y", TR + 1024 * k, TR + 1024 * k + 1024), "d%d" % (5 + k), LOAD + 3000)
 

@@ -11,27 +11,28 @@ M23 = 1.5 * 2.0 ** 23
 OFF = 2.0 ** 22
 SENT = -22528
 THETA = 7.05e8
-VF, VN, SK = (1, 5, 9, 11), ((0, 7),), ()
-PASSES, AHEAD, KA, KB, KC, CN = 2, 2, 13, 17, 21, 5
-ZS_ = 0
-NS = 3
-NV = 64
+VF, KN, KF, VN, W1ST = (0, 1, 7, 11), 4, 0, (5,), 8
+PASSES, AHEAD, KA, KB, KC, CN = 2, 2, 6, 10, 14, 1
+YN, SA, SB, SC, D0, D1, G0 = 2, 0, 0, 0, 5, 3, [(0, 1), (1, 3), (3, 7), (7, 12)]
+SE, KD, KE = 4, 11, 3
+NS = 4
+NV = 96
 
 _DT = {"f": "float32", "b": "bfloat16", "h": "float16", "i": "int32", "u": "uint16"}
 _SBUF = """
 f X:2368 Y:2368 J:256 col:32 sw:20 swa:20 swb:20 U:136 dm:16 fo:16 fo2:16 Sx:256 Ks:256 hb:16 rk:16 cc:256 CHf:256 xg:256
-f iv:16 iv2:16 own:16 R4:4,32 R50:5,32 R51:5,32 SL0:2304 SL1:2304 LA0:320 LA1:320 dd:3840 iv3:20 w1:320
-f MX:16 Q1:480 iv4:20 xq:320 ft:320 cq:320 xm:320 cn:320 DS:320 t3:20 IF:128
-i XI:2048 X1:2048 pp_i:1 pq_i:1 pr_i:1 hp:16 hq:16 vi:16 vv:16 ch:16 ow:16 ah:24 Z0:10 Z1:30 st0:10 st1:30 pm:20 Zi0:64 Zm0:64 Zi1:192 Zm1:192 KM:240
-i hi:2,16 ha:2,16 ci:4,8 ca:4,8 ai5:5,8 aa5:5,8
-h EB:128 cb:16 Dh:16,16 VK:256 VV:256 TK:256 VB:256 R1:256 m1:256 CH:16,16 s9:153 A16:20,16 uh:24 ZH:240 pvs:320 pv0:320 P0:320 PB:4,80
+f iv:16 iv2:16 own:16 R4:4,32 R50:2,32 R51:3,32 R52:5,32 SL0:2304 SL1:2304 LA0:320 LA1:320 dd:3840 iv3:20 w1:320
+f MX:16 s9:144 Q1:480 iv4:20 xq:320 ft:320 cq:320 xm:320 cn:320 DS:320 t3:20 IF:128
+i XI:2048 X1:2048 pp_i:1 pq_i:1 pr_i:1 hp:16 hq:16 vi:16 vv:16 ch:16 ow:16 ah:24 Z0:4 Z1:6 Z2:60 st0:4 st1:6 st2:60 pm:20 Zi0:32 Zm0:32 Zi1:48 Zm1:48 Zi2:192 Zm2:192 KM:240
+i hi:2,16 ha:2,16 ci:4,8 ca:4,8 ai5:5,10 aa5:5,10
+h EB:128 cb:16 Dh:16,16 VK:256 VV:256 TK:256 VB:256 R1:16,16 m1:16,16 CH:16,16 A16:20,16 uh:24 ZH0:12,5 ZH1:12,15 pvs:320 pv0:320 P0:320 PB:4,80
 b HM:4096 NZ:2048 SG:2048 SR:2064 Lb:130 PL:130 cmp:2048 G:256 Cb:256 sC:256 Fb:256 Fl:256 Lg:4096 Mn:16,256 db:3840 th:256 sD:16,16
-b sE:256 ab:256 fsq:256 fsg:256 O:153 m17:153 sq:3840 k1:240 k2:240 ckb:320 esq:320 EQ:320 EQ3:16,64
-b Jb:256 JI:320 JG:128 PD:128 zero:128 ones:256 BH:128 ZS:144 MK:4 WL:8 base:64 kx:128 kc:128 e0:128 TI:128 NU:128
-b SU:128 SD:128 PAR:128 PA2:128 AL:128 I592:8 WT:16 EH:144 OH:144 E1:144 O1:144 CQ:128 CR1:128 CR2:128 c9:16
-b m16:320 dk:256 RX:2048 IM:1408 cz0:64 cz1:192 kc2:240 mB:240 cT:20 I1:128 Im1:128 I256n:128 I256:128 I4kn:128
-b I64k:128 I16kn:128 I32kn:128 NUn:128
-u cu:16 plu:16 fou:16 Du:256 slu:16 zu0:64 zu1:192 pu:20 eou:4,6
+b sE:256 ab:256 fsq:256 fsg:256 O:144 m9:144 sq:3840 ka0:12,5 kb0:12,5 ka1:12,15 kb1:12,15 ckb:320 esq:320 EQ:320 EQ3:16,64
+b Jb:256 JI:320 JG:128 PD:128 zero:128 ones:256 BH:128 ZS:144 MK:4 WL:8 base:64 kx:128 kc:128 e0:128 TI:128
+b SU:128 SD:128 PAR:128 PA2:128 AL:128 I592:8 B592:128 Ca:64 WT:16 EH:144 OH:144 ER:144 OR:144 EM:144 OM:144 E1:144 O1:144 CQ:128 CR1:128 CR2:128 c9:144
+b m16:320 dk:256 RX:2048 IM:1408 cz0:32 cz1:48 cz2:192 kc2:240 mB:240 cT:20 I1:128 Im1:128 I256n:128 I256:128 I4kn:128
+b I32kn:128 NUn:128
+u cu:16 plu:16 fou:16 Du:256 slu:16 zu0:32 zu1:48 zu2:192 pu:20 eou:4,6
 """
 _ALL, SCRATCH, _AT = {}, {}, {}
 for _line in _SBUF.split("\n"):
@@ -54,7 +55,7 @@ for _d, _c in _wide.items():
 SEMAPHORES = ["sv", "ss", "sp", "sg", "loc", "ar0", "ar1", "an0", "an1"] + ["d%d" % k for k in range(7)]
 
 CYC, PE, WAKE, GATHER, SCATTER = 0.83, 0.42, 200.0, 1.56, 3.0
-ACT, DRAIN, LOAD, SEND, NEAR, FAR, FIRST = 65.0, 0.0, 1000.0, 700.0, 2200.0, 2800.0, 2500.0
+ACT, DRAIN, LOAD, SEND, NEAR, FAR, FIRST = 65.0, 0.0, 1000.0, 600.0, 1300.0, 1700.0, 1300.0
 
 
 def routes(src, T, topo):
@@ -231,7 +232,7 @@ def rank_program(g, core, T, topo):
     def q4(k):
         return 512 * k, 512 * k + 512
 
-    blocks = ((0, 640), (640, 1280), (1280, 1792), (1792, V))
+    blocks = ((0, 384), (384, 960), (960, 1536), (1536, V))
     for k, (lo, hi) in enumerate(blocks):
         queue["y"].dma_start(out=T.XI[:, lo:hi], in_=T.det[:, lo:hi]).then_inc(T.sem["d%d" % k], 16)
         op("r", None, [b("XI", lo, hi)], [], 0.0, LOAD + 80 * (k + 1) + 0.64 * hi, ("d%d" % k, 16))
@@ -239,7 +240,7 @@ def rank_program(g, core, T, topo):
     op("r", None, [b("HM")], [], 0.0, LOAD + 3500, ("d4", 16))
 
     cell = [divmod(STEP * (t + 1), 16) for t in range(RO)]
-    PP, PI, PG, PG16, OD, SIG, SI2, W1, W2, PGE, PGO, CE, CO, CE1, CO1, FIRSTROW = [b("col", k, k + 1) for k in range(16)]
+    PP, PI, PG, PG16, OD, SIG, SI2, W1, W2, PGE, PGO, CE, CO, CE1, CO1, FIRSTROW, N15, WR1, WR2, WM1, WM2 = [b("col", k, k + 1) for k in range(21)]
     diag = [[-1, 128]]
     blk = [[-16, 8], [0, 16]]
     iota(b("pp_i"), [[0, 1]], 0, 1)
@@ -260,6 +261,7 @@ def rank_program(g, core, T, topo):
     ts(b("I1"), b("PD"), 0.0, None, A.is_equal)
     ts(b("e0"), b("ones", 0, 128), PP, 0.0, A.mult, A.is_equal)
     sel(b("TI"), b("BH"), [[1, 128]], A.is_ge, 0.0, 0, -1)
+    sel(b("TI"), b("TI"), diag, A.not_equal, 4096.0, 0, 1)
     act(b("J"), b("Jb"))
     ts(b("sw"), b("Jb", 0, 20), 16.0, PI, A.mult, A.add)
     for t, (c0, r0) in enumerate(cell):
@@ -271,11 +273,11 @@ def rank_program(g, core, T, topo):
         act(b("WL", 4 * t + 2, 4 * t + 4), b("WL", 4 * t, 4 * t + 2), scale=0.5)
         iota(b("base", 32 * t, 32 * t + 32), [[16 * c0, 2], [0, 16]], 0)
         iota(b("base", 32 * t + 16 - NS, 32 * t + 16), [[0, NS]], 64)
-    sel(b("NU"), b("BH"), diag, A.is_gt, 0.0, 0, 1)
-    ts(b("NUn"), b("NU"), -1.0, None, A.mult)
+    sel(b("NUn"), b("BH"), diag, A.is_gt, 0.0, 0, 1)
+    ts(b("NUn"), b("NUn"), -1.0, None, A.mult)
     iota(b("JI"), [[0, 20], [1, 16]], 0)
-    for n, c in (("I256n", -256.0), ("Im1", -1.0), ("IF", 256.0), ("I4kn", -4096.0), ("I256", 256.0), ("I64k", 65536.0),
-                 ("I16kn", -16384.0), ("I32kn", -32768.0)):
+    for n, c in (("I256n", -256.0), ("Im1", -1.0), ("IF", 256.0), ("I4kn", -4096.0), ("I256", 256.0),
+                 ("I32kn", -32768.0)):
         ts(b(n), b("I1"), c, None, A.mult)
     ts(b("pq_i"), b("pp_i"), 1, None, A.bitwise_and)
     ts(b("pr_i"), b("pr_i"), 1, None, A.bitwise_and)
@@ -286,15 +288,22 @@ def rank_program(g, core, T, topo):
     act(PGE, b("pr_i"), scale=100000.0, bias=PG16)
     act(OD, b("pr_i"), scale=-100000.0, bias=100000.0 - 16.0)
     act(PGO, OD, bias=PG16)
-    for pg, ce, c1, nh, n1 in ((PGE, CE, CE1, "EH", "E1"), (PGO, CO, CO1, "OH", "O1")):
+    ts(N15, PI, 15.0, None, A.is_lt)
+    ts(WR1, W1, 13.0, N15, A.add, A.mult)
+    ts(WR2, W2, -14.0, N15, A.add, A.mult)
+    ts(WM1, N15, -213.0, 200.0, A.mult, A.add)
+    ts(WM2, N15, -31.0, 45.0, A.mult, A.add)
+    for pg, ce, c1, side in ((PGE, CE, CE1, "E"), (PGO, CO, CO1, "O")):
         act(ce, pg, scale=0.5, bias=3.0)
         act(c1, pg, bias=11.0)
-        ts(b(nh, 0, 144, 2), b("Jb", 0, 72), ce, W1, A.is_equal, A.mult)
-        ts(b(nh, 1, 144, 2), b("Jb", 0, 72), ce, W2, A.is_equal, A.mult)
-        ts(b(n1), b("Jb", 0, 144), c1, SIG, A.is_equal, A.mult)
+        for n, ws in (("H", (W1, W2)), ("R", (WR1, WR2)), ("M", (WM1, WM2))):
+            for k in range(2):
+                ts(b(side + n, k, 144, 2), b("Jb", 0, 72), ce, ws[k], A.is_equal, A.mult)
+        ts(b(side + "1"), b("Jb", 0, 144), c1, SIG, A.is_equal, A.mult)
     act(b("WT", 0, 8), b("BH", 0, 128, 16), scale=W1)
     act(b("WT", 8, 16), b("BH", 0, 128, 16), scale=W2)
-    act(b("I592"), b("BH", 0, 128, 16), scale=592.0)
+    act(b("B592"), b("BH"), scale=592.0)
+    act(b("I592"), b("BH", 0, 128, 16), scale=-592.0)
     act(b("kc"), b("kx"), bias=7.5)
     act(b("PAR"), b("BH"), scale=SIG)
     act(b("PA2"), b("BH"), scale=SI2)
@@ -310,17 +319,16 @@ def rank_program(g, core, T, topo):
     act(b("VV"), b("ones"), scale=0.0)
     sel(b("CQ"), b("zero"), [[0, 128]], A.not_equal, M31, 0, 1)
     sel(b("CQ"), b("CQ"), [[0, 128]], A.not_equal, 524288.0 + OFF, -1, 1)
-    iota(b("c9", 0, 9), [[256, 9]], -1024)
-    iota(b("O", 0, 153, 17), [[0, 9]], 0)
-    sel(b("m17"), b("ones", 0, 153), [[0, 9], [1, 17]], A.not_equal, 0.0, -1, 0)
+    iota(b("c9"), [[0, 16], [256, 9]], -4096)
+    sel(b("m9"), b("ones", 0, 144), [[0, 16], [1, 9]], A.not_equal, 0.0, 0, 0)
     sel(b("AL"), b("zero"), blk, A.not_equal, OFF, 0, 1)
     sel(b("AL"), b("AL"), blk, A.not_equal, -128.0, -1, 1)
     for o in range(N):
         iota(b("SL0", 256 * o, 256 * o + CAP), [[0, CAP]], SENT)
-    for m in range(3, NP):
-        ts(b("IM", 128 * m - 384, 128 * m - 256), b("I1"), 2.0 * m, None, A.mult)
-    iota(b("cz0", 6, 61), [[1, 11], [0, 5]], 1)
-    iota(b("cz1", 16, 181), [[1, 11], [0, 15]], 1)
+    for m in range(1, NP):
+        ts(b("IM", 128 * m - 128, 128 * m), b("I1"), 2.0 * m, None, A.mult)
+    for k, w in enumerate((2, 3, 15)):
+        iota(b("cz%d" % k, w + w % 2, 12 * w + w % 2), [[1, 11], [0, w]], 1)
     iota(b("kc2"), [[0, 20], [2048, 12]], -81920)
     iota(b("cT"), [[0, 20]], TR)
     iota(b("mB"), [[0, 240]], 0)
@@ -342,7 +350,8 @@ def rank_program(g, core, T, topo):
     land = {d: landing(d, T, topo) for d in T.cores}
     near = sum(topo.chip(d) == topo.chip(core) for d in T.cores)
     BW = near * CAP // 16
-    PART = ((0, BW), (BW, AR // 16))
+    own = CAP // 16
+    PART = (((0, own), (own, BW)) if land[core][0] == me else ((BW - own, BW), (0, BW - own))) + ((BW, AR // 16),)
     sent = [0]
     I1, Im1 = b("I1"), b("Im1")
 
@@ -354,9 +363,9 @@ def rank_program(g, core, T, topo):
                 if q[1] < V:
                     act(b("NZ", *q), b("X1", *q), F.Square, bias=-128.0)
                 else:
-                    ts(b("NZ", *q), b("X1", *q), 128.0, None, A.not_equal)
+                    row([ts(b("NZ", q[0] + x, V, 4), b("X1", q[0] + x, V, 4), 128.0, None, A.not_equal) for x in range(4)])
             terms = [(zs(x), b("NZ", 16 * lo + x, 16 * hi, 16), b("B0", lo + d, hi + d))
-                     for lo, hi, d in ((0, c0 + 1, 0), (c0, 128, 1)) for x in range(16)]
+                     for lo, hi, d in ((0, c0 + 1, 0), (c0, 128, 1)) for x in sorted(range(16), key=lambda x: x % 4)]
             mm(b("B0", 0, 129), terms[:18] + [(I1, b("MK", 0, 2), b("B0", c0, c0 + 2))] + terms[18:])
             parts = ((c0 + 1, 129), (0, c0 + 1))
         else:
@@ -403,24 +412,30 @@ def rank_program(g, core, T, topo):
         dh = ts(b("Dh"), b("Du"), -2048.0, None, A.add)
         CB0 = -524288.0 - 128.0
         mm(b("B3", 0, S), [(b("IF"), b("Sx")), (b("I256n"), b("Dh"))])
-        first = act(b("C3", 0, S), b("B3", 0, S), F.Abs, bias=CB0)
+        first = [act(b("C3", 0, 192), b("B3", 0, 192), F.Abs, bias=CB0), act(b("Ca"), b("B3", 192, S), F.Abs, bias=CB0)]
         for h in range(2):
             mm(b("B0", 16 * h, 16 * h + 16), [(b("Dh", 128 * h, 128 * h + 128), b("WT"))])
         mine = [cp(b("Lg", 0, 16 * NV), ind(b("HM"), b("Du", 0, NV)))]
-        look = [act(b("Lg", 16 * lo, 16 * hi), ind(b("HM"), b("Du", lo, hi)), F.Copy) for lo, hi in ((NV, 128), (128, 192), (192, S))]
-        row(look[:1] + [first] + look[1:])
+        look = [act(b("Lg", 16 * lo, 16 * hi), ind(b("HM"), b("Du", lo, hi)), F.Copy) for lo, hi in ((NV, 128), (192, S), (128, 192))]
         least = [tt(b3("Mn", k, slice(lo, hi)), b("Lg", 16 * lo + k, 16 * hi, 16), b("C3", lo, hi), A.min)
-                 for lo, hi in ((0, 128), (128, 192), (192, S)) for k in range(16)]
-        for h in range(2):
-            bank = "B%d" % (1 + h)
-            mm(b(bank, 0, 128), [(b("e0"), b("kc"))]
-               + [(b3("Mn", k, slice(128 * h, 128 * h + 128)), b("I592"), b(bank, k, 128, 16)) for k in range(16)])
+                 for lo, hi in ((0, 64), (64, 128), (128, 192)) for k in range(16)]
+        over = []
+        for kk, bank in ((0, "C1"), (8, "C2")):
+            mm(b(bank), [x for k in range(8) for x in ((Im1, b("Lg", 3072 + kk + k, 4096, 16), b(bank, 64 * k, 64 * k + 64)),
+                                                       (I1, b("Ca"), b(bank, 64 * k, 64 * k + 64)))])
+            over.append(act(b3("Mn", slice(kk, kk + 8), slice(192, S)), b(bank), F.Relu))
+        row(look[:1] + first + look[1:] + over)
+        plus = b("B592", 0, 128, 16)
+        mm(b("B1", 0, 128), [(b("e0"), b("kc"))] + [(b3("Mn", k, slice(0, 128)), plus, b("B1", k, 128, 16)) for k in range(16)])
+        low = [(b3("Mn", k, slice(128, 192)), plus, rows(b("B2", k, 128, 16), 0, 64)) for k in range(16)]
+        high = [(b3("Mn", k, slice(192, S)), b("I592"), rows(b("B2", k, 128, 16), 64, 128)) for k in range(16)]
+        mm(b("B2", 0, 128), [(b("e0"), b("kc")), (b("Ca"), b("B592"), rows(b("B2", 0, 128), 64, 128))] + low[:2] + high[:8] + low[2:12] + high[8:] + low[12:])
         steps = [cp(b3("hi"), b("B0", 0, 32)),
                  ts(b3("ha"), b3("hi"), 4095, None, A.bitwise_and),
                  tt(b("hp"), b3("ha", full, slice(0, 8)), b3("ha", full, slice(8, 16)), A.mult),
                  ts(b("hq"), b("hp"), 5, None, A.arith_shift_right),
                  ts(b("hb"), b("hq"), 16.0, M27 + 16.0 * t, A.mult, A.add)]
-        row([dh] + mine + [x for k in range(5) for x in [steps[k]] + least[2 * k:2 * k + 2]] + least[10:])
+        row([dh] + mine + [x for k in range(5) for x in [steps[k]] + least[4 * k:4 * k + 4]] + least[20:])
         act(b("Cb"), b("B3", 0, 256), bias=CB0)
         for h in range(2):
             scan(b("Ks", 128 * h, 128 * h + 128), b("m16", 0, 128), b("B%d" % (1 + h), 0, 128), A.mult, A.max)
@@ -444,9 +459,9 @@ def rank_program(g, core, T, topo):
         tt(b("CH"), b("m1"), b("B1", 0, 256), A.max)
         mm(b("C1", 0, 256), [(I1, DH)] + turned("C1", "VB", Im1))
         act(b("sD"), b("C1", 0, 256), F.Sign)
-        mm(b("C2", 0, 128),
-           [(b(n, 3 - j, 131 - j), b3("sD", slice(j, None, 4)), b3("C2", slice(par, 8, 2))) for par, n in ((0, "E1"), (1, "O1")) for j in range(4)]
-           + [(b(n, 6 - 2 * j, 134 - 2 * j), b3("CH", slice(j, None, 4)), b3("C2", slice(par, 8, 2))) for par, n in ((0, "EH"), (1, "OH")) for j in range(4)])
+        mm(b("C2", 0, 128), [(b(n, at - k * j, 128 + at - k * j), b3(x, slice(j, None, 4)), b3("C2", slice(par, 8, 2)))
+                             for x, ns, at, k in (("R1", ("ER", "OR"), 6, 2), ("sD", ("E1", "O1"), 3, 1), ("m1", ("EM", "OM"), 6, 2))
+                             for par, n in enumerate(ns) for j in range(4)])
         mm(None, turned("C0", "TK", I1))
         act(b("th"), b("C0", 0, 256), F.Sign, bias=7.5)
         mm(b("B2", 0, 256), [(I1, b("R1"))] + turned("B2", "VB", Im1))
@@ -464,18 +479,16 @@ def rank_program(g, core, T, topo):
         ts(b3("ca"), b3("ci"), 4095, None, A.bitwise_and)
         tt(b("iv2"), b("iv"), b("dm"), A.min)
         tt(b("ch"), b3("ca", full, slice(0, 8, 2)), b3("ca", full, slice(1, 8, 2)), A.mult)
-        ts(b("O", 137, 153), b("iv2"), 0.0, None, A.is_lt)
+        ts(b("O", 8, 144, 9), b("iv2"), 0.0, None, A.is_lt)
         ts(b("ow"), b("ch"), 5, 7, A.arith_shift_right, A.bitwise_and)
         tt(b("own"), b("ow"), b("iv2"), A.add)
         for o in range(8):
-            ts(b("O", 17 * o + 1, 17 * o + 17), b("own"), float(o), None, A.is_equal)
-        mm(b("B3", 0, 153), [(b("TI"), b("O")), (b("e0"), b("c9", 0, 9), b("B3", 1, 153, 17)), (b("NU"), b("O", 0, 152), b("B3", 1, 153))])
-        scan(b("B0", 0, 153), b("m17"), b("B3", 0, 153), A.mult, A.add)
-        tt(b("s9"), b("O"), b("B0", 0, 153), A.mult)
-        mm(b("B1", 0, 16), [(I1, b("s9", 17 * o + 1, 17 * o + 17)) for o in range(9)])
-        ts(b("slu"), b("B1", 0, 16), 1023.0, None, A.add)
+            ts(b("O", o, 144, 9), b("own"), float(o), None, A.is_equal)
+        mm(b("B3", 0, 144), [(b("e0"), b("c9")), (b("TI"), b("O"))] + [(b("BH"), b("O", 0, 144 - 9 * d), b("B3", 9 * d, 144)) for d in range(1, 16)])
+        scan(b("s9"), b("m9"), b("B3", 0, 144), A.mult, A.max)
+        cp(b("slu"), b("s9", 8, 144, 9))
         SL, LA = "SL%d" % t, "LA%d" % t
-        tt(ind(b(SL), b("slu")), b("cc"), b("CHf"), A.add)
+        packed = tt(ind(b(SL), b("slu")), b("cc"), b("CHf"), A.add)
         sends = []
         for call in (0, 1):
             tr = []
@@ -509,108 +522,125 @@ def rank_program(g, core, T, topo):
         tt(b("fo2"), b("fo"), b("swa", 0, 16), A.max)
         ts(b("fou"), b("fo2"), float(TR), None, A.add)
 
+        done = []
+
         def flagged(out, in_, at, o):
             for k in range(4):
-                bank = "C0" if k % 2 and k < 3 - 2 * t else "C3"
+                bank = "C0" if k % 2 and not t else "C3"
                 mm(b(bank), [(b("AL"), b("SG", *q4(k)))])
                 for h in (0, 256):
                     lo = 512 * k + h
-                    tt(b(out, TR + lo, TR + lo + 256), b(in_, at + lo, at + lo + 256), b(bank, h, h + 256), o)
+                    done.append(tt(b(out, TR + lo, TR + lo + 256), b(in_, at + lo, at + lo + 256), b(bank, h, h + 256), o))
         if t == 0:
             flagged("X", "XI", 0, A.add)
-        cp(ind(b("X"), b("fou")), b("xg"))
+        faded = cp(ind(b("X"), b("fou")), b("xg"))
         if t == RO - 1:
             for k in range(4):
                 act(b("SG", *q4(k)), b("X", TR + 512 * k, TR + 512 * k + 512), F.Sign)
             flagged("Y", "X", TR, A.subtract)
 
-        banks, looks, fused, tests, score = ["C0", "C2", "C1", "C0"], [], [], [], [(b("e0"), b("kc2"))]
-        for part in range(2):
-            c1, c2 = PART[part]
+        banks, places, score = ["C0", "C0", "C2", "C1", "C0"], [], []
+        for which, (c1, c2) in enumerate(PART):
+            part = int(which == 2)
+            if which < 2:
+                row(looks + [] if which else [])
+                row(fused + [] if which else [])
+                looks, fused, tests = [], [], []
             w = c2 - c1
-            n, ways, a0, z0, s0, q0 = 16 * w, w // 5, 16 * c1, 960 * part, 16 - 16 * part, 6 - 6 * part
+            n, ways, a0, z0, q0 = 16 * w, 1 + 2 * part, 16 * c1, 16 * NP * c1, (6, 8, 0)[which]
+            nb = slice(0, w // ways)
             A16 = b3("A16", slice(c1, c2))
-            zu, Zi, Zm, cz, R, Z, st = [x + str(part) for x in ("zu", "Zi", "Zm", "cz", "R5", "Z", "st")]
+            zu, Zi, Zm, cz, R, Z, st = [x + str(which) for x in ("zu", "Zi", "Zm", "cz", "R5", "Z", "st")]
             k0, linear = NP * c1, []
-            at = [0] + [w + 1 + w * m for m in range(NP)]
-            u1, u2 = b3("aa5", full, slice(q0, q0 + 2 * ways, 2)), b3("aa5", full, slice(q0 + 1, q0 + 2 * ways, 2))
-            ai5, aa5 = [b3(x, full, slice(q0, q0 + 2 * ways)) for x in ("ai5", "aa5")]
-            ah, uh = [b(x, s0, s0 + w) for x in ("ah", "uh")]
+            at = [0] + [w + w % 2 + w * m for m in range(NP)]
+            u1, u2 = b3("aa5", nb, slice(q0, q0 + 2 * ways, 2)), b3("aa5", nb, slice(q0 + 1, q0 + 2 * ways, 2))
+            ai5, aa5 = [b3(x, nb, slice(q0, q0 + 2 * ways)) for x in ("ai5", "aa5")]
+            ah, uh = [b(x, c1, c2) for x in ("ah", "uh")]
             hb = "C%d" % (2 - part)
-            ts(A16, b(LA, a0, a0 + n), M23, -M23, A.add, A.add)
-            mm(b(hb, 0, 160), [(b(nh, 6 - 2 * j, 134 - 2 * j), b3("A16", slice(c1 + j, c2, ways)), b3(hb, slice(par, 10, 2)))
-                               for par, nh in ((0, "EH"), (1, "OH")) for j in range(ways)])
-            groups = [(0, 1), (1, 3), (3, 5), (5, 7), (7, 9), (9, 11), (11, 12)] if part else [(0, 1), (1, 3), (3, 7), (7, NP)]
-            Q = b("B0" if part else "B3", 0, n)
-            mm(Q, [(b("CQ"), b("ones", 0, n)), (b("I256"), A16)])
+            i = ts(A16, b(LA, a0, a0 + n), M23, -M23, A.add, A.add)
+            row(([faded, i], [], done[:YN] + [i])[which] if t else [])
+            mm(b(hb, 0, 32 * nb.stop), [(b(nh, 6 - 2 * j, 134 - 2 * j), b3("A16", slice(c1 + j, c2, ways)), b3(hb, slice(par, 2 * nb.stop, 2)))
+                                        for par, nh in ((0, "EH"), (1, "OH")) for j in range(ways)])
+            groups = [(0, 1), (1, 3), (3, 5), (5, 7), (7, 9), (9, 11), (11, 12)] if part else G0
+            Q, many = "B0" if part else "B3", 1 if part else 5
+            mm(b(Q, 0, n * many), [(b("CQ"), b("ones", 0, n * many))] + [(b("I256"), A16, b(Q, n * k, n * k + n)) for k in range(many)])
             for k in range(2 * part):
                 act(b("Q1", n * k, n * k + n), A16, bias=524288.0 + OFF - M31, scale=256.0)
-            vtr(b3(R), b(hb, 0, 160))
+            vtr(b3(R), b(hb, 0, 32 * nb.stop))
             cp(ai5, b3(R, full, slice(0, 2 * ways)))
             ts(aa5, ai5, 4095, None, A.bitwise_and)
             tt(ah, u1, u2, A.mult)
             ts(uh, u1, -2048.0, None, A.add)
-            for m in (1, 2):
-                ts(b(st, w * m - w, w * m), u1, 2.0 * m, float(m), A.mult, A.add)
-            for m in (0, 1):
+            near1 = D0 if part else D1
+            for m in range(1, near1):
+                if part and m > SE:
+                    act(b(st, w * m - w, w * m), u1, bias=float(m), scale=2.0 * m)
+                else:
+                    ts(b(st, w * m - w, w * m), u1, 2.0 * m, float(m), A.mult, A.add)
+            for m in range(max(1, near1 - 1)):
                 ts(b(Z, w * m, w * m + w), ah, 8, V - 1, A.arith_shift_right, A.bitwise_and)
             cp(b(zu, 0, w), b(Z, 0, w))
-            cp(b("ZH", k0, k0 + w), b(Z, 0, w))
-            for m0, m1, bank in ((1, 3, None), (3, NP, "B2")):
+
+            def by(name, m0, m1):
+                return b3(name + str(part), slice(m0, m1), slice(c1 - BW * part, c2 - BW * part))
+            cp(by("ZH", 0, 1), b(Z, 0, w))
+            for m0, m1, bank in ((1, near1, None), (near1, NP, "B2"))[near1 == 1:]:
                 r = (at[m0], at[m1])
                 if bank:
                     mm(b(bank, *r), [(b("e0"), b(cz, *r))]
-                       + [(b("IM", 128 * m - 384, 128 * m - 256), uh, b(bank, at[m], at[m] + w)) for m in range(m0, m1)]
-                       + [(I1, b("ZH", k0, k0 + w), b(bank, at[m], at[m] + w)) for m in range(m0, m1)])
-                    (act if part else cp)(b(Zi, *r), b(bank, *r))
+                       + [(b("IM", 128 * m - 128, 128 * m), uh, b(bank, at[m], at[m] + w)) for m in range(m0, m1)]
+                       + [(I1, by("ZH", 0, 1), b(bank, at[m], at[m] + w)) for m in range(m0, m1)])
+                    (act if part or SA else cp)(b(Zi, *r), b(bank, *r))
                 else:
-                    tt(b(Zi, *r), b(Z, 0, 2 * w), b(st, 0, 2 * w), A.add)
+                    tt(b(Zi, *r), b(Z, 0, r[1] - r[0]), b(st, 0, r[1] - r[0]), A.add)
                 ts(b(Zm, *r), b(Zi, *r), V - 1, None, A.bitwise_and)
-                (act if part and bank else cp)(b(zu, *r), b(Zm, *r))
-                (act if part and bank and ZS_ else cp)(b("ZH", k0 + w * m0, k0 + w * m1), b(zu, *r))
+                (act if (part or SA) and bank else cp)(b(zu, *r), b(Zm, *r))
+                (act if SB > part else cp)(by("ZH", m0, m1), b(zu, *r))
             for m0, m1 in groups:
                 d = (z0 + n * m0, z0 + n * m1)
                 look = ind(XW, b(zu, at[m0], at[m0] + w * (m1 - m0)))
                 if part and m0 in VF:
                     fused.append(tt(b("dd", *d), look, b("Q1", 0, n * (m1 - m0)), A.subtract))
-                    looks.append(act(b("sq", *d), b("dd", *d), F.Square, bias=-M31 / 1024.0, scale=1.0 / 1024.0))
+                    k = 2 if m1 == NP else 1
+                    looks += [act(b("sq", d[0] + x, d[1], k), b("dd", d[0] + x, d[1], k), F.Square, bias=-M31 / 1024.0, scale=1.0 / 1024.0)
+                              for x in range(k)]
                     continue
                 looks.insert(len(looks) - AHEAD * (part and m0 > 0), act(b("dd", *d), look, bias=M31))
-                for m in range(m0, m1):
-                    e = (z0 + n * m, z0 + n * m + n)
-                    fused.append(tt(b("db", *e), Q, b("dd", *e), A.subtract))
+                for m in range(m0, m1, many):
+                    e = (z0 + n * m, z0 + n * min(m1, m + many))
+                    fused.append(tt(b("db", *e), b(Q, 0, e[1] - e[0]), b("dd", *e), A.subtract))
                 if part or m1 == NP:
-                    d = d if part else (0, n * NP)
-                    if (part, m0) in VN:
-                        tests.append([ts(b("sq", *d), b("db", *d), 0.0, 37.0 * 2 ** 20, A.not_equal, A.mult)])
-                        linear += range(d[0] // n - 4 * part, d[1] // n - 4 * part)
+                    d = d if part else (z0, z0 + n * NP)
+                    if which == 1 and not SC or part and m0 in VN:
+                        i = ts(b("sq", *d), b("db", *d), 0.0, 37.0 * 2 ** 20, A.not_equal, A.mult)
+                        tests.append([i])
+                        linear += range(m0 * part, m1)
                     else:
                         looks.append(act(b("sq", *d), b("db", *d), F.Square, scale=1.0 / 1024.0))
-            if part:
-                mm(b("B2", 0, AR), [(b("IF"), b(LA)), (b("I256n"), b3("A16"))])
-                act(b("cq"), b("B2", 0, AR))
             for m0 in (0, 4, 8) if part else (0,):
-                bank = banks.pop(0)
-                k = (k0 + w * m0, k0 + w * m0 + 60)
-                ms = [m for m in linear if m0 <= m < m0 + 60 // w]
-                more = [(zs(x), b("db", z0 + n * ms[0] + x, z0 + n * ms[-1] + n, 16), b3(bank, slice(ms[0] - m0, ms[-1] - m0 + 1), slice(0, w)))
-                        for x in range(16)] if ms else []
-                bank = b3(bank, slice(0, 60 // w), slice(0, w))
-                terms = [(zs(x), b("sq", 16 * k[0] + x, 16 * k[1], 16)) for x in range(16)]
-                mm(bank, terms[:1] + more + terms[1:])
-                if (part, m0) in SK:
-                    act(b("k1", *k), bank, F.Sign)
-                    act(b("k2", *k), bank, F.Sign, bias=-THETA)
-                else:
-                    tests.append([ts(b("k1", *k), bank, 0.0, None, A.is_gt), ts(b("k2", *k), bank, THETA, -0.5, A.is_gt, A.add)])
-                for m in range(m0, m0 + 60 // w):
-                    k, into = (k0 + w * m, k0 + w * m + w), b("B1", k0 + m, NP * c2, NP)
-                    score.insert(1, (I1, b("ZH", *k), into))
-                    score += [(b("I64k"), b("k1", *k), into), (b("I16kn" if (part, m0) in SK else "I32kn"), b("k2", *k), into)]
+                m1 = m0 + 4 if part else NP
+                k = (k0 + w * m0, k0 + w * m1)
+                ms, bank = [m for m in linear if m0 <= m < m1], banks.pop(0)
+                more = [(zs(x), b("db", z0 + n * ms[0] + x, z0 + n * ms[-1] + n, 16), b3(bank, slice(ms[0] - m0, ms[-1] + 1 - m0), slice(0, w)))
+                        for x in range(16) if ms]
+                bank = b3(bank, slice(0, m1 - m0), slice(0, w))
+                mm(bank, [(b("zero"), b("ones", 0, k[1] - k[0]))] * (0 < len(ms) < m1 - m0) + more
+                   + [(zs(x), b("sq", 16 * k[0] + x, 16 * k[1], 16)) for x in sorted(range(16), key=lambda x: x % 2)])
+                tests.append([ts(by("ka", m0, m1), bank, 0.0, -2.0, A.is_gt, A.mult), ts(by("kb", m0, m1), bank, THETA, -0.5, A.is_gt, A.add)])
+                if m0 < 8:
+                    tt(by("kb", m0, m1), by("kb", m0, m1), by("ka", m0, m1), A.add)
+                for m in range(m0, m1) if which else ():
+                    into = b("B1", NP * BW * part + m, NP * (c2 if part else BW), NP)
+                    places.append((I1, b3("ZH%d" % part, m), into))
+                    score += [(b("I32kn"), b3(x + str(part), m), into) for x in ("ka", "kb")[m0 < 8:]]
         row(looks)
-        tests = [[]] * (5 - len(tests)) + tests
-        row(fused[:KA] + tests[0] + fused[KA:KB] + tests[1] + fused[KB:KC] + tests[2] + fused[KC:])
-        mm(b("B1", 0, 240), score[:1] + score[24:0:-1] + score[25:])
+        fused = fused[:KN] + fused[4:4 + KF] + fused[KN:4] + fused[4 + KF:]
+        tests = [[]] * SC + tests
+        row(fused[:KA] + tests[0] + fused[KA:KB] + tests[1] + fused[KB:KD] + tests[2] + fused[KD:KC] + tests[3] + fused[KC:])
+        mm(b("B1", 0, 240), [(b("e0"), b("kc2"))] + places + score)
+        mm(b("B2", 0, AR), [(b("I256n"), b3("A16")), (b("IF"), b(LA))])
+        row([len(calls) - KE, len(calls) - 1])
+        act(b("cq"), b("B2", 0, AR))
         scan(b("KM"), b("mB"), b("B1", 0, 240), A.add, A.min)
         km = b("KM", NP - 1, 240, NP)
         ts(b("pm"), km, V - 1, None, A.bitwise_and)
@@ -626,30 +656,31 @@ def rank_program(g, core, T, topo):
         scan(b("P0"), b("m16"), b("pv0"), A.mult, A.add)
         act(b("xm"), ind(XW, b("pu")), bias=M31)
         act(b("C0", 0, AR), b("xm"), bias=-M31)
-        w1 = tt(b("w1"), ind(XW, b("pu")), b("cq"), A.add)
+        w1 = [tt(b("w1", 16 * lo, 16 * hi), ind(XW, b("pu", lo, hi)), b("cq", 16 * lo, 16 * hi), A.add) for lo, hi in ((0, W1ST), (W1ST, 20))]
         cn = tt(b("cn"), b("w1"), b("C0", 0, AR), A.subtract)
         if t < RO - 1:
             act(b("esq"), b("cn"), F.Square)
-            ts(b("ckb"), b("cn"), 127.0, -127.0, A.min, A.max)
+            cut = [ts(b("ckb"), b("cn"), 127.0, -127.0, A.min, A.max)]
             mm(b("B3", 0, AR), [(b("I256"), b3("A16")), (I1, b("ckb"))])
             act(b("xq"), b("B3", 0, AR), bias=524288.0 + 256.0 - OFF)
             mm(b("C1", 0, AR), [(b("BH"), b("esq"))])
-            ts(b("ft"), b("C1", 0, AR), 0.5, 2.0 * (OFF - 128.0), A.is_gt, A.mult)
         else:
-            ts(b("ft"), b("cn"), 127.0, -127.0, A.min, A.max)
             act(b("xq"), b3("A16"), bias=524288.0 + 128.0, scale=256.0)
         same = ([tt(b("EQ"), b("P0"), b("C2", 0, AR), A.is_equal)]
             + [tt(b3("EQ3", slice(4 * d - 4, 4 * d), slice(16 * (k - d), 16 * (k - d + 1))), b3("PB", full, slice(16 * k, 16 * k + 16)),
                   b3("C2", slice(k - d, 20, BW)), A.is_equal) for d in range(1, BW) for k in range(d, BW)])
-        at = CN if t < RO - 1 else len(same)
-        row([w1] + same[:at] + [cn] + same[at:])
+        row(w1[:1] + same[:CN] + w1[1:] + same[CN:CN + 4] + [cn] + same[CN + 4:] + cut if t < RO - 1 else w1[:1] + same + w1[1:] + [cn])
         mm(b("B1", 0, AR), [(b("I4kn"), b("EQ")), (I1, pvh, b("B1", 0, AR, 16)), (b("e0"), b("cT"), b("B1", 0, AR, 16))]
            + [(b("I4kn"), b3("EQ3", 4 * d - 4 + k, slice(0, 16 * (BW - d))), b("B1", 16 * (BW * k + d), 16 * BW * (k + 1)))
               for d in range(1, BW) for k in range(4)])
-        scan(b("DS"), b("m16"), b("B1", 0, AR), A.mult, A.add)
-        tt(b3("eou", full, slice(0, BW)), b("DS", 15, AR, 16), b("sw"), A.max)
         for k in sorted(range(N // near), key=lambda k: -land[core][near * k]):
             q = (16 * BW * k, 16 * BW * (k + 1))
+            scan(b("DS", *q), b("m16", *q), b("B1", *q), A.mult, A.add)
+            tt(b3("eou", k, slice(0, BW)), b("DS", q[0] + 15, q[1], 16), b("sw", 0, BW), A.max)
+            if t < RO - 1:
+                ts(b("ft", *q), b("C1", *q), 0.5, 2.0 * (OFF - 128.0), A.is_gt, A.mult)
+            else:
+                ts(b("ft", *q), b("cn", *q), 127.0, -127.0, A.min, A.max)
             tt(ind(b("X" if t < RO - 1 else "Y"), b3("eou", k, slice(0, BW))), b("xq", *q), b("ft", *q), A.add)
     for k, e in ((0, "y"), (1, "s")):
         dma(e, hbm(T.y[:, 1024 * k:1024 * k + 1024]), b("Y", TR + 1024 * k, TR + 1024 * k + 1024), "d%d" % (5 + k), LOAD + 3000)

@@ -5,34 +5,37 @@ from concourse.mybir import AluOpType as A, AxisListType, ActivationFunctionType
 N, V, CAP, S, RO, STEP, NP = 8, 2048, 40, 256, 2, 950, 12
 AR = N * CAP
 TR = 320
-M31 = 1.5 * 2.0 ** 31
 M27 = 1.5 * 2.0 ** 27
 M23 = 1.5 * 2.0 ** 23
-OFF = 2.0 ** 22
-SENT = -22528
-THETA = 7.05e8
-VF, KN, KF, VN, W1ST = (0, 1, 7, 11), 4, 0, (5,), 8
-PASSES, AHEAD, KA, KB, KC, CN = 2, 2, 6, 10, 14, 1
-YN, SA, SB, SC, D0, D1, G0 = 2, 0, 0, 0, 5, 3, [(0, 1), (1, 3), (3, 7), (7, 12)]
-SE, KD, KE = 4, 11, 3
+B18 = 1.5 * 2.0 ** 18
+SENT = -36864
+LOW, RISE = 2.0 ** -110, 2.0 ** 13
+TOP = LOW * RISE ** 15
+XB = (0, 1, 2, 0)
+PASSES = 2
+W1ST, CN = 8, 1
 NS = 4
 NV = 96
+ZHS, RES = 0, ()
+VROW, SROW = "F SZ zo SL qo zn s0 zf g2 s1 qf s2 s3 s4 s5", "g0 g1 g3 g4 g5"
+FARP = ((("v", 48), ("s", 64), ("s", 64)), (("s", 64),))
+NEARP = "ss"
 
 _DT = {"f": "float32", "b": "bfloat16", "h": "float16", "i": "int32", "u": "uint16"}
 _SBUF = """
-f X:2368 Y:2368 J:256 col:32 sw:20 swa:20 swb:20 U:136 dm:16 fo:16 fo2:16 Sx:256 Ks:256 hb:16 rk:16 cc:256 CHf:256 xg:256
-f iv:16 iv2:16 own:16 R4:4,32 R50:2,32 R51:3,32 R52:5,32 SL0:2304 SL1:2304 LA0:320 LA1:320 dd:3840 iv3:20 w1:320
-f MX:16 s9:144 Q1:480 iv4:20 xq:320 ft:320 cq:320 xm:320 cn:320 DS:320 t3:20 IF:128
-i XI:2048 X1:2048 pp_i:1 pq_i:1 pr_i:1 hp:16 hq:16 vi:16 vv:16 ch:16 ow:16 ah:24 Z0:4 Z1:6 Z2:60 st0:4 st1:6 st2:60 pm:20 Zi0:32 Zm0:32 Zi1:48 Zm1:48 Zi2:192 Zm2:192 KM:240
-i hi:2,16 ha:2,16 ci:4,8 ca:4,8 ai5:5,10 aa5:5,10
-h EB:128 cb:16 Dh:16,16 VK:256 VV:256 TK:256 VB:256 R1:16,16 m1:16,16 CH:16,16 A16:20,16 uh:24 ZH0:12,5 ZH1:12,15 pvs:320 pv0:320 P0:320 PB:4,80
-b HM:4096 NZ:2048 SG:2048 SR:2064 Lb:130 PL:130 cmp:2048 G:256 Cb:256 sC:256 Fb:256 Fl:256 Lg:4096 Mn:16,256 db:3840 th:256 sD:16,16
-b sE:256 ab:256 fsq:256 fsg:256 O:144 m9:144 sq:3840 ka0:12,5 kb0:12,5 ka1:12,15 kb1:12,15 ckb:320 esq:320 EQ:320 EQ3:16,64
-b Jb:256 JI:320 JG:128 PD:128 zero:128 ones:256 BH:128 ZS:144 MK:4 WL:8 base:64 kx:128 kc:128 e0:128 TI:128
-b SU:128 SD:128 PAR:128 PA2:128 AL:128 I592:8 B592:128 Ca:64 WT:16 EH:144 OH:144 ER:144 OR:144 EM:144 OM:144 E1:144 O1:144 CQ:128 CR1:128 CR2:128 c9:144
-b m16:320 dk:256 RX:2048 IM:1408 cz0:32 cz1:48 cz2:192 kc2:240 mB:240 cT:20 I1:128 Im1:128 I256n:128 I256:128 I4kn:128
-b I32kn:128 NUn:128
-u cu:16 plu:16 fou:16 Du:256 slu:16 zu0:32 zu1:48 zu2:192 pu:20 eou:4,6
+f X:2368 Y:2368 J:256 col:32 sw:20 swa:20 U:136 dm:16 fo:16 fo2:16 Sx:256 Ks:256 hb:16 rk:16 cc:256 CHf:256 xg:256
+f iv:16 iv2:16 own:16 R4:4,32 SL0:2304 SL1:2304 LA0:320 LA1:320 SZ0:2304 SZ1:2304 LZ0:320 LZ1:320 w1:320
+f MX:16 s9:144 xq:320 ft:320 cq:320 cn:320 DS:320 IF:128 zf:256 pw:16 pw2:16 fsg:256 thr:320
+i XI:2048 X1:2048 pp_i:1 pq_i:1 pr_i:1 hp:16 hq:16 vi:16 vv:16 ch:16 ow:16 Hi:16 dd:5120 xm:320
+i hi:2,16 ha:2,16 ci:4,8 ca:4,8
+h EB:128 cb:16 Dh:16,16 VK:256 VV:256 TK:256 VB:256 R1:16,16 m1:16,16 CH:16,16 A16:20,16 uh:16 Hh:16 zh:320 re:320 rr:320 PB:4,80 db:3840
+b HM:4096 NZ:2048 SR:2064 Lb:130 PL:130 cmp:2048 G:256 Cb:256 sC:256 Fb:256 Fl:256 Lg:4096 Mn:16,256 th:256 sD:16,16
+b sE:256 ab:256 fsq:256 R15:128 O:144 m9:144 ckb:320 esq:320 EQ:320 EQ3:16,64 qb:256 ee:320 ff:320 tri:320
+b Jb:256 JI:320 JG:128 PD:128 zero:128 ones:320 BH:128 ZS:144 MK:4 WL:8 base:64 kx:128 kc:128 e0:128 TI:128
+b SU:128 SD:128 PAR:128 PA2:128 I592:8 B592:128 Ca:64 WT:16 ER:144 OR:144 EM:144 OM:144 E1:144 O1:144 CR1:128 CR2:128 c9:144
+b m16:320 dk:256 RX:2048 RM:2048 cT:20 I1:128 Im1:128 I256n:128 I256:128 I4kn:128 NUn:128
+b ZD:144 ZP:144 BP:128 WE:128 WA:128 I12:128 TE:128 TF:128 mr:128 B2m:128
+u cu:16 plu:16 fou:16 Du:256 slu:16 zu:320 pu:20 eou:4,6
 """
 _ALL, SCRATCH, _AT = {}, {}, {}
 for _line in _SBUF.split("\n"):
@@ -52,7 +55,8 @@ for _n, (_w, _sh, _d) in _ALL.items():
         SCRATCH[_n] = (_w, _sh, _d)
 for _d, _c in _wide.items():
     SCRATCH["pack_" + _d] = ("sbuf", [128, _c], _d)
-SEMAPHORES = ["sv", "ss", "sp", "sg", "loc", "ar0", "ar1", "an0", "an1"] + ["d%d" % k for k in range(7)]
+SEMAPHORES = (["sv", "ss", "sp", "sg", "loc"] + [x + str(t) for x in ("LZn", "LZf", "LAn", "LAf") for t in range(RO)]
+              + ["d%d" % k for k in range(7)])
 
 CYC, PE, WAKE, GATHER, SCATTER = 0.83, 0.42, 200.0, 1.56, 3.0
 ACT, DRAIN, LOAD, SEND, NEAR, FAR, FIRST = 65.0, 0.0, 1000.0, 600.0, 1300.0, 1700.0, 1300.0
@@ -81,7 +85,7 @@ def order_calls(calls):
     for i, c in enumerate(calls):
         for d in c[3]:
             users[d].append(i)
-    gap = lambda d, i: calls[d][1] - calls[d][2] if calls[d][0] == calls[i][0] == "p" or d == calls[i][5] else WAKE
+    gap = lambda d, i: calls[d][1] - calls[d][2] if calls[d][0] == calls[i][0] == "p" or d in calls[i][5] else WAKE
     left = [len(u) for u in users]
     turn = [i for i in range(n) if not left[i]]
     for i in turn:
@@ -124,7 +128,7 @@ def rank_program(g, core, T, topo):
         return
     queue = {"v": g.vector, "s": g.scalar, "p": g.tensor, "g": g, "y": g.sync}
     semof = {"v": "sv", "s": "ss", "p": "sp", "g": "sg"}
-    calls, emit, acc = [], [], {}
+    calls, emit, acc, before = [], [], {}, {}
     full = slice(None)
 
     def b3(n, *ix):
@@ -132,7 +136,7 @@ def rank_program(g, core, T, topo):
         ix = ix + (full,) * (len(sh) - 1 - len(ix))
         on = np.zeros(sh[1:], bool)
         on[ix] = True
-        bits = -1 if w == "psum" else int.from_bytes(np.packbits(on).tobytes(), "little")
+        bits = int.from_bytes(np.packbits(on).tobytes(), "little")
         return T[n][(full,) + ix], [(n, bits)], int(on.sum()), dt in ("bfloat16", "float16", "uint16"), w == "psum", False, ix[0]
 
     def b(n, lo=0, hi=None, step=1):
@@ -161,11 +165,17 @@ def rank_program(g, core, T, topo):
         for kind, keys in ((0, sum([x[1] for x in ins] + outs[1], [])), (1, sum(outs[0], []))):
             for n, bits in keys:
                 lst = acc.setdefault(n, [])
-                need.update(j for b2, k2, j, e2 in lst if bits & b2 and (kind or k2 or bits == -1 and e != e2) and j != i)
+                if SCRATCH[n][0] == "psum":
+                    if lst and lst[-1][3] != e:
+                        before[n] = [r[2] for r in lst]
+                        lst.clear()
+                    need.update(before.get(n, []))
+                    bits = -1 if e == "p" else bits
+                need.update(j for b2, k2, j, e2 in lst if bits & b2 and (kind or k2) and j != i)
                 if kind:
                     lst[:] = [r for r in lst if r[0] & ~bits]
                 lst.append((bits, kind, i, e))
-        calls.append([e, cost, cost if late is None else late, sorted(need), more, None])
+        calls.append([e, cost, cost if late is None else late, sorted(need), more, set()])
         emit.append((call, sem))
         return i
 
@@ -173,7 +183,7 @@ def rank_program(g, core, T, topo):
         for d, i in zip(ids, ids[1:]):
             if d not in calls[i][3]:
                 calls[i][3].append(d)
-                calls[i][5] = d
+                calls[i][5].add(d)
 
     def vec(out, ins, per, fix=50.0):
         if out[5]:
@@ -198,8 +208,11 @@ def rank_program(g, core, T, topo):
     def cp(out, in_):
         return op("v", lambda: g.vector.tensor_copy(out[0], in_[0]), [out], [in_], vec(out, [in_], half(out, in_)))
 
-    def scan(out, d0, d1, o0, o1):
-        op("v", lambda: g.vector.tensor_tensor_scan(out[0], d0[0], d1[0], 0.0, o0, o1), [out], [d0, d1], vec(out, [d0], half(out, d0, d1)))
+    def fill(out, c):
+        return op("v", lambda: g.vector.memset(out[0], c), [out], [], vec(out, [out], half(out)))
+
+    def scan(out, d0, d1, o0, o1, first=0.0):
+        op("v", lambda: g.vector.tensor_tensor_scan(out[0], d0[0], d1[0], first, o0, o1), [out], [d0, d1], vec(out, [d0], half(out, d0, d1)))
 
     def vtr(out, in_):
         op("v", lambda: g.vector.transpose(out[0], in_[0]), [out], [in_], vec(out, [in_], 1))
@@ -208,6 +221,9 @@ def rank_program(g, core, T, topo):
         ins = [in_] + [x for x in (bias, scale) if isinstance(x, tuple)]
         return op("s", lambda: g.scalar.activation(out[0], in_[0], f, bias=sc(bias), scale=sc(scale)), [out], ins,
                   vec(out, ins, 1, 65.0) if in_[5] else ACT + in_[2] * CYC)
+
+    def lin(e, out, in_, scale, bias):
+        return act(out, in_, bias=bias, scale=scale) if e == "s" else ts(out, in_, scale, bias, A.mult, A.add)
 
     def mm(out, terms):
         for k, (l, r, *part) in enumerate(terms):
@@ -240,16 +256,16 @@ def rank_program(g, core, T, topo):
     op("r", None, [b("HM")], [], 0.0, LOAD + 3500, ("d4", 16))
 
     cell = [divmod(STEP * (t + 1), 16) for t in range(RO)]
-    PP, PI, PG, PG16, OD, SIG, SI2, W1, W2, PGE, PGO, CE, CO, CE1, CO1, FIRSTROW, N15, WR1, WR2, WM1, WM2 = [b("col", k, k + 1) for k in range(21)]
+    (PP, PI, PG, PG16, OD, SIG, SI2, W1, W2, PGE, PGO, CE, CO, CE1, CO1, N12, N15, WR1, WR2, WM1, WM2,
+     PW, P15) = [b("col", k, k + 1) for k in range(23)]
     diag = [[-1, 128]]
-    blk = [[-16, 8], [0, 16]]
     iota(b("pp_i"), [[0, 1]], 0, 1)
     iota(b("Jb"), [[1, 256]], 0)
     iota(b("JG"), [[1, 8], [0, 16]], 0)
     iota(b("PD"), [[1, 128]], 0, -1)
     iota(b("kx"), [[0, 8], [-1, 16]], 0)
-    op("v", lambda: g.vector.memset(b("zero")[0], 0.0), [b("zero")], [], 64 * CYC)
-    op("v", lambda: g.vector.memset(b("ones")[0], 1.0), [b("ones")], [], 128 * CYC)
+    fill(b("zero"), 0.0)
+    fill(b("ones"), 1.0)
     ts(b("pq_i"), b("pp_i"), 15, None, A.bitwise_and)
     ts(b("pr_i"), b("pp_i"), 4, None, A.arith_shift_right)
     act(PP, b("pp_i"))
@@ -276,8 +292,7 @@ def rank_program(g, core, T, topo):
     sel(b("NUn"), b("BH"), diag, A.is_gt, 0.0, 0, 1)
     ts(b("NUn"), b("NUn"), -1.0, None, A.mult)
     iota(b("JI"), [[0, 20], [1, 16]], 0)
-    for n, c in (("I256n", -256.0), ("Im1", -1.0), ("IF", 256.0), ("I4kn", -4096.0), ("I256", 256.0),
-                 ("I32kn", -32768.0)):
+    for n, c in (("I256n", -256.0), ("Im1", -1.0), ("IF", 256.0), ("I4kn", -4096.0), ("I256", 256.0)):
         ts(b(n), b("I1"), c, None, A.mult)
     ts(b("pq_i"), b("pp_i"), 1, None, A.bitwise_and)
     ts(b("pr_i"), b("pr_i"), 1, None, A.bitwise_and)
@@ -296,7 +311,7 @@ def rank_program(g, core, T, topo):
     for pg, ce, c1, side in ((PGE, CE, CE1, "E"), (PGO, CO, CO1, "O")):
         act(ce, pg, scale=0.5, bias=3.0)
         act(c1, pg, bias=11.0)
-        for n, ws in (("H", (W1, W2)), ("R", (WR1, WR2)), ("M", (WM1, WM2))):
+        for n, ws in (("R", (WR1, WR2)), ("M", (WM1, WM2))):
             for k in range(2):
                 ts(b(side + n, k, 144, 2), b("Jb", 0, 72), ce, ws[k], A.is_equal, A.mult)
         ts(b(side + "1"), b("Jb", 0, 144), c1, SIG, A.is_equal, A.mult)
@@ -315,43 +330,49 @@ def rank_program(g, core, T, topo):
     iota(b("CR1"), [[0, 128]], -240)
     sel(b("CR1"), b("CR1"), [[0, 8], [1, 16]], A.not_equal, -176.0, -15, 0)
     sel(b("CR2"), b("zero"), [[0, 8], [1, 16]], A.not_equal, -64.0, 0, 0)
-    act(b("VK"), b("ones"), scale=-7.5)
-    act(b("VV"), b("ones"), scale=0.0)
-    sel(b("CQ"), b("zero"), [[0, 128]], A.not_equal, M31, 0, 1)
-    sel(b("CQ"), b("CQ"), [[0, 128]], A.not_equal, 524288.0 + OFF, -1, 1)
+    act(b("VK"), b("ones", 0, 256), scale=-7.5)
+    act(b("VV"), b("ones", 0, 256), scale=0.0)
     iota(b("c9"), [[0, 16], [256, 9]], -4096)
     sel(b("m9"), b("ones", 0, 144), [[0, 16], [1, 9]], A.not_equal, 0.0, 0, 0)
-    sel(b("AL"), b("zero"), blk, A.not_equal, OFF, 0, 1)
-    sel(b("AL"), b("AL"), blk, A.not_equal, -128.0, -1, 1)
-    for o in range(N):
-        iota(b("SL0", 256 * o, 256 * o + CAP), [[0, CAP]], SENT)
-    for m in range(1, NP):
-        ts(b("IM", 128 * m - 128, 128 * m), b("I1"), 2.0 * m, None, A.mult)
-    for k, w in enumerate((2, 3, 15)):
-        iota(b("cz%d" % k, w + w % 2, 12 * w + w % 2), [[1, 11], [0, w]], 1)
-    iota(b("kc2"), [[0, 20], [2048, 12]], -81920)
+    for t in range(RO):
+        for n, c in (("SZ", 0), ("SL", SENT)):
+            for o in range(N):
+                iota(b(n + str(t), 256 * o, 256 * o + CAP), [[0, CAP]], c)
     iota(b("cT"), [[0, 20]], TR)
-    iota(b("mB"), [[0, 240]], 0)
-    iota(b("mB", 0, 240, NP), [[0, 20]], 1 << 21)
-    ts(b("pvs"), b("JI"), 0.0, None, A.mult)
-    ts(b("pv0"), b("JI"), PI, 8192.0, A.is_equal, A.mult)
-    ts(FIRSTROW, PI, 0.0, 8192.0, A.is_equal, A.mult)
     ts(b("MX"), b("Jb", 0, 16), PI, None, A.is_equal)
+    tt(b("B2m"), b("BH"), b("kx"), A.mult)
+    ts(b("mr"), b("kx"), b("e0", 0, 1), -1.0, A.mult, A.mult)
     for x in range(16):
         ts(b("RX", 128 * x, 128 * x + 128), b("BH"), b("MX", x, x + 1), None, A.mult)
-    for o in range(N):
-        iota(b("SL1", 256 * o, 256 * o + CAP), [[0, CAP]], SENT)
+        ts(b("RM", 128 * x, 128 * x + 128), b("B2m"), b("MX", x, x + 1), -2.0, A.mult, A.mult)
+    ts(b("tri"), b("JI"), PI, 8192.0, A.is_ge, A.mult)
+    ts(b("pw"), b("Jb", 0, 16), PI, RISE - 1.0, A.is_lt, A.mult)
+    ts(b("pw"), b("pw"), 1.0, None, A.add)
+    scan(b("pw2"), b("pw"), b("zero", 0, 16), A.mult, A.add, LOW)
+    ts(b("ZD"), b("ZS"), b("pw2", 15, 16), None, A.mult)
+    ts(P15, PI, 15.0, TOP, A.is_equal, A.mult)
+    ts(b("R15"), b("BH"), P15, None, A.mult)
+    ts(N12, PI, float(NP), None, A.is_lt)
+    ts(PW, PI, float(NP), -4097.0, A.is_equal, A.mult)
+    act(PW, PW, bias=1.0)
+    ts(b("ZP"), b("ZS"), PW, None, A.mult)
+    ts(b("BP"), b("BH"), PW, None, A.mult)
+    ts(b("I12"), b("I1"), N12, None, A.mult)
+    ts(b("WA"), b("BH"), N12, -4096.0, A.mult, A.mult)
+    sel(b("WE"), b("WA"), [[1, 128]], A.is_ge, 0.0, 0, -1)
+    sel(b("WE"), b("WE"), diag, A.not_equal, 4096.0, 0, 1)
+    iota(b("TE"), [[0, 128]], -32)
+    sel(b("TF"), b("TE"), [[0, 8], [1, 16]], A.not_equal, 1.0 / 128.0, -NP, 0)
 
-    def zs(x):
-        return b("ZS", 15 - x, 143 - x)
+    def zs(x, n="ZS"):
+        return b(n, 15 - x, 143 - x)
 
     XW = b("X", TR, TR + V)
     plan = {d: routes(d, T, topo) for d in T.cores}
     land = {d: landing(d, T, topo) for d in T.cores}
     near = sum(topo.chip(d) == topo.chip(core) for d in T.cores)
     BW = near * CAP // 16
-    own = CAP // 16
-    PART = (((0, own), (own, BW)) if land[core][0] == me else ((BW - own, BW), (0, BW - own))) + ((BW, AR // 16),)
+    mine = CAP * land[core].index(me)
     sent = [0]
     I1, Im1 = b("I1"), b("Im1")
 
@@ -403,11 +424,14 @@ def rank_program(g, core, T, topo):
         ts(b("dm"), b("sw", 0, 16), b("U", 129, 130), -8192.0, A.is_ge, A.mult)
         if t == 0:
             for k in range(4):
-                mm(b("C%d" % k), [(b("BH"), b("NZ", *q4(k)))])
-                act(b("SG", *q4(k)), b("C%d" % k), F.Sign, bias=-0.5)
-        win, off = (b("XI"), 128.0) if t == 0 else (XW, OFF)
-        ts(b("Du"), ind(win, b("plu")), 1.0 / 256.0, -off / 256.0, A.mult, A.add)
-        act(b("Sx"), ind(win, b("plu")), F.Relu, bias=(128.0 - off) / 256.0, scale=1.0 / 256.0)
+                bank = "C%d" % XB[k]
+                mm(b(bank), [(b("BH"), b("NZ", *q4(k)))])
+                act(b(bank), b(bank), F.Sign, bias=-0.5)
+                for lo in (512 * k, 512 * k + 256):
+                    tt(b("X", TR + lo, TR + lo + 256), b("XI", lo, lo + 256), b(bank, lo % 512, lo % 512 + 256), A.mult)
+        win = b("XI") if t == 0 else XW
+        ts(b("Du"), ind(win, b("plu")), 1.0 / 256.0, -0.5, A.mult, A.add)
+        act(b("Sx"), ind(win, b("plu")), F.Relu, scale=1.0 / 256.0)
         tt(b("fo"), b("dm"), b("B2", 0, 16), A.add)
         dh = ts(b("Dh"), b("Du"), -2048.0, None, A.add)
         CB0 = -524288.0 - 128.0
@@ -415,7 +439,7 @@ def rank_program(g, core, T, topo):
         first = [act(b("C3", 0, 192), b("B3", 0, 192), F.Abs, bias=CB0), act(b("Ca"), b("B3", 192, S), F.Abs, bias=CB0)]
         for h in range(2):
             mm(b("B0", 16 * h, 16 * h + 16), [(b("Dh", 128 * h, 128 * h + 128), b("WT"))])
-        mine = [cp(b("Lg", 0, 16 * NV), ind(b("HM"), b("Du", 0, NV)))]
+        mineL = [cp(b("Lg", 0, 16 * NV), ind(b("HM"), b("Du", 0, NV)))]
         look = [act(b("Lg", 16 * lo, 16 * hi), ind(b("HM"), b("Du", lo, hi)), F.Copy) for lo, hi in ((NV, 128), (192, S), (128, 192))]
         least = [tt(b3("Mn", k, slice(lo, hi)), b("Lg", 16 * lo + k, 16 * hi, 16), b("C3", lo, hi), A.min)
                  for lo, hi in ((0, 64), (64, 128), (128, 192)) for k in range(16)]
@@ -435,7 +459,7 @@ def rank_program(g, core, T, topo):
                  tt(b("hp"), b3("ha", full, slice(0, 8)), b3("ha", full, slice(8, 16)), A.mult),
                  ts(b("hq"), b("hp"), 5, None, A.arith_shift_right),
                  ts(b("hb"), b("hq"), 16.0, M27 + 16.0 * t, A.mult, A.add)]
-        row([dh] + mine + [x for k in range(5) for x in [steps[k]] + least[4 * k:4 * k + 4]] + least[20:])
+        row([dh] + mineL + [x for k in range(5) for x in [steps[k]] + least[4 * k:4 * k + 4]] + least[20:])
         act(b("Cb"), b("B3", 0, 256), bias=CB0)
         for h in range(2):
             scan(b("Ks", 128 * h, 128 * h + 128), b("m16", 0, 128), b("B%d" % (1 + h), 0, 128), A.mult, A.max)
@@ -450,7 +474,7 @@ def rank_program(g, core, T, topo):
 
         def turned(bank, n, w):
             return [(b(n, h, h + 128), w, b(bank, h, h + 128)) for h in (0, 128)]
-        DH, ONE = b("Dh"), b("ones")
+        DH, ONE = b("Dh"), b("ones", 0, 256)
         mm(b("B0", 0, 256), [(b("SU"), DH), (b("CR1"), ONE)] + turned("B0", "TK", b("I4kn")))
         tt(b("R1"), DH, b("B0", 0, 256), A.max)
         mm(None, turned("B3", "VB", I1))
@@ -482,206 +506,135 @@ def rank_program(g, core, T, topo):
         ts(b("O", 8, 144, 9), b("iv2"), 0.0, None, A.is_lt)
         ts(b("ow"), b("ch"), 5, 7, A.arith_shift_right, A.bitwise_and)
         tt(b("own"), b("ow"), b("iv2"), A.add)
+        ts(b("uh"), b3("ca", full, slice(0, 8, 2)), -2048.0, None, A.add)
+        ts(b("Hi"), b("ch"), 8, V - 1, A.arith_shift_right, A.bitwise_and)
+        cp(b("Hh"), b("Hi"))
+        mm(b("B0", 0, S), [(b("mr"), ONE)] + [(b(n, 128 * x, 128 * x + 128), b(u), b("B0", x, S, 16))
+                                              for n, u in (("RM", "uh"), ("RX", "Hh")) for x in range(16)])
+        act(b("qb"), b("B0", 0, S), bias=B18 - 1023.5)
+        tt(b("zf"), b("B0", 0, S), b("qb"), A.subtract)
         for o in range(8):
             ts(b("O", o, 144, 9), b("own"), float(o), None, A.is_equal)
         mm(b("B3", 0, 144), [(b("e0"), b("c9")), (b("TI"), b("O"))] + [(b("BH"), b("O", 0, 144 - 9 * d), b("B3", 9 * d, 144)) for d in range(1, 16)])
         scan(b("s9"), b("m9"), b("B3", 0, 144), A.mult, A.max)
         cp(b("slu"), b("s9", 8, 144, 9))
-        SL, LA = "SL%d" % t, "LA%d" % t
-        packed = tt(ind(b(SL), b("slu")), b("cc"), b("CHf"), A.add)
+        SL, LA, SZ, LZ = [x + str(t) for x in ("SL", "LA", "SZ", "LZ")]
+        scat = [ts(ind(b(SZ), b("slu")), b("zf"), 1.0, B18, A.mult, A.add), tt(ind(b(SL), b("slu")), b("cc"), b("CHf"), A.add)]
         sends = []
-        for call in (0, 1):
-            tr = []
-            for cl, d, eng in plan[core]:
-                if cl != call:
-                    continue
-                o, at = T.rank_of(d), CAP * land[d].index(me)
-                tr.append(RemoteDMATransfer(
-                    dst_ids=[DstId(rid=topo.addr(d)[0], pnc=topo.addr(d)[1])], dma_engine_mask=sum(1 << e for e in eng),
-                    remote_sem=T.sem[("an%d" if topo.chip(d) == topo.chip(core) else "ar%d") % t],
-                    src=T[SL][:, 256 * o:256 * o + CAP], dst=T[LA][:, at:at + CAP]))
-                sent[0] += len(eng)
-            sends.append(op("g", lambda tr=tr: g.remote_dma_fused(tr, local_sem=T.sem.loc), [], [b(SL)], SEND, None, ("", 0)))
+        for src, dst in ((SZ, LZ), (SL, LA)):
+            for call in (0, 1):
+                tr = []
+                for cl, d, eng in plan[core]:
+                    if cl != call:
+                        continue
+                    o, at = T.rank_of(d), CAP * land[d].index(me)
+                    tr.append(RemoteDMATransfer(
+                        dst_ids=[DstId(rid=topo.addr(d)[0], pnc=topo.addr(d)[1])], dma_engine_mask=sum(1 << e for e in eng),
+                        remote_sem=T.sem[dst[:2] + "fn"[topo.chip(d) == topo.chip(core)] + str(t)],
+                        src=T[src][:, 256 * o:256 * o + CAP], dst=T[dst][:, at:at + CAP]))
+                    sent[0] += len(eng)
+                sends.append(op("g", lambda tr=tr: g.remote_dma_fused(tr, local_sem=T.sem.loc), [], [b(src)], SEND, None, ("", 0)))
+            for nr in (True, False):
+                there = [d for d in T.cores if d != core and (topo.chip(d) == topo.chip(core)) == nr]
+                tot = sum(len(e) for s in there for _, x, e in plan[s] if x == core)
+                at = [CAP * land[core].index(T.rank_of(d)) for d in there]
+                i = op("r", None, [b(dst, a, a + CAP) for a in at], [], 0.0, (NEAR if nr else FAR) + FIRST * (t == 0 and src == SZ),
+                       (dst[:2] + "fn"[nr] + str(t), tot))
+                calls[i][3].append(sends[-2 if nr else -1])
         row(sends)
-        for nr in (True, False):
-            there = [d for d in T.cores if d != core and (topo.chip(d) == topo.chip(core)) == nr]
-            tot = sum(len(e) for s in there for _, x, e in plan[s] if x == core)
-            at = [CAP * land[core].index(T.rank_of(d)) for d in there]
-            i = op("r", None, [b(LA, a, a + CAP) for a in at], [], 0.0, (NEAR if nr else FAR) + FIRST * (t == 0), (("an%d" if nr else "ar%d") % t, tot))
-            calls[i][3].append(sends[0 if nr else 1])
-        at = CAP * land[core].index(me)
-        act(b(LA, at, at + CAP), b(SL, 256 * me, 256 * me + CAP))
+        act(b(LA, mine, mine + CAP), b(SL, 256 * me, 256 * me + CAP))
         act(b("sC"), b("Cb"), F.Sign)
         fade = [(I1, b("Cb")), (Im1, b("sC"))]
         mm(b("C3", 0, 256), fade)
         act(b("fsq"), b("C3", 0, 256), F.Square)
         mm(b("C3", 0, 256), [(b("BH"), b("fsq"))])
         act(b("fsg"), b("C3", 0, 256), F.Sign, bias=-0.5)
-        mm(b("C3", 0, 256), fade + [(b("I256"), DH), (b("AL"), b("fsg"))])
+        mm(b("C3", 0, 256), fade + [(b("I256"), DH)])
         act(b("xg"), b("C3", 0, 256), bias=-CB0)
         tt(b("fo2"), b("fo"), b("swa", 0, 16), A.max)
         ts(b("fou"), b("fo2"), float(TR), None, A.add)
-
-        done = []
-
-        def flagged(out, in_, at, o):
-            for k in range(4):
-                bank = "C0" if k % 2 and not t else "C3"
-                mm(b(bank), [(b("AL"), b("SG", *q4(k)))])
-                for h in (0, 256):
-                    lo = 512 * k + h
-                    done.append(tt(b(out, TR + lo, TR + lo + 256), b(in_, at + lo, at + lo + 256), b(bank, h, h + 256), o))
-        if t == 0:
-            flagged("X", "XI", 0, A.add)
-        faded = cp(ind(b("X"), b("fou")), b("xg"))
+        faded = tt(ind(b("X"), b("fou")), b("xg"), b("fsg"), A.mult)
         if t == RO - 1:
             for k in range(4):
-                act(b("SG", *q4(k)), b("X", TR + 512 * k, TR + 512 * k + 512), F.Sign)
-            flagged("Y", "X", TR, A.subtract)
+                act(b("Y", TR + 512 * k, TR + 512 * k + 512), b("X", TR + 512 * k, TR + 512 * k + 512), F.Abs)
 
-        banks, places, score = ["C0", "C0", "C2", "C1", "C0"], [], []
-        for which, (c1, c2) in enumerate(PART):
-            part = int(which == 2)
-            if which < 2:
-                row(looks + [] if which else [])
-                row(fused + [] if which else [])
-                looks, fused, tests = [], [], []
-            w = c2 - c1
-            n, ways, a0, z0, q0 = 16 * w, 1 + 2 * part, 16 * c1, 16 * NP * c1, (6, 8, 0)[which]
-            nb = slice(0, w // ways)
-            A16 = b3("A16", slice(c1, c2))
-            zu, Zi, Zm, cz, R, Z, st = [x + str(which) for x in ("zu", "Zi", "Zm", "cz", "R5", "Z", "st")]
-            k0, linear = NP * c1, []
-            at = [0] + [w + w % 2 + w * m for m in range(NP)]
-            u1, u2 = b3("aa5", nb, slice(q0, q0 + 2 * ways, 2)), b3("aa5", nb, slice(q0 + 1, q0 + 2 * ways, 2))
-            ai5, aa5 = [b3(x, nb, slice(q0, q0 + 2 * ways)) for x in ("ai5", "aa5")]
-            ah, uh = [b(x, c1, c2) for x in ("ah", "uh")]
-            hb = "C%d" % (2 - part)
-            i = ts(A16, b(LA, a0, a0 + n), M23, -M23, A.add, A.add)
-            row(([faded, i], [], done[:YN] + [i])[which] if t else [])
-            mm(b(hb, 0, 32 * nb.stop), [(b(nh, 6 - 2 * j, 134 - 2 * j), b3("A16", slice(c1 + j, c2, ways)), b3(hb, slice(par, 2 * nb.stop, 2)))
-                                        for par, nh in ((0, "EH"), (1, "OH")) for j in range(ways)])
-            groups = [(0, 1), (1, 3), (3, 5), (5, 7), (7, 9), (9, 11), (11, 12)] if part else G0
-            Q, many = "B0" if part else "B3", 1 if part else 5
-            mm(b(Q, 0, n * many), [(b("CQ"), b("ones", 0, n * many))] + [(b("I256"), A16, b(Q, n * k, n * k + n)) for k in range(many)])
-            for k in range(2 * part):
-                act(b("Q1", n * k, n * k + n), A16, bias=524288.0 + OFF - M31, scale=256.0)
-            vtr(b3(R), b(hb, 0, 32 * nb.stop))
-            cp(ai5, b3(R, full, slice(0, 2 * ways)))
-            ts(aa5, ai5, 4095, None, A.bitwise_and)
-            tt(ah, u1, u2, A.mult)
-            ts(uh, u1, -2048.0, None, A.add)
-            near1 = D0 if part else D1
-            for m in range(1, near1):
-                if part and m > SE:
-                    act(b(st, w * m - w, w * m), u1, bias=float(m), scale=2.0 * m)
-                else:
-                    ts(b(st, w * m - w, w * m), u1, 2.0 * m, float(m), A.mult, A.add)
-            for m in range(max(1, near1 - 1)):
-                ts(b(Z, w * m, w * m + w), ah, 8, V - 1, A.arith_shift_right, A.bitwise_and)
-            cp(b(zu, 0, w), b(Z, 0, w))
-
-            def by(name, m0, m1):
-                return b3(name + str(part), slice(m0, m1), slice(c1 - BW * part, c2 - BW * part))
-            cp(by("ZH", 0, 1), b(Z, 0, w))
-            for m0, m1, bank in ((1, near1, None), (near1, NP, "B2"))[near1 == 1:]:
-                r = (at[m0], at[m1])
-                if bank:
-                    mm(b(bank, *r), [(b("e0"), b(cz, *r))]
-                       + [(b("IM", 128 * m - 128, 128 * m), uh, b(bank, at[m], at[m] + w)) for m in range(m0, m1)]
-                       + [(I1, by("ZH", 0, 1), b(bank, at[m], at[m] + w)) for m in range(m0, m1)])
-                    (act if part or SA else cp)(b(Zi, *r), b(bank, *r))
-                else:
-                    tt(b(Zi, *r), b(Z, 0, r[1] - r[0]), b(st, 0, r[1] - r[0]), A.add)
-                ts(b(Zm, *r), b(Zi, *r), V - 1, None, A.bitwise_and)
-                (act if (part or SA) and bank else cp)(b(zu, *r), b(Zm, *r))
-                (act if SB > part else cp)(by("ZH", m0, m1), b(zu, *r))
-            for m0, m1 in groups:
-                d = (z0 + n * m0, z0 + n * m1)
-                look = ind(XW, b(zu, at[m0], at[m0] + w * (m1 - m0)))
-                if part and m0 in VF:
-                    fused.append(tt(b("dd", *d), look, b("Q1", 0, n * (m1 - m0)), A.subtract))
-                    k = 2 if m1 == NP else 1
-                    looks += [act(b("sq", d[0] + x, d[1], k), b("dd", d[0] + x, d[1], k), F.Square, bias=-M31 / 1024.0, scale=1.0 / 1024.0)
-                              for x in range(k)]
-                    continue
-                looks.insert(len(looks) - AHEAD * (part and m0 > 0), act(b("dd", *d), look, bias=M31))
-                for m in range(m0, m1, many):
-                    e = (z0 + n * m, z0 + n * min(m1, m + many))
-                    fused.append(tt(b("db", *e), b(Q, 0, e[1] - e[0]), b("dd", *e), A.subtract))
-                if part or m1 == NP:
-                    d = d if part else (z0, z0 + n * NP)
-                    if which == 1 and not SC or part and m0 in VN:
-                        i = ts(b("sq", *d), b("db", *d), 0.0, 37.0 * 2 ** 20, A.not_equal, A.mult)
-                        tests.append([i])
-                        linear += range(m0 * part, m1)
-                    else:
-                        looks.append(act(b("sq", *d), b("db", *d), F.Square, scale=1.0 / 1024.0))
-            for m0 in (0, 4, 8) if part else (0,):
-                m1 = m0 + 4 if part else NP
-                k = (k0 + w * m0, k0 + w * m1)
-                ms, bank = [m for m in linear if m0 <= m < m1], banks.pop(0)
-                more = [(zs(x), b("db", z0 + n * ms[0] + x, z0 + n * ms[-1] + n, 16), b3(bank, slice(ms[0] - m0, ms[-1] + 1 - m0), slice(0, w)))
-                        for x in range(16) if ms]
-                bank = b3(bank, slice(0, m1 - m0), slice(0, w))
-                mm(bank, [(b("zero"), b("ones", 0, k[1] - k[0]))] * (0 < len(ms) < m1 - m0) + more
-                   + [(zs(x), b("sq", 16 * k[0] + x, 16 * k[1], 16)) for x in sorted(range(16), key=lambda x: x % 2)])
-                tests.append([ts(by("ka", m0, m1), bank, 0.0, -2.0, A.is_gt, A.mult), ts(by("kb", m0, m1), bank, THETA, -0.5, A.is_gt, A.add)])
-                if m0 < 8:
-                    tt(by("kb", m0, m1), by("kb", m0, m1), by("ka", m0, m1), A.add)
-                for m in range(m0, m1) if which else ():
-                    into = b("B1", NP * BW * part + m, NP * (c2 if part else BW), NP)
-                    places.append((I1, b3("ZH%d" % part, m), into))
-                    score += [(b("I32kn"), b3(x + str(part), m), into) for x in ("ka", "kb")[m0 < 8:]]
-        row(looks)
-        fused = fused[:KN] + fused[4:4 + KF] + fused[KN:4] + fused[4 + KF:]
-        tests = [[]] * SC + tests
-        row(fused[:KA] + tests[0] + fused[KA:KB] + tests[1] + fused[KB:KD] + tests[2] + fused[KD:KC] + tests[3] + fused[KC:])
-        mm(b("B1", 0, 240), [(b("e0"), b("kc2"))] + places + score)
-        mm(b("B2", 0, AR), [(b("I256n"), b3("A16")), (b("IF"), b(LA))])
-        row([len(calls) - KE, len(calls) - 1])
-        act(b("cq"), b("B2", 0, AR))
-        scan(b("KM"), b("mB"), b("B1", 0, 240), A.add, A.min)
-        km = b("KM", NP - 1, 240, NP)
-        ts(b("pm"), km, V - 1, None, A.bitwise_and)
-        ts(b("iv3"), km, 0.0, -4096.0, A.is_ge, A.mult)
-        ts(b("iv4"), b("iv3"), FIRSTROW, None, A.add)
-        pvh = b("pvs", 0, AR, 16)
-        tt(pvh, b("pm"), b("iv3"), A.add)
-        tt(b("pv0", 0, AR, 16), b("pm"), b("iv4"), A.add)
-        cp(b("pu"), b("pm"))
-        mm(None, [(b("RX", 128 * x, 128 * x + 128), pvh, b("C2", x, AR, 16)) for x in range(16)])
+        other = CAP - mine
+        did = dict(SZ=scat[:1], SL=scat[1:], F=[faded])
+        for x, lo, hi, z, rec in (("o", mine, mine + CAP, b(SZ, 256 * me, 256 * me + CAP), b(SL, 256 * me, 256 * me + CAP)),
+                                  ("n", other, other + CAP, b(LZ, other, other + CAP), b(LA, other, other + CAP)),
+                                  ("f", 2 * CAP, AR, b(LZ, 2 * CAP, AR), b(LA, 2 * CAP, AR))):
+            did["z" + x] = [cp(b("zu", lo, hi), z)]
+            did["q" + x] = [ts(b("B0", lo, hi), rec, M23 + 2048.0, -M23, A.add, A.add)]
+        groups, lo = [[(NEARP[0], mine, mine + CAP), (NEARP[1], other, other + CAP)]], 2 * CAP
+        for some in FARP:
+            groups.append([])
+            for e, n in some:
+                groups[-1].append((e, lo, lo + n))
+                lo += n
+        for k, (e, lo, hi) in enumerate(sum(groups, [])):
+            did["g%d" % k] = [lin(e, b("dd", 16 * lo, 16 * hi), ind(XW, b("zu", lo, hi)), 1.0 / 256.0, -0.5)]
+            did["s%d" % k] = [tt(b("db", at, at + hi - lo), b("B0", lo, hi), b("dd", 16 * lo + m, 16 * hi, 16), A.subtract)
+                              for m in range(NP) for at in [NP * lo + m * (hi - lo)]]
+        for x, lo, hi in (("n", 0, 2 * CAP), ("f", 2 * CAP, AR)):
+            did["a" + x] = [ts(b("A16", lo, hi), b(LA, lo, hi), M23, -M23, A.add, A.add)]
+            did["h" + x] = [(act if ZHS else cp)(b("zh", lo, hi), b("zu", lo, hi))]
+            mm(b("C3", 0, hi - lo), [(b("R15"), b("A16", lo, hi))])
+            did["t" + x] = [act(b("thr", lo, hi), b("C3", 0, hi - lo), F.Relu, bias=2048.0 * TOP)]
+        for k, (some, bank, tb) in enumerate(zip(groups, ("B3", "C2", "C0"), ("C1", "B", "C1"))):
+            lo, hi = min(x[1] for x in some), max(x[2] for x in some)
+            n = hi - lo
+            TE, TF = (b("B1", 0, n), b("B2", 0, n)) if tb == "B" else (b(tb, 0, n), b(tb, n, 2 * n))
+            mm(b(bank, 0, n), [(zs(m, "ZD"), b("db", NP * p + m * (q - p), NP * p + (m + 1) * (q - p)), b(bank, p - lo, q - lo))
+                               for e, p, q in some for m in range(NP)])
+            did["e%d" % k] = [ts(b("ee", lo, hi), b(bank, 0, n), 0.0, None, A.is_equal),
+                              tt(b("ff", lo, hi), b(bank, 0, n), b("thr", lo, hi), A.is_gt)]
+            one, zh, ee, ff = [b(x, lo, hi) for x in ("ones", "zh", "ee", "ff")]
+            te = [(b("TE"), one, TE), (b("I12"), zh, TE), (b("WE"), ee, TE)]
+            tf = [(b("TF"), one, TF), (b("I12"), zh, TF), (b("WA"), ee, TF), (b("WE"), ff, TF)]
+            if tb == "B":
+                mm(TE, te)
+                mm(TF, tf)
+            else:
+                mm(b(tb, 0, 2 * n), te[:2] + tf[:2] + te[2:] + tf[2:])
+            did["r%d" % k] = [act(b("re", lo, hi), TE, F.Relu) if k in RES else ts(b("re", lo, hi), TE, 0.0, None, A.max)]
+            did["x%d" % k] = [tt(b("rr", lo, hi), TF, b("re", lo, hi), A.max)]
+        for line in (VROW, SROW):
+            row(sum([did[x] for x in line.split()], []))
+        mm(b("C3", 0, AR), [(b("I256n"), b3("A16")), (b("IF"), b(LA))])
+        act(b("cq"), b("C3", 0, AR))
+        mm(b("B3", 0, AR), [(b("zero"), b("ones"))] + [(zs(x, "ZP"), b("rr", x, AR, 16), b("B3", 0, AR, 16)) for x in range(16)])
+        mm(b("C1", 0, AR), [(I1, b("tri")), (b("BP"), b("rr"))])
+        mm(b("C0", 0, AR), [(b("BP"), b("rr"))])
+        cp(b("pu"), b("B3", 0, AR, 16))
         for k in range(4):
-            scan(b3("PB", k), b("m16", 0, 80), b("pvs", 80 * k, 80 * k + 80), A.mult, A.add)
-        scan(b("P0"), b("m16"), b("pv0"), A.mult, A.add)
-        act(b("xm"), ind(XW, b("pu")), bias=M31)
-        act(b("C0", 0, AR), b("xm"), bias=-M31)
+            scan(b3("PB", k), b("m16", 0, 80), b("B3", 80 * k, 80 * k + 80), A.mult, A.add)
+        act(b("xm"), ind(XW, b("pu")), bias=-0.5, scale=1.0 / 256.0)
+        act(b("B0", 0, AR), b("xm"), bias=128.0, scale=256.0)
         w1 = [tt(b("w1", 16 * lo, 16 * hi), ind(XW, b("pu", lo, hi)), b("cq", 16 * lo, 16 * hi), A.add) for lo, hi in ((0, W1ST), (W1ST, 20))]
-        cn = tt(b("cn"), b("w1"), b("C0", 0, AR), A.subtract)
+        cn = tt(b("cn"), b("w1"), b("B0", 0, AR), A.subtract)
         if t < RO - 1:
             act(b("esq"), b("cn"), F.Square)
             cut = [ts(b("ckb"), b("cn"), 127.0, -127.0, A.min, A.max)]
-            mm(b("B3", 0, AR), [(b("I256"), b3("A16")), (I1, b("ckb"))])
-            act(b("xq"), b("B3", 0, AR), bias=524288.0 + 256.0 - OFF)
-            mm(b("C1", 0, AR), [(b("BH"), b("esq"))])
+            mm(b("B2", 0, AR), [(b("I256"), b3("A16")), (I1, b("ckb"))])
+            act(b("xq"), b("B2", 0, AR), bias=524288.0 + 128.0)
+            mm(b("C2", 0, AR), [(b("BH"), b("esq"))])
+            act(b("ft"), b("C2", 0, AR), F.Sign, bias=-0.5)
         else:
             act(b("xq"), b3("A16"), bias=524288.0 + 128.0, scale=256.0)
-        same = ([tt(b("EQ"), b("P0"), b("C2", 0, AR), A.is_equal)]
+        same = ([tt(b("EQ"), b("PB"), b("C1", 0, AR), A.is_equal)]
             + [tt(b3("EQ3", slice(4 * d - 4, 4 * d), slice(16 * (k - d), 16 * (k - d + 1))), b3("PB", full, slice(16 * k, 16 * k + 16)),
-                  b3("C2", slice(k - d, 20, BW)), A.is_equal) for d in range(1, BW) for k in range(d, BW)])
+                  b3("C0", slice(k - d, 20, BW)), A.is_equal) for d in range(1, BW) for k in range(d, BW)])
         row(w1[:1] + same[:CN] + w1[1:] + same[CN:CN + 4] + [cn] + same[CN + 4:] + cut if t < RO - 1 else w1[:1] + same + w1[1:] + [cn])
-        mm(b("B1", 0, AR), [(b("I4kn"), b("EQ")), (I1, pvh, b("B1", 0, AR, 16)), (b("e0"), b("cT"), b("B1", 0, AR, 16))]
+        mm(b("B1", 0, AR), [(b("I4kn"), b("EQ")), (I1, b3("PB", full, slice(0, 80, 16)), b("B1", 0, AR, 16)), (b("e0"), b("cT"), b("B1", 0, AR, 16))]
            + [(b("I4kn"), b3("EQ3", 4 * d - 4 + k, slice(0, 16 * (BW - d))), b("B1", 16 * (BW * k + d), 16 * BW * (k + 1)))
               for d in range(1, BW) for k in range(4)])
         for k in sorted(range(N // near), key=lambda k: -land[core][near * k]):
             q = (16 * BW * k, 16 * BW * (k + 1))
             scan(b("DS", *q), b("m16", *q), b("B1", *q), A.mult, A.add)
             tt(b3("eou", k, slice(0, BW)), b("DS", q[0] + 15, q[1], 16), b("sw", 0, BW), A.max)
-            if t < RO - 1:
-                ts(b("ft", *q), b("C1", *q), 0.5, 2.0 * (OFF - 128.0), A.is_gt, A.mult)
-            else:
+            if t == RO - 1:
                 ts(b("ft", *q), b("cn", *q), 127.0, -127.0, A.min, A.max)
-            tt(ind(b("X" if t < RO - 1 else "Y"), b3("eou", k, slice(0, BW))), b("xq", *q), b("ft", *q), A.add)
+            tt(ind(b("X" if t < RO - 1 else "Y"), b3("eou", k, slice(0, BW))), b("xq", *q), b("ft", *q), A.add if t else A.mult)
     for k, e in ((0, "y"), (1, "s")):
         dma(e, hbm(T.y[:, 1024 * k:1024 * k + 1024]), b("Y", TR + 1024 * k, TR + 1024 * k + 1024), "d%d" % (5 + k), LOAD + 3000)
 
@@ -694,7 +647,7 @@ def rank_program(g, core, T, topo):
             mark[i] = (sem[0], sem[1], {})
             continue
         kn = known[e]
-        for s, v, seen in sorted((mark[d] for d in calls[i][3] if not (e == calls[d][0] == "p" or d == calls[i][5])), key=lambda x: (x[0] == semof.get(e), -x[1])):
+        for s, v, seen in sorted((mark[d] for d in calls[i][3] if not (e == calls[d][0] == "p" or d in calls[i][5])), key=lambda x: (x[0] == semof.get(e), -x[1])):
             if s and kn.get(s, 0) < v:
                 queue[e].wait_ge(T.sem[s], v)
                 for s2, v2 in list(seen.items()) + [(s, v)]:

@@ -7,7 +7,7 @@ AR = N * CAP
 TR = 320
 M27 = 1.5 * 2.0 ** 27
 M23 = 1.5 * 2.0 ** 23
-B18 = 1.5 * 2.0 ** 18
+B30 = 1.5 * 2.0 ** 30
 SENT = -36864
 LOW, RISE = 2.0 ** -110, 2.0 ** 13
 TOP = LOW * RISE ** 15
@@ -15,27 +15,33 @@ XB = (0, 1, 2, 0)
 PASSES = 2
 W1ST, CN = 8, 1
 NS = 4
-NV = 96
-ZHS, RES = 0, ()
-VROW, SROW = "F SZ zo SL qo zn s0 zf g2 s1 qf s2 s3 s4 s5", "g0 g1 g3 g4 g5"
-FARP = ((("v", 48), ("s", 64), ("s", 64)), (("s", 64),))
-NEARP = "ss"
+NV = 90
+RES, ZHS, PUS, RS, RN, IS = (0, 1, 2, 3), (), (0, 1, 2), (), 16, ("IF1",)
+DENSE = (3,)
+GB, SB = ("B3", "B1", "B2", "C0"), ("C1", "C2", "C1", "C2")
+ROWS = [[x + " z01 s00 z10 z20 z30 h30 h10 h20 g10 c30 s01 s10 s20 s30", "Y0 g00 L g01 t0 g11 g20 t1 g30 Y1 Y2 Y3"] for x in ("SZ F z00", "F SZ z00 SL")]
+GATH = ((("s", 40), ("s", 40)), (("v", 56), ("s", 24)), (("s", 80),), (("s", 80),))
 
 _DT = {"f": "float32", "b": "bfloat16", "h": "float16", "i": "int32", "u": "uint16"}
 _SBUF = """
-f X:2368 Y:2368 J:256 col:32 sw:20 swa:20 U:136 dm:16 fo:16 fo2:16 Sx:256 Ks:256 hb:16 rk:16 cc:256 CHf:256 xg:256
-f iv:16 iv2:16 own:16 R4:4,32 SL0:2304 SL1:2304 LA0:320 LA1:320 SZ0:2304 SZ1:2304 LZ0:320 LZ1:320 w1:320
-f MX:16 s9:144 xq:320 ft:320 cq:320 cn:320 DS:320 IF:128 zf:256 pw:16 pw2:16 fsg:256 thr:320
-i XI:2048 X1:2048 pp_i:1 pq_i:1 pr_i:1 hp:16 hq:16 vi:16 vv:16 ch:16 ow:16 Hi:16 dd:5120 xm:320
+f X:2368 Y:2368 J:256 col:32 sw:20 swa:20 U:136 dm:16 fo:16 fo2:16 Sx:256 CH:256 xg:256
+i Ks:256 HI:256 KI:256 VI:256
+h hx:256 pm0:256 pm1:256
+b m8:128 BD:128 I4k:128 I16:128
+f iv:16 IVs:128 IV:128 R4:4,32 SZ0:2304 SZ1:2304 LZ0:320 LZ1:320 w1:320
+b SL0:2304 SL1:2304 LA0:320 LA1:320 sg:256
+f MX:16 s9:144 xq:320 ft:320 cn:320 DS:320 IF:128 IF1:128 R15f:128 zf:256 pw:16 pw2:16 fsg:256 thr:320
+i XI:2048 X1:2048 pp_i:1 pq_i:1 pr_i:1 hp:16 ch:16 ow:16 Hi:16 dd:5120 xm:320
 i hi:2,16 ha:2,16 ci:4,8 ca:4,8
-h EB:128 cb:16 Dh:16,16 VK:256 VV:256 TK:256 VB:256 R1:16,16 m1:16,16 CH:16,16 A16:20,16 uh:16 Hh:16 zh:320 re:320 rr:320 PB:4,80 db:3840
+h EB:128 cb:16 Dh:16,16 TK:256 VB:256 R1:16,16 m1:16,16 uh:16 Hh:16 zh:320 A16:320 rr:640 db:3840
 b HM:4096 NZ:2048 SR:2064 Lb:130 PL:130 cmp:2048 G:256 Cb:256 sC:256 Fb:256 Fl:256 Lg:4096 Mn:16,256 th:256 sD:16,16
-b sE:256 ab:256 fsq:256 R15:128 O:144 m9:144 ckb:320 esq:320 EQ:320 EQ3:16,64 qb:256 ee:320 ff:320 tri:320
+b sE:256 ab:256 fsq:256 R15:128 O:144 m9:144 ckb:320 EQ:960 qb:256 ee:320 ff:320
 b Jb:256 JI:320 JG:128 PD:128 zero:128 ones:320 BH:128 ZS:144 MK:4 WL:8 base:64 kx:128 kc:128 e0:128 TI:128
-b SU:128 SD:128 PAR:128 PA2:128 I592:8 B592:128 Ca:64 WT:16 ER:144 OR:144 EM:144 OM:144 E1:144 O1:144 CR1:128 CR2:128 c9:144
-b m16:320 dk:256 RX:2048 RM:2048 cT:20 I1:128 Im1:128 I256n:128 I256:128 I4kn:128 NUn:128
-b ZD:144 ZP:144 BP:128 WE:128 WA:128 I12:128 TE:128 TF:128 mr:128 B2m:128
-u cu:16 plu:16 fou:16 Du:256 slu:16 zu:320 pu:20 eou:4,6
+b SU:128 SD:128 PAR:128 PA2:128 I592:8 B592:128 Ca:128 WT:16 ER:144 OR:144 EM:144 OM:144 E1:144 O1:144 CR1:128 CR2:128 c9:144
+b m16:320 dk:256 RX:2048 RM:2048 I1:128 Im1:128 I256n:128 I256:128 I4kn:128 NUn:128
+f PB:320
+b ZD:144 dg1:160 dg2:80 B4kn:128 BP:128 WE:128 WA:128 I12:128 X16:128 k2:128 BN:128 SH:768 mr:128 B2m:128
+u cu:16 plu:16 fou:16 Du:256 slu:16 zu:320 zc:320 pu:4,6 eou:4,6
 """
 _ALL, SCRATCH, _AT = {}, {}, {}
 for _line in _SBUF.split("\n"):
@@ -45,7 +51,7 @@ for _line in _SBUF.split("\n"):
         _ALL[_n] = ("sbuf", [128] + [int(_k) for _k in _s.split(",")], _DT[_w[0]])
 for _k in range(4):
     _ALL["B%d" % _k] = ("psum", [128, 512], "float32")
-    _ALL["C%d" % _k] = ("psum", [128, 32, 16], "float32")
+    _ALL["C%d" % _k] = ("psum", [128, 32, 16] if _k == 2 else [128, 512], "float32")
 _wide = {}
 for _n, (_w, _sh, _d) in _ALL.items():
     if _w == "sbuf" and len(_sh) == 2 and _sh[1] <= 144:
@@ -103,7 +109,10 @@ def order_calls(calls):
                 t = max([at[u] + calls[u][1] + gap(i, u) for u in users[i]], default=0.0) + c[2] - c[1]
             else:
                 t = max([at[d] + calls[d][2] + gap(d, i) for d in c[3]], default=0.0)
-            line, k = busy.setdefault(c[0], []), 0
+            line = busy.setdefault(c[0], [])
+            k, hi = 0, len(line)
+            while k < hi:
+                k, hi = ((k + hi) // 2 + 1, hi) if line[(k + hi) // 2][1] <= t else (k, (k + hi) // 2)
             while k < len(line) and line[k][0] < t + c[1]:
                 t, k = max(t, line[k][1]), k + 1
             line.insert(k, (t, t + c[1]))
@@ -119,7 +128,7 @@ def order_calls(calls):
     return sorted(range(n), key=lambda i: (best[1][i], i))
 
 
-_ORDER = []
+_ORDER = {}
 
 
 def rank_program(g, core, T, topo):
@@ -212,7 +221,7 @@ def rank_program(g, core, T, topo):
         return op("v", lambda: g.vector.memset(out[0], c), [out], [], vec(out, [out], half(out)))
 
     def scan(out, d0, d1, o0, o1, first=0.0):
-        op("v", lambda: g.vector.tensor_tensor_scan(out[0], d0[0], d1[0], first, o0, o1), [out], [d0, d1], vec(out, [d0], half(out, d0, d1)))
+        return op("v", lambda: g.vector.tensor_tensor_scan(out[0], d0[0], d1[0], first, o0, o1), [out], [d0, d1], vec(out, [d0], half(out, d0, d1)))
 
     def vtr(out, in_):
         op("v", lambda: g.vector.transpose(out[0], in_[0]), [out], [in_], vec(out, [in_], 1))
@@ -228,8 +237,7 @@ def rank_program(g, core, T, topo):
     def mm(out, terms):
         for k, (l, r, *part) in enumerate(terms):
             o, cost = part[0] if part else out, max(min(64, l[2]), r[2]) * PE * (1 if l[3] else 4)
-            stop = not out or k == len(terms) - 1 or len(o) > 7 and all(x[2][7:] != o[7:] for x in terms[k + 1:])
-            op("p", lambda o=o, l=l, r=r, k=k, stop=stop: g.tensor.matmul(o[0], l[0], r[0], k == 0 or not out, stop),
+            op("p", lambda o=o, l=l, r=r, k=k: g.tensor.matmul(o[0], l[0], r[0], k == 0 or not out, k == len(terms) - 1 or not out),
                [o], [l, r], cost, cost + DRAIN, more=len(terms) - 1 - k)
 
     def iota(out, pat, base, cm=0):
@@ -257,7 +265,7 @@ def rank_program(g, core, T, topo):
 
     cell = [divmod(STEP * (t + 1), 16) for t in range(RO)]
     (PP, PI, PG, PG16, OD, SIG, SI2, W1, W2, PGE, PGO, CE, CO, CE1, CO1, N12, N15, WR1, WR2, WM1, WM2,
-     PW, P15) = [b("col", k, k + 1) for k in range(23)]
+     PW, P15, N13) = [b("col", k, k + 1) for k in range(24)]
     diag = [[-1, 128]]
     iota(b("pp_i"), [[0, 1]], 0, 1)
     iota(b("Jb"), [[1, 256]], 0)
@@ -292,12 +300,12 @@ def rank_program(g, core, T, topo):
     sel(b("NUn"), b("BH"), diag, A.is_gt, 0.0, 0, 1)
     ts(b("NUn"), b("NUn"), -1.0, None, A.mult)
     iota(b("JI"), [[0, 20], [1, 16]], 0)
-    for n, c in (("I256n", -256.0), ("Im1", -1.0), ("IF", 256.0), ("I4kn", -4096.0), ("I256", 256.0)):
-        ts(b(n), b("I1"), c, None, A.mult)
+    for n, c in (("I256n", -256.0), ("Im1", -1.0), ("IF", 256.0), ("IF1", 1.0), ("I4k", 4096.0), ("I16", 16.0), ("I4kn", -4096.0), ("I256", 256.0)):
+        lin("s" if n in IS else "v", b(n), b("I1"), c, 0.0)
     ts(b("pq_i"), b("pp_i"), 1, None, A.bitwise_and)
     ts(b("pr_i"), b("pr_i"), 1, None, A.bitwise_and)
     act(SIG, b("pq_i"), scale=-2.0, bias=1.0)
-    act(SI2, b("pq_i"), scale=4.0, bias=-2.0)
+    act(SI2, b("pq_i"), scale=-4.0, bias=2.0)
     act(W1, PI, scale=13.0, bias=5.0)
     act(W2, PI, scale=-14.0, bias=255.0)
     act(PGE, b("pr_i"), scale=100000.0, bias=PG16)
@@ -319,50 +327,68 @@ def rank_program(g, core, T, topo):
     act(b("WT", 8, 16), b("BH", 0, 128, 16), scale=W2)
     act(b("B592"), b("BH"), scale=592.0)
     act(b("I592"), b("BH", 0, 128, 16), scale=-592.0)
-    act(b("kc"), b("kx"), bias=7.5)
+    ts(b("kc"), b("kx"), 15.0, b("e0", 0, 1), A.add, A.mult)
+    sel(b("kc"), b("kc"), [[0, 128]], A.not_equal, 32768.0, -1, 1)
     act(b("PAR"), b("BH"), scale=SIG)
     act(b("PA2"), b("BH"), scale=SI2)
     act(b("swa"), b("sw"), bias=-float(TR))
     ts(b("m16"), b("JI"), 0.0, None, A.is_gt)
-    ts(b("dk"), b("m16", 0, 256), 1023.0, -1024.0, A.mult, A.add)
+    ts(b("dk"), b("m16", 0, 256), -1023.0, 1024.0, A.mult, A.add)
+    for t in range(RO):
+        lin("vs"[t], b("pm%d" % t), b("m16", 0, 256), 6144.0 - t, t - 2048.0)
     sel(b("SU"), b("BH"), diag, A.is_equal, 0.0, -1, 1)
     sel(b("SD"), b("BH"), diag, A.is_equal, 0.0, 1, 1)
-    iota(b("CR1"), [[0, 128]], -240)
-    sel(b("CR1"), b("CR1"), [[0, 8], [1, 16]], A.not_equal, -176.0, -15, 0)
+    iota(b("CR1"), [[0, 128]], -480)
+    sel(b("CR1"), b("CR1"), [[0, 8], [1, 16]], A.not_equal, -416.0, -15, 0)
     sel(b("CR2"), b("zero"), [[0, 8], [1, 16]], A.not_equal, -64.0, 0, 0)
-    act(b("VK"), b("ones", 0, 256), scale=-7.5)
-    act(b("VV"), b("ones", 0, 256), scale=0.0)
+    for n, c in (("HI", 0.0), ("KI", 15.0), ("VI", 0.0)):
+        act(b(n), b("ones", 0, 256), scale=c)
+    act(b("IVs"), b("ones", 0, 128))
+    sel(b("m8"), b("ones", 0, 128), [[0, 16], [1, 8]], A.not_equal, 0.0, 0, 0)
     iota(b("c9"), [[0, 16], [256, 9]], -4096)
     sel(b("m9"), b("ones", 0, 144), [[0, 16], [1, 9]], A.not_equal, 0.0, 0, 0)
     for t in range(RO):
-        for n, c in (("SZ", 0), ("SL", SENT)):
+        for n, c in (("SZ", SENT), ("SL", 0)):
             for o in range(N):
                 iota(b(n + str(t), 256 * o, 256 * o + CAP), [[0, CAP]], c)
-    iota(b("cT"), [[0, 20]], TR)
-    ts(b("MX"), b("Jb", 0, 16), PI, None, A.is_equal)
-    tt(b("B2m"), b("BH"), b("kx"), A.mult)
-    ts(b("mr"), b("kx"), b("e0", 0, 1), -1.0, A.mult, A.mult)
+    ts(b("MX"), b("Jb", 0, 16), PI, 4096.0, A.is_equal, A.mult)
+    iota(b("k2"), [[0, 8], [2, 16]], -2)
+    tt(b("B2m"), b("BH"), b("k2"), A.mult)
+    ts(b("mr"), b("k2"), b("e0", 0, 1), 2048.0, A.mult, A.mult)
+    sel(b("mr"), b("mr"), [[0, 128]], A.not_equal, B30, -1, 1)
+    sel(b("mr"), b("mr"), [[0, 128]], A.not_equal, 2048.0, -2, 1)
     for x in range(16):
-        ts(b("RX", 128 * x, 128 * x + 128), b("BH"), b("MX", x, x + 1), None, A.mult)
-        ts(b("RM", 128 * x, 128 * x + 128), b("B2m"), b("MX", x, x + 1), -2.0, A.mult, A.mult)
-    ts(b("tri"), b("JI"), PI, 8192.0, A.is_ge, A.mult)
+        for n, w in (("RX", "BH"), ("RM", "B2m")):
+            lin("s" if n in RS and x < RN else "v", b(n, 128 * x, 128 * x + 128), b(w), b("MX", x, x + 1), 0.0)
+    sel(b("X16"), b("ones", 0, 128), [[0, 8], [1, 16]], A.is_equal, 0.0, 0, -1)
+    five = [[0, 5], [1, 16]]
+    iota(b("dg2"), [[0, 80]], -8192)
+    sel(b("dg1", 0, 80), b("dg2"), five, A.not_equal, 1.0, 0, -1)
+    sel(b("dg1", 80, 160), b("ones", 0, 80), five, A.is_gt, 8192.0, 0, -1)
+    sel(b("dg2"), b("dg2"), five, A.not_equal, float(TR), 0, -1)
+    act(b("B4kn"), b("BH"), scale=-4096.0)
     ts(b("pw"), b("Jb", 0, 16), PI, RISE - 1.0, A.is_lt, A.mult)
-    ts(b("pw"), b("pw"), 1.0, None, A.add)
+    act(b("pw"), b("pw"), bias=1.0)
     scan(b("pw2"), b("pw"), b("zero", 0, 16), A.mult, A.add, LOW)
-    ts(b("ZD"), b("ZS"), b("pw2", 15, 16), None, A.mult)
+    act(b("ZD"), b("ZS"), scale=b("pw2", 15, 16))
+    act(b("BD"), b("BH"), scale=b("pw2", 15, 16))
     ts(P15, PI, 15.0, TOP, A.is_equal, A.mult)
-    ts(b("R15"), b("BH"), P15, None, A.mult)
-    ts(N12, PI, float(NP), None, A.is_lt)
-    ts(PW, PI, float(NP), -4097.0, A.is_equal, A.mult)
-    act(PW, PW, bias=1.0)
-    ts(b("ZP"), b("ZS"), PW, None, A.mult)
-    ts(b("BP"), b("BH"), PW, None, A.mult)
-    ts(b("I12"), b("I1"), N12, None, A.mult)
-    ts(b("WA"), b("BH"), N12, -4096.0, A.mult, A.mult)
+    act(b("R15f"), b("BH"), scale=P15)
+    act(b("R15"), b("R15f"), scale=-4096.0)
+    ts(N13, PI, float(NP), -4096.0, A.is_le, A.mult)
+    ts(N12, PI, 0.0, N13, A.is_gt, A.mult)
+    act(N12, N12, scale=-1.0 / 4096.0)
+    ts(PW, PI, NP + 1.0, -4096.0, A.is_equal, A.mult)
+    act(PW, PW, bias=N12)
+    act(b("BP"), b("BH"), scale=PW)
+    act(b("I12"), b("I1"), scale=N12)
+    act(b("BN"), b("BH"), scale=N12)
+    for i, d in enumerate((0, 12, -4, 8, -8, 4)):
+        sel(b("SH", 128 * i, 128 * i + 128), b("BN"), [[1, 128]], A.is_equal, 0.0, 1 - d, -1)
+    act(b("WA"), b("BH"), scale=N13)
     sel(b("WE"), b("WA"), [[1, 128]], A.is_ge, 0.0, 0, -1)
     sel(b("WE"), b("WE"), diag, A.not_equal, 4096.0, 0, 1)
-    iota(b("TE"), [[0, 128]], -32)
-    sel(b("TF"), b("TE"), [[0, 8], [1, 16]], A.not_equal, 1.0 / 128.0, -NP, 0)
+    sel(b("WA"), b("WA"), [[-16, 8], [256, 16]], A.not_equal, 1.0, -256 * (NP + 1), 1)
 
     def zs(x, n="ZS"):
         return b(n, 15 - x, 143 - x)
@@ -436,46 +462,45 @@ def rank_program(g, core, T, topo):
         dh = ts(b("Dh"), b("Du"), -2048.0, None, A.add)
         CB0 = -524288.0 - 128.0
         mm(b("B3", 0, S), [(b("IF"), b("Sx")), (b("I256n"), b("Dh"))])
-        first = [act(b("C3", 0, 192), b("B3", 0, 192), F.Abs, bias=CB0), act(b("Ca"), b("B3", 192, S), F.Abs, bias=CB0)]
+        first = [act(b("C3", 0, 128), b("B3", 0, 128), F.Abs, bias=CB0), act(b("Ca"), b("B3", 128, S), F.Abs, bias=CB0)]
         for h in range(2):
             mm(b("B0", 16 * h, 16 * h + 16), [(b("Dh", 128 * h, 128 * h + 128), b("WT"))])
         mineL = [cp(b("Lg", 0, 16 * NV), ind(b("HM"), b("Du", 0, NV)))]
-        look = [act(b("Lg", 16 * lo, 16 * hi), ind(b("HM"), b("Du", lo, hi)), F.Copy) for lo, hi in ((NV, 128), (192, S), (128, 192))]
-        least = [tt(b3("Mn", k, slice(lo, hi)), b("Lg", 16 * lo + k, 16 * hi, 16), b("C3", lo, hi), A.min)
-                 for lo, hi in ((0, 64), (64, 128), (128, 192)) for k in range(16)]
+        look = [act(b("Lg", 16 * lo, 16 * hi), ind(b("HM"), b("Du", lo, hi)), scale=c) for lo, hi, c in ((NV, 128, 1.0), (192, S, 1.0), (128, 192, -1.0))]
+        steps = [cp(b3("hi"), b("B0", 0, 32))]
+        mm(b("B0", 128, 192), [(Im1, b("Ca", 0, 64))])
+        least = [tt(b3("Mn", k, slice(lo, lo + 64)), b("Lg", 16 * lo + k, 16 * lo + 1024, 16), b(bank, lo, lo + 64), o)
+                 for lo, bank, o in ((0, "C3", A.min), (64, "C3", A.min), (128, "B0", A.max)) for k in range(16)]
         over = []
         for kk, bank in ((0, "C1"), (8, "C2")):
             mm(b(bank), [x for k in range(8) for x in ((Im1, b("Lg", 3072 + kk + k, 4096, 16), b(bank, 64 * k, 64 * k + 64)),
-                                                       (I1, b("Ca"), b(bank, 64 * k, 64 * k + 64)))])
+                                                       (I1, b("Ca", 64, 128), b(bank, 64 * k, 64 * k + 64)))])
             over.append(act(b3("Mn", slice(kk, kk + 8), slice(192, S)), b(bank), F.Relu))
         row(look[:1] + first + look[1:] + over)
-        plus = b("B592", 0, 128, 16)
-        mm(b("B1", 0, 128), [(b("e0"), b("kc"))] + [(b3("Mn", k, slice(0, 128)), plus, b("B1", k, 128, 16)) for k in range(16)])
-        low = [(b3("Mn", k, slice(128, 192)), plus, rows(b("B2", k, 128, 16), 0, 64)) for k in range(16)]
-        high = [(b3("Mn", k, slice(192, S)), b("I592"), rows(b("B2", k, 128, 16), 64, 128)) for k in range(16)]
-        mm(b("B2", 0, 128), [(b("e0"), b("kc")), (b("Ca"), b("B592"), rows(b("B2", 0, 128), 64, 128))] + low[:2] + high[:8] + low[2:12] + high[8:] + low[12:])
-        steps = [cp(b3("hi"), b("B0", 0, 32)),
+        steps += [
                  ts(b3("ha"), b3("hi"), 4095, None, A.bitwise_and),
                  tt(b("hp"), b3("ha", full, slice(0, 8)), b3("ha", full, slice(8, 16)), A.mult),
-                 ts(b("hq"), b("hp"), 5, None, A.arith_shift_right),
-                 ts(b("hb"), b("hq"), 16.0, M27 + 16.0 * t, A.mult, A.add)]
+                 ts(b("HI", 0, 256, 16), b("hp"), 5, 4095, A.arith_shift_right, A.bitwise_and),
+                 scan(b("hx"), b("pm%d" % t), b("HI"), A.min, A.add)]
+        plus = b("B592", 0, 128, 16)
+        const = [[(b("ones", 0, 128), b("kc")), (b("I16"), b("hx", 128 * h, 128 * h + 128), b("B%d" % (1 + h), 0, 128))] for h in (0, 1)]
+        mm(b("B1", 0, 128), const[0] + [(b3("Mn", k, slice(0, 128)), plus, b("B1", k, 128, 16)) for k in range(16)])
+        mm(b("B2", 0, 128), const[1] + [(b("Ca", 64, 128), b("B592"), rows(b("B2", 0, 128), 64, 128))]
+           + [(b3("Mn", k, slice(128, S)), b("I592"), b("B2", k, 128, 16)) for k in range(16)])
         row([dh] + mineL + [x for k in range(5) for x in [steps[k]] + least[4 * k:4 * k + 4]] + least[20:])
         act(b("Cb"), b("B3", 0, 256), bias=CB0)
         for h in range(2):
             scan(b("Ks", 128 * h, 128 * h + 128), b("m16", 0, 128), b("B%d" % (1 + h), 0, 128), A.mult, A.max)
         kmx = b("Ks", 15, 256, 16)
-        ts(b("rk"), kmx, M27, -M27, A.add, A.add)
-        tt(b("vi"), kmx, b("hb"), A.add)
-        tt(b("VK", 0, 256, 16), b("rk"), kmx, A.subtract)
-        ts(b("vv"), b("vi"), 4, 4095, A.arith_shift_right, A.bitwise_and)
-        scan(b("TK"), b("dk"), b("VK"), A.add, A.max)
-        ts(b("VV", 0, 256, 16), b("vv"), -2048.0, None, A.add)
-        scan(b("VB"), b("m16", 0, 256), b("VV"), A.mult, A.add)
+        ts(b("KI", 0, 256, 16), kmx, 15, None, A.bitwise_and)
+        ts(b("VI", 0, 256, 16), kmx, 4, 4095, A.arith_shift_right, A.bitwise_and)
+        scan(b("TK"), b("dk"), b("KI"), A.add, A.min)
+        scan(b("VB"), b("pm0"), b("VI"), A.min, A.add)
 
         def turned(bank, n, w):
             return [(b(n, h, h + 128), w, b(bank, h, h + 128)) for h in (0, 128)]
         DH, ONE = b("Dh"), b("ones", 0, 256)
-        mm(b("B0", 0, 256), [(b("SU"), DH), (b("CR1"), ONE)] + turned("B0", "TK", b("I4kn")))
+        mm(b("B0", 0, 256), [(b("SU"), DH), (b("CR1"), ONE)] + turned("B0", "TK", b("I4k")))
         tt(b("R1"), DH, b("B0", 0, 256), A.max)
         mm(None, turned("B3", "VB", I1))
         mm(b("B1", 0, 256), [(b("CR2"), ONE), (b("SD"), b("R1"))])
@@ -487,39 +512,38 @@ def rank_program(g, core, T, topo):
                              for x, ns, at, k in (("R1", ("ER", "OR"), 6, 2), ("sD", ("E1", "O1"), 3, 1), ("m1", ("EM", "OM"), 6, 2))
                              for par, n in enumerate(ns) for j in range(4)])
         mm(None, turned("C0", "TK", I1))
-        act(b("th"), b("C0", 0, 256), F.Sign, bias=7.5)
+        act(b("th"), b("C0", 0, 256), F.Sign, bias=-15.0)
         mm(b("B2", 0, 256), [(I1, b("R1"))] + turned("B2", "VB", Im1))
         act(b("sE"), b("B2", 0, 256), F.Sign)
         mm(b("C0", 0, 256), [(b("PA2"), b("th")), (b("PAR"), b("sE"))])
         act(b("ab"), b("C0", 0, 256), F.Abs, bias=2.0)
-        act(b("C1", 0, 256), b("ab"), bias=-1.0 / 256.0, scale=1.0 / 256.0)
+        act(b("sg"), b("ab"), bias=-1.0)
         act(b("Fb"), b("Cb"), bias=191.625, scale=0.25)
         act(b("Fl"), b("Fb"), bias=-192.0)
-        act(b("CHf"), b("CH"))
-        tt(b("cc"), b("Fl"), b("C1", 0, 256), A.mult)
         vtr(b3("R4"), b("C2", 0, 128))
         cp(b3("ci"), b3("R4", full, slice(0, 8)))
         ts(b("iv"), b3("R4", full, slice(8, 12)), -1.0, -8192.0, A.is_equal, A.mult)
         ts(b3("ca"), b3("ci"), 4095, None, A.bitwise_and)
-        tt(b("iv2"), b("iv"), b("dm"), A.min)
+        iv2 = b("IVs", 0, 128, 8)
+        tt(iv2, b("iv"), b("dm"), A.min)
+        scan(b("IV"), b("m8"), b("IVs"), A.mult, A.add)
         tt(b("ch"), b3("ca", full, slice(0, 8, 2)), b3("ca", full, slice(1, 8, 2)), A.mult)
-        ts(b("O", 8, 144, 9), b("iv2"), 0.0, None, A.is_lt)
+        ts(b("O", 8, 144, 9), iv2, 0.0, None, A.is_lt)
         ts(b("ow"), b("ch"), 5, 7, A.arith_shift_right, A.bitwise_and)
-        tt(b("own"), b("ow"), b("iv2"), A.add)
         ts(b("uh"), b3("ca", full, slice(0, 8, 2)), -2048.0, None, A.add)
         ts(b("Hi"), b("ch"), 8, V - 1, A.arith_shift_right, A.bitwise_and)
         cp(b("Hh"), b("Hi"))
         mm(b("B0", 0, S), [(b("mr"), ONE)] + [(b(n, 128 * x, 128 * x + 128), b(u), b("B0", x, S, 16))
                                               for n, u in (("RM", "uh"), ("RX", "Hh")) for x in range(16)])
-        act(b("qb"), b("B0", 0, S), bias=B18 - 1023.5)
+        act(b("qb"), b("B0", 0, S), bias=-1024.0 * 4096.0)
         tt(b("zf"), b("B0", 0, S), b("qb"), A.subtract)
         for o in range(8):
-            ts(b("O", o, 144, 9), b("own"), float(o), None, A.is_equal)
+            tt(b("O", o, 144, 9), b("ow"), b("IV", o, 128, 8), A.is_equal)
         mm(b("B3", 0, 144), [(b("e0"), b("c9")), (b("TI"), b("O"))] + [(b("BH"), b("O", 0, 144 - 9 * d), b("B3", 9 * d, 144)) for d in range(1, 16)])
         scan(b("s9"), b("m9"), b("B3", 0, 144), A.mult, A.max)
         cp(b("slu"), b("s9", 8, 144, 9))
         SL, LA, SZ, LZ = [x + str(t) for x in ("SL", "LA", "SZ", "LZ")]
-        scat = [ts(ind(b(SZ), b("slu")), b("zf"), 1.0, B18, A.mult, A.add), tt(ind(b(SL), b("slu")), b("cc"), b("CHf"), A.add)]
+        scat = [tt(ind(b(SZ), b("slu")), b("zf"), b("CH"), A.add), tt(ind(b(SL), b("slu")), b("Fl"), b("sg"), A.mult)]
         sends = []
         for src, dst in ((SZ, LZ), (SL, LA)):
             for call in (0, 1):
@@ -542,7 +566,7 @@ def rank_program(g, core, T, topo):
                        (dst[:2] + "fn"[nr] + str(t), tot))
                 calls[i][3].append(sends[-2 if nr else -1])
         row(sends)
-        act(b(LA, mine, mine + CAP), b(SL, 256 * me, 256 * me + CAP))
+        kept = act(b(LA, mine, mine + CAP), b(SL, 256 * me, 256 * me + CAP))
         act(b("sC"), b("Cb"), F.Sign)
         fade = [(I1, b("Cb")), (Im1, b("sC"))]
         mm(b("C3", 0, 256), fade)
@@ -554,94 +578,94 @@ def rank_program(g, core, T, topo):
         tt(b("fo2"), b("fo"), b("swa", 0, 16), A.max)
         ts(b("fou"), b("fo2"), float(TR), None, A.add)
         faded = tt(ind(b("X"), b("fou")), b("xg"), b("fsg"), A.mult)
-        if t == RO - 1:
-            for k in range(4):
-                act(b("Y", TR + 512 * k, TR + 512 * k + 512), b("X", TR + 512 * k, TR + 512 * k + 512), F.Abs)
+        out = [act(b("Y", TR + 512 * k, TR + 512 * k + 512), b("X", TR + 512 * k, TR + 512 * k + 512), F.Abs) for k in range(4 * (t == RO - 1))]
 
-        other = CAP - mine
-        did = dict(SZ=scat[:1], SL=scat[1:], F=[faded])
-        for x, lo, hi, z, rec in (("o", mine, mine + CAP, b(SZ, 256 * me, 256 * me + CAP), b(SL, 256 * me, 256 * me + CAP)),
-                                  ("n", other, other + CAP, b(LZ, other, other + CAP), b(LA, other, other + CAP)),
-                                  ("f", 2 * CAP, AR, b(LZ, 2 * CAP, AR), b(LA, 2 * CAP, AR))):
-            did["z" + x] = [cp(b("zu", lo, hi), z)]
-            did["q" + x] = [ts(b("B0", lo, hi), rec, M23 + 2048.0, -M23, A.add, A.add)]
-        groups, lo = [[(NEARP[0], mine, mine + CAP), (NEARP[1], other, other + CAP)]], 2 * CAP
-        for some in FARP:
-            groups.append([])
-            for e, n in some:
-                groups[-1].append((e, lo, lo + n))
-                lo += n
-        for k, (e, lo, hi) in enumerate(sum(groups, [])):
-            did["g%d" % k] = [lin(e, b("dd", 16 * lo, 16 * hi), ind(XW, b("zu", lo, hi)), 1.0 / 256.0, -0.5)]
-            did["s%d" % k] = [tt(b("db", at, at + hi - lo), b("B0", lo, hi), b("dd", 16 * lo + m, 16 * hi, 16), A.subtract)
-                              for m in range(NP) for at in [NP * lo + m * (hi - lo)]]
-        for x, lo, hi in (("n", 0, 2 * CAP), ("f", 2 * CAP, AR)):
-            did["a" + x] = [ts(b("A16", lo, hi), b(LA, lo, hi), M23, -M23, A.add, A.add)]
-            did["h" + x] = [(act if ZHS else cp)(b("zh", lo, hi), b("zu", lo, hi))]
-            mm(b("C3", 0, hi - lo), [(b("R15"), b("A16", lo, hi))])
-            did["t" + x] = [act(b("thr", lo, hi), b("C3", 0, hi - lo), F.Relu, bias=2048.0 * TOP)]
-        for k, (some, bank, tb) in enumerate(zip(groups, ("B3", "C2", "C0"), ("C1", "B", "C1"))):
-            lo, hi = min(x[1] for x in some), max(x[2] for x in some)
-            n = hi - lo
-            TE, TF = (b("B1", 0, n), b("B2", 0, n)) if tb == "B" else (b(tb, 0, n), b(tb, n, 2 * n))
-            mm(b(bank, 0, n), [(zs(m, "ZD"), b("db", NP * p + m * (q - p), NP * p + (m + 1) * (q - p)), b(bank, p - lo, q - lo))
-                               for e, p, q in some for m in range(NP)])
-            did["e%d" % k] = [ts(b("ee", lo, hi), b(bank, 0, n), 0.0, None, A.is_equal),
-                              tt(b("ff", lo, hi), b(bank, 0, n), b("thr", lo, hi), A.is_gt)]
-            one, zh, ee, ff = [b(x, lo, hi) for x in ("ones", "zh", "ee", "ff")]
-            te = [(b("TE"), one, TE), (b("I12"), zh, TE), (b("WE"), ee, TE)]
-            tf = [(b("TF"), one, TF), (b("I12"), zh, TF), (b("WA"), ee, TF), (b("WE"), ff, TF)]
-            if tb == "B":
-                mm(TE, te)
-                mm(TF, tf)
+        other, W = CAP - mine, near * CAP
+        did = dict(SZ=scat[:1], SL=scat[1:], F=[faded], L=[kept], Y0=out[:1], Y1=out[1:2], Y2=out[2:3], Y3=out[3:])
+        turn = [0] + list(range(N // near - 1, 0, -1))
+        recs = {0: [(mine, mine + CAP, b(SZ, 256 * me, 256 * me + CAP)), (other, other + CAP, b(LZ, other, other + CAP))]}
+        recs.update({k: [(W * k, W * k + W, b(LZ, W * k, W * k + W))] for k in turn[1:]})
+
+        def Q(lo, hi):
+            return b("B0", lo, hi) if lo < W else b("C3", lo - W, hi - W)
+
+        def split(out, big, small, k):
+            return [(w, y, out(lo, hi)) for lo, hi, rec in recs[k] for w, y in ((b(big), rec), (b(small), b("zh", lo, hi)))]
+        for j, k in enumerate(turn):
+            for x, (lo, hi, rec) in enumerate(recs[k]):
+                did["z%d%d" % (j, x)] = [ts(b("zu", lo, hi), rec, 1.0 / 4096.0, -2047.5 / 4096.0, A.mult, A.add)]
+                did["h%d%d" % (j, x)] = [(act if j in ZHS else cp)(b("zh", lo, hi), b("zu", lo, hi))]
+        for some in (turn[:1], turn[1:]):
+            lo, hi = W * min(some), W * max(some) + W
+            mm(b("C1", lo, hi), [x for k in some for x in split(lambda lo, hi: b("C1", lo, hi), "R15f", "R15", k)])
+            did["t%d" % (lo > 0)] = [act(b("thr", lo, hi), b("C1", lo, hi), F.Relu)]
+        mm(Q(W, AR), [x for k in turn[1:] for x in split(Q, "IF1", "I4kn", k)])
+        for j, k in enumerate(turn):
+            at, sums, n16 = W * k, [], NP if j in DENSE else 16
+            for x, (p, q, rec) in enumerate(recs[k] if j in DENSE else []):
+                n = (q - p) * 3 // 4
+                mm(b(GB[j], 0, n), [(b("SH", 128 * i, 128 * i + 128), b("zh", p + (i + 1) // 2, q, 4), b(GB[j], i // 2, n, 3)) for i in range(6)])
+                did["c%d%d" % (j, x)] = [cp(b("zc", p, p + n), b(GB[j], 0, n))]
+            for x, (e, n) in enumerate(GATH[j]):
+                at = recs[k][x][0] if j == 0 and x < 2 else at
+                base = recs[k][min(x, 1)][0] if j == 0 else W * k
+                c0, c1 = [base + (y - base) * n16 // 16 for y in (at, at + n)]
+                did["g%d%d" % (j, x)] = [lin(e, b("dd", 16 * c0, 16 * c1), ind(XW, b("zc" if j in DENSE else "zu", c0, c1)), 1.0 / 256.0, -0.5)]
+                at += n
+            for x, (p, q, rec) in enumerate(recs[k]):
+                if j == 0:
+                    mm(Q(p, q), [(b("IF1"), rec), (b("I4kn"), b("zh", p, q))])
+                db = [b("db", NP * p + m * (q - p), NP * p + (m + 1) * (q - p)) for m in range(NP)]
+                did["s%d%d" % (j, x)] = [tt(db[m], Q(p, q), b("dd", 16 * p + m + (n16 > NP), 16 * p + n16 * (q - p), n16), A.subtract) for m in range(NP)]
+                sums += [(zs(m + 1, "ZD"), db[m], b(GB[j], p - W * k, q - W * k)) for m in range(NP)]
+            mm(b(GB[j], 0, W), sums)
+        for lo, hi in ((0, W), (W, AR)):
+            if t < RO - 1:
+                act(b("A16", lo, hi), Q(lo, hi), bias=-2048.0)
             else:
-                mm(b(tb, 0, 2 * n), te[:2] + tf[:2] + te[2:] + tf[2:])
-            did["r%d" % k] = [act(b("re", lo, hi), TE, F.Relu) if k in RES else ts(b("re", lo, hi), TE, 0.0, None, A.max)]
-            did["x%d" % k] = [tt(b("rr", lo, hi), TF, b("re", lo, hi), A.max)]
-        for line in (VROW, SROW):
+                act(b("xq", lo, hi), Q(lo, hi), bias=128.0, scale=256.0)
+        for j, k in enumerate(turn):
+            lo, hi, bank, side = W * k, W * k + W, GB[j], SB[j]
+            S0, TE, TF, WP, CM, CP = [b(bank, W * x, W * x + W) for x in range(6)]
+            zh, ee, ff, PB, cn, ckb, ft, xq = [b(x, lo, hi) for x in "zh ee ff PB cn ckb ft xq".split()]
+            did["e%d" % j] = [ts(ee, S0, 0.0, None, A.is_equal), tt(ff, S0, b("thr", lo, hi), A.is_gt)]
+            mm(TE, [(b("I12"), zh, TE), (b("WE"), ee, TE), (b("I12"), zh, TF), (b("WA"), ee, TF), (b("WE"), ff, TF)])
+            both, rr = b(bank, W, 3 * W), [b("rr", 2 * lo + x, 2 * lo + x + W) for x in (0, W)]
+            did["r%d" % j] = [act(b("rr", 2 * lo, 2 * hi), both, F.Relu) if j in RES else ts(b("rr", 2 * lo, 2 * hi), both, 0.0, None, A.max)]
+            mm(b(bank, 3 * W, 5 * W), [(b("X16"), b("dg1"))] + [(b("BP"), r, x) for x in (WP, CM, CP) for r in rr])
+            pu = b3("pu", k, slice(0, BW))
+            did["p%d" % j] = [scan(PB, b("m16", 0, W), WP, A.mult, A.max), lin("s" if j in PUS else "v", pu, b("PB", lo + 15, hi, 16), 1.0, -1.0)]
+            XQ = lambda p, q: b(side, p - lo, q - lo)
+            act(b("xm", lo, hi), ind(XW, pu), bias=-0.5, scale=1.0 / 256.0)
+            act(XQ(lo, hi), b("xm", lo, hi), bias=128.0, scale=256.0)
+            tt(b("w1", lo, hi), ind(XW, pu), b(LA, lo, hi), A.add)
+            tt(cn, b("w1", lo, hi), XQ(lo, hi), A.subtract)
+            EQ = [b("EQ", 3 * lo + W * d - 8 * d * (d - 1), 3 * lo + W * (d + 1) - 8 * d * (d + 1)) for d in range(BW)]
+            did["q%d" % j] = [tt(EQ[0], PB, CM, A.is_equal)] + [
+                ts(EQ[d], b(bank, 5 * W + 16 * d, 6 * W), 1.0, b("PB", lo + 16 * d - 1, lo + 16 * d), A.add, A.is_equal) for d in range(1, BW)]
+            mm(S0, [(b("X16"), b("dg2"))] + [(b("BP"), r) for r in rr] + [(b("B4kn"), EQ[d], b(bank, 16 * d, W)) for d in range(BW)])
+            scan(b("DS", lo, hi), b("m16", 0, W), S0, A.mult, A.max)
+            tt(b3("eou", k, slice(0, BW)), b("DS", lo + 15, hi, 16), b("sw", 0, BW), A.max)
+            if t < RO - 1:
+                ts(ckb, cn, 127.0, -127.0, A.min, A.max)
+                mm(XQ(lo, hi), [(b("I256"), b("A16", lo, hi)), (I1, ckb), (b("BD"), ckb, b(side, W, 2 * W))])
+                ts(ft, b(side, W, 2 * W), 0.0, -0.5, A.not_equal, A.add)
+                act(xq, XQ(lo, hi), bias=2.0 * (524288.0 + 128.0), scale=2.0)
+            else:
+                ts(ft, cn, 127.0, -127.0, A.min, A.max)
+        for line in ROWS[t]:
             row(sum([did[x] for x in line.split()], []))
-        mm(b("C3", 0, AR), [(b("I256n"), b3("A16")), (b("IF"), b(LA))])
-        act(b("cq"), b("C3", 0, AR))
-        mm(b("B3", 0, AR), [(b("zero"), b("ones"))] + [(zs(x, "ZP"), b("rr", x, AR, 16), b("B3", 0, AR, 16)) for x in range(16)])
-        mm(b("C1", 0, AR), [(I1, b("tri")), (b("BP"), b("rr"))])
-        mm(b("C0", 0, AR), [(b("BP"), b("rr"))])
-        cp(b("pu"), b("B3", 0, AR, 16))
-        for k in range(4):
-            scan(b3("PB", k), b("m16", 0, 80), b("B3", 80 * k, 80 * k + 80), A.mult, A.add)
-        act(b("xm"), ind(XW, b("pu")), bias=-0.5, scale=1.0 / 256.0)
-        act(b("B0", 0, AR), b("xm"), bias=128.0, scale=256.0)
-        w1 = [tt(b("w1", 16 * lo, 16 * hi), ind(XW, b("pu", lo, hi)), b("cq", 16 * lo, 16 * hi), A.add) for lo, hi in ((0, W1ST), (W1ST, 20))]
-        cn = tt(b("cn"), b("w1"), b("B0", 0, AR), A.subtract)
-        if t < RO - 1:
-            act(b("esq"), b("cn"), F.Square)
-            cut = [ts(b("ckb"), b("cn"), 127.0, -127.0, A.min, A.max)]
-            mm(b("B2", 0, AR), [(b("I256"), b3("A16")), (I1, b("ckb"))])
-            act(b("xq"), b("B2", 0, AR), bias=524288.0 + 128.0)
-            mm(b("C2", 0, AR), [(b("BH"), b("esq"))])
-            act(b("ft"), b("C2", 0, AR), F.Sign, bias=-0.5)
-        else:
-            act(b("xq"), b3("A16"), bias=524288.0 + 128.0, scale=256.0)
-        same = ([tt(b("EQ"), b("PB"), b("C1", 0, AR), A.is_equal)]
-            + [tt(b3("EQ3", slice(4 * d - 4, 4 * d), slice(16 * (k - d), 16 * (k - d + 1))), b3("PB", full, slice(16 * k, 16 * k + 16)),
-                  b3("C0", slice(k - d, 20, BW)), A.is_equal) for d in range(1, BW) for k in range(d, BW)])
-        row(w1[:1] + same[:CN] + w1[1:] + same[CN:CN + 4] + [cn] + same[CN + 4:] + cut if t < RO - 1 else w1[:1] + same + w1[1:] + [cn])
-        mm(b("B1", 0, AR), [(b("I4kn"), b("EQ")), (I1, b3("PB", full, slice(0, 80, 16)), b("B1", 0, AR, 16)), (b("e0"), b("cT"), b("B1", 0, AR, 16))]
-           + [(b("I4kn"), b3("EQ3", 4 * d - 4 + k, slice(0, 16 * (BW - d))), b("B1", 16 * (BW * k + d), 16 * BW * (k + 1)))
-              for d in range(1, BW) for k in range(4)])
-        for k in sorted(range(N // near), key=lambda k: -land[core][near * k]):
-            q = (16 * BW * k, 16 * BW * (k + 1))
-            scan(b("DS", *q), b("m16", *q), b("B1", *q), A.mult, A.add)
-            tt(b3("eou", k, slice(0, BW)), b("DS", q[0] + 15, q[1], 16), b("sw", 0, BW), A.max)
-            if t == RO - 1:
-                ts(b("ft", *q), b("cn", *q), 127.0, -127.0, A.min, A.max)
+        for k in sorted(turn, key=lambda k: -land[core][near * k]):
+            q = (W * k, W * k + W)
             tt(ind(b("X" if t < RO - 1 else "Y"), b3("eou", k, slice(0, BW))), b("xq", *q), b("ft", *q), A.add if t else A.mult)
     for k, e in ((0, "y"), (1, "s")):
         dma(e, hbm(T.y[:, 1024 * k:1024 * k + 1024]), b("Y", TR + 1024 * k, TR + 1024 * k + 1024), "d%d" % (5 + k), LOAD + 3000)
 
-    if not _ORDER:
-        _ORDER.extend(order_calls(calls))
+    kind = land[core][0]
+    if kind not in _ORDER:
+        _ORDER[kind] = order_calls(calls)
     cnt, known, mark = {}, {e: {} for e in queue}, {}
-    for i in _ORDER:
+    for i in _ORDER[kind]:
         e, (call, sem) = calls[i][0], emit[i]
         if e == "r":
             mark[i] = (sem[0], sem[1], {})

import numpy as np
from concourse.bass import DstId, RemoteDMATransfer
from concourse.mybir import AluOpType as A, AxisListType, ActivationFunctionType as F

N, V, CAP, S, RO, STEP, NP = 8, 2048, 40, 256, 2, 950, 12
AR = N * CAP
TR = 320
M27 = 1.5 * 2.0 ** 27
M23 = 1.5 * 2.0 ** 23
B30 = 1.5 * 2.0 ** 30
SENT = -36864
LOW, RISE = 2.0 ** -110, 2.0 ** 13
TOP = LOW * RISE ** 15
XB = (0, 1, 2, 0)
PASSES = 2
W1ST, CN = 8, 1
NS = 4
NV = 90
RES, ZHS, PUS, RS, RN, IS = (0, 1, 2, 3), (), (0, 1, 2), (), 16, ("IF1",)
DENSE = (3,)
GB, SB = ("B3", "B1", "B2", "C0"), ("C1", "C2", "C1", "C2")
ROWS = [[x + " z01 s00 z10 z20 z30 h30 h10 h20 g10 c30 s01 s10 s20 s30", "Y0 g00 L g01 t0 g11 g20 t1 g30 Y1 Y2 Y3"] for x in ("SZ F z00", "F SZ z00 SL")]
GATH = ((("s", 40), ("s", 40)), (("v", 56), ("s", 24)), (("s", 80),), (("s", 80),))

_DT = {"f": "float32", "b": "bfloat16", "h": "float16", "i": "int32", "u": "uint16"}
_SBUF = """
f X:2368 Y:2368 J:256 col:32 sw:20 swa:20 U:136 dm:16 fo:16 fo2:16 Sx:256 CH:256 xg:256
i Ks:256 HI:256 KI:256 VI:256
h hx:256 pm0:256 pm1:256
b m8:128 BD:128 I4k:128 I16:128
f iv:16 IVs:128 IV:128 R4:4,32 SZ0:2304 SZ1:2304 LZ0:320 LZ1:320 w1:320
b SL0:2304 SL1:2304 LA0:320 LA1:320 sg:256
f MX:16 s9:144 xq:320 ft:320 cn:320 DS:320 IF:128 IF1:128 R15f:128 zf:256 pw:16 pw2:16 fsg:256 thr:320
i XI:2048 X1:2048 pp_i:1 pq_i:1 pr_i:1 hp:16 ch:16 ow:16 Hi:16 dd:5120 xm:320
i hi:2,16 ha:2,16 ci:4,8 ca:4,8
h EB:128 cb:16 Dh:16,16 TK:256 VB:256 R1:16,16 m1:16,16 uh:16 Hh:16 zh:320 A16:320 rr:640 db:3840
b HM:4096 NZ:2048 SR:2064 Lb:130 PL:130 cmp:2048 G:256 Cb:256 sC:256 Fb:256 Fl:256 Lg:4096 Mn:16,256 th:256 sD:16,16
b sE:256 ab:256 fsq:256 R15:128 O:144 m9:144 ckb:320 EQ:960 qb:256 ee:320 ff:320
b Jb:256 JI:320 JG:128 PD:128 zero:128 ones:320 BH:128 ZS:144 MK:4 WL:8 base:64 kx:128 kc:128 e0:128 TI:128
b SU:128 SD:128 PAR:128 PA2:128 I592:8 B592:128 Ca:128 WT:16 ER:144 OR:144 EM:144 OM:144 E1:144 O1:144 CR1:128 CR2:128 c9:144
b m16:320 dk:256 RX:2048 RM:2048 I1:128 Im1:128 I256n:128 I256:128 I4kn:128 NUn:128
f PB:320
b ZD:144 dg1:160 dg2:80 B4kn:128 BP:128 WE:128 WA:128 I12:128 X16:128 k2:128 BN:128 SH:768 mr:128 B2m:128
u cu:16 plu:16 fou:16 Du:256 slu:16 zu:320 zc:320 pu:4,6 eou:4,6
"""
_ALL, SCRATCH, _AT = {}, {}, {}
for _line in _SBUF.split("\n"):
    _w = _line.split()
    for _e in _w[1:]:
        _n, _s = _e.split(":")
        _ALL[_n] = ("sbuf", [128] + [int(_k) for _k in _s.split(",")], _DT[_w[0]])
for _k in range(4):
    _ALL["B%d" % _k] = ("psum", [128, 512], "float32")
    _ALL["C%d" % _k] = ("psum", [128, 32, 16] if _k == 2 else [128, 512], "float32")
_wide = {}
for _n, (_w, _sh, _d) in _ALL.items():
    if _w == "sbuf" and len(_sh) == 2 and _sh[1] <= 144:
        _AT[_n] = ("pack_" + _d, _wide.get(_d, 0))
        _wide[_d] = _AT[_n][1] + -(-_sh[1] // 16) * 16
    else:
        SCRATCH[_n] = (_w, _sh, _d)
for _d, _c in _wide.items():
    SCRATCH["pack_" + _d] = ("sbuf", [128, _c], _d)
SEMAPHORES = (["sv", "ss", "sp", "sg", "loc"] + [x + str(t) for x in ("LZn", "LZf", "LAn", "LAf") for t in range(RO)]
              + ["d%d" % k for k in range(7)])

CYC, PE, WAKE, GATHER, SCATTER = 0.83, 0.42, 200.0, 1.56, 3.0
ACT, DRAIN, LOAD, SEND, NEAR, FAR, FIRST = 65.0, 0.0, 1000.0, 600.0, 1300.0, 1700.0, 1300.0


def routes(src, T, topo):
    r = T.rank_of(src)
    ring = [T.cores[(r + k) % N] for k in range(1, N)]
    near = [d for d in ring if topo.chip(d) == topo.chip(src)]
    far = [d for d in ring if topo.chip(d) != topo.chip(src)]
    eng = topo.engines(src, far[0])
    n = len(eng)
    out = [(0, d, eng[k * n // 4:(k + 1) * n // 4]) for k, d in enumerate(far[:4])]
    out += [(1, d, eng[k * n // 2:(k + 1) * n // 2]) for k, d in enumerate(far[4:])]
    return out + [(0, d, [e for e in topo.engines(src, d) if e not in eng][::2]) for d in near]


def landing(dst, T, topo):
    near = [c for c in T.cores if topo.chip(c) == topo.chip(dst)]
    return [T.rank_of(c) for c in near + [c for c in T.cores if c not in near]]


def order_calls(calls):
    n = len(calls)
    tail, users = [0.0] * n, [[] for _ in range(n)]
    for i, c in enumerate(calls):
        for d in c[3]:
            users[d].append(i)
    gap = lambda d, i: calls[d][1] - calls[d][2] if calls[d][0] == calls[i][0] == "p" or d in calls[i][5] else WAKE
    left = [len(u) for u in users]
    turn = [i for i in range(n) if not left[i]]
    for i in turn:
        tail[i] = calls[i][2] + max([tail[u] + gap(i, u) for u in users[i]], default=0.0)
        for d in calls[i][3]:
            left[d] -= 1
            if not left[d]:
                turn.append(d)

    def place(turn, back):
        at, busy = [0.0] * n, {}
        for i in turn:
            c = calls[i]
            if back:
                t = max([at[u] + calls[u][1] + gap(i, u) for u in users[i]], default=0.0) + c[2] - c[1]
            else:
                t = max([at[d] + calls[d][2] + gap(d, i) for d in c[3]], default=0.0)
            line = busy.setdefault(c[0], [])
            k, hi = 0, len(line)
            while k < hi:
                k, hi = ((k + hi) // 2 + 1, hi) if line[(k + hi) // 2][1] <= t else (k, (k + hi) // 2)
            while k < len(line) and line[k][0] < t + c[1]:
                t, k = max(t, line[k][1]), k + 1
            line.insert(k, (t, t + c[1]))
            at[i] = t
        return at

    at = place(sorted(range(n), key=lambda i: (-tail[i + calls[i][4]], i)), False)
    best = (max(at), at)
    for _ in range(PASSES):
        late = place(sorted(range(n), key=lambda i: (-at[i] - calls[i][1], -i)), True)
        at = place(sorted(range(n), key=lambda i: (-late[i] - calls[i][1], i)), False)
        best = min(best, (max(at), at))
    return sorted(range(n), key=lambda i: (best[1][i], i))


_ORDER = {}


def rank_program(g, core, T, topo):
    me = T.rank_of(core)
    if me is None:
        return
    queue = {"v": g.vector, "s": g.scalar, "p": g.tensor, "g": g, "y": g.sync}
    semof = {"v": "sv", "s": "ss", "p": "sp", "g": "sg"}
    calls, emit, acc, before = [], [], {}, {}
    full = slice(None)

    def b3(n, *ix):
        w, sh, dt = SCRATCH[n]
        ix = ix + (full,) * (len(sh) - 1 - len(ix))
        on = np.zeros(sh[1:], bool)
        on[ix] = True
        bits = int.from_bytes(np.packbits(on).tobytes(), "little")
        return T[n][(full,) + ix], [(n, bits)], int(on.sum()), dt in ("bfloat16", "float16", "uint16"), w == "psum", False, ix[0]

    def b(n, lo=0, hi=None, step=1):
        sh = _ALL[n][1]
        if hi is None:
            hi = int(np.prod(sh[1:]))
        if n in _AT:
            w, at = _AT[n]
            return b3(w, slice(at + lo, at + hi, step))
        if len(sh) == 2:
            return b3(n, slice(lo, hi, step))
        k = sh[2]
        if step == 1:
            return b3(n, slice(lo // k, hi // k))
        return b3(n, slice(lo // k, -(-hi // k)), lo % k)

    def rows(x, lo, hi):
        return (T[x[1][0][0]][lo:hi, x[6]],) + x[1:] + (lo,)

    def ind(w, o):
        return w[0].indirect(o[0]), w[1] + o[1], 16 * o[2], False, False, True

    def op(e, call, outs, ins, cost, late=None, sem=None, more=0):
        i, need = len(calls), set()
        outs = [(x[1][:1] if x[5] else x[1]) for x in outs], [x[1][1:] for x in outs if x[5]]
        for kind, keys in ((0, sum([x[1] for x in ins] + outs[1], [])), (1, sum(outs[0], []))):
            for n, bits in keys:
                lst = acc.setdefault(n, [])
                if SCRATCH[n][0] == "psum":
                    if lst and lst[-1][3] != e:
                        before[n] = [r[2] for r in lst]
                        lst.clear()
                    need.update(before.get(n, []))
                    bits = -1 if e == "p" else bits
                need.update(j for b2, k2, j, e2 in lst if bits & b2 and (kind or k2) and j != i)
                if kind:
                    lst[:] = [r for r in lst if r[0] & ~bits]
                lst.append((bits, kind, i, e))
        calls.append([e, cost, cost if late is None else late, sorted(need), more, set()])
        emit.append((call, sem))
        return i

    def row(ids):
        for d, i in zip(ids, ids[1:]):
            if d not in calls[i][3]:
                calls[i][3].append(d)
                calls[i][5].add(d)

    def vec(out, ins, per, fix=50.0):
        if out[5]:
            return fix + out[2] * SCATTER * CYC
        return fix + out[2] * GATHER * CYC if ins[0][5] else max(64, ins[0][2] * per) * CYC

    def half(*x):
        return 0.5 if all(k[3] for k in x) else 1.0

    def sc(x):
        return x[0] if isinstance(x, tuple) else x

    def ts(out, in0, s1, s2, op0, op1=None):
        ins = [in0] + [x for x in (s1, s2) if isinstance(x, tuple)]
        more = () if op1 is None else (op1,)
        return op("v", lambda: g.vector.tensor_scalar(out[0], in0[0], sc(s1), sc(s2), op0, *more), [out], ins, vec(out, ins, half(out, in0)))

    def tt(out, in0, in1, o):
        return op("v", lambda: g.vector.tensor_tensor(out[0], in0[0], in1[0], o), [out], [in0, in1],
                  vec(out, [in0], 1 if in0[4] or in1[4] else 2) + in0[5] * in0[2] * (2 - GATHER) * CYC)

    def cp(out, in_):
        return op("v", lambda: g.vector.tensor_copy(out[0], in_[0]), [out], [in_], vec(out, [in_], half(out, in_)))

    def fill(out, c):
        return op("v", lambda: g.vector.memset(out[0], c), [out], [], vec(out, [out], half(out)))

    def scan(out, d0, d1, o0, o1, first=0.0):
        return op("v", lambda: g.vector.tensor_tensor_scan(out[0], d0[0], d1[0], first, o0, o1), [out], [d0, d1], vec(out, [d0], half(out, d0, d1)))

    def vtr(out, in_):
        op("v", lambda: g.vector.transpose(out[0], in_[0]), [out], [in_], vec(out, [in_], 1))

    def act(out, in_, f=F.Identity, bias=0.0, scale=1.0):
        ins = [in_] + [x for x in (bias, scale) if isinstance(x, tuple)]
        return op("s", lambda: g.scalar.activation(out[0], in_[0], f, bias=sc(bias), scale=sc(scale)), [out], ins,
                  vec(out, ins, 1, 65.0) if in_[5] else ACT + in_[2] * CYC)

    def lin(e, out, in_, scale, bias):
        return act(out, in_, bias=bias, scale=scale) if e == "s" else ts(out, in_, scale, bias, A.mult, A.add)

    def mm(out, terms):
        for k, (l, r, *part) in enumerate(terms):
            o, cost = part[0] if part else out, max(min(64, l[2]), r[2]) * PE * (1 if l[3] else 4)
            op("p", lambda o=o, l=l, r=r, k=k: g.tensor.matmul(o[0], l[0], r[0], k == 0 or not out, k == len(terms) - 1 or not out),
               [o], [l, r], cost, cost + DRAIN, more=len(terms) - 1 - k)

    def iota(out, pat, base, cm=0):
        small = {} if out[1][0][0] == "pack_int32" else {"allow_small_or_imprecise_dtypes": True}
        op("g", lambda: g.iota(out[0], pat, base, cm, **small), [out], [], 130 + 2 * CYC * out[2])

    def sel(out, in_, pat, cmp_, fill, base, cm):
        op("g", lambda: g.affine_select(out[0], in_[0], pat, cmp_, fill, base, cm), [out], [in_], 170 + 2 * CYC * out[2])

    def dma(e, out, in_, sem, late):
        op(e, lambda: queue[e].dma_start(out=out[0], in_=in_[0]), [out], [in_], 50.0, late, (sem, 16))

    def hbm(ap):
        return ap, [], 0, False, False, False

    def q4(k):
        return 512 * k, 512 * k + 512

    blocks = ((0, 384), (384, 960), (960, 1536), (1536, V))
    for k, (lo, hi) in enumerate(blocks):
        queue["y"].dma_start(out=T.XI[:, lo:hi], in_=T.det[:, lo:hi]).then_inc(T.sem["d%d" % k], 16)
        op("r", None, [b("XI", lo, hi)], [], 0.0, LOAD + 80 * (k + 1) + 0.64 * hi, ("d%d" % k, 16))
    queue["y"].dma_start(out=T.HM[:], in_=T.ham[:]).then_inc(T.sem.d4, 16)
    op("r", None, [b("HM")], [], 0.0, LOAD + 3500, ("d4", 16))

    cell = [divmod(STEP * (t + 1), 16) for t in range(RO)]
    (PP, PI, PG, PG16, OD, SIG, SI2, W1, W2, PGE, PGO, CE, CO, CE1, CO1, N12, N15, WR1, WR2, WM1, WM2,
     PW, P15, N13) = [b("col", k, k + 1) for k in range(24)]
    diag = [[-1, 128]]
    iota(b("pp_i"), [[0, 1]], 0, 1)
    iota(b("Jb"), [[1, 256]], 0)
    iota(b("JG"), [[1, 8], [0, 16]], 0)
    iota(b("PD"), [[1, 128]], 0, -1)
    iota(b("kx"), [[0, 8], [-1, 16]], 0)
    fill(b("zero"), 0.0)
    fill(b("ones"), 1.0)
    ts(b("pq_i"), b("pp_i"), 15, None, A.bitwise_and)
    ts(b("pr_i"), b("pp_i"), 4, None, A.arith_shift_right)
    act(PP, b("pp_i"))
    act(PI, b("pq_i"))
    act(PG, b("pr_i"))
    act(PG16, b("pr_i"), scale=16.0)
    ts(b("ZS"), b("Jb", 0, 144), -15.0, PG16, A.add, A.is_equal)
    ts(b("BH"), b("JG"), PG, None, A.is_equal)
    ts(b("I1"), b("PD"), 0.0, None, A.is_equal)
    ts(b("e0"), b("ones", 0, 128), PP, 0.0, A.mult, A.is_equal)
    sel(b("TI"), b("BH"), [[1, 128]], A.is_ge, 0.0, 0, -1)
    sel(b("TI"), b("TI"), diag, A.not_equal, 4096.0, 0, 1)
    act(b("J"), b("Jb"))
    ts(b("sw"), b("Jb", 0, 20), 16.0, PI, A.mult, A.add)
    for t, (c0, r0) in enumerate(cell):
        ts(b("MK", 3 * t, 3 * t + 1), PI, float(r0), -2.0 ** 19, A.is_ge, A.mult)
        ts(b("MK", t + 1, t + 2), PI, float(r0), -2.0 ** 19, A.is_lt, A.mult)
        w0, w1 = b("WL", 4 * t, 4 * t + 1), b("WL", 4 * t + 1, 4 * t + 2)
        iota(b("WL", 4 * t, 4 * t + 2), [[15, 2]], 1)
        sel(w1, w1, [[0, 1]], A.not_equal, -2032.0, c0 - 127, 1)
        act(b("WL", 4 * t + 2, 4 * t + 4), b("WL", 4 * t, 4 * t + 2), scale=0.5)
        iota(b("base", 32 * t, 32 * t + 32), [[16 * c0, 2], [0, 16]], 0)
        iota(b("base", 32 * t + 16 - NS, 32 * t + 16), [[0, NS]], 64)
    sel(b("NUn"), b("BH"), diag, A.is_gt, 0.0, 0, 1)
    ts(b("NUn"), b("NUn"), -1.0, None, A.mult)
    iota(b("JI"), [[0, 20], [1, 16]], 0)
    for n, c in (("I256n", -256.0), ("Im1", -1.0), ("IF", 256.0), ("IF1", 1.0), ("I4k", 4096.0), ("I16", 16.0), ("I4kn", -4096.0), ("I256", 256.0)):
        lin("s" if n in IS else "v", b(n), b("I1"), c, 0.0)
    ts(b("pq_i"), b("pp_i"), 1, None, A.bitwise_and)
    ts(b("pr_i"), b("pr_i"), 1, None, A.bitwise_and)
    act(SIG, b("pq_i"), scale=-2.0, bias=1.0)
    act(SI2, b("pq_i"), scale=-4.0, bias=2.0)
    act(W1, PI, scale=13.0, bias=5.0)
    act(W2, PI, scale=-14.0, bias=255.0)
    act(PGE, b("pr_i"), scale=100000.0, bias=PG16)
    act(OD, b("pr_i"), scale=-100000.0, bias=100000.0 - 16.0)
    act(PGO, OD, bias=PG16)
    ts(N15, PI, 15.0, None, A.is_lt)
    ts(WR1, W1, 13.0, N15, A.add, A.mult)
    ts(WR2, W2, -14.0, N15, A.add, A.mult)
    ts(WM1, N15, -213.0, 200.0, A.mult, A.add)
    ts(WM2, N15, -31.0, 45.0, A.mult, A.add)
    for pg, ce, c1, side in ((PGE, CE, CE1, "E"), (PGO, CO, CO1, "O")):
        act(ce, pg, scale=0.5, bias=3.0)
        act(c1, pg, bias=11.0)
        for n, ws in (("R", (WR1, WR2)), ("M", (WM1, WM2))):
            for k in range(2):
                ts(b(side + n, k, 144, 2), b("Jb", 0, 72), ce, ws[k], A.is_equal, A.mult)
        ts(b(side + "1"), b("Jb", 0, 144), c1, SIG, A.is_equal, A.mult)
    act(b("WT", 0, 8), b("BH", 0, 128, 16), scale=W1)
    act(b("WT", 8, 16), b("BH", 0, 128, 16), scale=W2)
    act(b("B592"), b("BH"), scale=592.0)
    act(b("I592"), b("BH", 0, 128, 16), scale=-592.0)
    ts(b("kc"), b("kx"), 15.0, b("e0", 0, 1), A.add, A.mult)
    sel(b("kc"), b("kc"), [[0, 128]], A.not_equal, 32768.0, -1, 1)
    act(b("PAR"), b("BH"), scale=SIG)
    act(b("PA2"), b("BH"), scale=SI2)
    act(b("swa"), b("sw"), bias=-float(TR))
    ts(b("m16"), b("JI"), 0.0, None, A.is_gt)
    ts(b("dk"), b("m16", 0, 256), -1023.0, 1024.0, A.mult, A.add)
    for t in range(RO):
        lin("vs"[t], b("pm%d" % t), b("m16", 0, 256), 6144.0 - t, t - 2048.0)
    sel(b("SU"), b("BH"), diag, A.is_equal, 0.0, -1, 1)
    sel(b("SD"), b("BH"), diag, A.is_equal, 0.0, 1, 1)
    iota(b("CR1"), [[0, 128]], -480)
    sel(b("CR1"), b("CR1"), [[0, 8], [1, 16]], A.not_equal, -416.0, -15, 0)
    sel(b("CR2"), b("zero"), [[0, 8], [1, 16]], A.not_equal, -64.0, 0, 0)
    for n, c in (("HI", 0.0), ("KI", 15.0), ("VI", 0.0)):
        act(b(n), b("ones", 0, 256), scale=c)
    act(b("IVs"), b("ones", 0, 128))
    sel(b("m8"), b("ones", 0, 128), [[0, 16], [1, 8]], A.not_equal, 0.0, 0, 0)
    iota(b("c9"), [[0, 16], [256, 9]], -4096)
    sel(b("m9"), b("ones", 0, 144), [[0, 16], [1, 9]], A.not_equal, 0.0, 0, 0)
    for t in range(RO):
        for n, c in (("SZ", SENT), ("SL", 0)):
            for o in range(N):
                iota(b(n + str(t), 256 * o, 256 * o + CAP), [[0, CAP]], c)
    ts(b("MX"), b("Jb", 0, 16), PI, 4096.0, A.is_equal, A.mult)
    iota(b("k2"), [[0, 8], [2, 16]], -2)
    tt(b("B2m"), b("BH"), b("k2"), A.mult)
    ts(b("mr"), b("k2"), b("e0", 0, 1), 2048.0, A.mult, A.mult)
    sel(b("mr"), b("mr"), [[0, 128]], A.not_equal, B30, -1, 1)
    sel(b("mr"), b("mr"), [[0, 128]], A.not_equal, 2048.0, -2, 1)
    for x in range(16):
        for n, w in (("RX", "BH"), ("RM", "B2m")):
            lin("s" if n in RS and x < RN else "v", b(n, 128 * x, 128 * x + 128), b(w), b("MX", x, x + 1), 0.0)
    sel(b("X16"), b("ones", 0, 128), [[0, 8], [1, 16]], A.is_equal, 0.0, 0, -1)
    five = [[0, 5], [1, 16]]
    iota(b("dg2"), [[0, 80]], -8192)
    sel(b("dg1", 0, 80), b("dg2"), five, A.not_equal, 1.0, 0, -1)
    sel(b("dg1", 80, 160), b("ones", 0, 80), five, A.is_gt, 8192.0, 0, -1)
    sel(b("dg2"), b("dg2"), five, A.not_equal, float(TR), 0, -1)
    act(b("B4kn"), b("BH"), scale=-4096.0)
    ts(b("pw"), b("Jb", 0, 16), PI, RISE - 1.0, A.is_lt, A.mult)
    act(b("pw"), b("pw"), bias=1.0)
    scan(b("pw2"), b("pw"), b("zero", 0, 16), A.mult, A.add, LOW)
    act(b("ZD"), b("ZS"), scale=b("pw2", 15, 16))
    act(b("BD"), b("BH"), scale=b("pw2", 15, 16))
    ts(P15, PI, 15.0, TOP, A.is_equal, A.mult)
    act(b("R15f"), b("BH"), scale=P15)
    act(b("R15"), b("R15f"), scale=-4096.0)
    ts(N13, PI, float(NP), -4096.0, A.is_le, A.mult)
    ts(N12, PI, 0.0, N13, A.is_gt, A.mult)
    act(N12, N12, scale=-1.0 / 4096.0)
    ts(PW, PI, NP + 1.0, -4096.0, A.is_equal, A.mult)
    act(PW, PW, bias=N12)
    act(b("BP"), b("BH"), scale=PW)
    act(b("I12"), b("I1"), scale=N12)
    act(b("BN"), b("BH"), scale=N12)
    for i, d in enumerate((0, 12, -4, 8, -8, 4)):
        sel(b("SH", 128 * i, 128 * i + 128), b("BN"), [[1, 128]], A.is_equal, 0.0, 1 - d, -1)
    act(b("WA"), b("BH"), scale=N13)
    sel(b("WE"), b("WA"), [[1, 128]], A.is_ge, 0.0, 0, -1)
    sel(b("WE"), b("WE"), diag, A.not_equal, 4096.0, 0, 1)
    sel(b("WA"), b("WA"), [[-16, 8], [256, 16]], A.not_equal, 1.0, -256 * (NP + 1), 1)

    def zs(x, n="ZS"):
        return b(n, 15 - x, 143 - x)

    XW = b("X", TR, TR + V)
    plan = {d: routes(d, T, topo) for d in T.cores}
    land = {d: landing(d, T, topo) for d in T.cores}
    near = sum(topo.chip(d) == topo.chip(core) for d in T.cores)
    BW = near * CAP // 16
    mine = CAP * land[core].index(me)
    sent = [0]
    I1, Im1 = b("I1"), b("Im1")

    for t in range(RO):
        c0, r0 = cell[t]
        if t == 0:
            for q in blocks:
                ts(b("X1", *q), b("XI", *q), 255, None, A.bitwise_and)
                if q[1] < V:
                    act(b("NZ", *q), b("X1", *q), F.Square, bias=-128.0)
                else:
                    row([ts(b("NZ", q[0] + x, V, 4), b("X1", q[0] + x, V, 4), 128.0, None, A.not_equal) for x in range(4)])
            terms = [(zs(x), b("NZ", 16 * lo + x, 16 * hi, 16), b("B0", lo + d, hi + d))
                     for lo, hi, d in ((0, c0 + 1, 0), (c0, 128, 1)) for x in sorted(range(16), key=lambda x: x % 4)]
            mm(b("B0", 0, 129), terms[:18] + [(I1, b("MK", 0, 2), b("B0", c0, c0 + 2))] + terms[18:])
            parts = ((c0 + 1, 129), (0, c0 + 1))
        else:
            act(b("SR", 128, 16 * 129, 129), b("X", TR + 16 * c0, TR + 16 * c0 + 16), F.Sign)
            for x in range(16):
                o, i = b("SR", 129 * x, 129 * x + 128), b("X", TR + x, TR + V, 16)
                act(o, i, F.Sign) if x % 8 in (1, 4, 6) else ts(o, i, 0.0, None, A.is_gt)
            terms = [(zs(x), b("SR", 129 * x, 129 * x + 129)) for x in range(16)]
            mm(b("B0", 0, 129), terms[:1] + [(I1, b("MK", 2, 4), b("B0", c0, 129, 128 - c0))] + terms[1:])
            parts = ((c0, 128), (0, c0), (128, 129))
        at = 0
        for lo, hi in parts:
            ts(b("Lb", at, at + hi - lo), b("B0", lo, hi), 0.0, None, A.is_gt)
            at += hi - lo
        scan(b("PL", 0, 129), b("ones", 0, 129), b("Lb", 0, 129), A.mult, A.add)
        mm(b("B2", 0, 128), [(b("e0"), b("kx")), (b("PL", 0, 128), b("BH"))])
        mm(b("B0", 0, 130), [(b("BH"), b("PL", 0, 129), b("B0", 0, 129)), (b("NUn"), b("Lb", 0, 129), b("B0", 0, 129)),
                             (b("BH"), b("PL", 128, 129), b("B0", 129, 130))])
        cp(b("EB"), b("B2", 0, 128))
        act(b("U", 0, 130), b("B0", 0, 130))
        for j in range(16):
            o = b("cmp", 128 * j, 128 * j + 128)
            if j < 16 - NS:
                ts(o, b("EB"), 16.0 * j, None, A.is_le)
            else:
                act(o, b("EB"), F.Sign, bias=16.0 * j + 0.5, scale=-1.0)
        turn = sorted(range(16), key=lambda j: j if j < 16 - NS else 4 * (j - 16 + NS) + 2.5)
        mm(b("B1", 0, 32), [(b("e0"), b("base", 32 * t, 32 * t + 32))]
           + [(b("cmp", 128 * j, 128 * j + 128), b("WL", 4 * t + 2 * (j >= 16 - NS), 4 * t + 2 * (j >= 16 - NS) + 2), b("B1", j, 32, 16)) for j in turn])
        cp(b("cu"), b("B1", 0, 16))
        act(b("cb"), b("B1", 16, 32))
        tt(b("G"), ind(b("U", 0, 130), b("cu")), b("J"), A.is_le)
        mm(b("B2", 0, 16), [(I1, b("cb"))] + [(zs(x), b("G", x, 256, 16)) for x in range(16)])
        cp(b("plu"), b("B2", 0, 16))
        ts(b("dm"), b("sw", 0, 16), b("U", 129, 130), -8192.0, A.is_ge, A.mult)
        if t == 0:
            for k in range(4):
                bank = "C%d" % XB[k]
                mm(b(bank), [(b("BH"), b("NZ", *q4(k)))])
                act(b(bank), b(bank), F.Sign, bias=-0.5)
                for lo in (512 * k, 512 * k + 256):
                    tt(b("X", TR + lo, TR + lo + 256), b("XI", lo, lo + 256), b(bank, lo % 512, lo % 512 + 256), A.mult)
        win = b("XI") if t == 0 else XW
        ts(b("Du"), ind(win, b("plu")), 1.0 / 256.0, -0.5, A.mult, A.add)
        act(b("Sx"), ind(win, b("plu")), F.Relu, scale=1.0 / 256.0)
        tt(b("fo"), b("dm"), b("B2", 0, 16), A.add)
        dh = ts(b("Dh"), b("Du"), -2048.0, None, A.add)
        CB0 = -524288.0 - 128.0
        mm(b("B3", 0, S), [(b("IF"), b("Sx")), (b("I256n"), b("Dh"))])
        first = [act(b("C3", 0, 128), b("B3", 0, 128), F.Abs, bias=CB0), act(b("Ca"), b("B3", 128, S), F.Abs, bias=CB0)]
        for h in range(2):
            mm(b("B0", 16 * h, 16 * h + 16), [(b("Dh", 128 * h, 128 * h + 128), b("WT"))])
        mineL = [cp(b("Lg", 0, 16 * NV), ind(b("HM"), b("Du", 0, NV)))]
        look = [act(b("Lg", 16 * lo, 16 * hi), ind(b("HM"), b("Du", lo, hi)), scale=c) for lo, hi, c in ((NV, 128, 1.0), (192, S, 1.0), (128, 192, -1.0))]
        steps = [cp(b3("hi"), b("B0", 0, 32))]
        mm(b("B0", 128, 192), [(Im1, b("Ca", 0, 64))])
        least = [tt(b3("Mn", k, slice(lo, lo + 64)), b("Lg", 16 * lo + k, 16 * lo + 1024, 16), b(bank, lo, lo + 64), o)
                 for lo, bank, o in ((0, "C3", A.min), (64, "C3", A.min), (128, "B0", A.max)) for k in range(16)]
        over = []
        for kk, bank in ((0, "C1"), (8, "C2")):
            mm(b(bank), [x for k in range(8) for x in ((Im1, b("Lg", 3072 + kk + k, 4096, 16), b(bank, 64 * k, 64 * k + 64)),
                                                       (I1, b("Ca", 64, 128), b(bank, 64 * k, 64 * k + 64)))])
            over.append(act(b3("Mn", slice(kk, kk + 8), slice(192, S)), b(bank), F.Relu))
        row(look[:1] + first + look[1:] + over)
        steps += [
                 ts(b3("ha"), b3("hi"), 4095, None, A.bitwise_and),
                 tt(b("hp"), b3("ha", full, slice(0, 8)), b3("ha", full, slice(8, 16)), A.mult),
                 ts(b("HI", 0, 256, 16), b("hp"), 5, 4095, A.arith_shift_right, A.bitwise_and),
                 scan(b("hx"), b("pm%d" % t), b("HI"), A.min, A.add)]
        plus = b("B592", 0, 128, 16)
        const = [[(b("ones", 0, 128), b("kc")), (b("I16"), b("hx", 128 * h, 128 * h + 128), b("B%d" % (1 + h), 0, 128))] for h in (0, 1)]
        mm(b("B1", 0, 128), const[0] + [(b3("Mn", k, slice(0, 128)), plus, b("B1", k, 128, 16)) for k in range(16)])
        mm(b("B2", 0, 128), const[1] + [(b("Ca", 64, 128), b("B592"), rows(b("B2", 0, 128), 64, 128))]
           + [(b3("Mn", k, slice(128, S)), b("I592"), b("B2", k, 128, 16)) for k in range(16)])
        row([dh] + mineL + [x for k in range(5) for x in [steps[k]] + least[4 * k:4 * k + 4]] + least[20:])
        act(b("Cb"), b("B3", 0, 256), bias=CB0)
        for h in range(2):
            scan(b("Ks", 128 * h, 128 * h + 128), b("m16", 0, 128), b("B%d" % (1 + h), 0, 128), A.mult, A.max)
        kmx = b("Ks", 15, 256, 16)
        ts(b("KI", 0, 256, 16), kmx, 15, None, A.bitwise_and)
        ts(b("VI", 0, 256, 16), kmx, 4, 4095, A.arith_shift_right, A.bitwise_and)
        scan(b("TK"), b("dk"), b("KI"), A.add, A.min)
        scan(b("VB"), b("pm0"), b("VI"), A.min, A.add)

        def turned(bank, n, w):
            return [(b(n, h, h + 128), w, b(bank, h, h + 128)) for h in (0, 128)]
        DH, ONE = b("Dh"), b("ones", 0, 256)
        mm(b("B0", 0, 256), [(b("SU"), DH), (b("CR1"), ONE)] + turned("B0", "TK", b("I4k")))
        tt(b("R1"), DH, b("B0", 0, 256), A.max)
        mm(None, turned("B3", "VB", I1))
        mm(b("B1", 0, 256), [(b("CR2"), ONE), (b("SD"), b("R1"))])
        tt(b("m1"), b("R1"), b("B3", 0, 256), A.min)
        tt(b("CH"), b("m1"), b("B1", 0, 256), A.max)
        mm(b("C1", 0, 256), [(I1, DH)] + turned("C1", "VB", Im1))
        act(b("sD"), b("C1", 0, 256), F.Sign)
        mm(b("C2", 0, 128), [(b(n, at - k * j, 128 + at - k * j), b3(x, slice(j, None, 4)), b3("C2", slice(par, 8, 2)))
                             for x, ns, at, k in (("R1", ("ER", "OR"), 6, 2), ("sD", ("E1", "O1"), 3, 1), ("m1", ("EM", "OM"), 6, 2))
                             for par, n in enumerate(ns) for j in range(4)])
        mm(None, turned("C0", "TK", I1))
        act(b("th"), b("C0", 0, 256), F.Sign, bias=-15.0)
        mm(b("B2", 0, 256), [(I1, b("R1"))] + turned("B2", "VB", Im1))
        act(b("sE"), b("B2", 0, 256), F.Sign)
        mm(b("C0", 0, 256), [(b("PA2"), b("th")), (b("PAR"), b("sE"))])
        act(b("ab"), b("C0", 0, 256), F.Abs, bias=2.0)
        act(b("sg"), b("ab"), bias=-1.0)
        act(b("Fb"), b("Cb"), bias=191.625, scale=0.25)
        act(b("Fl"), b("Fb"), bias=-192.0)
        vtr(b3("R4"), b("C2", 0, 128))
        cp(b3("ci"), b3("R4", full, slice(0, 8)))
        ts(b("iv"), b3("R4", full, slice(8, 12)), -1.0, -8192.0, A.is_equal, A.mult)
        ts(b3("ca"), b3("ci"), 4095, None, A.bitwise_and)
        iv2 = b("IVs", 0, 128, 8)
        tt(iv2, b("iv"), b("dm"), A.min)
        scan(b("IV"), b("m8"), b("IVs"), A.mult, A.add)
        tt(b("ch"), b3("ca", full, slice(0, 8, 2)), b3("ca", full, slice(1, 8, 2)), A.mult)
        ts(b("O", 8, 144, 9), iv2, 0.0, None, A.is_lt)
        ts(b("ow"), b("ch"), 5, 7, A.arith_shift_right, A.bitwise_and)
        ts(b("uh"), b3("ca", full, slice(0, 8, 2)), -2048.0, None, A.add)
        ts(b("Hi"), b("ch"), 8, V - 1, A.arith_shift_right, A.bitwise_and)
        cp(b("Hh"), b("Hi"))
        mm(b("B0", 0, S), [(b("mr"), ONE)] + [(b(n, 128 * x, 128 * x + 128), b(u), b("B0", x, S, 16))
                                              for n, u in (("RM", "uh"), ("RX", "Hh")) for x in range(16)])
        act(b("qb"), b("B0", 0, S), bias=-1024.0 * 4096.0)
        tt(b("zf"), b("B0", 0, S), b("qb"), A.subtract)
        for o in range(8):
            tt(b("O", o, 144, 9), b("ow"), b("IV", o, 128, 8), A.is_equal)
        mm(b("B3", 0, 144), [(b("e0"), b("c9")), (b("TI"), b("O"))] + [(b("BH"), b("O", 0, 144 - 9 * d), b("B3", 9 * d, 144)) for d in range(1, 16)])
        scan(b("s9"), b("m9"), b("B3", 0, 144), A.mult, A.max)
        cp(b("slu"), b("s9", 8, 144, 9))
        SL, LA, SZ, LZ = [x + str(t) for x in ("SL", "LA", "SZ", "LZ")]
        scat = [tt(ind(b(SZ), b("slu")), b("zf"), b("CH"), A.add), tt(ind(b(SL), b("slu")), b("Fl"), b("sg"), A.mult)]
        sends = []
        for src, dst in ((SZ, LZ), (SL, LA)):
            for call in (0, 1):
                tr = []
                for cl, d, eng in plan[core]:
                    if cl != call:
                        continue
                    o, at = T.rank_of(d), CAP * land[d].index(me)
                    tr.append(RemoteDMATransfer(
                        dst_ids=[DstId(rid=topo.addr(d)[0], pnc=topo.addr(d)[1])], dma_engine_mask=sum(1 << e for e in eng),
                        remote_sem=T.sem[dst[:2] + "fn"[topo.chip(d) == topo.chip(core)] + str(t)],
                        src=T[src][:, 256 * o:256 * o + CAP], dst=T[dst][:, at:at + CAP]))
                    sent[0] += len(eng)
                sends.append(op("g", lambda tr=tr: g.remote_dma_fused(tr, local_sem=T.sem.loc), [], [b(src)], SEND, None, ("", 0)))
            for nr in (True, False):
                there = [d for d in T.cores if d != core and (topo.chip(d) == topo.chip(core)) == nr]
                tot = sum(len(e) for s in there for _, x, e in plan[s] if x == core)
                at = [CAP * land[core].index(T.rank_of(d)) for d in there]
                i = op("r", None, [b(dst, a, a + CAP) for a in at], [], 0.0, (NEAR if nr else FAR) + FIRST * (t == 0 and src == SZ),
                       (dst[:2] + "fn"[nr] + str(t), tot))
                calls[i][3].append(sends[-2 if nr else -1])
        row(sends)
        kept = act(b(LA, mine, mine + CAP), b(SL, 256 * me, 256 * me + CAP))
        act(b("sC"), b("Cb"), F.Sign)
        fade = [(I1, b("Cb")), (Im1, b("sC"))]
        mm(b("C3", 0, 256), fade)
        act(b("fsq"), b("C3", 0, 256), F.Square)
        mm(b("C3", 0, 256), [(b("BH"), b("fsq"))])
        act(b("fsg"), b("C3", 0, 256), F.Sign, bias=-0.5)
        mm(b("C3", 0, 256), fade + [(b("I256"), DH)])
        act(b("xg"), b("C3", 0, 256), bias=-CB0)
        tt(b("fo2"), b("fo"), b("swa", 0, 16), A.max)
        ts(b("fou"), b("fo2"), float(TR), None, A.add)
        faded = tt(ind(b("X"), b("fou")), b("xg"), b("fsg"), A.mult)
        out = [act(b("Y", TR + 512 * k, TR + 512 * k + 512), b("X", TR + 512 * k, TR + 512 * k + 512), F.Abs) for k in range(4 * (t == RO - 1))]

        other, W = CAP - mine, near * CAP
        did = dict(SZ=scat[:1], SL=scat[1:], F=[faded], L=[kept], Y0=out[:1], Y1=out[1:2], Y2=out[2:3], Y3=out[3:])
        turn = [0] + list(range(N // near - 1, 0, -1))
        recs = {0: [(mine, mine + CAP, b(SZ, 256 * me, 256 * me + CAP)), (other, other + CAP, b(LZ, other, other + CAP))]}
        recs.update({k: [(W * k, W * k + W, b(LZ, W * k, W * k + W))] for k in turn[1:]})

        def Q(lo, hi):
            return b("B0", lo, hi) if lo < W else b("C3", lo - W, hi - W)

        def split(out, big, small, k):
            return [(w, y, out(lo, hi)) for lo, hi, rec in recs[k] for w, y in ((b(big), rec), (b(small), b("zh", lo, hi)))]
        for j, k in enumerate(turn):
            for x, (lo, hi, rec) in enumerate(recs[k]):
                did["z%d%d" % (j, x)] = [ts(b("zu", lo, hi), rec, 1.0 / 4096.0, -2047.5 / 4096.0, A.mult, A.add)]
                did["h%d%d" % (j, x)] = [(act if j in ZHS else cp)(b("zh", lo, hi), b("zu", lo, hi))]
        for some in (turn[:1], turn[1:]):
            lo, hi = W * min(some), W * max(some) + W
            mm(b("C1", lo, hi), [x for k in some for x in split(lambda lo, hi: b("C1", lo, hi), "R15f", "R15", k)])
            did["t%d" % (lo > 0)] = [act(b("thr", lo, hi), b("C1", lo, hi), F.Relu)]
        mm(Q(W, AR), [x for k in turn[1:] for x in split(Q, "IF1", "I4kn", k)])
        for j, k in enumerate(turn):
            at, sums, n16 = W * k, [], NP if j in DENSE else 16
            for x, (p, q, rec) in enumerate(recs[k] if j in DENSE else []):
                n = (q - p) * 3 // 4
                mm(b(GB[j], 0, n), [(b("SH", 128 * i, 128 * i + 128), b("zh", p + (i + 1) // 2, q, 4), b(GB[j], i // 2, n, 3)) for i in range(6)])
                did["c%d%d" % (j, x)] = [cp(b("zc", p, p + n), b(GB[j], 0, n))]
            for x, (e, n) in enumerate(GATH[j]):
                at = recs[k][x][0] if j == 0 and x < 2 else at
                base = recs[k][min(x, 1)][0] if j == 0 else W * k
                c0, c1 = [base + (y - base) * n16 // 16 for y in (at, at + n)]
                did["g%d%d" % (j, x)] = [lin(e, b("dd", 16 * c0, 16 * c1), ind(XW, b("zc" if j in DENSE else "zu", c0, c1)), 1.0 / 256.0, -0.5)]
                at += n
            for x, (p, q, rec) in enumerate(recs[k]):
                if j == 0:
                    mm(Q(p, q), [(b("IF1"), rec), (b("I4kn"), b("zh", p, q))])
                db = [b("db", NP * p + m * (q - p), NP * p + (m + 1) * (q - p)) for m in range(NP)]
                did["s%d%d" % (j, x)] = [tt(db[m], Q(p, q), b("dd", 16 * p + m + (n16 > NP), 16 * p + n16 * (q - p), n16), A.subtract) for m in range(NP)]
                sums += [(zs(m + 1, "ZD"), db[m], b(GB[j], p - W * k, q - W * k)) for m in range(NP)]
            mm(b(GB[j], 0, W), sums)
        for lo, hi in ((0, W), (W, AR)):
            if t < RO - 1:
                act(b("A16", lo, hi), Q(lo, hi), bias=-2048.0)
            else:
                act(b("xq", lo, hi), Q(lo, hi), bias=128.0, scale=256.0)
        for j, k in enumerate(turn):
            lo, hi, bank, side = W * k, W * k + W, GB[j], SB[j]
            S0, TE, TF, WP, CM, CP = [b(bank, W * x, W * x + W) for x in range(6)]
            zh, ee, ff, PB, cn, ckb, ft, xq = [b(x, lo, hi) for x in "zh ee ff PB cn ckb ft xq".split()]
            did["e%d" % j] = [ts(ee, S0, 0.0, None, A.is_equal), tt(ff, S0, b("thr", lo, hi), A.is_gt)]
            mm(TE, [(b("I12"), zh, TE), (b("WE"), ee, TE), (b("I12"), zh, TF), (b("WA"), ee, TF), (b("WE"), ff, TF)])
            both, rr = b(bank, W, 3 * W), [b("rr", 2 * lo + x, 2 * lo + x + W) for x in (0, W)]
            did["r%d" % j] = [act(b("rr", 2 * lo, 2 * hi), both, F.Relu) if j in RES else ts(b("rr", 2 * lo, 2 * hi), both, 0.0, None, A.max)]
            mm(b(bank, 3 * W, 5 * W), [(b("X16"), b("dg1"))] + [(b("BP"), r, x) for x in (WP, CM, CP) for r in rr])
            pu = b3("pu", k, slice(0, BW))
            did["p%d" % j] = [scan(PB, b("m16", 0, W), WP, A.mult, A.max), lin("s" if j in PUS else "v", pu, b("PB", lo + 15, hi, 16), 1.0, -1.0)]
            XQ = lambda p, q: b(side, p - lo, q - lo)
            act(b("xm", lo, hi), ind(XW, pu), bias=-0.5, scale=1.0 / 256.0)
            act(XQ(lo, hi), b("xm", lo, hi), bias=128.0, scale=256.0)
            tt(b("w1", lo, hi), ind(XW, pu), b(LA, lo, hi), A.add)
            tt(cn, b("w1", lo, hi), XQ(lo, hi), A.subtract)
            EQ = [b("EQ", 3 * lo + W * d - 8 * d * (d - 1), 3 * lo + W * (d + 1) - 8 * d * (d + 1)) for d in range(BW)]
            did["q%d" % j] = [tt(EQ[0], PB, CM, A.is_equal)] + [
                ts(EQ[d], b(bank, 5 * W + 16 * d, 6 * W), 1.0, b("PB", lo + 16 * d - 1, lo + 16 * d), A.add, A.is_equal) for d in range(1, BW)]
            mm(S0, [(b("X16"), b("dg2"))] + [(b("BP"), r) for r in rr] + [(b("B4kn"), EQ[d], b(bank, 16 * d, W)) for d in range(BW)])
            scan(b("DS", lo, hi), b("m16", 0, W), S0, A.mult, A.max)
            tt(b3("eou", k, slice(0, BW)), b("DS", lo + 15, hi, 16), b("sw", 0, BW), A.max)
            if t < RO - 1:
                ts(ckb, cn, 127.0, -127.0, A.min, A.max)
                mm(XQ(lo, hi), [(b("I256"), b("A16", lo, hi)), (I1, ckb), (b("BD"), ckb, b(side, W, 2 * W))])
                ts(ft, b(side, W, 2 * W), 0.0, -0.5, A.not_equal, A.add)
                act(xq, XQ(lo, hi), bias=2.0 * (524288.0 + 128.0), scale=2.0)
            else:
                ts(ft, cn, 127.0, -127.0, A.min, A.max)
        for line in ROWS[t]:
            row(sum([did[x] for x in line.split()], []))
        for k in sorted(turn, key=lambda k: -land[core][near * k]):
            q = (W * k, W * k + W)
            tt(ind(b("X" if t < RO - 1 else "Y"), b3("eou", k, slice(0, BW))), b("xq", *q), b("ft", *q), A.add if t else A.mult)
    for k, e in ((0, "y"), (1, "s")):
        dma(e, hbm(T.y[:, 1024 * k:1024 * k + 1024]), b("Y", TR + 1024 * k, TR + 1024 * k + 1024), "d%d" % (5 + k), LOAD + 3000)

    kind = land[core][0]
    if kind not in _ORDER:
        _ORDER[kind] = order_calls(calls)
    cnt, known, mark = {}, {e: {} for e in queue}, {}
    for i in _ORDER[kind]:
        e, (call, sem) = calls[i][0], emit[i]
        if e == "r":
            mark[i] = (sem[0], sem[1], {})
            continue
        kn = known[e]
        for s, v, seen in sorted((mark[d] for d in calls[i][3] if not (e == calls[d][0] == "p" or d in calls[i][5])), key=lambda x: (x[0] == semof.get(e), -x[1])):
            if s and kn.get(s, 0) < v:
                queue[e].wait_ge(T.sem[s], v)
                for s2, v2 in list(seen.items()) + [(s, v)]:
                    kn[s2] = max(kn.get(s2, 0), v2)
        if sem is None:
            cnt[e] = cnt.get(e, 0) + 1
            sem = (semof[e], cnt[e])
            call().then_inc(T.sem[sem[0]], 1)
        elif sem[0]:
            call().then_inc(T.sem[sem[0]], sem[1])
        else:
            call()
        mark[i] = (sem[0], sem[1], dict(kn))
    for e in semof:
        g.wait_ge(T.sem[semof[e]], cnt[e])
    for k in range(7):
        g.wait_ge(T.sem["d%d" % k], 16)
    g.wait_ge(T.sem.loc, sent[0])
